import numpy as np, ml_dtypes
CORES = [48,51,52,55]
N = 4
BF = ml_dtypes.bfloat16
V, C, T, S, VT, DR, DG = 4096, 256, 6, 32, 9, 1, 1
def start(s0, w0):
    H = np.full((N, 8, 16, C), -1, np.int64); H[:, :, 0] = s0; live = s0 >= 0
    return H, np.where(live[:, :, None], w0, np.float32(0)), live
def grow(t, H, W, live, nt, qt, u):
    nk = np.take_along_axis(nt, np.where(live, H[:, :, t], 0)[:, :, None, :], 3)
    shut = np.zeros(nk.shape, bool)
    for p in range(t + 1): shut |= nk == H[:, :, p:p + 1]
    x = np.take_along_axis(qt, nk.reshape(N, 8, 1, 16 * C), 3).reshape(N, 8, 16, 16, C)
    P = np.add.accumulate(np.where(shut[:, :, None], 0, x), axis=3); full = P[:, :, :, 15]
    votes = np.sum(256 * P > u[:, :, None, None, :] * full[:, :, :, None], axis=2)
    k = np.argmax((votes >= VT) & ~shut, axis=2); site = np.take_along_axis(nk, k[:, :, None, :], 2)[:, :, 0]
    moved = live & ~np.all(shut, axis=2)
    H = H.copy(); H[:, :, t + 1] = np.where(moved, site, -1)
    W = np.where(moved[:, :, None], W * full.astype(np.float32) * np.float32(2.0 ** -11), np.float32(0))
    return H, W, moved
def breed(H, W, live, old, lo, hi, coin):
    low = live & (np.sum(W < lo[..., None], axis=2) >= VT); high = live & (np.sum(W > hi[..., None], axis=2) >= VT)
    W = np.where(high[:, :, None], W * np.float32(0.5), np.where(low[:, :, None], W * np.float32(2), W))
    live = live & ~(low & (coin == 0)); H = H.copy()
    up = np.sum(high, axis=(0, 2)) > np.sum(old & ~live, axis=(0, 2))
    over, left = {}, {}
    for a in range(N):
        for g in range(8):
            src = np.flatnonzero(high[a, g]); hole = np.flatnonzero(~live[a, g]); n = min(len(src), len(hole))
            H[a, g][:, hole[:n]] = H[a, g][:, src[:n]]; W[a, g][:, hole[:n]] = W[a, g][:, src[:n]]; live[a, g, hole[:n]] = True
            over[a, g] = (H[a, g][:, src[n:n + S]], W[a, g][:, src[n:n + S]]); left[a, g] = hole[n:]
    for a in range(N):
        for g in range(8):
            h, w = over[(a - DR) % N, (g - DG) % 8]; hole = left[a, g][:h.shape[1]]; m = len(hole)
            H[a, g][:, hole] = h[:, :m]; W[a, g][:, hole] = w[:, :m]; live[a, g, hole] = True
    return H, W, live, up
def land(rng, traps):
    ring = np.argsort(rng.random((N, 8, V)), axis=-1); x = np.arange(V); sh = (N, 8, 16, V)
    to = np.where(rng.random(sh) < 0.4, (x + rng.integers(-6, 7, sh)) % V, rng.integers(0, V, sh))
    m = np.repeat(rng.integers(1, 5, (N, 8, V // 4)), 4, axis=-1)[:, :, None]; trap = np.repeat(rng.random((N, 8, V // 4)) < traps, 4, axis=-1)[:, :, None]
    to = np.where(trap, 4 * (x // 4) + (rng.random(sh) * m).astype(np.int64), to)
    return np.take_along_axis(np.take_along_axis(ring[:, :, None], to, 3), np.argsort(ring, axis=-1)[:, :, None], 3)
def base(rng, traps, dead):
    qt = np.clip(np.rint(rng.uniform(40, 200, (N, 8, 1, V)) * rng.uniform(0.6, 1.4, (N, 8, 16, V))), 16, 255).astype(np.int32)
    s0 = np.where(rng.random((N, 8, C)) < dead * rng.random((N, 8, 1)), -1, rng.integers(0, V, (N, 8, C)))
    w0 = np.exp2(rng.uniform(-2, 2, (N, 8, 1, C)) + rng.uniform(-1, 1, (N, 8, 16, 1)) + rng.uniform(-0.2, 0.2, (N, 8, 16, C))).astype(np.float32)
    return dict(nt=land(rng, traps), qt=qt, s0=s0, w0=w0, u=rng.integers(0, 256, (N, 8, T, C)), coin=rng.integers(0, 2, (N, 8, T, C)))
def limits(rng, W, live, na, nh, sharp):
    lo = np.ones((N, 8, 16), np.float32); hi = np.ones((N, 8, 16), np.float32); tiny = np.float32(0); huge = np.float32(2.0 ** 100)
    for a in range(N):
        for g in range(8):
            m = np.flatnonzero(live[a, g]); n = len(m)
            if n == 0: continue
            w = W[a, g][:, m]; o = np.argsort(np.add.reduce(np.log2(w), axis=0), kind="stable"); i = int(na[a, g]); j = n - 1 - int(nh[a, g])
            least = np.minimum.reduce(w, axis=1) * np.float32(0.5); most = np.maximum.reduce(w, axis=1) * np.float32(2)
            r1 = rng.permutation(16) < rng.choice(np.array([0, VT - 1, VT, 16])); r2 = rng.permutation(16) < rng.choice(np.array([0, VT - 1, VT, 16]))
            if i < 0: l = least
            elif i >= n: l = most
            elif sharp[a, g]: l = np.where(r1, np.nextafter(w[:, o[i]], huge), w[:, o[i]])
            else: l = w[:, o[i]] * np.float32(0.25)
            if j >= n: h = most
            elif j < 0: h = least
            elif sharp[a, g] == 2:
                v = np.sort(w, axis=0)[16 - VT]
                h = np.full(16, np.max(v[v < np.max(v)], initial=np.min(v) * np.float32(0.5)), np.float32)
            elif sharp[a, g]: h = np.where(r2, np.nextafter(w[:, o[j]], tiny), w[:, o[j]])
            else: h = w[:, o[j]] * np.float32(4)
            lo[a, g] = np.minimum(l, h); hi[a, g] = h
    return lo, hi
def tilt(rng, coin, W, live, old, lo, hi, tip):
    low = live & (np.sum(W < lo[..., None], axis=2) >= VT); high = live & (np.sum(W > hi[..., None], axis=2) >= VT)
    for g in tip:
        m = np.flatnonzero(low[:, g].reshape(-1)); k = int(np.sum(high[:, g])) - int(np.sum(old[:, g] & ~live[:, g])) - tip[g]
        z = coin[:, g].copy().reshape(-1); z[m] = 1; z[rng.permutation(m)[:max(k, 0)]] = 0
        coin[:, g] = z.reshape(N, C)
def finish(rng, d, goal):
    H, W, live = start(d["s0"], d["w0"]); f = np.ones(8, np.float32); lo = np.ones((N, 8, 16, T), np.float32); hi = np.ones((N, 8, 16, T), np.float32)
    for t in range(T):
        old = live
        H, W, live = grow(t, H, W, live, d["nt"], d["qt"], d["u"][:, :, t])
        aim = goal(t, np.sum(live, axis=2))
        l, h = limits(rng, W, live, aim[0], aim[1], aim[2])
        if len(aim) > 3: tilt(rng, d["coin"][:, :, t], W, live, old, l, h, aim[3])
        lo[..., t] = l * f[:, None]; hi[..., t] = h * f[:, None]
        H, W, live, up = breed(H, W, live, old, l, h, d["coin"][:, :, t])
        f = np.where(up, f * np.float32(0.5), f)
    return {"nb": np.ascontiguousarray(d["nt"].reshape(N, 128, V)).astype(np.int32), "qs": d["qt"].reshape(N, 128, V).astype(np.float32).astype(BF),
            "s0": d["s0"].astype(np.int32), "w0": np.ascontiguousarray(d["w0"].reshape(N, 128, C)).astype(np.float32),
            "us": np.ascontiguousarray(d["u"].reshape(N, 8, T * C)).astype(np.int32), "coin": np.ascontiguousarray(d["coin"].reshape(N, 8, T * C)).astype(np.int32),
            "lo": lo.reshape(N, 128, T), "hi": hi.reshape(N, 128, T)}
def sway(rng, n, k):
    up = (rng.permutation(8) < k)[None, :]
    a = np.where(up, rng.uniform(0.03, 0.12, (N, 8)), rng.uniform(0.3, 0.5, (N, 8))); b = np.where(up, rng.uniform(0.25, 0.45, (N, 8)), rng.uniform(0.03, 0.12, (N, 8)))
    return (a * n).astype(np.int64), (b * n).astype(np.int64), np.ones((N, 8), bool)
def setup_inputs(rng):
    return finish(rng, base(rng, 0.1, 0.3), lambda t, n: sway(rng, n, 4))
def setup_inputs_calm(rng):
    o = rng.permutation(8); num = np.zeros(8, np.int64); few = np.zeros(8, bool); num[o] = np.arange(8) % 4; few[o[:4]] = True
    d = base(rng, np.where(few, 0.0, 0.05)[:, None], 0.0)
    odd = (np.arange(N)[:, None] + np.arange(8)[None, :]) % 2 == 1
    d["qt"] = np.where(odd[:, :, None, None], rng.integers(60, 200, (N, 8, 16, 1)), d["qt"]).astype(np.int32)
    d["u"] = np.where(odd[:, :, None, None], 16 * rng.integers(0, 16, (N, 8, T, C)), d["u"])
    def goal(t, n):
        rich = (np.arange(N)[:, None] + t + num[None, :]) % 2 == 0; tip = {}
        a = np.where(few[None, :], 0.3, np.where(rich, 0.12, 0.5)) * rng.uniform(0.9, 1.0, (N, 8)); b = np.where(rich, 0.3, 0.05) * rng.uniform(0.9, 1.0, (N, 8))
        na = (a * n).astype(np.int64); nh = (b * n).astype(np.int64); sharp = np.ones((N, 8), np.int64)
        for g in range(8):
            k = int(num[g])
            if few[g]:
                c = 1 + t % 3 if t < k else (t + k) % 4
                q = rng.permutation(N)[:c]; nh[:, g] = -1; nh[q, g] = 1; sharp[q, g] = 2
                tip[g] = 1 if t < k else 0
            else: tip[g] = 1 + (t + g) % 3 if t < k else -((t + k) % 2)
        return na, nh, sharp, tip
    return finish(rng, d, goal)
def setup_inputs_corners(rng):
    d = base(rng, 0.0, 0.0); d["s0"] = rng.integers(0, V, (N, 8, C))
    d["w0"] = np.exp2(rng.uniform(-0.4, 0.4, (N, 8, 1, C)) + rng.uniform(-1, 1, (N, 8, 16, 1))).astype(np.float32)
    d["u"] = np.where(rng.random(d["u"].shape) < 0.3, 255 * rng.integers(0, 2, d["u"].shape), d["u"])
    cases = [(0, 0, S), (0, 0, C), (C, 0, 0), (C - 1, 0, 1), (40, 24, 64), (40, 24, 65 + S), (40, 24, 63 + S), (40, 24, 64 - S), (40, 24, 65 - S), (0, C, 0), (0, C - 1, 0), (0, 0, 0)]
    kind = rng.integers(0, 12, (N, 8)); o = rng.permutation(8)
    for a in range(N): kind[a, a % 8] = 5
    for i in range(8):
        kind[0, o[i]] = (0, 1, 5, 6, 0, 5, 1, 6)[i]; kind[DR % N, (o[i] + DG) % 8] = (7, 8, 7, 8, 2, 3, 4, 7)[i]
    na = np.zeros((N, 8), np.int64); nh = np.zeros((N, 8), np.int64)
    for a in range(N):
        for g in range(8):
            z, k, m = cases[kind[a, g]]; p = rng.permutation(C); na[a, g] = k; nh[a, g] = m
            d["s0"][a, g, p[:z]] = -1; d["coin"][a, g, 0, p[z:z + k]] = 0
            d["w0"][a, g][:, p[z:z + k]] *= np.float32(2.0 ** -6); d["w0"][a, g][:, p[z + k:z + k + m]] *= np.float32(64)
    return finish(rng, d, lambda t, n: (na, nh, np.zeros((N, 8), bool)) if t == 0 else sway(rng, n, 4))
def setup_inputs_crowd(rng):
    d = base(rng, 0.0, 0.0); kind = [list("ABDFGHIJ")[i] for i in rng.permutation(8)]; far = int(rng.integers(0, N))
    i = kind.index("A"); j = (kind.index("D") - DG) % 8; kind[i], kind[j] = kind[j], kind[i]
    fall = rng.permutation(N)[:(N // 2 if C > 255 else N - 2)].tolist()
    d["w0"] = np.exp2(rng.uniform(-0.4, 0.4, (N, 8, 1, C)) + rng.uniform(-1, 1, (N, 8, 16, 1))).astype(np.float32)
    na = np.full((N, 8), -1, np.int64); nh = np.full((N, 8), -1, np.int64); big = np.float32(64); small = np.float32(2.0 ** -6)
    for a in range(N):
        for g in range(8):
            c = kind[g]; one = (0, C - 1, int(rng.integers(0, C)))[int(rng.integers(0, 3))]; w = d["w0"][a, g]
            if c == "A":
                nh[a, g] = C
                if a % 2 == 0: d["s0"][a, g] = V - 1
            elif c == "B": nh[a, g] = C - 1; w[:, one] *= small
            elif (c == "H" and a % 2 == 0) or (c == "J" and a not in fall): nh[a, g] = C
            elif c == "D" or c == "J": d["coin"][a, g, 0] = 0; na[a, g] = C
            elif c == "H": d["coin"][a, g, 0] = 0; na[a, g] = C - 1; w[:, one] *= big
            elif c == "G":
                b = C // 4; p = rng.permutation(C); v = int(rng.integers(1, V - 1)); s = d["s0"][a, g]
                s[s == v] = 0; s[p[:b]] = v; d["nt"][a, g][:, v] = v
                na[a, g] = b; nh[a, g] = C - 2 * b; d["coin"][a, g, 0] = 0; w[:, p[b:2 * b]] *= small; w[:, p[2 * b:]] *= big
            else:
                k = C // 2; m = C - k; p = rng.permutation(C)
                if a == far and c == "F": k = k - 1
                if a == far and c == "I": m = m - 1
                na[a, g] = k; nh[a, g] = m
                d["coin"][a, g, 0] = 0; w[:, p[:k]] *= small; w[:, p[C - m:]] *= big
    def goal(t, n):
        if t == 0: return na, nh, np.zeros((N, 8), bool)
        a, b, s = sway(rng, n, 4)
        for g in range(8):
            if t < T - 1 and (kind[g] == "A" or kind[g] == "B"): a[:, g] = -1; b[:, g] = -1 if (kind[g] == "B" and t == 1) else C
        return a, b, s
    return finish(rng, d, goal)
def setup_inputs_ends(rng):
    d = base(rng, 0.0, 0.0); sh = (N, 8, 16, V)
    end = rng.random(sh) < np.where(rng.random((N, 8, 1, V)) < 0.3, 1.0, 0.55)
    d["nt"] = np.where(end, (V - 1) * rng.integers(0, 2, sh), d["nt"])
    bit = np.where(rng.random((N, 8, 1, V)) < 0.5, rng.integers(0, 2, (N, 8, 1, V)), rng.integers(0, 2, sh))
    d["qt"] = (16 + 239 * bit).astype(np.int32)
    d["w0"] = np.ascontiguousarray(np.broadcast_to(np.exp2(32.0 * rng.integers(0, 2, (N, 8, 1, C)) - 16), (N, 8, 16, C))).astype(np.float32)
    for a in range(N):
        for g in range(8):
            p = 1 + rng.permutation(V - 2)[:40]; nt = d["nt"][a, g]; qt = d["qt"][a, g]; m = (a + g) % 4
            nt[::2, p] = rng.integers(1, V - 1, (8, 40)); nt[:, 0] = p[17:33]; qt[:, p[17:32]] = 255; qt[:, p[32]] = rng.integers(144, 255, 16)
            d["w0"][a, g][:, [0, C - 1]] = np.float32(2.0 ** 16 if m % 2 == 0 else 2.0 ** -16)
            if m % 2 == 0:
                nt[:, V - 1] = p[:16]; qt[:, p[:16]] = 255
                if m == 0: nt[:, p[:16]] = p[17:33][:, None]; nt[:, p[17:33]] = p[:16][:, None]
            else:
                nt[:, V - 1] = V - 1; nt[15, V - 1] = p[16]; qt[:, p[16]] = 16; nt[:, p[16]] = p[:16]
                if m == 1:
                    way = [V - 1, int(p[16])] + p[33:32 + T].tolist()
                    for j in range(T):
                        nt[:, way[j]] = way[j]; nt[15 if j == 0 else int(rng.integers(0, 16)), way[j]] = way[j + 1]; qt[:, way[j + 1]] = 16
                    d["coin"][a, g][:, ::3] = 1; d["coin"][a, g][:, C - 1] = 1
    r = rng.random((N, 8, C)); d["s0"] = np.where(r < 0.2, -1, np.where(r < 0.55, V - 1, np.where(r < 0.75, 0, rng.integers(0, V, (N, 8, C))))); d["s0"][..., 0] = V - 1; d["s0"][..., 1] = 0; d["s0"][..., C - 1] = V - 1
    d["u"] = np.where(rng.random(d["u"].shape) < 0.85, 255 * rng.integers(0, 2, d["u"].shape), d["u"])
    return finish(rng, d, lambda t, n: sway(rng, n, 6))
def setup_inputs_spread(rng):
    d = base(rng, 0.08, 0.3)
    d["qt"] = np.clip(np.rint(np.exp2(4 + 4 * rng.random((N, 8, 1, V)) + rng.uniform(-1, 1, (N, 8, 16, V)))), 16, 255).astype(np.int32)
    d["u"] = (256 * rng.random((N, 8, T, C)) ** 3).astype(np.int64)
    d["w0"] = np.exp2(rng.uniform(-6, 6, (N, 8, 1, C)) + rng.uniform(-2, 2, (N, 8, 16, 1)) + rng.uniform(-0.3, 0.3, (N, 8, 16, C))).astype(np.float32)
    return finish(rng, d, lambda t, n: sway(rng, n, 4))
def check_inputs(d):
    bad = []
    for k, a, b in (("nb", 0, V - 1), ("qs", 16, 255), ("s0", -1, V - 1), ("us", 0, 255), ("coin", 0, 1), ("w0", 2.0 ** -16, 2.0 ** 16), ("lo", 2.0 ** -90, 2.0 ** 90), ("hi", 2.0 ** -90, 2.0 ** 90)):
        v = np.asarray(d[k]).astype(np.float64)
        if not (np.min(v) >= a and np.max(v) <= b): bad.append("range of " + k)
    v = np.asarray(d["qs"]).astype(np.float64)
    if not np.all(v == np.floor(v)): bad.append("qs not whole")
    if not np.all(np.asarray(d["lo"]) <= np.asarray(d["hi"])): bad.append("lo over hi")
    return bad
def reference(nb, qs, s0, w0, us, coin, lo, hi):
    nt = nb.reshape(N, 8, 16, V); qt = qs.astype(np.float32).astype(np.int32).reshape(N, 8, 16, V)
    u = us.astype(np.int64).reshape(N, 8, T, C); cn = coin.reshape(N, 8, T, C)
    l = lo.astype(np.float32).reshape(N, 8, 16, T); h = hi.astype(np.float32).reshape(N, 8, 16, T)
    H, W, live = start(s0.astype(np.int64), w0.astype(np.float32).reshape(N, 8, 16, C)); F = np.ones(8, np.float32)
    for t in range(T):
        old = live
        H, W, live = grow(t, H, W, live, nt, qt, u[:, :, t])
        H, W, live, up = breed(H, W, live, old, l[..., t] * F[:, None], h[..., t] * F[:, None], cn[:, :, t])
        F = np.where(up, F * np.float32(2), F)
    H = np.where(live[:, :, None], H, -1); W = np.where(live[:, :, None], W, np.float32(0))
    return {"yh": H.reshape(N, 128, C).astype(np.float32), "yw": W.reshape(N, 128, C).astype(np.float32)}

@@ -1,0 +1,829 @@
+import math
+from concourse.bass import DstId, RemoteDMATransfer
+from concourse.mybir import AluOpType as ALU, AxisListType, ActivationFunctionType as ACT
+
+NS = 6
+F32, BF, F16, I32, U16 = "float32", "bfloat16", "float16", "int32", "uint16"
+EXT, IDS = 1024, 1280
+PW = 100
+
+SB = {
+    "NB": (4096, I32), "QT": (4112, BF), "W0": (256, F32), "LO": (6, F32), "HI": (6, F32),
+    "SI": (256, I32), "UI": (1536, I32), "CI": (1536, I32),
+    "S0F": (256, F32), "UB": (1536, BF), "CB": (1792, BF), "CW": (96, BF),
+    "PI": (1, I32), "PJ": (4, I32), "PF": (8, F32), "GQ": (144, F32), "IQ": (144, F32),
+    "C16": (256, F32), "Q4": (256, F32), "IOT": (256, F32), "TMP": (256, F32), "TM2": (256, F32),
+    "EW32": (160, F32), "EWB": (160, BF), "BO32": (144, F32), "BOB": (128, BF), "RM": (16, F32),
+    "UH": (6 * 144, F16), "UB16": (2048, BF), "I32W": (144, F32), "I16W": (144, F16), "IB": (128, BF),
+    "I4": (128, BF), "I16": (128, BF), "I4096": (128, BF), "IM256": (128, BF), "IM1024": (128, BF), "I64": (128, BF), "IM32": (128, BF),
+    "ZB": (128, BF), "TB": (128, BF), "TBR": (128, BF), "VJ": (384, BF), "D32": (128, F32),
+    "MASK": (256, BF), "MASKN": (256, BF), "RST": (256, F32), "RS4": (256, F32), "RS32": (32, F32),
+    "C3": (64, F32), "C4": (64, F32), "CIN": (34, F32), "M16": (16, BF), "THR": (1, F32),
+    "G8": (128, BF), "G832": (128, F32), "E8": (144, BF), "HB": (1, F32),
+    "X": (4608, BF), "PT": (4608, F32), "TS": (256, F32), "US": (256, F32), "PG": (256, F32),
+    "CMP": (768, BF), "LT": (48, BF), "LL": (48, U16), "L4": (64, U16), "SB16": (16, BF),
+    "BS": (16, BF), "R": (256, F32), "XG": (768, BF), "C2": (768, BF), "GE": (256, F32), "M": (256, F32),
+    "SC": (288, F32), "LW": (18, U16), "NK": (288, F32), "EQ": (6 * 288, BF), "OU": (288, U16),
+    "OF": (256, F32), "WT": (296, F32), "HT": (296, F32), "WG": (256, F32), "HC": (256, F32), "H16": (288, F16),
+    "FL": (512, BF), "CL": (256, BF), "FG": (32, BF), "SN": (32, BF), "E1": (16, BF), "POS": (16, U16),
+    "TT": (1536, F32), "SM1": (32, F32), "SM2": (32, F32), "SL": (2, U16), "NL": (16, BF),
+    "SV": (16, F32), "FF": (1, F32), "LF": (2, F32), "LH": (12, F32),
+    "IDX": (16, U16), "SRB": (256, BF), "SRC": (16, U16), "FW": (16, BF), "YW": (256, F32), "YH": (256, F32),
+    "SC_O": (NS * 4, F32), "SC_I": (NS * 12, F32), "SP_O": (NS * PW, F32), "SP_I": (NS * PW, F32),
+}
+SB.update({"W0": (816, F32), "W1": (816, F32), "NK": (288, F16), "OT": (288, F32), "THB": (256, F32), "LL": (64, U16), "L4": (96, U16),
+           "C4": (96, F32), "FL": (768, BF), "FG": (48, BF), "I512": (128, BF), "PJ3": (768, F32)})
+for _n in ("US", "UB16", "MASKN", "WT", "BS", "CL", "SRC"):
+    del SB[_n]
+PACK = {n: 16 * i for i, n in enumerate(["FA", "FB", "FC", "FD", "FE", "Q1", "Q2", "Q3", "Q5", "Q6", "CWR", "IDC", "M16F"])}
+SB["SMALL"] = (16 * len(PACK), F32)
+SCRATCH = {k: ("sbuf", [128, v[0]], v[1]) for k, v in SB.items()}
+for _k in range(8):
+    SCRATCH["K%d" % _k] = ("psum", [128, 512], F32)
+
+NDMA = 24
+SEMAPHORES = (["ev", "es", "et", "eg", "sent"] + ["d%d" % i for i in range(NDMA)]
+              + ["rc%d" % t for t in range(NS - 1)] + ["rp%d" % t for t in range(NS)] + ["rw%d" % (NS - 1)])
+
+PAR = dict(
+    pieces=[("s", 0, 64), ("s", 64, 128), ("v", 128, 160), ("v", 160, 192), ("s", 192, 240), ("v", 256, 288), ("s", 240, 256)],
+    halves=[(0, 128), (128, 256)], soft=False, vj=-1, rounds=8000, seed=2)
+COST = dict(cyc=1.04, pe=0.55, gat=1.56, sca=3.8, hop=90.0, dma=2000.0, rem=2600.0, iss=900.0, look=60.0)
+
+
+def A(name, c0=0, c1=None, step=1, p0=0, p1=128):
+    if name in PACK:
+        return ("SMALL", p0, p1, PACK[name], PACK[name] + 16, 1)
+    if c1 is None:
+        c1 = SCRATCH[name][1][1]
+    return (name, p0, p1, c0, c1, step)
+
+
+def IND(win, off):
+    return ("@", win, off)
+
+
+def width(a):
+    if a[0] == "@":
+        return 16 * width(a[2])
+    return (a[4] - a[3] + a[5] - 1) // a[5]
+
+
+def is_ap(a):
+    return isinstance(a, tuple)
+
+
+def size(a):
+    return {F32: 4, I32: 4}.get(SCRATCH[a[0]][2], 2)
+
+
+def plan():
+    ops, now = [], [-1]
+
+    def add(eng, kind, args, outs, ins, ns, lat=0.0):
+        rd, wr = [], []
+        for a in ins:
+            if is_ap(a):
+                rd += [a[1], a[2]] if a[0] == "@" else [a]
+        for a in outs:
+            if a[0] == "@":
+                wr.append(a[1])
+                rd.append(a[2])
+            else:
+                wr.append(a)
+        ops.append(dict(step=now[0], eng=eng, kind=kind, args=args, rd=rd, wr=wr, ns=ns, lat=lat))
+        return ops[-1]
+
+    def vcost(out, ins, k=1.0):
+        n = width(out)
+        if out[0] == "@":
+            return 50 + n * COST["sca"] * COST["cyc"]
+        if ins[0][0] == "@":
+            return 55 + n * COST["gat"] * COST["cyc"]
+        if k == 1.0 and all(size(a) == 2 for a in [out] + ins):
+            k = 0.5
+        return max(64, n * k) * COST["cyc"]
+
+    def cp(out, in_):
+        add("v", "cp", (out, in_), [out], [in_], vcost(out, [in_]))
+
+    def tt(out, a, b, op):
+        k = 2.0 if a[0][0] != "K" and b[0][0] != "K" else 1.001
+        add("v", "tt", (out, a, b, op), [out], [a, b], vcost(out, [a, b], k))
+
+    def ts(out, a, s1, op0, s2=None, op1=None):
+        add("v", "ts", (out, a, s1, s2, op0, op1), [out], [a, s1, s2], vcost(out, [a]))
+
+    def scan(out, d0, d1, op0, op1):
+        add("v", "scan", (out, d0, d1, op0, op1), [out], [d0, d1], vcost(out, [d0, d1]))
+
+    def mset(out, c):
+        add("v", "mset", (out, c), [out], [], max(64, width(out) * size(out) / 4) * COST["cyc"])
+
+    def act(out, in_, func=ACT.Identity, bias=0.0, scale=1.0):
+        add("s", "act", (out, in_, func, bias, scale), [out], [in_, bias, scale], vcost(out, [in_], 1.001) + 15)
+
+    def iota(out, pat, base=0, ch=0):
+        add("g", "iota", (out, pat, base, ch), [out], [], 130 + 2 * width(out) * COST["cyc"])
+
+    def mm(items, start, stop=True):
+        ns = sum(max(64, width(r)) * (4 if size(r) == 4 else 1) * COST["pe"] for o, l, r in items)
+        tok = ("grp" + items[0][0][0], 0, 128, 0, 1, 1)
+        op = add("t", "mm", (items, start, stop), [o for o, l, r in items], [x for o, l, r in items for x in (l, r)], ns, 40.0)
+        op["wr"].append(tok)
+
+    def dma(eng, out, in_, ns, outs, ins):
+        add(eng, "dma", (out, in_), outs, ins, 60.0, ns)
+
+    def send(kind, t, src, land):
+        tok = ("tok%s%d" % (kind, t), 0, 128, 0, 1, 1)
+        add("g", "send", (kind, t, src), [tok], [src], COST["iss"])
+        add("x", "recv", (kind, t), [land], [tok], 0.0, COST["rem"] - COST["iss"])
+
+    def K(b, c0, c1, step=1):
+        return A("K%d" % b, c0, c1, step)
+
+    sel = lambda r: A("EWB", 31 - r, 159 - r)
+    sel32 = lambda r: A("EW32", 31 - r, 159 - r)
+    unw = lambda r: A("UB16", 128 * r, 128 * r + 128)
+    col = lambda n, j: A(n, j, j + 1)
+    P_, PG, PR, PNZ = col("PF", 0), col("PF", 1), col("PF", 2), col("PF", 3)
+    BO, IW = A("BO32", 16, 144), A("I32W", 16, 144)
+    IQ = A("IQ", 16, 144)
+
+    dma("y", A("SI", p1=8), ("in", "s0"), 1800, [A("SI", p1=8)], [])
+    dma("y", A("NB"), ("in", "nb"), 8500, [A("NB")], [])
+    dma("y", A("QT", 0, 4096), ("in", "qs"), 12000, [A("QT", 0, 4096)], [])
+    for n, s in ((A("CI", p1=8), "coin"), (A("UI", p1=8), "us"), (A("W1", 0, 256), "w0"), (A("LO"), "lo"), (A("HI"), "hi")):
+        dma("s", n, ("in", s), 2500, [n], [])
+
+    iota(A("PI"), [[0, 1]], 0, 1)
+    iota(A("C16"), [[0, 16], [1, 16]])
+    iota(A("GQ", 16, 144), [[16, 8], [0, 16]])
+    iota(A("IOT"), [[1, 256]])
+    iota(A("Q4"), [[0, 64], [1, 4]])
+    iota(A("M16F"), [[16, 16]])
+    iota(A("C3", 0, 48), [[-1, 3], [0, 16]], 2304 + 3)
+    iota(A("C4", 0, 64), [[4, 4], [0, 16]], 2304 + 3)
+    S160 = A("IOT", 0, 160)
+    mset(A("GQ", 0, 16), 112.0)
+    mset(A("C3", 48, 64), 0.0)
+    cp(IQ, A("IOT", 0, 128))
+    cp(A("IQ", 0, 16), A("IOT", 112, 128))
+    ts(col("PJ", 0), A("PI"), 112, ALU.bitwise_and)
+    ts(col("PJ", 1), A("PI"), 15, ALU.bitwise_and)
+    ts(col("PJ", 2), A("PI"), 12, ALU.bitwise_and)
+    ts(col("PJ", 3), A("PI"), 3, ALU.bitwise_and)
+    cp(P_, A("PI"))
+    cp(A("PF", 1, 3), A("PJ", 0, 2))
+    cp(A("PF", 4, 6), A("PJ", 2, 4))
+    ts(PNZ, PR, 0.5, ALU.is_gt)
+    ts(col("PF", 6), col("PF", 5), 3.0, ALU.is_equal, -2.0, ALU.mult)
+    ts(col("PF", 7), col("PF", 4), -1.0, ALU.mult, 8.5 / 8, ALU.add)
+    tt(A("THR"), col("PF", 6), col("PF", 7), ALU.add)
+    ts(A("BO32"), A("GQ"), PG, ALU.is_equal)
+    act(A("BOB"), BO)
+    ts(A("RM"), A("IOT", 0, 16), PR, ALU.is_equal)
+    ts(A("I32W"), A("IQ"), P_, ALU.is_equal)
+    ts(A("I16W"), A("IQ"), P_, ALU.is_equal)
+    for n, c in (("IB", 1.0), ("I4096", 4096.0), ("I4", 4.0), ("I16", 16.0), ("IM256", -256.0), ("IM1024", -1024.0),
+                 ("I64", 64.0), ("IM32", -32.0), ("ZB", 0.0), ("I512", 512.0)):
+        act(A(n), IW, scale=c)
+    ts(A("TMP", 0, 160), S160, PG, ALU.subtract, 31.0, ALU.is_equal)
+    ts(A("TM2", 0, 160), S160, PG, ALU.subtract, -97.0, ALU.is_equal)
+    tt(A("EW32"), A("TMP", 0, 160), A("TM2", 0, 160), ALU.add)
+    act(A("EWB"), A("EW32"))
+    ts(A("MASK"), A("C16"), PR, ALU.not_equal, 8192.0, ALU.mult)
+    ts(A("RST"), A("C16"), 0.0, ALU.is_equal, 65536.0, ALU.mult)
+    ts(A("RS4"), A("Q4"), 0.5, ALU.is_gt)
+    ts(A("RS32"), A("C16", 0, 32), 0.5, ALU.is_gt)
+    ts(A("GE", 0, 128, p1=8), A("GQ", 16, 144, p1=8), 1.0 / 16, ALU.mult)
+    ts(A("G832", p1=8), A("GE", 0, 128, p1=8), A("PF", 0, 1, p1=8), ALU.is_equal)
+    ts(A("G8", p1=8), A("G832", p1=8), 8.0, ALU.mult)
+    ts(A("R", 0, 144, p1=8), A("IOT", 0, 144, p1=8), -15.0, ALU.add, 1.0 / 16, ALU.mult)
+    ts(A("E8", p1=8), A("R", 0, 144, p1=8), A("PF", 0, 1, p1=8), ALU.is_equal)
+    ts(A("HB"), PR, 6.5, ALU.is_lt, 2049.0, ALU.mult)
+    ts(A("HB"), A("HB"), -1.0, ALU.add)
+    mset(A("QT", 4096, 4112), 0.0)
+    mset(A("W0", 800, 816), 0.0)
+    mset(A("W1", 800, 816), 0.0)
+    mset(A("C4", 64, 96), 144.0)
+    mset(A("OT", 256, 288), 0.0)
+    mset(A("HT", 256, 296), -1.0)
+    mset(A("X", 4096, 4608), 0.0)
+    for j in range(1, 4):
+        mset(A("SP_O", j, NS * PW, PW), 0.0)
+    for j in range(18):
+        act(A("PT", 256 * j, 256 * j + 256), A("C16"), scale=0.0)
+    ts(A("TS", 0, 128), IQ, 1.0, ALU.add, P_, ALU.is_equal)
+    ts(A("TS", 128, 256), A("TS", 0, 128), PNZ, ALU.mult)
+    tt(A("D32"), IW, A("TS", 128, 256), ALU.subtract)
+    for p in range(5):
+        ts(A("UH", 144 * p, 144 * p + 144), A("BO32"), col("RM", p), ALU.mult)
+    for j in range(3):
+        x = A("OF", 128 * (j % 2), 128 * (j % 2) + 128)
+        ts(x, A("Q4", 0, 128), float(j), ALU.is_equal, 0.125, ALU.mult)
+        tt(A("VJ", 128 * j, 128 * j + 128), x, BO, ALU.mult)
+    ts(A("WG", 0, 128), IQ, P_, ALU.is_lt, -1.0, ALU.mult)
+    tt(A("TB"), A("WG", 0, 128), BO, ALU.mult)
+    ts(A("WG", 128, 256), IW, PR, ALU.mult)
+    tt(A("TBR"), A("TB"), A("WG", 128, 256), ALU.subtract)
+    ts(A("CWR"), A("M16F"), PR, ALU.add)
+    ts(A("SB16"), A("CWR"), -144.0, ALU.add)
+    mset(A("CIN", 0, 16), 1024.0)
+    ts(A("CIN", 16, 32), A("CWR"), 511.0, ALU.add)
+    mset(A("CIN", 32, 34), 0.0)
+    ts(A("IDC"), A("CWR"), float(IDS), ALU.add)
+    ts(A("M16"), A("M16F"), -1.0, ALU.mult)
+    for j in range(4):
+        act(A("TT", 256 * j, 256 * j + 256), A("C16"), scale=0.0)
+    ts(A("TT", EXT, IDS), A("IOT"), 256.0, ALU.add, 287.0, ALU.min)
+    act(A("TT", IDS, 1536), A("IOT"))
+    mset(A("FF"), 1.0)
+
+    ts(A("S0F", p1=8), A("SI", p1=8), -2048.0, ALU.add)
+    mm([(K(0, 0, 256), A("G832", p1=8), A("S0F", p1=8))], True)
+    ts(A("M"), K(0, 0, 256), col("RM", 0), ALU.mult)
+    cp(A("UB", p1=8), A("UI", p1=8))
+    cp(A("CB", 0, 1536, p1=8), A("CI", p1=8))
+    ts(A("CB", 1536, 1792, p1=8), A("S0F", p1=8), -2048.5, ALU.is_lt)
+    mm([(K(7, 0, 112), A("E8", 15 - r, 143 - r, p1=8), A("CB", r, 1792, 16, p1=8)) for r in range(16)], True)
+    cp(A("CW"), K(7, 0, 96))
+    cp(A("NL"), K(7, 96, 112))
+    mm([(K(7, 128, 144), A("BOB"), A("NL"))], True)
+    add("v", "red", (col("SV", 2), K(7, 128, 144)), [col("SV", 2)], [K(7, 128, 144)], 64 * COST["cyc"])
+    cp(A("LH", 0, 6), A("LO"))
+    cp(A("LH", 6, 12), A("HI"))
+    cp(A("LF"), A("LH", 0, 12, 6))
+    DD, NDN, QQ, TH = col("SV", 0), col("SV", 2), col("SV", 3), col("SV", 4)
+
+    def history(t):
+        it = [(K(4, 0, 256), A("I16W", 16, 144), A("H16", 0, 256))] if t >= 0 else []
+        mm(it + [(K(4, 0, 256), sel32(t + 1), A("M"))], True)
+        act(A("HT", 0, 256), K(4, 0, 256), bias=A("HB") if t == NS - 1 else 0.0)
+
+    def neighbours(t, a, b, m, bo, uo, sm, hb, of):
+        w = b - a
+        mm([(sm, A("IB"), A("MASK", 0, w))], True, False)
+        mm([(sm, bo, m)], False)
+        scan(A("SC", a, b), A("RST", 0, w), sm, ALU.add, ALU.min)
+        lw = A("LW", a // 16, b // 16)
+        ts(lw, A("SC", a + 15, b, 16), 2048.0, ALU.add, 4095.0, ALU.min)
+        mm([(hb(t + 1), bo, m)], True)
+        nk = A("NK", a, b)
+        ts(nk, IND(A("NB"), lw), -2048.0, ALU.add)
+        mm([(of, A("I16W", 16, 144), nk)], True, False)
+        for p in range(t + 2):
+            e = A("EQ", 288 * p + a, 288 * p + b)
+            tt(e, nk, hb(p), ALU.is_equal)
+            mm([(of, A("I4096"), e)], False, p == t + 1)
+        ts(A("OU", a, b), of, 2048.0, ALU.add, 4096.0, ALU.min)
+        act(A("OT", a, b), of)
+
+    def own(t):
+        for p in range(t + 1):
+            mm([(K(p // 2, 256 * (p % 2), 256 * (p % 2) + 256), A("UH", 144 * p + 16, 144 * p + 144), A("H16", 0, 256))], True)
+        for h, (a, b) in enumerate(PAR["halves"]):
+            neighbours(t, a, b, A("M", a, b), BO, 16, K(5 + h % 2, a, b),
+                       lambda p: K(p // 2, 256 * (p % 2) + a, 256 * (p % 2) + b), K(3, 256 + a, 256 + b))
+
+    def lists(t):
+        last = t == NS - 1
+        it = [(K(7, 160, 256), IW, A("C4"))]
+        it += [(K(7, 160 + 16 * j, 176 + 16 * j), A("I16" if j < 4 else "IB"), A("SB16")) for j in range(4 if last else 0, 6)]
+        if t >= 0:
+            it += [(K(7, 240, 256), A("I512"), A("FW"))]
+        if last:
+            mm(it, True, False)
+            mm([(K(7, 224, 240), A("I4096"), A("NL")), (K(7, 240, 256), A("I4096"), A("NL"))], False)
+            ts(SRC, K(7, 224, 240), 288.0, ALU.min)
+            ts(WL, K(7, 240, 256), 800.0, ALU.min)
+        else:
+            mm(it, True)
+            cp(A("L4"), K(7, 160, 256))
+
+    SRC, WL = A("L4", 64, 80), A("L4", 80, 96)
+    own(-1)
+    history(-1)
+    lists(-1)
+    act(A("HC"), A("HT", 0, 256))
+    act(A("OF"), A("OT", 0, 256))
+
+    for t in range(NS):
+        last = t == NS - 1
+        now[0] = t
+        mm([(K(4, 0, 256), A("G8", p1=8), A("UB", 256 * t, 256 * t + 256, p1=8))], True)
+        for i, (e, a, b) in enumerate(PAR["pieces"]):
+            if a >= 256 and t == 0:
+                continue
+            o, x = A("X", 16 * a, 16 * b), IND(A("QT"), A("OU", a, b))
+            if e == "v":
+                cp(o, x)
+            else:
+                act(o, x)
+            k = K(i % 4, 0, 4 * (b - a))
+            mm([(k, A("IB"), A("X", 16 * a + j, 16 * b, 4)) for j in range(4)], True)
+            scan(A("PT", 16 * a + 3, 16 * b, 4), A("RS4", 0, 4 * (b - a)), k, ALU.mult, ALU.add)
+        mm([(K(4, 256, 512), A("D32"), A("OF"))], True)
+        cp(A("H16", 0, 256), A("HC"))
+        mm([(K(6, 0, 48), A("ZB"), A("MASK", 0, 48)), (K(6, 32, 48), A("I64"), A("NL")),
+            (K(6, 0, 16), A("IM32"), A("CW", 16 * t, 16 * t + 16)), (K(6, 16, 32), A("IM32"), A("NL"))], True, False)
+        pt = lambda j: IND(A("PT"), A("L4", 16 * j, 16 * j + 16))
+        wn, wo = "W%d" % (t % 2), "W%d" % (1 - t % 2)
+        act(A("PG"), pt(3), scale=2.0 ** -11)
+        tt(K(4, 0, 256), A("PG"), K(4, 0, 256), ALU.mult)
+        for j in range(3):
+            pj = A("PJ3", 256 * j, 256 * j + 256)
+            if j == PAR["vj"]:
+                cp(pj, pt(j))
+            else:
+                act(pj, pt(j))
+            tt(A("CMP", 256 * j, 256 * j + 256), pj, K(4, 0, 256), ALU.is_gt)
+        act(A("TS"), K(4, 0, 256))
+        act(A("FL", 512, 768), A("PG"), ACT.Relu, 1.0, -2048.0)
+        tt(A(wn, 0, 256), IND(A(wo, 0, 816 if t else 256), WL), A("PG"), ALU.mult)
+        ts(A("FL", 0, 256), A(wn, 0, 256), col("LF", 0), ALU.is_lt)
+        ts(A("FL", 256, 512), A(wn, 0, 256), col("LF", 1), ALU.is_gt)
+        act(A(wn, 512, 768), A(wn, 0, 256), scale=0.5)
+        act(A(wn, 256, 512), A(wn, 0, 256), scale=2.0)
+        mm([(K(1, 256, 320), IW, A("C3"))] + [(K(1, 256 + 16 * j, 272 + 16 * j), A("I16"), A("SB16")) for j in range(3)], True, False)
+        mm([(K(0, 256, 304), sel(r), A("CMP", r, 768, 16)) for r in range(16)], True)
+        ts(A("LT"), K(0, 256, 304), 8.5, ALU.is_lt)
+        mm([(K(1, 256 + a, 256 + b), A("I4"), A("LT", c, c + b - a))
+            for a, b, c in ((0, 48, 0), (0, 32, 16), (32, 64, 0), (0, 16, 32), (16, 48, 0), (48, 64, 0), (48, 64, 32))], False)
+        cp(A("LL"), K(1, 256, 320))
+        mm([(K(6, 0, 48), sel(r), A("FL", r, 768, 16)) for r in range(16)], False)
+        mm([(K(7, 0, 34), IW, A("CIN"))], True, False)
+        ts(A("FG"), K(6, 0, 48), 8.5, ALU.is_gt)
+        HOLE, HIGH = A("FG", 0, 16), A("FG", 16, 32)
+        tt(HOLE, HOLE, A("FG", 32, 48), ALU.max)
+        scan(A("SN"), A("RS32"), A("FG", 0, 32), ALU.mult, ALU.add)
+        tt(A("E1"), HIGH, A("M16"), ALU.mult)
+        mm([(K(7, 0, 16), A("TB"), HOLE), (K(7, 0, 16), A("IM1024"), HOLE), (K(7, 16, 32), A("TBR"), HIGH),
+            (K(7, 16, 32), A("IM256"), HIGH), (K(7, 16, 32), A("IB"), A("E1"))], False, False)
+        mm([(K(7, 0, 32), A("BOB"), A("SN")), (K(7, 32, 34), A("BOB"), A("SN", 15, 32, 16))], False)
+        NH, NC, HX = K(7, 32, 33), K(7, 33, 34), K(7, 0, 16)
+        po = PW * t
+        ts(A("POS"), K(7, 16, 32), NH, ALU.subtract)
+        act(col("SV", 6), NH, bias=255.0, scale=-1.0)
+        act(DD, NC, bias=col("SV", 6))
+        act(col("SP_O", po), DD, ACT.Relu, -255.0)
+        act(A("Q2"), HX, bias=col("SV", 6))
+        cp(IND(A("TT", 0, EXT), A("POS")), A("IOT"))
+        tt(A("SM1"), A("TT", 256, 288), A("MASK", 0, 32), ALU.add)
+        scan(A("SM2"), A("RST", 0, 32), A("SM1"), ALU.add, ALU.min)
+        cp(A("SL"), A("SM2", 15, 32, 16))
+        act(A("SP_O", po + 4, po + 36), IND(A(wn, 512, 768), A("SL")))
+        act(A("SP_O", po + 36, po + 68), IND(A("HC"), A("SL")))
+        if last:
+            send("w", t, A("SP_O", po, po + 68), A("SP_I", po, po + 68))
+        ts(A("FA"), K(6, 0, 16), -23.5, ALU.is_gt, 0.5, ALU.mult)
+        ts(A("FB"), K(6, 0, 16), -15.5, ALU.is_gt, 0.5, ALU.mult)
+        tt(A("R"), IND(A("PT"), A("LL", 0, 16)), A("TS"), ALU.subtract)
+        xg = lambda i: A("XG", 256 * i, 256 * i + 256)
+        for i in range(3):
+            act(xg(i), IND(A("X"), A("LL", 16 * i, 16 * i + 16)))
+        for i in range(3):
+            mm([(K(i, 0, 256), A("IB"), xg(j)) for j in range(i + 1)], True)
+            c2 = A("C2", 256 * i, 256 * i + 256)
+            tt(c2, K(i, 0, 256), A("R"), ALU.is_lt)
+            mm([(K(3, 0, 256), A("VJ", 128 * (2 - i), 128 * (3 - i)), c2)], i == 0, i == 2)
+        act(A("THB"), IND(A("IOT"), A("LL", 48, 64)), bias=A("THR"))
+        for a, b in PAR["halves"]:
+            tt(A("GE", a, b), K(3, a, b), A("THB", a, b), ALU.is_gt)
+            tt(A("M", a, b), A("GE", a, b), K(4, 256 + a, 256 + b), ALU.mult)
+        cp(A("SP_O", po + 68, po + PW), IND(A("M"), A("SL")))
+        p0 = po + 68 if last else po
+        send("p", t, A("SP_O", p0, po + PW), A("SP_I", p0, po + PW))
+        if not last:
+            act(col("SC_O", 4 * t), NDN, bias=DD, scale=-1.0)
+            send("c", t, col("SC_O", 4 * t), A("SC_I", 12 * t, 12 * t + 12))
+            own(t)
+        history(t)
+        act(QQ, DD, bias=float(EXT - 1), scale=-1.0)
+        ts(A("Q1"), HX, NC, ALU.is_gt, QQ, ALU.mult)
+        tt(A("Q3"), A("Q1"), A("Q2"), ALU.add)
+        tt(A("Q5"), A("Q3"), A("IDC"), ALU.min)
+        cp(A("IDX"), A("Q5"))
+        act(A("SRB"), IND(A("TT"), A("IDX")), bias=-144.0)
+        tt(A("FC"), HOLE, HIGH, ALU.add)
+        tt(A("FE"), A("FA"), A("FB"), ALU.subtract)
+        tt(A("FW"), A("FE"), A("FC"), ALU.max)
+        mm([(K(7, 96, 112), sel(r), A("SRB", r, 256, 16)) for r in range(16)], True)
+        act(A("SB16"), K(7, 96, 112), scale=1.0 / 16)
+        if not last:
+            lists(t)
+        wi = A("SP_I", po + 4, po + 36)
+        dma("y", A(wn, 768, 800, p0=16), A("SP_I", po + 4, po + 36, p1=112), COST["dma"], [A(wn, 768, 800, p0=16)], [wi])
+        dma("y", A(wn, 768, 800, p1=16), A("SP_I", po + 4, po + 36, p0=112), COST["dma"], [A(wn, 768, 800, p1=16)], [wi])
+        cp(A("H16", 256, 288), A("SP_I", po + 36, po + 68))
+        mi = A("SP_I", po + 68, po + PW)
+        if not last:
+            for p in range(t + 1):
+                mm([(K(6, 320 + 32 * p, 352 + 32 * p), A("UH", 144 * p, 144 * p + 128), A("H16", 256, 288))], True)
+            neighbours(t, 256, 288, mi, A("BO32", 0, 128), 0, K(5, 0, 32), lambda p: K(6, 320 + 32 * p, 352 + 32 * p), K(5, 64, 96))
+            act(A("OF"), IND(A("OT"), SRC))
+        mm([(K(6, 288, 320), A("I16W", 0, 128), A("H16", 256, 288)), (K(6, 288, 320), sel32(t + 17), mi)], True)
+        act(A("HT", 256, 288), K(6, 288, 320), bias=A("HB") if last else 0.0)
+        mm([(K(6, 65, 66), A("I32W", 0, 128), col("SP_I", po))], True)
+        ts(TH, K(6, 65, 66), 32.0, ALU.min, NC, ALU.add)
+        ts(A("Q6"), HX, TH, ALU.is_le)
+        tt(A("NL"), HOLE, A("Q6"), ALU.subtract)
+        if not last:
+            ts(NDN, TH, NH, ALU.subtract, 0.0, ALU.min)
+            mm([(K(6, 64, 65), IW, x) for x in [col("SC_O", 4 * t)] + [col("SC_I", 12 * t + 4 * j) for j in range(3)]], True)
+            act(col("SV", 7), K(6, 64, 65), ACT.Sign, -4 * 255.0 - 0.5)
+            act(col("SV", 5), col("SV", 7), bias=1.5, scale=0.5)
+            act(A("FF"), A("FF"), scale=col("SV", 5))
+            act(A("LF"), A("LH", t + 1, 12, 6), scale=A("FF"))
+            act(A("HC"), IND(A("HT"), SRC))
+        else:
+            lists(t)
+            act(A("YH"), IND(A("HT"), SRC))
+            cp(A("YW"), IND(A(wn), WL))
+            dma("s", ("out", "yh"), A("YH"), COST["dma"], [], [A("YH")])
+            dma("y", ("out", "yw"), A("YW"), COST["dma"], [], [A("YW")])
+    return ops
+
+
+def meet(a, b):
+    return a[0] == b[0] and a[1] < b[2] and b[1] < a[2] and a[3] < b[4] and b[3] < a[4]
+
+
+def sign(o):
+    a = (o["wr"] or o["rd"])[0]
+    c = {"SP_O": a[3] % PW, "SC_O": 0, "EQ": a[3] % 288, "SP_I": a[3] % PW, "SC_I": 0}.get(a[0], a[3])
+    if o["kind"] == "mm":
+        l, r = o["rd"][0], o["rd"][1]
+        if r[0] == "X":
+            return "mm.sum.%d" % r[3]
+        if l[0] == "UH":
+            return "mm.hb.%d" % r[3]
+        if l[0] == "BO32" and a[0] in ("K0", "K1", "K2") or (a[0] == "K6" and a[3] >= 320):
+            return "mm.hbm.%d" % (r[3] if r[0] == "M" else 256)
+        return "mm.%s.%d.%s" % (a[0], c, o["rd"][1][0][:3])
+    return "%s.%s.%d" % (o["kind"], "W" if a[0] in ("W0", "W1") else a[0][:4], c)
+
+
+BIAS = {"dma.SI.0": 2e6, "dma.NB.0": 1e6}
+
+
+def depend(ops):
+    seen = {}
+    for i, o in enumerate(ops):
+        d, raw = set(), set()
+        for a in o["rd"]:
+            raw.update(j for j, b, w in seen.get(a[0], []) if w and meet(a, b))
+        for a in o["wr"]:
+            d.update(j for j, b, w in seen.get(a[0], []) if meet(a, b))
+        d |= raw
+        d.discard(i)
+        o["dep"] = d
+        same = {j for j in d if ops[j]["eng"] == o["eng"]}
+        if o["eng"] == "t":
+            o["soft"] = same
+        elif o["eng"] in "vs" and o["kind"] != "dma" and PAR["soft"]:
+            o["soft"] = {j for j in same - raw if ops[j]["kind"] != "dma"}
+        else:
+            o["soft"] = set()
+        for a in o["wr"]:
+            keep = [e for e in seen.get(a[0], []) if not (a[5] == 1 and a[1] <= e[1][1] and e[1][2] <= a[2] and a[3] <= e[1][3] and e[1][4] <= a[4] and e[0] != i)]
+            seen[a[0]] = keep + [(i, a, True)]
+        for a in o["rd"]:
+            seen.setdefault(a[0], []).append((i, a, False))
+        o["banks"] = sorted({a[0] for a in o["rd"] + o["wr"] if a[0][0] == "K"})
+
+
+def schedule(ops):
+    n = len(ops)
+    depend(ops)
+    users = [[] for _ in range(n)]
+    for i, o in enumerate(ops):
+        for j in o["dep"]:
+            users[j].append(i)
+    hop = COST["hop"]
+    prio = [0.0] * n
+    for i in range(n - 1, -1, -1):
+        prio[i] = ops[i]["ns"] + max([prio[u] + (0.0 if i in ops[u]["soft"] else hop + ops[i]["lat"]) for u in users[i]], default=ops[i]["lat"])
+    for i, o in enumerate(ops):
+        prio[i] += BIAS.get(sign(o), 0.0)
+    left = [len(o["dep"]) for o in ops]
+    done = [0.0] * n
+    free, bank, order = {}, {}, []
+    cand = [i for i in range(n) if left[i] == 0]
+
+    def ready(i):
+        o = ops[i]
+        r = max([0.0 if j in o["soft"] else done[j] + hop for j in o["dep"]], default=0.0)
+        for b in o["banks"]:
+            if b in bank and ops[bank[b]]["eng"] != o["eng"]:
+                r = max(r, done[bank[b]] + hop)
+        return max(r, free.get(o["eng"], 0.0))
+    while cand:
+        st = {i: ready(i) for i in cand}
+        first = min(cand, key=lambda i: (st[i], -prio[i]))
+        e = ops[first]["eng"]
+        mine = [i for i in cand if ops[i]["eng"] == e]
+        now = [i for i in mine if st[i] <= st[first] + 1e-6]
+        pick = max(now, key=lambda i: prio[i])
+        if e not in "xy":
+            while True:
+                b = [i for i in mine if prio[i] > prio[pick] + ops[pick]["ns"] and st[i] < st[pick] + ops[pick]["ns"] - COST["look"]]
+                if not b:
+                    break
+                lim = min(st[i] for i in b)
+                fit = [i for i in now if st[i] + ops[i]["ns"] <= lim + COST["look"]]
+                if fit:
+                    pick = max(fit, key=lambda i: prio[i])
+                    break
+                pick = min(b, key=lambda i: (st[i], -prio[i]))
+        o = ops[pick]
+        for b in o["banks"]:
+            if b in bank and ops[bank[b]]["eng"] != o["eng"]:
+                o["dep"].add(bank[b])
+            bank[b] = pick
+        o["t0"] = st[pick]
+        free[o["eng"]] = st[pick] + o["ns"]
+        done[pick] = st[pick] + o["ns"] + o["lat"]
+        order.append(pick)
+        cand.remove(pick)
+        for u in users[pick]:
+            left[u] -= 1
+            if left[u] == 0:
+                cand.append(u)
+    return order, max(done)
+
+
+PERIOD, FIRST = 16000.0, 12000.0
+ORDER = {
+    "v": "cp.X.2048:100 scan.PT.3:230 cp.X.2560:240 cp.X.4096:330 scan.PT.2051:335 scan.PT.1027:420 cp.X.3840:430 scan.PT.2563:440 "
+         "scan.PT.4099:480 scan.PT.3843:490 scan.PT.3075:520 cp.PJ3.0:560 cp.PJ3.256:560 cp.PJ3.512:560 tt.K4.0:610 tt.CMP.0:640 tt.W.0:660 tt.CMP.256:700 "
+         "tt.CMP.512:730 ts.FL.0:760 ts.FL.256:790 ts.LT.0:820 cp.LL.0:870 tt.R.0:885 ts.FG.0:930 tt.FG.0:935 scan.SN.0:940 tt.E1.0:945 "
+         "ts.SMAL.0:950 ts.SMAL.16:955 tt.SMAL.32:960 cp.H16.0:825 ts.POS.0:990 cp.TT.0:1000 tt.C2.0:1100 tt.C2.256:1110 tt.SM1.0:1115 tt.C2.512:1120 "
+         "scan.SM2.0:1150 ts.SMAL.80:1155 cp.SL.0:1160 tt.SMAL.112:1165 tt.GE.0:1200 tt.M.0:1210 tt.SMAL.128:1215 tt.GE.128:1220 tt.M.128:1230 cp.IDX.0:1235 "
+         "cp.SP_O.68:1240 scan.SC.0:1250 tt.SMAL.64:1255 ts.LW.0:1260 scan.SC.128:1265 ts.NK.0:1270 ts.LW.8:1275 tt.FW.0:1278 tt.EQ.0:1280 ts.NK.128:1290 "
+         "ts.OU.0:1300 tt.EQ.128:1310 ts.OU.128:1650 cp.H16.256:1690 scan.SC.256:1710 ts.LW.16:1720 ts.NK.256:1810 tt.EQ.256:1820 "
+         "ts.OU.256:1850 cp.L4.0:1900 ts.SV.4:2060 ts.SMAL.144:2070 tt.NL.0:2080 ts.SV.2:2090 ts.L4.64:2100 ts.L4.80:2095 cp.YW.0:2110",
+    "s": "act.X.0:0 act.X.1024:175 act.X.3072:350 act.X.2048:350 act.X.4096:400 act.PG.0:560 act.PJ3.0:600 act.PJ3.256:610 act.PJ3.512:660 act.FL.512:710 act.TS.0:770 "
+         "act.W.512:780 act.XG.0:885 act.XG.256:935 act.XG.512:985 act.THB.0:1035 act.SV.6:1080 act.SV.0:1085 act.SV.3:1090 act.SMAL.96:1095 "
+         "act.SP_O.0:1100 act.W.256:1110 act.SP_O.4:1170 act.SP_O.36:1180 act.SC_O.0:1190 act.SRB.0:1240 act.SB16.0:1300 "
+         "act.HT.0:2090 act.HT.256:2100 act.SV.7:2110 act.SV.5:2120 act.FF.0:2130 act.LF.0:2140 act.OT.0:2150 act.OT.128:2320 act.OT.256:2330 "
+         "act.OF.0:2390 act.HC.0:2395 act.YH.0:2200",
+    "t": "mm.K0.0.X:180 mm.K2.0.X:190 mm.K3.0.X:330 mm.K1.0.X:350 mm.K4.0.UB:530 mm.K1.256.C3:600 mm.K6.0.MAS:610 mm.K7.0.CIN:620 "
+         "mm.K0.256.CMP:750 mm.K1.256.LT:835 mm.K6.0.FL:860 mm.K4.256.OF:920 mm.K0.0.XG:935 mm.K7.0.FG:950 mm.K7.0.SN:955 mm.K1.0.XG:985 "
+         "mm.K2.0.XG:1035 mm.K5.0.MAS:1040 mm.K6.128.MAS:1045 mm.K3.0.C2:1130 mm.hb.0:1190 mm.K5.0.M:1215 mm.K6.128.M:1235 mm.hbm.0:1240 mm.K7.96.SRB:1260 "
+         "mm.K3.256.NK:1275 mm.K3.256.EQ:1285 mm.hbm.128:1290 mm.K3.384.NK:1295 mm.K3.384.EQ:1315 mm.K7.160.C4:1660 mm.K5.0.SP_:1700 mm.hb.256:1705 "
+         "mm.hbm.256:1710 mm.K4.0.H16:1730 mm.K5.64.NK:1815 mm.K5.64.EQ:1825 mm.K6.288.H16:1850 mm.K6.65.SP_:1860 mm.K6.64.SC_:1900 mm.K7.224.NL:2090",
+    "g": "send.tokw.0:1185 send.tokp.0:1245 send.tokc.0:1300",
+    "x": "recv.SP_I.0:1250 recv.SP_I.68:1260 recv.SC_I.0:1310",
+}
+TAU = {e + w.split(":")[0]: 10.0 * int(w.split(":")[1]) for e, s in ORDER.items() for w in s.split()
+       if ".X" not in w and "scan.PT" not in w}
+EARLY = ("vtt.K4.0:610 vtt.W.0:620 vts.FL.0:650 vts.FL.256:680 vtt.CMP.0:700 vtt.CMP.256:730 vtt.CMP.512:760 vts.FG.0:775 vtt.FG.0:780 "
+         "vscan.SN.0:785 vtt.E1.0:790 vts.SMAL.0:795 vts.SMAL.16:800 vtt.SMAL.32:805 vts.LT.0:850 vts.POS.0:870 vcp.LL.0:890 vtt.R.0:900 "
+         "vcp.TT.0:950 vcp.H16.0:860 sact.FL.512:600 sact.PJ3.0:610 sact.PJ3.256:650 sact.PJ3.512:700 sact.TS.0:800 sact.W.512:810 "
+         "sact.HC.0:2380 sact.OT.0:2100 sact.OT.128:2105 sact.OT.256:2110 sact.OF.0:2400 tmm.K6.0.MAS:500 tmm.K6.0.FL:720 tmm.K0.256.CMP:790 "
+         "tmm.K7.0.FG:850 tmm.K7.0.SN:855 tmm.K1.256.LT:860 vtt.NL.0:2000 vts.SV.4:1990 vts.SMAL.144:1995 sact.SV.7:1940 sact.SV.5:1945 "
+         "sact.FF.0:1950 sact.LF.0:1955")
+TAU.update({w.split(":")[0]: 10.0 * int(w.split(":")[1]) for w in EARLY.split()})
+
+
+def label(o):
+    return ("p" if o["step"] < 0 else "") + o["eng"] + sign(o)
+
+
+def simulate(ops, tau, fix=False):
+    hop = COST["hop"]
+    seq, key = {}, []
+    for i, o in enumerate(ops):
+        k = tau[o["id"]] + (0.0 if o["step"] < 0 else FIRST + PERIOD * o["step"])
+        for j in o["dep"]:
+            if j < i and key[j] > k:
+                k = key[j]
+        key.append(k)
+        seq.setdefault(o["eng"], []).append((k, i))
+    qs = [[i for k, i in sorted(v)] for v in seq.values()]
+    pos, free, done, bank, order = [0] * len(qs), [0.0] * len(qs), [-1.0] * len(ops), {}, []
+    rdy = [None] * len(qs)
+    for _ in range(len(ops)):
+        best, bs = -1, 1e18
+        for q in range(len(qs)):
+            if pos[q] == len(qs[q]):
+                continue
+            o = ops[qs[q][pos[q]]]
+            r = rdy[q]
+            if r is None:
+                r = free[q]
+                for j in o["hard"]:
+                    d = done[j]
+                    if d < 0:
+                        r = None
+                        break
+                    if d + hop > r:
+                        r = d + hop
+                if r is None or any(done[j] < 0 for j in o["soft"]):
+                    continue
+                rdy[q] = r
+            for b in o["banks"]:
+                if b in bank and bank[b][0] != q and done[bank[b][1]] + hop > r:
+                    r = done[bank[b][1]] + hop
+            if r < bs:
+                best, bs = q, r
+        if best < 0:
+            return None, 1e18
+        i = qs[best][pos[best]]
+        o = ops[i]
+        for b in o["banks"]:
+            if fix and b in bank and bank[b][0] != best:
+                o["dep"].add(bank[b][1])
+            bank[b] = (best, i)
+        o["t0"] = bs
+        free[best] = bs + o["ns"]
+        done[i] = bs + o["ns"] + o["lat"]
+        pos[best] += 1
+        rdy[best] = None
+        order.append(i)
+    return order, max(done)
+
+
+def prepared():
+    ops = plan()
+    ref = plan()
+    schedule(ref)
+    depend(ops)
+    tau = {}
+    mid = min(o["t0"] for o in ref if o["step"] == 3 and o["kind"] == "send")
+    for s in (-1, 3, 4, 5, 0):
+        t0 = 0.0 if s < 0 else min(o["t0"] for o in ref if o["step"] == s and o["kind"] == "send" and o["args"][0] == "p")
+        for o in ref:
+            if o["step"] == s:
+                tau.setdefault(label(o), o["t0"] - t0 + (0.0 if s < 0 else 12450.0))
+    at = {"s": 0.0, "v": 1000.0}
+    for e, a, b in PAR["pieces"]:
+        d = 60 + 26.0 * (b - a)
+        tau[e + ("cp" if e == "v" else "act") + ".X.%d" % (16 * a)] = at[e]
+        tau["tmm.sum.%d" % (16 * a)] = at[e] + d + 50
+        tau["vscan.PT.%d" % (16 * a + 3)] = at[e] + d + 700
+        at[e] += d + (500.0 if e == "v" else 0.0)
+    tau.update(TAU)
+    for o in ops:
+        o["id"] = label(o)
+        o["hard"] = sorted(o["dep"] - o["soft"])
+    return ops, tau
+
+
+def refine(ops, tau, rounds, seed=12345):
+    st = sorted(k for k in tau if k[0] != "p")
+    pr = sorted(k for k in tau if k[0] == "p" and "dma" not in k)
+    x = [seed]
+
+    def rnd():
+        x[0] = (x[0] * 6364136223846793005 + 1442695040888963407) % (1 << 64)
+        return (x[0] >> 11) / float(1 << 53)
+    best = simulate(ops, tau)[1]
+    for _ in range(rounds):
+        pool = pr if rnd() < 0.12 else st
+        old = {}
+        for _k in range(2 if rnd() < 0.3 else 1):
+            k = pool[int(rnd() * len(pool))]
+            old.setdefault(k, tau[k])
+            tau[k] += (1 if rnd() < 0.5 else -1) * math.exp(4 + rnd() * (3.6 if pool is st else 4.5))
+        v = simulate(ops, tau)[1]
+        if v <= best + 5:
+            best = v
+        else:
+            tau.update(old)
+    return best
+
+
+_CACHE = {}
+
+
+def rank_program(g, core, T, topo):
+    rank = T.rank_of(core)
+    if rank is None:
+        return
+    if not _CACHE:
+        _CACHE["ops"], tau = prepared()
+        refine(_CACHE["ops"], tau, PAR["rounds"], PAR["seed"])
+        _CACHE["order"] = simulate(_CACHE["ops"], tau, True)[0]
+    ops, order = _CACHE["ops"], _CACHE["order"]
+    cores = list(T.cores)
+    n = len(cores)
+    Q = {"v": g.vector, "s": g.scalar, "t": g.tensor, "g": g, "y": g.sync}
+
+    def ap(a):
+        if not is_ap(a):
+            return a
+        if a[0] == "@":
+            return ap(a[1]).indirect(ap(a[2]))
+        if a[0] in ("in", "out"):
+            return T[a[1]][:]
+        if a[5] == 1:
+            return T[a[0]][a[1]:a[2], a[3]:a[4]]
+        return T[a[0]][a[1]:a[2], a[3]:a[4]:a[5]]
+
+    def maskof(es):
+        return sum(1 << e for e in es)
+
+    def peers(kind):
+        return list(range(1, n)) if kind == "c" else [1]
+
+    def share(src, dst, kind, d):
+        es = topo.engines(src, dst)
+        if kind == "c":
+            k = len(es) // 4
+            return es[k * (d - 1):k * d]
+        return es
+
+    needed = set()
+    for o in ops:
+        needed |= o["dep"] - o["soft"]
+    count = {e: 0 for e in "vstg"}
+    mark, known, totals, clock = {}, {e: {} for e in Q}, {}, {}
+    nd = [0]
+    for i in order:
+        o = ops[i]
+        e, k, a = o["eng"], o["kind"], o["args"]
+        if k == "recv":
+            tot = sum(len(share(cores[(rank - d) % n], core, a[0], d)) for d in peers(a[0]))
+            mark[i] = ("r%s%d" % a, tot)
+            totals[mark[i][0]] = tot
+            clock[i] = {}
+            continue
+        q, kn = Q[e], known[e]
+        want = {}
+        for j in o["dep"] - o["soft"]:
+            s, v = mark[j]
+            if v > want.get(s, (0, 0))[0]:
+                want[s] = (v, j)
+        for s, (v, j) in sorted(want.items(), key=lambda x: -ops[x[1][1]]["t0"]):
+            if kn.get(s, 0) < v:
+                q.wait_ge(T.sem[s], v)
+                kn[s] = v
+                for s2, v2 in clock[j].items():
+                    if kn.get(s2, 0) < v2:
+                        kn[s2] = v2
+        clock[i] = dict(kn)
+        if k == "send":
+            kind, t, src = a
+            tr = []
+            for d in peers(kind):
+                dst = cores[(rank + d) % n]
+                rid, pid, _ = topo.addr(dst)
+                es = share(core, dst, kind, d)
+                if kind == "c":
+                    land = A("SC_I", 12 * t + 4 * (d - 1), 12 * t + 4 * (d - 1) + 1)
+                else:
+                    land = ("SP_I",) + src[1:]
+                tr.append((rid, pid, es, land))
+                totals["sent"] = totals.get("sent", 0) + len(es)
+            sem = T.sem["r%s%d" % (kind, t)]
+            if len(tr) == 1:
+                rid, pid, es, land = tr[0]
+                g.remote_dma(ap(land), ap(src), sem, T.sem.sent, pid, rid, maskof(es))
+            else:
+                g.remote_dma_fused([RemoteDMATransfer(dst_ids=[DstId(rid=rid, pnc=pid)], dma_engine_mask=maskof(es), remote_sem=sem,
+                                                      src=ap(src), dst=ap(land)) for rid, pid, es, land in tr], local_sem=T.sem.sent)
+            continue
+        if k == "dma":
+            s = "d%d" % nd[0]
+            nd[0] += 1
+            q.dma_start(ap(a[0]), ap(a[1])).then_inc(T.sem[s], 16)
+            mark[i] = (s, 16)
+            totals[s] = 16
+            continue
+        if k == "cp":
+            r = q.tensor_copy(ap(a[0]), ap(a[1]))
+        elif k == "tt":
+            r = q.tensor_tensor(ap(a[0]), ap(a[1]), ap(a[2]), a[3])
+        elif k == "ts":
+            if a[5] is None:
+                r = q.tensor_scalar(ap(a[0]), ap(a[1]), ap(a[2]), None, a[4])
+            else:
+                r = q.tensor_scalar(ap(a[0]), ap(a[1]), ap(a[2]), ap(a[3]), a[4], a[5])
+        elif k == "scan":
+            r = q.tensor_tensor_scan(ap(a[0]), ap(a[1]), ap(a[2]), 0.0, a[3], a[4])
+        elif k == "mset":
+            r = q.memset(ap(a[0]), a[1])
+        elif k == "red":
+            r = q.tensor_reduce(ap(a[0]), ap(a[1]), AxisListType.X, ALU.add, negate=True)
+        elif k == "act":
+            r = q.activation(ap(a[0]), ap(a[1]), a[2], bias=ap(a[3]), scale=ap(a[4]))
+        elif k == "iota":
+            if SCRATCH[a[0][0]][2] == I32:
+                r = q.iota(ap(a[0]), a[1], a[2], a[3])
+            else:
+                r = q.iota(ap(a[0]), a[1], a[2], a[3], allow_small_or_imprecise_dtypes=True)
+        else:
+            its = a[0]
+            for m, (x, l, y) in enumerate(its):
+                r = q.matmul(ap(x), ap(l), ap(y), a[1] and m == 0, a[2] and m == len(its) - 1)
+        if i in needed:
+            count[e] += 1
+            r.then_inc(T.sem["e" + e], 1)
+            mark[i] = ("e" + e, count[e])
+            totals["e" + e] = count[e]
+    for s, v in totals.items():
+        if known["g"].get(s, 0) < v:
+            g.wait_ge(T.sem[s], v)

@@ -4,59 +4,55 @@ from concourse.mybir import AluOpType as ALU, AxisListType, ActivationFunctionTy
 
 NS = 6
 F32, BF, F16, I32, U16 = "float32", "bfloat16", "float16", "int32", "uint16"
-EXT, IDS = 1024, 1280
-PW = 100
+DEAD = 288
+NW = 304
+ZR = 1536
+BIG, LOWER = 32768.0, -16384.0
 
 SB = {
-    "NB": (4096, I32), "QT": (4112, BF), "W0": (256, F32), "LO": (6, F32), "HI": (6, F32),
-    "SI": (256, I32), "UI": (1536, I32), "CI": (1536, I32),
-    "S0F": (256, F32), "UB": (1536, BF), "CB": (1792, BF), "CW": (96, BF),
-    "PI": (1, I32), "PJ": (4, I32), "PF": (8, F32), "GQ": (144, F32), "IQ": (144, F32),
-    "C16": (256, F32), "Q4": (256, F32), "IOT": (256, F32), "TMP": (256, F32), "TM2": (256, F32),
-    "EW32": (160, F32), "EWB": (160, BF), "BO32": (144, F32), "BOB": (128, BF), "RM": (16, F32),
-    "UH": (6 * 144, F16), "UB16": (2048, BF), "I32W": (144, F32), "I16W": (144, F16), "IB": (128, BF),
-    "I4": (128, BF), "I16": (128, BF), "I4096": (128, BF), "IM256": (128, BF), "IM1024": (128, BF), "I64": (128, BF), "IM32": (128, BF),
-    "ZB": (128, BF), "TB": (128, BF), "TBR": (128, BF), "VJ": (384, BF), "D32": (128, F32),
-    "MASK": (256, BF), "MASKN": (256, BF), "RST": (256, F32), "RS4": (256, F32), "RS32": (32, F32),
-    "C3": (64, F32), "C4": (64, F32), "CIN": (34, F32), "M16": (16, BF), "THR": (1, F32),
-    "G8": (128, BF), "G832": (128, F32), "E8": (144, BF), "HB": (1, F32),
-    "X": (4608, BF), "PT": (4608, F32), "TS": (256, F32), "US": (256, F32), "PG": (256, F32),
-    "CMP": (768, BF), "LT": (48, BF), "LL": (48, U16), "L4": (64, U16), "SB16": (16, BF),
-    "BS": (16, BF), "R": (256, F32), "XG": (768, BF), "C2": (768, BF), "GE": (256, F32), "M": (256, F32),
-    "SC": (288, F32), "LW": (18, U16), "NK": (288, F32), "EQ": (6 * 288, BF), "OU": (288, U16),
-    "OF": (256, F32), "WT": (296, F32), "HT": (296, F32), "WG": (256, F32), "HC": (256, F32), "H16": (288, F16),
-    "FL": (512, BF), "CL": (256, BF), "FG": (32, BF), "SN": (32, BF), "E1": (16, BF), "POS": (16, U16),
-    "TT": (1536, F32), "SM1": (32, F32), "SM2": (32, F32), "SL": (2, U16), "NL": (16, BF),
-    "SV": (16, F32), "FF": (1, F32), "LF": (2, F32), "LH": (12, F32),
-    "IDX": (16, U16), "SRB": (256, BF), "SRC": (16, U16), "FW": (16, BF), "YW": (256, F32), "YH": (256, F32),
-    "SC_O": (NS * 4, F32), "SC_I": (NS * 12, F32), "SP_O": (NS * PW, F32), "SP_I": (NS * PW, F32),
+    "NB": (4096, I32), "QT": (4112, BF), "LH": (16, F32), "SI": (256, I32), "UI": (1536, I32), "CI": (1536, I32),
+    "S0F": (256, F32), "U8": (1536, BF), "CB": (1792, BF), "PJ3": (768, F32), "TH": (288, F32), "TH2": (96, F32),
+    "PI": (1, I32), "PJ": (4, I32), "PF": (8, F32), "GQ": (144, F32), "IQ": (144, F32), "C16": (48, F32),
+    "IOT": (256, F32), "IOB": (256, F32), "IOX": (288, F32), "TMP": (64, F32), "PK": (128, F32),
+    "EWB": (144, BF), "E0B": (144, BF), "BO32": (144, F32), "BOB": (128, BF), "BON": (128, BF), "RM": (16, F32),
+    "UH": (16 * 144, F16), "I32W": (144, F32), "IBW": (144, BF),
+    "I4": (128, BF), "I16": (128, BF), "I4096": (128, BF), "IMW": (144, BF), "IMH": (128, BF),
+    "I16F": (144, F16), "D32": (128, F16), "VJ": (384, BF), "THR": (1, F32), "EW32": (160, F32), "B4": (1160, F32),
+    "THB": (256, F32), "GE": (256, F32), "M": (296, F32), "OF": (256, F16), "DG": (128, BF), "TBZ": (128, BF), "TBR": (128, BF),
+    "RS4": (256, F32), "RS48": (48, F32), "C64": (64, BF), "C80": (80, BF), "CIN": (52, BF), "M16": (48, F32), "TBP": (128, BF), "G": (16, BF), "CWB": (16, BF),
+    "CW": (32, F32), "G8": (128, BF), "G832": (128, F32), "E8": (144, BF),
+    "X": (4624, BF), "PT": (1160, F32), "TS": (256, F32), "PG": (256, F32), "CMP": (768, BF), "LT": (48, BF), "LT2": (48, BF),
+    "LL": (64, U16), "L": (80, U16), "LS": (16, U16), "SB16": (16, BF), "R": (256, F32), "XG": (768, BF), "C2": (768, BF),
+    "SC": (288, F32), "LW": (18, U16), "NK": (NW, F32), "EQ": (6 * 288, BF), "OU": (288, U16),
+    "WT": (296, F32), "WN": (296, F32), "HT": (296, F32), "HC": (256, F16), "FL": (768, BF), "FG": (48, BF), "DB": (16, BF),
+    "SN": (48, BF), "E": (48, BF), "HF": (296, F32), "WG": (256, F32), "PO": (32, U16), "TT": (2048, F32), "SM": (32, F32), "SL": (2, U16), "SV": (8, F32),
+    "SRB": (256, BF), "FW": (16, F16), "YW": (256, F32), "YH": (256, F32),
+    "SC_O": (NS * 8, BF), "SC_I": (NS * 24, BF), "SP_O": (NS * 96, F32), "SP_I": (NS * 96, F32),
+    "HA": (32, F16),
 }
-SB.update({"W0": (816, F32), "W1": (816, F32), "NK": (288, F16), "OT": (288, F32), "THB": (256, F32), "LL": (64, U16), "L4": (96, U16),
-           "C4": (96, F32), "FL": (768, BF), "FG": (48, BF), "I512": (128, BF), "PJ3": (768, F32)})
-for _n in ("US", "UB16", "MASKN", "WT", "BS", "CL", "SRC"):
-    del SB[_n]
-PACK = {n: 16 * i for i, n in enumerate(["FA", "FB", "FC", "FD", "FE", "Q1", "Q2", "Q3", "Q5", "Q6", "CWR", "IDC", "M16F"])}
-SB["SMALL"] = (16 * len(PACK), F32)
 SCRATCH = {k: ("sbuf", [128, v[0]], v[1]) for k, v in SB.items()}
 for _k in range(8):
     SCRATCH["K%d" % _k] = ("psum", [128, 512], F32)
 
-NDMA = 24
+NDMA = 32
 SEMAPHORES = (["ev", "es", "et", "eg", "sent"] + ["d%d" % i for i in range(NDMA)]
-              + ["rc%d" % t for t in range(NS - 1)] + ["rp%d" % t for t in range(NS)] + ["rw%d" % (NS - 1)])
+              + ["rc%d" % t for t in range(NS - 1)] + ["r%s%d" % (k, t) for k in "p" for t in range(NS)])
 
 PAR = dict(
-    pieces=[("s", 0, 64), ("s", 64, 128), ("v", 128, 160), ("v", 160, 192), ("s", 192, 240), ("v", 256, 288), ("s", 240, 256)],
-    halves=[(0, 128), (128, 256)], soft=False, vj=-1, rounds=8000, seed=2)
-COST = dict(cyc=1.04, pe=0.55, gat=1.56, sca=3.8, hop=90.0, dma=2000.0, rem=2600.0, iss=900.0, look=60.0)
+    pieces=[("*", a, a + 32) for a in range(0, 256, 32)] + [("*", 256, 272), ("*", 272, 288)], l1="ssss", wg=False,
+    c1=[(0, 128), (128, 256)], c3=[(0, 128), (128, 256)], c4=[(0, 128), (128, 256)], nk="*", nka="*", hc="*", xg="***", rounds=(8000, 20000, 15000, 5000),
+    bank=dict(sums=[(4, 0), (3, 0), (4, 128), (3, 128), (5, 0), (4, 256), (5, 128), (3, 0), (5, 256), (4, 0)], t=(3, 0),
+              hb=[(0, 0), (0, 256), (1, 0), (1, 256), (2, 256)], xs=[[(4, 0), (4, 128), (4, 256)], [(5, 0), (5, 128), (5, 256)]],
+              v1=[(4, 384), (5, 384)], ge=[(6, 128), (7, 128)], ll=[(6, 0), (7, 0)], hn=[(4, 384), (5, 384)], d=(3, 256), ht=(3, 0),
+              of=[(6, 128), (7, 128)], fl=(2, 0), rank=(2, 48), sb=(2, 100), l=(2, 116), fw=(2, 196), cnt=(7, 304), rot=(7, 320),
+              fb=(0, 0), ha=(1, 0), hna=(2, 224), ofa=(6, 256)))
+COST = dict(cyc=0.92, pe=0.48, gat=1.56, sca=3.8, hop=165.0, dma=2000.0, rem=3000.0, iss=1100.0, look=60.0)
 
 
-def A(name, c0=0, c1=None, step=1, p0=0, p1=128):
-    if name in PACK:
-        return ("SMALL", p0, p1, PACK[name], PACK[name] + 16, 1)
+def A(name, c0=0, c1=None, step=1, p0=0, p1=128, ps=1):
     if c1 is None:
         c1 = SCRATCH[name][1][1]
-    return (name, p0, p1, c0, c1, step)
+    return (name, p0, p1, c0, c1, step, ps)
 
 
 def IND(win, off):
@@ -77,8 +73,17 @@ def size(a):
     return {F32: 4, I32: 4}.get(SCRATCH[a[0]][2], 2)
 
 
+def landing(kind, t, src, d):
+    if kind == "c":
+        return A("SC_I", 24 * t + 8 * (d - 1), 24 * t + 8 * (d - 1) + 2)
+    return (src[0][:3] + "I",) + src[1:]
+
+
 def plan():
-    ops, now = [], [-1]
+    ops, now, tag, B = [], [-1], ["", {}], PAR["bank"]
+
+    def at(name):
+        tag[0] = name
 
     def add(eng, kind, args, outs, ins, ns, lat=0.0):
         rd, wr = [], []
@@ -91,7 +96,10 @@ def plan():
                 rd.append(a[2])
             else:
                 wr.append(a)
-        ops.append(dict(step=now[0], eng=eng, kind=kind, args=args, rd=rd, wr=wr, ns=ns, lat=lat))
+        key = (now[0], eng, tag[0])
+        tag[1][key] = tag[1].get(key, -1) + 1
+        name = "%s%s.%s%d" % ({-1: "p", NS - 1: "z"}.get(now[0], ""), eng, tag[0], tag[1][key])
+        ops.append(dict(step=now[0], eng=eng, kind=kind, args=args, rd=rd, wr=wr, ns=ns, lat=lat, id=name))
         return ops[-1]
 
     def vcost(out, ins, k=1.0):
@@ -114,8 +122,8 @@ def plan():
     def ts(out, a, s1, op0, s2=None, op1=None):
         add("v", "ts", (out, a, s1, s2, op0, op1), [out], [a, s1, s2], vcost(out, [a]))
 
-    def scan(out, d0, d1, op0, op1):
-        add("v", "scan", (out, d0, d1, op0, op1), [out], [d0, d1], vcost(out, [d0, d1]))
+    def scan(out, d0, d1, op0, op1, first=0.0):
+        add("v", "scan", (out, d0, d1, op0, op1, first), [out], [d0, d1], vcost(out, [d0, d1]))
 
     def mset(out, c):
         add("v", "mset", (out, c), [out], [], max(64, width(out) * size(out) / 4) * COST["cyc"])
@@ -123,17 +131,39 @@ def plan():
     def act(out, in_, func=ACT.Identity, bias=0.0, scale=1.0):
         add("s", "act", (out, in_, func, bias, scale), [out], [in_, bias, scale], vcost(out, [in_], 1.001) + 15)
 
+    def move(e, out, in_, bias=0.0, scale=1.0):
+        if e == "s":
+            act(out, in_, bias=bias, scale=scale)
+            return
+        if bias == 0.0 and scale == 1.0:
+            cp(out, in_)
+        elif scale == 1.0:
+            ts(out, in_, bias, ALU.add)
+        elif bias == 0.0:
+            ts(out, in_, scale, ALU.mult)
+        else:
+            ts(out, in_, scale, ALU.mult, bias, ALU.add)
+        if e == "*":
+            either((out, in_, ACT.Identity, bias, scale))
+
+    def either(args):
+        o = ops[-1]
+        o["alt"] = [(o["eng"], o["kind"], o["args"], o["ns"]), ("s", "act", args, vcost(args[0], [args[1]], 1.001) + 15)]
+
     def iota(out, pat, base=0, ch=0):
         add("g", "iota", (out, pat, base, ch), [out], [], 130 + 2 * width(out) * COST["cyc"])
 
-    def mm(items, start, stop=True):
+    def mm(items, start=True, stop=True):
         ns = sum(max(64, width(r)) * (4 if size(r) == 4 else 1) * COST["pe"] for o, l, r in items)
         tok = ("grp" + items[0][0][0], 0, 128, 0, 1, 1)
         op = add("t", "mm", (items, start, stop), [o for o, l, r in items], [x for o, l, r in items for x in (l, r)], ns, 40.0)
-        op["wr"].append(tok)
+        if tok[0] in ("grpK6", "grpK7"):
+            op["wr"].append(tok)
+        else:
+            assert start and stop
 
-    def dma(eng, out, in_, ns, outs, ins):
-        add(eng, "dma", (out, in_), outs, ins, 60.0, ns)
+    def dma(eng, out, in_, ns=COST["dma"]):
+        add(eng, "dma", (out, in_), [out] if out[0] != "out" else [], [in_] if in_[0] != "in" else [], 60.0, ns)
 
     def send(kind, t, src, land):
         tok = ("tok%s%d" % (kind, t), 0, 128, 0, 1, 1)
@@ -141,308 +171,351 @@ def plan():
         add("x", "recv", (kind, t), [land], [tok], 0.0, COST["rem"] - COST["iss"])
 
     def K(b, c0, c1, step=1):
+        if is_ap(b):
+            b, c0, c1 = b[0], b[1] + c0, b[1] + c1
         return A("K%d" % b, c0, c1, step)
 
-    sel = lambda r: A("EWB", 31 - r, 159 - r)
-    sel32 = lambda r: A("EW32", 31 - r, 159 - r)
-    unw = lambda r: A("UB16", 128 * r, 128 * r + 128)
+    sel = lambda r: A("EWB", 15 - r, 143 - r)
+    sel0 = lambda r: A("E0B", 15 - r, 143 - r)
+    uh = lambda r, turn=0: A("UH", 144 * r + 16 - turn, 144 * r + 144 - turn)
     col = lambda n, j: A(n, j, j + 1)
-    P_, PG, PR, PNZ = col("PF", 0), col("PF", 1), col("PF", 2), col("PF", 3)
-    BO, IW = A("BO32", 16, 144), A("I32W", 16, 144)
-    IQ = A("IQ", 16, 144)
+    P_, PG, PR, LWB, SLB, HB = [col("PF", j) for j in range(6)]
+    BO, IW, IB, IQ = A("BO32", 16, 144), A("I32W", 16, 144), A("IBW", 16, 144), A("IQ", 16, 144)
+    SRC = A("L", 64, 80)
+    IM1 = A("IMW", 16, 144)
 
-    dma("y", A("SI", p1=8), ("in", "s0"), 1800, [A("SI", p1=8)], [])
-    dma("y", A("NB"), ("in", "nb"), 8500, [A("NB")], [])
-    dma("y", A("QT", 0, 4096), ("in", "qs"), 12000, [A("QT", 0, 4096)], [])
-    for n, s in ((A("CI", p1=8), "coin"), (A("UI", p1=8), "us"), (A("W1", 0, 256), "w0"), (A("LO"), "lo"), (A("HI"), "hi")):
-        dma("s", n, ("in", s), 2500, [n], [])
+    at("load")
+    mset(A("LH"), 0.0)
+    dma("y", A("SI", p1=8), ("in", "s0"), 1800)
+    dma("y", A("NB"), ("in", "nb"), 8500)
+    dma("y", A("QT", 0, 4096), ("in", "qs"), 12000)
+    for n, s in ((A("CI", p1=8), "coin"), (A("UI", p1=8), "us"), (A("WT", 0, 256), "w0"), (A("LH", 0, 6), "lo"), (A("LH", 8, 14), "hi")):
+        dma("s", n, ("in", s), 2500)
 
+    at("c")
     iota(A("PI"), [[0, 1]], 0, 1)
-    iota(A("C16"), [[0, 16], [1, 16]])
     iota(A("GQ", 16, 144), [[16, 8], [0, 16]])
     iota(A("IOT"), [[1, 256]])
-    iota(A("Q4"), [[0, 64], [1, 4]])
-    iota(A("M16F"), [[16, 16]])
-    iota(A("C3", 0, 48), [[-1, 3], [0, 16]], 2304 + 3)
-    iota(A("C4", 0, 64), [[4, 4], [0, 16]], 2304 + 3)
-    S160 = A("IOT", 0, 160)
+    iota(A("C16"), [[0, 3], [1, 16]])
+    iota(A("M16", 0, 32), [[704, 2], [16, 16]], -144)
+    iota(A("M16", 32, 48), [[16, 16]], -144)
+    iota(A("C64", 16, 64), [[-1, 3], [0, 16]], 3)
+    iota(A("C80", 0, 64), [[1, 4], [0, 16]])
     mset(A("GQ", 0, 16), 112.0)
-    mset(A("C3", 48, 64), 0.0)
-    cp(IQ, A("IOT", 0, 128))
-    cp(A("IQ", 0, 16), A("IOT", 112, 128))
+    move("*", IQ, A("IOT", 0, 128))
+    move("*", A("IQ", 0, 16), A("IOT", 112, 128))
     ts(col("PJ", 0), A("PI"), 112, ALU.bitwise_and)
     ts(col("PJ", 1), A("PI"), 15, ALU.bitwise_and)
-    ts(col("PJ", 2), A("PI"), 12, ALU.bitwise_and)
-    ts(col("PJ", 3), A("PI"), 3, ALU.bitwise_and)
     cp(P_, A("PI"))
     cp(A("PF", 1, 3), A("PJ", 0, 2))
-    cp(A("PF", 4, 6), A("PJ", 2, 4))
-    ts(PNZ, PR, 0.5, ALU.is_gt)
-    ts(col("PF", 6), col("PF", 5), 3.0, ALU.is_equal, -2.0, ALU.mult)
-    ts(col("PF", 7), col("PF", 4), -1.0, ALU.mult, 8.5 / 8, ALU.add)
-    tt(A("THR"), col("PF", 6), col("PF", 7), ALU.add)
     ts(A("BO32"), A("GQ"), PG, ALU.is_equal)
-    act(A("BOB"), BO)
+    move("*", A("BOB"), BO)
+    move("*", A("BON"), BO, scale=-1.0)
     ts(A("RM"), A("IOT", 0, 16), PR, ALU.is_equal)
     ts(A("I32W"), A("IQ"), P_, ALU.is_equal)
-    ts(A("I16W"), A("IQ"), P_, ALU.is_equal)
-    for n, c in (("IB", 1.0), ("I4096", 4096.0), ("I4", 4.0), ("I16", 16.0), ("IM256", -256.0), ("IM1024", -1024.0),
-                 ("I64", 64.0), ("IM32", -32.0), ("ZB", 0.0), ("I512", 512.0)):
-        act(A(n), IW, scale=c)
-    ts(A("TMP", 0, 160), S160, PG, ALU.subtract, 31.0, ALU.is_equal)
-    ts(A("TM2", 0, 160), S160, PG, ALU.subtract, -97.0, ALU.is_equal)
-    tt(A("EW32"), A("TMP", 0, 160), A("TM2", 0, 160), ALU.add)
-    act(A("EWB"), A("EW32"))
-    ts(A("MASK"), A("C16"), PR, ALU.not_equal, 8192.0, ALU.mult)
-    ts(A("RST"), A("C16"), 0.0, ALU.is_equal, 65536.0, ALU.mult)
-    ts(A("RS4"), A("Q4"), 0.5, ALU.is_gt)
-    ts(A("RS32"), A("C16", 0, 32), 0.5, ALU.is_gt)
-    ts(A("GE", 0, 128, p1=8), A("GQ", 16, 144, p1=8), 1.0 / 16, ALU.mult)
-    ts(A("G832", p1=8), A("GE", 0, 128, p1=8), A("PF", 0, 1, p1=8), ALU.is_equal)
-    ts(A("G8", p1=8), A("G832", p1=8), 8.0, ALU.mult)
-    ts(A("R", 0, 144, p1=8), A("IOT", 0, 144, p1=8), -15.0, ALU.add, 1.0 / 16, ALU.mult)
-    ts(A("E8", p1=8), A("R", 0, 144, p1=8), A("PF", 0, 1, p1=8), ALU.is_equal)
-    ts(A("HB"), PR, 6.5, ALU.is_lt, 2049.0, ALU.mult)
-    ts(A("HB"), A("HB"), -1.0, ALU.add)
-    mset(A("QT", 4096, 4112), 0.0)
-    mset(A("W0", 800, 816), 0.0)
-    mset(A("W1", 800, 816), 0.0)
-    mset(A("C4", 64, 96), 144.0)
-    mset(A("OT", 256, 288), 0.0)
-    mset(A("HT", 256, 296), -1.0)
-    mset(A("X", 4096, 4608), 0.0)
-    for j in range(1, 4):
-        mset(A("SP_O", j, NS * PW, PW), 0.0)
-    for j in range(18):
-        act(A("PT", 256 * j, 256 * j + 256), A("C16"), scale=0.0)
-    ts(A("TS", 0, 128), IQ, 1.0, ALU.add, P_, ALU.is_equal)
-    ts(A("TS", 128, 256), A("TS", 0, 128), PNZ, ALU.mult)
-    tt(A("D32"), IW, A("TS", 128, 256), ALU.subtract)
-    for p in range(5):
-        ts(A("UH", 144 * p, 144 * p + 144), A("BO32"), col("RM", p), ALU.mult)
+    move("*", A("IBW"), A("I32W"))
+    move("*", A("IMW"), A("I32W"), scale=-1.0)
+    for n, c in (("I4096", 4096.0), ("I4", 4.0), ("I16", 16.0), ("IMH", -0.5)):
+        move("*", A(n), IW, scale=c)
+    ts(A("YW", 0, 160), A("IOT", 0, 160), PG, ALU.subtract, 31.0, ALU.is_equal)
+    ts(A("M", 0, 160), A("IOT", 0, 160), PG, ALU.subtract, -97.0, ALU.is_equal)
+    tt(A("EW32"), A("YW", 0, 160), A("M", 0, 160), ALU.add)
+    move("*", A("EWB"), A("EW32", 16, 160))
+    move("*", A("E0B"), A("EW32", 16, 160), scale=col("RM", 0))
+    mset(A("M", 256, 296), 0.0)
+    mset(A("HF", 256, 296), -4096.0)
+    for p in range(16):
+        move("*", A("UH", 144 * p, 144 * p + 144), A("BO32"), scale=col("RM", p))
+    ts(col("PF", 6), PR, 15.0, ALU.add)
+    ts(col("PF", 7), PR, -1.0, ALU.add)
+    c16 = A("C16", 0, 16)
+    ts(A("TMP", 0, 16), c16, PR, ALU.is_equal, LOWER, ALU.mult)
+    ts(A("TMP", 16, 32), c16, col("PF", 6), ALU.is_equal, BIG, ALU.mult)
+    ts(A("TMP", 32, 48), c16, col("PF", 7), ALU.is_equal, BIG, ALU.mult)
+    tt(A("TMP", 48, 64), A("TMP", 0, 16), A("TMP", 16, 32), ALU.add)
+    tt(A("PK", 0, 16), A("TMP", 48, 64), A("TMP", 32, 48), ALU.add)
+    for n in (16, 32, 64):
+        move("*", A("PK", n, 2 * n), A("PK", 0, n))
+    ts(LWB, col("RM", 0), -BIG, ALU.mult, 2048.0 - LOWER, ALU.add)
+    ts(SLB, col("RM", 0), -BIG, ALU.mult, 0.25 - 64.0 - LOWER, ALU.add)
+    ts(HB, PR, 6.5, ALU.is_lt, 2049.0, ALU.mult)
+    ts(HB, HB, -1.0, ALU.add)
+    mset(A("RS4"), 1.0)
+    mset(A("RS4", 0, 256, 4), 0.0)
+    ts(A("RS48"), A("C16"), 0.5, ALU.is_gt)
+    ts(A("SV", 3, 4, p1=8), A("PF", 0, 1, p1=8), 16.0, ALU.mult)
+    ts(A("G832", p1=8), A("GQ", 16, 144, p1=8), A("SV", 3, 4, p1=8), ALU.is_equal)
+    move("*", A("G8", p1=8), A("G832", p1=8), scale=8.0)
+    ts(A("E8", p1=8), A("IOT", 0, 144, p1=8), -15.0, ALU.add, A("SV", 3, 4, p1=8), ALU.is_equal)
+    ts(A("PG", 0, 128), IQ, P_, ALU.is_lt, -1.0, ALU.mult)
+    tt(A("PG", 128, 256), A("PG", 0, 128), BO, ALU.mult)
+    move("*", A("YW", 0, 128), IW, scale=-float(ZR))
+    tt(A("TBZ"), A("PG", 128, 256), A("YW", 0, 128), ALU.add)
+    ts(A("DG"), IW, PR, ALU.mult, -1.0, ALU.mult)
+    tt(A("TBR"), A("PG", 128, 256), A("DG"), ALU.add)
+    move("*", A("CW", 0, 16), A("M16", 0, 16), PR)
+    move("*", A("CWB"), A("CW", 0, 16))
+    mset(A("CIN", 0, 16), float(ZR))
+    mset(A("CIN", 16, 32), 704.0)
+    mset(A("CIN", 32, 36), 0.0)
+    mset(A("CIN", 36, 52), -1024.0)
+    move("*", A("YH", 0, 128), IW, scale=1024.0)
+    tt(A("TBP"), A("PG", 128, 256), A("YH", 0, 128), ALU.add)
+    mset(A("C64", 0, 16), 576.0 - 2304)
+    mset(A("C80", 64, 80), 144.0 - 576)
+    act(A("IOB"), A("IOT"), ACT.Silu, 64.0)
+    ops[-1]["ns"] += 1600.0
+    mset(A("IOX", 0, 256), 208.0 + 111)
+    mset(A("IOX", 256, 288), 64.0 + DEAD)
+    move("*", A("I16F"), A("I32W"))
+    ts(A("GE", 0, 128), IQ, 1.0, ALU.add, P_, ALU.is_equal)
+    ts(col("SV", 4), PR, 0.5, ALU.is_gt)
+    move("*", A("GE", 128, 256), A("GE", 0, 128), scale=col("SV", 4))
+    tt(A("D32"), IW, A("GE", 128, 256), ALU.subtract)
+    mset(A("VJ"), 0.0)
     for j in range(3):
-        x = A("OF", 128 * (j % 2), 128 * (j % 2) + 128)
-        ts(x, A("Q4", 0, 128), float(j), ALU.is_equal, 0.125, ALU.mult)
-        tt(A("VJ", 128 * j, 128 * j + 128), x, BO, ALU.mult)
-    ts(A("WG", 0, 128), IQ, P_, ALU.is_lt, -1.0, ALU.mult)
-    tt(A("TB"), A("WG", 0, 128), BO, ALU.mult)
-    ts(A("WG", 128, 256), IW, PR, ALU.mult)
-    tt(A("TBR"), A("TB"), A("WG", 128, 256), ALU.subtract)
-    ts(A("CWR"), A("M16F"), PR, ALU.add)
-    ts(A("SB16"), A("CWR"), -144.0, ALU.add)
-    mset(A("CIN", 0, 16), 1024.0)
-    ts(A("CIN", 16, 32), A("CWR"), 511.0, ALU.add)
-    mset(A("CIN", 32, 34), 0.0)
-    ts(A("IDC"), A("CWR"), float(IDS), ALU.add)
-    ts(A("M16"), A("M16F"), -1.0, ALU.mult)
-    for j in range(4):
-        act(A("TT", 256 * j, 256 * j + 256), A("C16"), scale=0.0)
-    ts(A("TT", EXT, IDS), A("IOT"), 256.0, ALU.add, 287.0, ALU.min)
-    act(A("TT", IDS, 1536), A("IOT"))
-    mset(A("FF"), 1.0)
+        move("*", A("VJ", 129 * j, 128 * j + 128, 4), A("BOB", j, 128, 4), scale=0.125)
+    ts(col("PJ", 2), A("PI"), 12, ALU.bitwise_and)
+    ts(col("PJ", 3), A("PI"), 3, ALU.bitwise_and)
+    cp(A("SV", 5, 7), A("PJ", 2, 4))
+    ts(col("SV", 6), col("SV", 6), 3.0, ALU.is_equal, -2.0, ALU.mult)
+    ts(col("SV", 5), col("SV", 5), -1.0, ALU.mult, 8.5 / 8, ALU.add)
+    tt(A("THR"), col("SV", 5), col("SV", 6), ALU.add)
+    mset(A("QT", 4096, 4112), 0.0)
+    mset(A("WT", 256, 296), 0.0)
+    mset(A("WN", 256, 296), 0.0)
+    mset(A("HT", 256, 296), -4096.0)
+    mset(A("NK", 256, NW), 0.0)
+    mset(A("X", 4096, 4624), 0.0)
+    mset(A("PT", 1024, 1160), 0.0)
+    mset(A("TH"), 8.5)
+    mset(A("SC_O"), 0.0)
+    at("flat")
+    iota(A("B4"), [[0, 290], [4, 4]])
+    iota(A("TT"), [[0, 2048]], 208)
 
-    ts(A("S0F", p1=8), A("SI", p1=8), -2048.0, ALU.add)
-    mm([(K(0, 0, 256), A("G832", p1=8), A("S0F", p1=8))], True)
-    ts(A("M"), K(0, 0, 256), col("RM", 0), ALU.mult)
-    cp(A("UB", p1=8), A("UI", p1=8))
-    cp(A("CB", 0, 1536, p1=8), A("CI", p1=8))
+    at("s")
+    move("*", A("S0F", p1=8), A("SI", p1=8), -2048.0)
+    mm([(K(0, 0, 256), A("G832", p1=8), A("S0F", p1=8))])
+    move("*", A("HT", 0, 256), K(0, 0, 256), scale=col("RM", 0))
+    for j in range(0, 1536, 512):
+        move("*", A("U8", j, j + 512, p1=8), A("UI", j, j + 512, p1=8))
+        move("*", A("CB", j, j + 512, p1=8), A("CI", j, j + 512, p1=8))
     ts(A("CB", 1536, 1792, p1=8), A("S0F", p1=8), -2048.5, ALU.is_lt)
-    mm([(K(7, 0, 112), A("E8", 15 - r, 143 - r, p1=8), A("CB", r, 1792, 16, p1=8)) for r in range(16)], True)
-    cp(A("CW"), K(7, 0, 96))
-    cp(A("NL"), K(7, 96, 112))
-    mm([(K(7, 128, 144), A("BOB"), A("NL"))], True)
+    mm([(K(7, 0, 112), A("E8", 15 - r, 143 - r, p1=8), A("CB", r, 1792, 16, p1=8)) for r in range(16)])
+    for t in range(NS):
+        move("*", A("TH", 48 * t, 48 * t + 16), K(7, 16 * t, 16 * t + 16), 8.5, 100.0)
+        move("*", A("TH", 48 * t + 32, 48 * t + 48), K(7, 16 * t, 16 * t + 16), 108.5, -100.0)
+    move("*", A("DB"), K(7, 96, 112))
+    move("*", A("CW", 16, 32), K(7, 96, 112), scale=1024.0)
+    tt(A("CW", 16, 32), A("CW", 16, 32), A("CW", 0, 16), ALU.add)
+    ts(A("SB16"), A("CW", 16, 32), 144.0, ALU.min)
+    mm([(K(7, 128, 144), A("BOB"), A("DB"))])
     add("v", "red", (col("SV", 2), K(7, 128, 144)), [col("SV", 2)], [K(7, 128, 144)], 64 * COST["cyc"])
-    cp(A("LH", 0, 6), A("LO"))
-    cp(A("LH", 6, 12), A("HI"))
-    cp(A("LF"), A("LH", 0, 12, 6))
-    DD, NDN, QQ, TH = col("SV", 0), col("SV", 2), col("SV", 3), col("SV", 4)
+    cp(col("SC_O", 1), col("SV", 2))
 
-    def history(t):
-        it = [(K(4, 0, 256), A("I16W", 16, 144), A("H16", 0, 256))] if t >= 0 else []
-        mm(it + [(K(4, 0, 256), sel32(t + 1), A("M"))], True)
-        act(A("HT", 0, 256), K(4, 0, 256), bias=A("HB") if t == NS - 1 else 0.0)
-
-    def neighbours(t, a, b, m, bo, uo, sm, hb, of):
-        w = b - a
-        mm([(sm, A("IB"), A("MASK", 0, w))], True, False)
-        mm([(sm, bo, m)], False)
-        scan(A("SC", a, b), A("RST", 0, w), sm, ALU.add, ALU.min)
+    def neighbours(t, a, b, hb, of, e):
+        scan(A("SC", a, b), hb(t + 1), A("PK", 0, b - a), ALU.min, ALU.add, BIG)
         lw = A("LW", a // 16, b // 16)
-        ts(lw, A("SC", a + 15, b, 16), 2048.0, ALU.add, 4095.0, ALU.min)
-        mm([(hb(t + 1), bo, m)], True)
+        ts(lw, A("SC", a + 15, b, 16), LWB, ALU.add, 4095.0, ALU.min)
         nk = A("NK", a, b)
-        ts(nk, IND(A("NB"), lw), -2048.0, ALU.add)
-        mm([(of, A("I16W", 16, 144), nk)], True, False)
-        for p in range(t + 2):
-            e = A("EQ", 288 * p + a, 288 * p + b)
-            tt(e, nk, hb(p), ALU.is_equal)
-            mm([(of, A("I4096"), e)], False, p == t + 1)
+        move(e, nk, IND(A("NB"), lw), -2048.0)
+        mm([(of, IW, nk)], True, False)
+        name = tag[0]
+        at(name + "e")
+        for p in range(t + 1, -1, -1):
+            eq = A("EQ", 288 * p + a, 288 * p + b)
+            tt(eq, nk, hb(p), ALU.is_equal)
+            mm([(of, A("I4096"), eq)], False, p == 0)
+        at(name + "o")
         ts(A("OU", a, b), of, 2048.0, ALU.add, 4096.0, ALU.min)
-        act(A("OT", a, b), of)
 
     def own(t):
+        at("hb")
         for p in range(t + 1):
-            mm([(K(p // 2, 256 * (p % 2), 256 * (p % 2) + 256), A("UH", 144 * p + 16, 144 * p + 144), A("H16", 0, 256))], True)
-        for h, (a, b) in enumerate(PAR["halves"]):
-            neighbours(t, a, b, A("M", a, b), BO, 16, K(5 + h % 2, a, b),
-                       lambda p: K(p // 2, 256 * (p % 2) + a, 256 * (p % 2) + b), K(3, 256 + a, 256 + b))
+            mm([(K(B["hb"][p], 0, 256), uh(p), A("HC"))])
+        for h, (a, b) in enumerate(PAR["c3"]):
+            at("n%d_" % h)
+            hn = K(B["hn"][h % 2], 0, b - a)
+            mm([(hn, BO, A("M" if t >= 0 else "HT", a, b))])
+            neighbours(t, a, b, lambda p: hn if p == t + 1 else K(B["hb"][p], a, b), K(B["of"][h % 2], 0, b - a), PAR["nk"])
 
-    def lists(t):
-        last = t == NS - 1
-        it = [(K(7, 160, 256), IW, A("C4"))]
-        it += [(K(7, 160 + 16 * j, 176 + 16 * j), A("I16" if j < 4 else "IB"), A("SB16")) for j in range(4 if last else 0, 6)]
-        if t >= 0:
-            it += [(K(7, 240, 256), A("I512"), A("FW"))]
-        if last:
-            mm(it, True, False)
-            mm([(K(7, 224, 240), A("I4096"), A("NL")), (K(7, 240, 256), A("I4096"), A("NL"))], False)
-            ts(SRC, K(7, 224, 240), 288.0, ALU.min)
-            ts(WL, K(7, 240, 256), 800.0, ALU.min)
-        else:
-            mm(it, True)
-            cp(A("L4"), K(7, 160, 256))
+    def lists():
+        at("l")
+        mm([(K(B["l"], 0, 80), IB, A("C80"))] + [(K(B["l"], 16 * j, 16 * j + 16), A("I4") if j < 4 else IB, A("SB16")) for j in range(5)])
+        ts(A("L"), K(B["l"], 0, 80), 576.25, ALU.add)
 
-    SRC, WL = A("L4", 64, 80), A("L4", 80, 96)
+    def steps():
+        at("d")
+        move("*", A("OF"), IND(A("NK"), SRC))
+        mm([(K(B["d"], 0, 256), A("D32"), A("OF"))])
+
+    def history():
+        move("*", A("HF", 0, 256), IND(A("HT"), SRC))
+        move("*", A("HC"), A("HF", 0, 256))
+        if PAR["wg"]:
+            move("*", A("WG"), IND(A("WT"), SRC), scale=2.0 ** -11)
+
     own(-1)
-    history(-1)
-    lists(-1)
-    act(A("HC"), A("HT", 0, 256))
-    act(A("OF"), A("OT", 0, 256))
+    lists()
+    steps()
+    at("f")
+    history()
 
     for t in range(NS):
         last = t == NS - 1
         now[0] = t
-        mm([(K(4, 0, 256), A("G8", p1=8), A("UB", 256 * t, 256 * t + 256, p1=8))], True)
         for i, (e, a, b) in enumerate(PAR["pieces"]):
             if a >= 256 and t == 0:
                 continue
-            o, x = A("X", 16 * a, 16 * b), IND(A("QT"), A("OU", a, b))
-            if e == "v":
-                cp(o, x)
-            else:
-                act(o, x)
-            k = K(i % 4, 0, 4 * (b - a))
-            mm([(k, A("IB"), A("X", 16 * a + j, 16 * b, 4)) for j in range(4)], True)
-            scan(A("PT", 16 * a + 3, 16 * b, 4), A("RS4", 0, 4 * (b - a)), k, ALU.mult, ALU.add)
-        mm([(K(4, 256, 512), A("D32"), A("OF"))], True)
-        cp(A("H16", 0, 256), A("HC"))
-        mm([(K(6, 0, 48), A("ZB"), A("MASK", 0, 48)), (K(6, 32, 48), A("I64"), A("NL")),
-            (K(6, 0, 16), A("IM32"), A("CW", 16 * t, 16 * t + 16)), (K(6, 16, 32), A("IM32"), A("NL"))], True, False)
-        pt = lambda j: IND(A("PT"), A("L4", 16 * j, 16 * j + 16))
-        wn, wo = "W%d" % (t % 2), "W%d" % (1 - t % 2)
-        act(A("PG"), pt(3), scale=2.0 ** -11)
-        tt(K(4, 0, 256), A("PG"), K(4, 0, 256), ALU.mult)
-        for j in range(3):
-            pj = A("PJ3", 256 * j, 256 * j + 256)
-            if j == PAR["vj"]:
-                cp(pj, pt(j))
-            else:
-                act(pj, pt(j))
-            tt(A("CMP", 256 * j, 256 * j + 256), pj, K(4, 0, 256), ALU.is_gt)
-        act(A("TS"), K(4, 0, 256))
-        act(A("FL", 512, 768), A("PG"), ACT.Relu, 1.0, -2048.0)
-        tt(A(wn, 0, 256), IND(A(wo, 0, 816 if t else 256), WL), A("PG"), ALU.mult)
-        ts(A("FL", 0, 256), A(wn, 0, 256), col("LF", 0), ALU.is_lt)
-        ts(A("FL", 256, 512), A(wn, 0, 256), col("LF", 1), ALU.is_gt)
-        act(A(wn, 512, 768), A(wn, 0, 256), scale=0.5)
-        act(A(wn, 256, 512), A(wn, 0, 256), scale=2.0)
-        mm([(K(1, 256, 320), IW, A("C3"))] + [(K(1, 256 + 16 * j, 272 + 16 * j), A("I16"), A("SB16")) for j in range(3)], True, False)
-        mm([(K(0, 256, 304), sel(r), A("CMP", r, 768, 16)) for r in range(16)], True)
-        ts(A("LT"), K(0, 256, 304), 8.5, ALU.is_lt)
-        mm([(K(1, 256 + a, 256 + b), A("I4"), A("LT", c, c + b - a))
-            for a, b, c in ((0, 48, 0), (0, 32, 16), (32, 64, 0), (0, 16, 32), (16, 48, 0), (48, 64, 0), (48, 64, 32))], False)
-        cp(A("LL"), K(1, 256, 320))
-        mm([(K(6, 0, 48), sel(r), A("FL", r, 768, 16)) for r in range(16)], False)
-        mm([(K(7, 0, 34), IW, A("CIN"))], True, False)
-        ts(A("FG"), K(6, 0, 48), 8.5, ALU.is_gt)
-        HOLE, HIGH = A("FG", 0, 16), A("FG", 16, 32)
-        tt(HOLE, HOLE, A("FG", 32, 48), ALU.max)
-        scan(A("SN"), A("RS32"), A("FG", 0, 32), ALU.mult, ALU.add)
-        tt(A("E1"), HIGH, A("M16"), ALU.mult)
-        mm([(K(7, 0, 16), A("TB"), HOLE), (K(7, 0, 16), A("IM1024"), HOLE), (K(7, 16, 32), A("TBR"), HIGH),
-            (K(7, 16, 32), A("IM256"), HIGH), (K(7, 16, 32), A("IB"), A("E1"))], False, False)
-        mm([(K(7, 0, 32), A("BOB"), A("SN")), (K(7, 32, 34), A("BOB"), A("SN", 15, 32, 16))], False)
-        NH, NC, HX = K(7, 32, 33), K(7, 33, 34), K(7, 0, 16)
-        po = PW * t
-        ts(A("POS"), K(7, 16, 32), NH, ALU.subtract)
-        act(col("SV", 6), NH, bias=255.0, scale=-1.0)
-        act(DD, NC, bias=col("SV", 6))
-        act(col("SP_O", po), DD, ACT.Relu, -255.0)
-        act(A("Q2"), HX, bias=col("SV", 6))
-        cp(IND(A("TT", 0, EXT), A("POS")), A("IOT"))
-        tt(A("SM1"), A("TT", 256, 288), A("MASK", 0, 32), ALU.add)
-        scan(A("SM2"), A("RST", 0, 32), A("SM1"), ALU.add, ALU.min)
-        cp(A("SL"), A("SM2", 15, 32, 16))
-        act(A("SP_O", po + 4, po + 36), IND(A(wn, 512, 768), A("SL")))
-        act(A("SP_O", po + 36, po + 68), IND(A("HC"), A("SL")))
-        if last:
-            send("w", t, A("SP_O", po, po + 68), A("SP_I", po, po + 68))
-        ts(A("FA"), K(6, 0, 16), -23.5, ALU.is_gt, 0.5, ALU.mult)
-        ts(A("FB"), K(6, 0, 16), -15.5, ALU.is_gt, 0.5, ALU.mult)
-        tt(A("R"), IND(A("PT"), A("LL", 0, 16)), A("TS"), ALU.subtract)
-        xg = lambda i: A("XG", 256 * i, 256 * i + 256)
-        for i in range(3):
-            act(xg(i), IND(A("X"), A("LL", 16 * i, 16 * i + 16)))
-        for i in range(3):
-            mm([(K(i, 0, 256), A("IB"), xg(j)) for j in range(i + 1)], True)
-            c2 = A("C2", 256 * i, 256 * i + 256)
-            tt(c2, K(i, 0, 256), A("R"), ALU.is_lt)
-            mm([(K(3, 0, 256), A("VJ", 128 * (2 - i), 128 * (3 - i)), c2)], i == 0, i == 2)
-        act(A("THB"), IND(A("IOT"), A("LL", 48, 64)), bias=A("THR"))
-        for a, b in PAR["halves"]:
-            tt(A("GE", a, b), K(3, a, b), A("THB", a, b), ALU.is_gt)
-            tt(A("M", a, b), A("GE", a, b), K(4, 256 + a, 256 + b), ALU.mult)
-        cp(A("SP_O", po + 68, po + PW), IND(A("M"), A("SL")))
-        p0 = po + 68 if last else po
-        send("p", t, A("SP_O", p0, po + PW), A("SP_I", p0, po + PW))
-        if not last:
-            act(col("SC_O", 4 * t), NDN, bias=DD, scale=-1.0)
-            send("c", t, col("SC_O", 4 * t), A("SC_I", 12 * t, 12 * t + 12))
-            own(t)
-        history(t)
-        act(QQ, DD, bias=float(EXT - 1), scale=-1.0)
-        ts(A("Q1"), HX, NC, ALU.is_gt, QQ, ALU.mult)
-        tt(A("Q3"), A("Q1"), A("Q2"), ALU.add)
-        tt(A("Q5"), A("Q3"), A("IDC"), ALU.min)
-        cp(A("IDX"), A("Q5"))
-        act(A("SRB"), IND(A("TT"), A("IDX")), bias=-144.0)
-        tt(A("FC"), HOLE, HIGH, ALU.add)
-        tt(A("FE"), A("FA"), A("FB"), ALU.subtract)
-        tt(A("FW"), A("FE"), A("FC"), ALU.max)
-        mm([(K(7, 96, 112), sel(r), A("SRB", r, 256, 16)) for r in range(16)], True)
-        act(A("SB16"), K(7, 96, 112), scale=1.0 / 16)
-        if not last:
-            lists(t)
-        wi = A("SP_I", po + 4, po + 36)
-        dma("y", A(wn, 768, 800, p0=16), A("SP_I", po + 4, po + 36, p1=112), COST["dma"], [A(wn, 768, 800, p0=16)], [wi])
-        dma("y", A(wn, 768, 800, p1=16), A("SP_I", po + 4, po + 36, p0=112), COST["dma"], [A(wn, 768, 800, p1=16)], [wi])
-        cp(A("H16", 256, 288), A("SP_I", po + 36, po + 68))
-        mi = A("SP_I", po + 68, po + PW)
-        if not last:
-            for p in range(t + 1):
-                mm([(K(6, 320 + 32 * p, 352 + 32 * p), A("UH", 144 * p, 144 * p + 128), A("H16", 256, 288))], True)
-            neighbours(t, 256, 288, mi, A("BO32", 0, 128), 0, K(5, 0, 32), lambda p: K(6, 320 + 32 * p, 352 + 32 * p), K(5, 64, 96))
-            act(A("OF"), IND(A("OT"), SRC))
-        mm([(K(6, 288, 320), A("I16W", 0, 128), A("H16", 256, 288)), (K(6, 288, 320), sel32(t + 17), mi)], True)
-        act(A("HT", 256, 288), K(6, 288, 320), bias=A("HB") if last else 0.0)
-        mm([(K(6, 65, 66), A("I32W", 0, 128), col("SP_I", po))], True)
-        ts(TH, K(6, 65, 66), 32.0, ALU.min, NC, ALU.add)
-        ts(A("Q6"), HX, TH, ALU.is_le)
-        tt(A("NL"), HOLE, A("Q6"), ALU.subtract)
-        if not last:
-            ts(NDN, TH, NH, ALU.subtract, 0.0, ALU.min)
-            mm([(K(6, 64, 65), IW, x) for x in [col("SC_O", 4 * t)] + [col("SC_I", 12 * t + 4 * j) for j in range(3)]], True)
-            act(col("SV", 7), K(6, 64, 65), ACT.Sign, -4 * 255.0 - 0.5)
-            act(col("SV", 5), col("SV", 7), bias=1.5, scale=0.5)
-            act(A("FF"), A("FF"), scale=col("SV", 5))
-            act(A("LF"), A("LH", t + 1, 12, 6), scale=A("FF"))
-            act(A("HC"), IND(A("HT"), SRC))
+            at("x%d_" % i)
+            move(e, A("X", 16 * a, 16 * b), IND(A("QT"), A("OU", a, b)))
+            k = K(B["sums"][i % len(B["sums"])], 0, 4 * (b - a))
+            mm([(k, IB, A("X", 16 * a + j, 16 * b, 4)) for j in range(4)])
+            scan(A("PT", 4 * a, 4 * b), A("RS4", 0, 4 * (b - a)), k, ALU.mult, ALU.add)
+        pt = lambda j, a, b: IND(A("PT"), A("L", 16 * j + a // 16, 16 * j + b // 16))
+        for h, (a, b) in enumerate(PAR["c1"]):
+            at("a%d_" % h)
+            w, th = b - a, K(B["t"], a, b)
+            move("*", A("PG", a, b), pt(3, a, b), scale=2.0 ** -11)
+            mm([(th, A("G8", p1=8), A("U8", 256 * t + a, 256 * t + b, p1=8))])
+            tt(th, A("PG", a, b), th, ALU.mult)
+            if "v" in PAR["l1"]:
+                move("*", A("TS", a, b), th)
+            for j in range(3):
+                c = A("CMP", 3 * a + w * j, 3 * a + w * j + w)
+                if PAR["l1"][j] == "v":
+                    tt(c, pt(j, a, b), A("TS", a, b), ALU.is_gt)
+                else:
+                    pj = A("PJ3", 256 * j + a, 256 * j + b)
+                    move("*", pj, pt(j, a, b))
+                    tt(c, pj, th, ALU.is_gt)
+            v1 = K(B["v1"][h % 2], 0, 3 * w // 16)
+            mm([(v1, sel(r), A("CMP", 3 * a + r, 3 * b, 16)) for r in range(16)])
+            ts(A("LT", 3 * a // 16, 3 * b // 16), v1, 8.5, ALU.is_lt)
+        at("w")
+        if PAR["wg"]:
+            tt(A("WN", 0, 256), pt(3, 0, 256), A("WG"), ALU.mult)
         else:
-            lists(t)
-            act(A("YH"), IND(A("HT"), SRC))
-            cp(A("YW"), IND(A(wn), WL))
-            dma("s", ("out", "yh"), A("YH"), COST["dma"], [], [A("YH")])
-            dma("y", ("out", "yw"), A("YW"), COST["dma"], [], [A("YW")])
+            tt(A("WN", 0, 256), IND(A("WT"), SRC), A("PG"), ALU.mult)
+        ts(A("FL", 0, 256), A("WN", 0, 256), col("LH", t), ALU.is_lt)
+        ts(A("FL", 256, 512), A("WN", 0, 256), col("LH", 8 + t), ALU.is_gt)
+        ts(A("FL", 512, 768), A("WN", 0, 256), 0.0, ALU.is_equal)
+        either((A("FL", 512, 768), A("WN", 0, 256), ACT.Relu, 1.0, -2.0 ** 85))
+        fl, rk = B["fl"], B["rank"]
+        mm([(K(fl, 0, 48), sel(r), A("FL", r, 768, 16)) for r in range(16)])
+        at("r")
+        tt(A("FG"), K(fl, 0, 48), A("TH", 48 * t, 48 * t + 48), ALU.is_gt)
+        HIGH, HOLES = A("FG", 16, 32), (0, 32)
+        scan(A("SN"), A("RS48"), A("FG"), ALU.mult, ALU.add)
+        tt(A("E"), A("FG"), A("M16"), ALU.mult)
+        mm([(K(rk, 0, 36), IB, A("CIN", 0, 36)), (K(rk, 16, 32), IB, A("CWB")), (K(rk, 16, 32), A("TBR"), HIGH),
+            (K(rk, 16, 32), IM1, A("E", 16, 32)), (K(rk, 0, 32), A("BOB"), A("SN", 0, 32)), (K(rk, 0, 16), A("BOB"), A("SN", 32, 48)),
+            (K(rk, 32, 34), A("BOB"), A("SN", 15, 32, 16)), (K(rk, 32, 33), A("BOB"), col("SN", 47))]
+           + [(K(rk, 0, 16), A("TBZ"), A("FG", j, j + 16)) for j in HOLES])
+        ts(A("PO"), K(rk, 0, 32), K(rk, 32, 33), ALU.subtract, 255.0, ALU.add)
+        DD = col("SC_O", 8 * t)
+        ts(DD, K(rk, 32, 33), K(rk, 33, 34), ALU.subtract)
+        mm([(K(rk, 36, 52), IB, A("CIN", 36, 52))] + [x for j in HOLES for x in ((K(rk, 36, 52), A("BOB"), A("SN", j, j + 16)),
+                                                                               (K(rk, 36, 52), A("TBP"), A("FG", j, j + 16)))])
+        ts(A("G"), K(rk, 36, 52), K(rk, 33, 34), ALU.subtract, 0.0, ALU.max)
+        move("*", A("TT", 0, 288), A("IOX"))
+        at("p")
+        cp(IND(A("TT", 0, 1328), A("PO", 16, 32)), A("IOB"))
+        either((IND(A("TT", 0, 1328), A("PO", 16, 32)), A("IOB"), ACT.Silu, 0.0, 1.0))
+        scan(A("SM"), A("TT", 256, 288), A("PK", 0, 32), ALU.min, ALU.add, BIG)
+        ts(A("SL"), A("SM", 15, 32, 16), SLB, ALU.add, float(DEAD), ALU.min)
+        po = 96 * t
+        move("*", A("SP_O", po, po + 32), IND(A("WN"), A("SL")), scale=0.5)
+        for h, (a, b) in enumerate(PAR["c1"]):
+            at("b%d_" % h)
+            w, m, ll = b - a, (b - a) // 16, B["ll"][h % 2]
+            lt = lambda j, n=1: A("LT", 3 * a // 16 + j * m, 3 * a // 16 + (j + n) * m)
+            sb = A("SB16", a // 16, b // 16)
+            mm([(K(ll, 0, 4 * m), IB, A("C64", 0, 64, 16 // m))]
+               + [(K(ll, m * j, m * j + m), A("I16") if j else A("I4"), sb) for j in range(4)], True, False)
+            mm([(K(ll, 0, m), IB, lt(i)) for i in range(3)]
+               + [(K(ll, m * j, m * (j + n)), A("I4"), lt(i, n)) for j, i, n in ((1, 0, 3), (1, 1, 2), (3, 0, 1), (1, 2, 1), (2, 0, 2))], False)
+            L2 = lambda j: A("LL", a // 4 + m * j, a // 4 + m * j + m)
+            ts(A("LL", a // 4, b // 4), K(ll, 0, 4 * m), 2304.25, ALU.add)
+            if PAR["l1"][3] == "v":
+                tt(A("R", a, b), IND(A("PT"), L2(0)), A("TS", a, b), ALU.subtract)
+            else:
+                move("*", A("PJ3", a, b), IND(A("PT"), L2(0)))
+                tt(A("R", a, b), A("PJ3", a, b), K(B["t"], a, b), ALU.subtract)
+            xg = lambda i: A("XG", 256 * i + a, 256 * i + b)
+            for i in range(3):
+                move(PAR["xg"][i], xg(i), IND(A("X"), L2(i + 1)))
+            for i in range(3):
+                k = K(B["xs"][h % 2][i], 0, w)
+                mm([(k, IB, xg(j)) for j in range(i + 1)])
+                tt(A("C2", 3 * a + w * i, 3 * a + w * i + w), k, A("R", a, b), ALU.is_lt)
+                mm([(K(B["ge"][h % 2], 0, w), A("VJ", 128 * (2 - i), 128 * (3 - i)), A("C2", 3 * a + w * i, 3 * a + w * i + w))], i == 0, i == 2)
+            move("*", A("THB", a, b), IND(A("B4"), L2(0)), A("THR"))
+            for c, d in PAR["c3"]:
+                if a <= c and d <= b:
+                    at("h%d_" % (c // 32))
+                    tt(A("GE", c, d), K(B["ge"][h % 2], c - a, d - a), A("THB", c, d), ALU.is_gt)
+                    tt(A("M", c, d), A("GE", c, d), K(B["d"], c, d), ALU.mult)
+        at("q")
+        move("*", A("SP_O", po + 32, po + 64), IND(A("HF"), A("SL")))
+        move("*", A("SP_O", po + 64, po + 96), IND(A("M"), A("SL")))
+        send("p", t, A("SP_O", po, po + 96), A("SP_I", po, po + 96))
+        at("u")
+        for a, b in PAR["c4"]:
+            mm([(K(B["ht"], a, b), A("I16F", 16, 144), A("HC", a, b)), (K(B["ht"], a, b), A("EW32", 30 - t, 158 - t), A("M", a, b))])
+            move("*", A("HT", a, b), K(B["ht"], a, b))
+        if not last:
+            at("c")
+            send("c", t, A("SC_O", 8 * t, 8 * t + 2), A("SC_I", 24 * t, 24 * t + 24))
+            own(t)
+        at("f")
+        tt(A("DB"), K(fl, 0, 16), A("TH", 48 * t + 32, 48 * t + 48), ALU.is_gt)
+        mm([(K(B["fw"], 0, 16), IB, A("DB")), (K(B["fw"], 0, 16), A("IMH"), HIGH)])
+        ts(A("FW"), K(B["fw"], 0, 16), 1.0, ALU.add)
+        mm([(K(B["fb"], r, 256, 16), uh(r), A("FW")) for r in range(16)], "each")
+        tt(A("WT", 0, 256), A("WN", 0, 256), K(B["fb"], 0, 256), ALU.mult)
+        at("s")
+        move("*", A("SRB"), IND(A("TT"), A("PO", 0, 16)), -208.0)
+        sb = K(B["sb"], 0, 16)
+        mm([(sb, IB, A("CWB")), (sb, IB, A("G"))]
+           + [x for j in HOLES for x in ((sb, A("DG"), A("FG", j, j + 16)), (sb, IM1, A("E", j, j + 16)))]
+           + [(sb, sel0(r), A("SRB", r, 256, 16)) for r in range(16)])
+        ts(A("SB16"), sb, 144.0, ALU.min)
+        lists()
+        at("i")
+        mi = A("SP_I", po + 64, po + 96)
+        move("*", A("HA"), A("SP_I", po + 32, po + 64))
+        if not last:
+            ha = lambda p: K(B["hna"], 0, 32) if p == t + 1 else K(B["ha"], 32 * p, 32 * p + 32)
+            mm([(ha(t + 1), A("BO32", 0, 128), mi)])
+            mm([(ha(p), uh(p, 16), A("HA")) for p in range(t + 1)], "each")
+            at("in")
+            neighbours(t, 256, 288, ha, K(B["ofa"], 0, 32), PAR["nka"])
+            steps()
+        at("j")
+        mm([(K(B["rot"], 0, 32), A("I32W", 0, 128), A("SP_I", po, po + 32))])
+        move("*", A("WT", 256, 288), K(B["rot"], 0, 32))
+        mm([(K(B["rot"], 32, 64), A("I32W", 0, 128), A("SP_I", po + 32, po + 64)), (K(B["rot"], 32, 64), A("EW32", 14 - t, 142 - t), mi)])
+        move("*", A("HT", 256, 288), K(B["rot"], 32, 64))
+        if not last:
+            history()
+            at("k")
+            cn = B["cnt"]
+            got = [A("SC_O", 8 * t, 8 * t + 2)] + [A("SC_I", 24 * t + 8 * j, 24 * t + 8 * j + 2) for j in range(3)]
+            mm([(K(cn, 0, 1), IM1, A(x[0], x[3] + j, x[3] + j + 1)) for x in got for j in range(2)])
+            ts(col("SV", 0), K(cn, 0, 1), 0.5, ALU.is_gt, 1.0, ALU.add)
+            ts(A("LH", 0, 14), A("LH", 0, 14), col("SV", 0), ALU.mult)
+            if t < NS - 2:
+                mm([(K(cn, 1, 2), A("IMW", 0, 128), col("SC_I", 24 * t))])
+                ts(col("SV", 1), K(cn, 1, 2), 0.0, ALU.max, 32.0, ALU.min)
+                ts(col("SC_O", 8 * t + 9), col("SV", 1), DD, ALU.subtract, 0.0, ALU.min)
+        else:
+            at("y")
+            ts(A("YH"), IND(A("HT"), SRC), HB, ALU.add, -1.0, ALU.max)
+            act(A("YW"), IND(A("WT"), SRC))
+            dma("y", ("out", "yh"), A("YH"))
+            dma("s", ("out", "yw"), A("YW"))
     return ops
 
 
@@ -450,44 +523,27 @@ def meet(a, b):
     return a[0] == b[0] and a[1] < b[2] and b[1] < a[2] and a[3] < b[4] and b[3] < a[4]
 
 
-def sign(o):
-    a = (o["wr"] or o["rd"])[0]
-    c = {"SP_O": a[3] % PW, "SC_O": 0, "EQ": a[3] % 288, "SP_I": a[3] % PW, "SC_I": 0}.get(a[0], a[3])
-    if o["kind"] == "mm":
-        l, r = o["rd"][0], o["rd"][1]
-        if r[0] == "X":
-            return "mm.sum.%d" % r[3]
-        if l[0] == "UH":
-            return "mm.hb.%d" % r[3]
-        if l[0] == "BO32" and a[0] in ("K0", "K1", "K2") or (a[0] == "K6" and a[3] >= 320):
-            return "mm.hbm.%d" % (r[3] if r[0] == "M" else 256)
-        return "mm.%s.%d.%s" % (a[0], c, o["rd"][1][0][:3])
-    return "%s.%s.%d" % (o["kind"], "W" if a[0] in ("W0", "W1") else a[0][:4], c)
+def whole(a):
+    return a[5] == 1 and (len(a) < 7 or a[6] == 1)
 
 
-BIAS = {"dma.SI.0": 2e6, "dma.NB.0": 1e6}
+BIAS = {"py.load0": 2e6, "py.load1": 1e6}
 
 
 def depend(ops):
     seen = {}
     for i, o in enumerate(ops):
-        d, raw = set(), set()
+        d = set()
         for a in o["rd"]:
-            raw.update(j for j, b, w in seen.get(a[0], []) if w and meet(a, b))
+            d.update(j for j, b, w in seen.get(a[0], []) if w and meet(a, b))
         for a in o["wr"]:
             d.update(j for j, b, w in seen.get(a[0], []) if meet(a, b))
-        d |= raw
         d.discard(i)
         o["dep"] = d
-        same = {j for j in d if ops[j]["eng"] == o["eng"]}
-        if o["eng"] == "t":
-            o["soft"] = same
-        elif o["eng"] in "vs" and o["kind"] != "dma" and PAR["soft"]:
-            o["soft"] = {j for j in same - raw if ops[j]["kind"] != "dma"}
-        else:
-            o["soft"] = set()
+        o["soft"] = {j for j in d if ops[j]["kind"] == o["kind"]} if o["kind"] in ("mm", "send") else set()
+        o["hard"] = sorted(d - o["soft"])
         for a in o["wr"]:
-            keep = [e for e in seen.get(a[0], []) if not (a[5] == 1 and a[1] <= e[1][1] and e[1][2] <= a[2] and a[3] <= e[1][3] and e[1][4] <= a[4] and e[0] != i)]
+            keep = [e for e in seen.get(a[0], []) if not (whole(a) and a[1] <= e[1][1] and e[1][2] <= a[2] and a[3] <= e[1][3] and e[1][4] <= a[4] and e[0] != i)]
             seen[a[0]] = keep + [(i, a, True)]
         for a in o["rd"]:
             seen.setdefault(a[0], []).append((i, a, False))
@@ -506,10 +562,10 @@ def schedule(ops):
     for i in range(n - 1, -1, -1):
         prio[i] = ops[i]["ns"] + max([prio[u] + (0.0 if i in ops[u]["soft"] else hop + ops[i]["lat"]) for u in users[i]], default=ops[i]["lat"])
     for i, o in enumerate(ops):
-        prio[i] += BIAS.get(sign(o), 0.0)
+        prio[i] += BIAS.get(o["id"], 0.0)
     left = [len(o["dep"]) for o in ops]
     done = [0.0] * n
-    free, bank, order = {}, {}, []
+    free, bank = {}, {}
     cand = [i for i in range(n) if left[i] == 0]
 
     def ready(i):
@@ -539,64 +595,26 @@ def schedule(ops):
                 pick = min(b, key=lambda i: (st[i], -prio[i]))
         o = ops[pick]
         for b in o["banks"]:
-            if b in bank and ops[bank[b]]["eng"] != o["eng"]:
-                o["dep"].add(bank[b])
             bank[b] = pick
         o["t0"] = st[pick]
         free[o["eng"]] = st[pick] + o["ns"]
         done[pick] = st[pick] + o["ns"] + o["lat"]
-        order.append(pick)
         cand.remove(pick)
         for u in users[pick]:
             left[u] -= 1
             if left[u] == 0:
                 cand.append(u)
-    return order, max(done)
+    return max(done)
 
 
-PERIOD, FIRST = 16000.0, 12000.0
-ORDER = {
-    "v": "cp.X.2048:100 scan.PT.3:230 cp.X.2560:240 cp.X.4096:330 scan.PT.2051:335 scan.PT.1027:420 cp.X.3840:430 scan.PT.2563:440 "
-         "scan.PT.4099:480 scan.PT.3843:490 scan.PT.3075:520 cp.PJ3.0:560 cp.PJ3.256:560 cp.PJ3.512:560 tt.K4.0:610 tt.CMP.0:640 tt.W.0:660 tt.CMP.256:700 "
-         "tt.CMP.512:730 ts.FL.0:760 ts.FL.256:790 ts.LT.0:820 cp.LL.0:870 tt.R.0:885 ts.FG.0:930 tt.FG.0:935 scan.SN.0:940 tt.E1.0:945 "
-         "ts.SMAL.0:950 ts.SMAL.16:955 tt.SMAL.32:960 cp.H16.0:825 ts.POS.0:990 cp.TT.0:1000 tt.C2.0:1100 tt.C2.256:1110 tt.SM1.0:1115 tt.C2.512:1120 "
-         "scan.SM2.0:1150 ts.SMAL.80:1155 cp.SL.0:1160 tt.SMAL.112:1165 tt.GE.0:1200 tt.M.0:1210 tt.SMAL.128:1215 tt.GE.128:1220 tt.M.128:1230 cp.IDX.0:1235 "
-         "cp.SP_O.68:1240 scan.SC.0:1250 tt.SMAL.64:1255 ts.LW.0:1260 scan.SC.128:1265 ts.NK.0:1270 ts.LW.8:1275 tt.FW.0:1278 tt.EQ.0:1280 ts.NK.128:1290 "
-         "ts.OU.0:1300 tt.EQ.128:1310 ts.OU.128:1650 cp.H16.256:1690 scan.SC.256:1710 ts.LW.16:1720 ts.NK.256:1810 tt.EQ.256:1820 "
-         "ts.OU.256:1850 cp.L4.0:1900 ts.SV.4:2060 ts.SMAL.144:2070 tt.NL.0:2080 ts.SV.2:2090 ts.L4.64:2100 ts.L4.80:2095 cp.YW.0:2110",
-    "s": "act.X.0:0 act.X.1024:175 act.X.3072:350 act.X.2048:350 act.X.4096:400 act.PG.0:560 act.PJ3.0:600 act.PJ3.256:610 act.PJ3.512:660 act.FL.512:710 act.TS.0:770 "
-         "act.W.512:780 act.XG.0:885 act.XG.256:935 act.XG.512:985 act.THB.0:1035 act.SV.6:1080 act.SV.0:1085 act.SV.3:1090 act.SMAL.96:1095 "
-         "act.SP_O.0:1100 act.W.256:1110 act.SP_O.4:1170 act.SP_O.36:1180 act.SC_O.0:1190 act.SRB.0:1240 act.SB16.0:1300 "
-         "act.HT.0:2090 act.HT.256:2100 act.SV.7:2110 act.SV.5:2120 act.FF.0:2130 act.LF.0:2140 act.OT.0:2150 act.OT.128:2320 act.OT.256:2330 "
-         "act.OF.0:2390 act.HC.0:2395 act.YH.0:2200",
-    "t": "mm.K0.0.X:180 mm.K2.0.X:190 mm.K3.0.X:330 mm.K1.0.X:350 mm.K4.0.UB:530 mm.K1.256.C3:600 mm.K6.0.MAS:610 mm.K7.0.CIN:620 "
-         "mm.K0.256.CMP:750 mm.K1.256.LT:835 mm.K6.0.FL:860 mm.K4.256.OF:920 mm.K0.0.XG:935 mm.K7.0.FG:950 mm.K7.0.SN:955 mm.K1.0.XG:985 "
-         "mm.K2.0.XG:1035 mm.K5.0.MAS:1040 mm.K6.128.MAS:1045 mm.K3.0.C2:1130 mm.hb.0:1190 mm.K5.0.M:1215 mm.K6.128.M:1235 mm.hbm.0:1240 mm.K7.96.SRB:1260 "
-         "mm.K3.256.NK:1275 mm.K3.256.EQ:1285 mm.hbm.128:1290 mm.K3.384.NK:1295 mm.K3.384.EQ:1315 mm.K7.160.C4:1660 mm.K5.0.SP_:1700 mm.hb.256:1705 "
-         "mm.hbm.256:1710 mm.K4.0.H16:1730 mm.K5.64.NK:1815 mm.K5.64.EQ:1825 mm.K6.288.H16:1850 mm.K6.65.SP_:1860 mm.K6.64.SC_:1900 mm.K7.224.NL:2090",
-    "g": "send.tokw.0:1185 send.tokp.0:1245 send.tokc.0:1300",
-    "x": "recv.SP_I.0:1250 recv.SP_I.68:1260 recv.SC_I.0:1310",
-}
-TAU = {e + w.split(":")[0]: 10.0 * int(w.split(":")[1]) for e, s in ORDER.items() for w in s.split()
-       if ".X" not in w and "scan.PT" not in w}
-EARLY = ("vtt.K4.0:610 vtt.W.0:620 vts.FL.0:650 vts.FL.256:680 vtt.CMP.0:700 vtt.CMP.256:730 vtt.CMP.512:760 vts.FG.0:775 vtt.FG.0:780 "
-         "vscan.SN.0:785 vtt.E1.0:790 vts.SMAL.0:795 vts.SMAL.16:800 vtt.SMAL.32:805 vts.LT.0:850 vts.POS.0:870 vcp.LL.0:890 vtt.R.0:900 "
-         "vcp.TT.0:950 vcp.H16.0:860 sact.FL.512:600 sact.PJ3.0:610 sact.PJ3.256:650 sact.PJ3.512:700 sact.TS.0:800 sact.W.512:810 "
-         "sact.HC.0:2380 sact.OT.0:2100 sact.OT.128:2105 sact.OT.256:2110 sact.OF.0:2400 tmm.K6.0.MAS:500 tmm.K6.0.FL:720 tmm.K0.256.CMP:790 "
-         "tmm.K7.0.FG:850 tmm.K7.0.SN:855 tmm.K1.256.LT:860 vtt.NL.0:2000 vts.SV.4:1990 vts.SMAL.144:1995 sact.SV.7:1940 sact.SV.5:1945 "
-         "sact.FF.0:1950 sact.LF.0:1955")
-TAU.update({w.split(":")[0]: 10.0 * int(w.split(":")[1]) for w in EARLY.split()})
-
-
-def label(o):
-    return ("p" if o["step"] < 0 else "") + o["eng"] + sign(o)
+PERIOD = 13000.0
 
 
 def simulate(ops, tau, fix=False):
     hop = COST["hop"]
     seq, key = {}, []
     for i, o in enumerate(ops):
-        k = tau[o["id"]] + (0.0 if o["step"] < 0 else FIRST + PERIOD * o["step"])
+        k = tau[o["id"]] + PERIOD * o["step"]
         for j in o["dep"]:
             if j < i and key[j] > k:
                 k = key[j]
@@ -648,33 +666,20 @@ def simulate(ops, tau, fix=False):
 
 def prepared():
     ops = plan()
-    ref = plan()
-    schedule(ref)
-    depend(ops)
+    schedule(ops)
+    sent = {o["step"]: o["t0"] for o in ops if o["kind"] == "send" and o["args"][0] == "p"}
+    sent[-1] = sent[0] - PERIOD
     tau = {}
-    mid = min(o["t0"] for o in ref if o["step"] == 3 and o["kind"] == "send")
-    for s in (-1, 3, 4, 5, 0):
-        t0 = 0.0 if s < 0 else min(o["t0"] for o in ref if o["step"] == s and o["kind"] == "send" and o["args"][0] == "p")
-        for o in ref:
+    for s in (3, 4, 5, 2, 1, 0, -1):
+        for o in ops:
             if o["step"] == s:
-                tau.setdefault(label(o), o["t0"] - t0 + (0.0 if s < 0 else 12450.0))
-    at = {"s": 0.0, "v": 1000.0}
-    for e, a, b in PAR["pieces"]:
-        d = 60 + 26.0 * (b - a)
-        tau[e + ("cp" if e == "v" else "act") + ".X.%d" % (16 * a)] = at[e]
-        tau["tmm.sum.%d" % (16 * a)] = at[e] + d + 50
-        tau["vscan.PT.%d" % (16 * a + 3)] = at[e] + d + 700
-        at[e] += d + (500.0 if e == "v" else 0.0)
-    tau.update(TAU)
-    for o in ops:
-        o["id"] = label(o)
-        o["hard"] = sorted(o["dep"] - o["soft"])
+                tau.setdefault(o["id"], o["t0"] - sent[s])
     return ops, tau
 
 
 def refine(ops, tau, rounds, seed=12345):
     st = sorted(k for k in tau if k[0] != "p")
-    pr = sorted(k for k in tau if k[0] == "p" and "dma" not in k)
+    pr = sorted(k for k in tau if k[0] == "p" and "load" not in k)
     x = [seed]
 
     def rnd():
@@ -696,6 +701,249 @@ def refine(ops, tau, rounds, seed=12345):
     return best
 
 
+def place(ops, key, before, after, back, lean, way):
+    n, hop = len(ops), COST["hop"]
+    left = [len(b) for b in before]
+    pend = sorted((key[i], i) for i in range(n) if left[i] == 0)
+    start, early, lines = [0.0] * n, [0.0] * n, {}
+    while pend:
+        i = pend.pop(0)[1]
+        o = ops[i]
+        tail = o["lat"] + hop
+        pick = None
+        for w, (e, ns) in enumerate([(a[0], a[3]) for a in o["alt"]] if "alt" in o else [(o["eng"], o["ns"])]):
+            t = early[i] if early[i] or not back else o["lat"]
+            need = ([] if e == "x" else [(e, 0.0, ns)]) + [(b, -tail if back else 0.0, ns if back else ns + tail) for b in o["banks"]]
+            moved = True
+            while moved:
+                moved = False
+                for r, lo, hi in need:
+                    for s, f, who in reversed(lines.get(r, ())):
+                        if f <= t + lo + 0.01:
+                            break
+                        if s + 0.01 < t + hi and (who != e or r == e):
+                            t, moved = f - lo, True
+            v = t + ns + (lean[i] if w == 0 else 0.0)
+            if pick is None or v < pick[0]:
+                pick = (v, t, ns, e, need, w)
+        v, t, ns, e, need, way[i] = pick
+        start[i], o["ns"] = t, ns
+        for r, lo, hi in need:
+            line = lines.setdefault(r, [])
+            k = len(line)
+            while k and line[k - 1][1] > t + hi:
+                k -= 1
+            line.insert(k, (t + lo, t + hi, e))
+        for u, d in after[i]:
+            if t + ns + d > early[u]:
+                early[u] = t + ns + d
+            left[u] -= 1
+            if left[u] == 0:
+                k, v = len(pend), (key[u], u)
+                while k and pend[k - 1] > v:
+                    k -= 1
+                pend.insert(k, v)
+    return start
+
+
+def arrange(ops, rounds, seed):
+    depend(ops)
+    n, x = len(ops), [seed]
+
+    def rnd():
+        x[0] = (x[0] * 6364136223846793005 + 1442695040888963407) % (1 << 64)
+        return (x[0] >> 11) / float(1 << 53)
+    pre, post = [[] for _ in ops], [[] for _ in ops]
+    for i, o in enumerate(ops):
+        for j in o["dep"]:
+            d = 0.0 if j in o["soft"] else ops[j]["lat"] + COST["hop"]
+            pre[i].append((j, d))
+            post[j].append((i, d))
+    best, keep = 1e18, [float(i) for i in range(n)]
+    key, lean, way = keep, [PAR["lean"]] * n, [0] * n
+    good = lean
+    for r in range(rounds):
+        f = place(ops, key, pre, post, False, lean, way)
+        v = max(f[i] + ops[i]["ns"] + ops[i]["lat"] for i in range(n))
+        if v < best:
+            best, keep, ways, good = v, f, list(way), lean
+        if r % 3 == 2:
+            amp = 50.0 + 700.0 * rnd()
+            lo = best * rnd()
+            f = [s + amp * rnd() if lo < s < lo + PAR["span"] else s for s in keep]
+            lean = [(3 * rnd() - 1) * PAR["lean"] if lo < keep[i] < lo + PAR["span"] and rnd() < 0.3 else good[i] for i in range(n)]
+        b = place(ops, [-(f[i] + ops[i]["ns"]) for i in range(n)], post, pre, True, lean, way)
+        key = [-(b[i] + ops[i]["ns"]) - BIAS.get(ops[i]["id"], 0.0) for i in range(n)]
+    for i, o in enumerate(ops):
+        o["id"] = i
+        if "alt" in o:
+            o["eng"], o["kind"], o["args"], o["ns"] = o["alt"][ways[i]]
+    return {i: keep[i] - PERIOD * ops[i]["step"] for i in range(n)}, best
+
+
+ORDER = """
+v.a0_4!:-439 v.x1_0:-414 t.x2_0:-389 t.x1_0:-319 v.x4_0:-317 v.x3_0!:-303 v.x2_0!:-302 t.a0_0:-301 t.x5_0:-246 v.x2_1:-222 t.x0_0:-218 t.x3_0:-162 t.x8_0:-157 v.x3_1:-150 v.x1_1:-150 v.x7_0:-123 t.x6_0:-120 t.x4_0:-63 v.a0_0:-55 v.x0_0!:-46 v.x6_0!:-46 v.x5_0!:-41 t.x7_0:-27 v.x6_1:-16 v.x4_1:-15 v.b0_0:-14 v.x8_0!:-14 v.x0_1:23 v.x5_1:31 v.a0_2!:33 v.p0!:35 v.w1:51 v.a1_0!:57 v.x7_1:58 t.a1_0:60 t.hb2:60 v.x8_1:61 t.r0:64 v.a1_2!:66 t.hb4:72 t.hb3:73 t.a0_1:96 v.a0_1:112 t.hb0:113 v.a0_6:130 v.a0_3:134 t.b0_0:134 v.a0_7:134 v.a0_5:134 v.w0:135 v.p3!:136 v.a1_6!:154 v.a1_4!:161 v.w3!:176 v.b0_3!:178 v.a0_8:181 t.hb1:192 v.w2:193 v.a1_1:194 t.b0_1:194 v.a1_7:198 v.b1_4!:201 v.a1_3:207 x.c0:207 t.b1_0:218 v.b0_1!:226 v.b0_6:243 v.r6!:245 v.a1_5:246 t.w0:253 t.b0_2:253 g.c0:258 v.q2:260 v.b0_4!:263 t.n1_0:273 v.b0_9:276 v.b0_2:288 v.r1:289 t.a1_1:292 v.r0:295 v.a1_8:295 v.b0_5!:303 v.b1_9!:310 t.b1_4:322 v.f0:331 t.b0_4:348 t.b0_6:349 v.r3:357 t.b0_7:357 t.b1_1:365 v.b0_8:368 t.f0:369 t.b0_3:378 t.b0_5:383 v.b0_7:388 v.b1_0:388 v.r2:391 v.b1_3:411 v.b1_5!:417 t.b1_7:423 v.h0_0:433 v.h4_1:434 v.h0_1:438 t.n0_1:445 v.r5:461 x.p0:468 v.b1_1:477 v.r4:483 t.b1_2:488 v.b1_2:492 v.n0_0:496 t.n0_0:510 t.b1_6:526 t.n0_e2:538 t.q0:550 v.b1_6:573 v.n0_1:574 v.b1_7:574 v.b1_8:578 t.b1_5:578 t.b1_3:578 v.n0_2:581 v.h4_0:593 v.q0!:599 v.p1:600 v.p2:615 v.n0_e2:615 v.n0_e0:615 v.s0!:616 g.p0:620 t.n0_e5:625 t.k1:636 v.n0_o0:667 v.n0_e1:668 v.n0_e3:669 v.n1_0:670 t.q1:683 x.q0:685 v.n0_e4:694 v.n1_1:694 t.n0_e1:694 t.n0_e0:695 t.n0_e3:698 v.q1!:698 t.n0_e4:701 t.s0:711 v.n1_2!:776 v.n1_e2:776 v.n0_e5:799 t.n1_e3:807 t.n1_1:818 v.n1_e1:853 v.n1_e4:853 v.n1_e0:854 t.n1_e5:881 v.n1_e5:882 v.n1_e3:884 g.q0:915 t.n1_e4:919 t.n1_e2:929 v.f1:934 t.n1_e0:936 v.in0:939 v.s1:941 t.n1_e1:955 t.f1:960 v.n1_o0:965 v.f2:1000 t.l0:1000 t.j0:1006 t.ine5:1086 v.ino0:1109 t.ine4:1110 t.i0:1113 v.i0:1113 t.i1:1120 v.ine0:1129 v.l0:1147 v.in1:1148 t.k0:1158 v.ine5:1169 t.ine0:1177 t.j1:1179 v.in2:1193 v.ine2:1193 v.ine4:1193 v.ine1:1194 v.ine3:1194 t.in0:1242 t.ine3:1243 t.ine2:1243 t.ine1:1244 v.j1!:1406 v.j0!:1418 v.j2!:1424 v.k0:1424 v.k1:1444 v.d0!:1491 t.d0:1508 v.k2:1553 v.k3:1641
+"""
+ORDER = """
+v.a0_4!:-575.5 v.x2_0!:-530.8 t.x2_0:-484.3 v.x3_0!:-454.3 t.a0_0:-392.8 v.x1_0:-354 v.x6_0!:-351.6 v.x0_0!:-351 t.x1_0:-312.7 v.x2_1:-312.5 v.x4_0:-303.9 t.x3_0:-295.8 v.w3!:-283.9 v.w1:-278.5 t.x4_0:-210.9 t.r0:-163 v.a1_6!:-152.2 v.b0_0:-107 v.a1_0!:-105.2 v.b0_6:-80.1 v.x1_1:-76.7 v.x3_1:-76.4 t.x5_0:-55.8 v.p0!:-47.8 t.a0_1:-29.2 t.x6_0:-17.7 v.a0_2!:-12.3 t.x0_0:-6.2 t.a1_0:14.4 v.x5_0!:16.2 v.x7_0:18.2 t.hb3:22.1 t.x7_0:24.2 t.f0:24.5 t.x8_0:31.8 v.x6_1:31.9 v.x4_1:32 x.c0:34.9 v.x8_0!:43.6 v.x5_1:49.4 v.a0_0:49.7 v.x0_1:52 v.x7_1:52.5 v.x8_1:52.5 v.a0_6:52.5 v.a0_1:71.1 t.hb4:78 t.hb2:84.4 t.b1_0:105.4 t.hb0:115 v.h0_1:115.7 t.b0_0:119.3 v.a1_4!:122.1 v.a1_2!:123.6 v.a0_5:129.2 v.a0_7:129.5 v.a0_3:130.3 v.w0:135 v.a0_8:154.9 t.n0_0:164.5 g.c0:173.8 v.b1_5!:185.7 t.hb1:186.5 v.w2:193 v.a1_1:194 t.b0_1:194 v.b0_3!:198.4 v.a1_5:202.7 v.r1:209.9 v.a1_7:213.4 v.b0_1!:224.6 v.a1_3:234.2 t.w0:235.3 v.b0_4!:239.8 t.b0_2:241 t.b0_7:254.2 t.a1_1:264.1 t.b0_6:267.3 v.b0_9:275.7 v.b0_2:294.3 t.b1_5:301.4 v.r0:302.1 v.a1_8:303.7 t.b0_4:305.2 v.r3:306.3 t.b1_7:309.7 v.b0_5!:314.3 t.b1_1:317.1 t.b1_2:325.2 v.r6!:340.3 v.f0:358.6 t.b0_5:361.9 v.b0_8:377.3 v.b1_2:379.7 v.b0_7:387.3 v.b1_4!:392.5 v.b1_0:395.5 t.b0_3:401.2 t.b1_3:407 v.r2:410.1 t.n1_0:413.9 t.q1:457.3 v.r5!:467.2 x.p0:468 v.b1_3:468.8 v.b1_9!:475.2 t.b1_4:477.3 v.h0_0:483 v.b1_1:484.4 v.h4_1:498.6 v.r4:511.8 v.n0_0:516.6 t.b1_6:524.4 t.n0_e5:525 t.q0:553.1 v.s0!:555.3 t.n0_1:572.9 v.b1_6:573.3 v.b1_7:573.5 v.n0_1:574.7 v.b1_8:578 g.q0:580.8 v.n0_2:581 v.h4_0:581.1 x.q0:586 v.p1:596.6 v.n0_e1:612.5 v.n0_e4:614.5 v.q2:617.1 g.p0:620 v.n0_e0:632.1 v.q1!:646.4 v.p2:672.2 v.n0_e2:673.4 v.n0_e3:678.8 v.n1_0:682.1 v.q0!:699.4 t.n0_e4:700 v.p3!:712.1 v.n0_e5:724.8 t.n0_e0:824.2 t.n0_e1:824.2 t.n0_e2:824.2 v.n0_o0:824.2 v.n1_1:824.5 t.n1_e4:835.8 t.n0_e3:836 t.n1_1:849.3 t.s0:853 v.n1_2:872.1 t.n1_e0:900.4 t.n1_e1:911.7 v.n1_e3:947.6 v.n1_e4:948 v.n1_e2:960.3 t.n1_e2:975.4 v.n1_e1:981.3 v.s1:996.4 v.f1:1002.8 t.n1_e3:1011.4 v.n1_e0:1015.5 v.n1_o0:1037.4 t.f1:1037.8 v.ino0:1044.6 t.l0:1047.1 v.in0:1069.1 t.n1_e5:1092.9 v.f2:1106.5 v.n1_e5:1108.3 t.i0:1121.7 v.i0:1122.5 t.j0:1123.2 t.ine4:1128.5 t.i1:1144.4 t.ine1:1167.3 v.in1:1176 t.j1:1179 v.l0:1179 t.in0:1232.6 v.in2:1241.9 v.j1!:1259.2 v.ine0:1275.9 v.ine1:1276 v.ine2:1276.1 v.ine3:1277 v.ine4:1277.1 t.ine0:1315 t.ine3:1327.4 t.ine2:1330.6 v.ine5:1373.8 t.ine5:1373.8 t.k0:1374 v.j2!:1415.7 v.k0:1419.9 v.j0:1422.4 t.k1:1454.3 v.d0!:1463.8 v.k1:1466.8 t.d0:1512.7 v.k2:1536.5 v.k3:1682
+"""
+ORDER = """
+v.a1_6!:-1118.5 v.w3!:-681.9 v.a1_0!:-467.6 t.x8_0:-349.3 g.c0:-297.5 t.a0_1:-281.1 v.x3_0!:-155.5 v.x5_0!:-155.2 v.x1_0:-147.1 v.x2_0!:-110.6 t.x3_0:-91.7 v.x4_0:-79.7 g.q0:-77.2 v.a0_2!:-70.1 v.a1_2!:-69.8 v.x0_0!:-69.6 v.x5_1:-55 t.b0_1:-42.3 v.x3_1:-29.7 v.a1_4!:-23.6 t.x6_0:-23.2 t.b1_0:-12.9 t.hb4:-12 t.x5_0:-3.1 v.a0_4!:1.6 t.x1_0:28.2 t.x2_0:29.4 t.x0_0:29.4 t.x4_0:29.5 v.x7_0:30.1 t.x9_0:31.3 v.x6_0!:31.5 v.x8_0!:32.7 v.x1_1:39.7 x.c0:44.4 v.x2_1:47.2 v.x0_1:48.5 t.x7_0:50.8 v.p0!:57.5 t.hb3:65.4 v.x9_0!:67.3 t.hb1:72.4 t.hb2:79 v.b0_4!:86.1 t.a0_0:111.4 v.x4_1:137.7 v.x6_1:137.8 v.x8_1:147.6 v.x7_1:149.6 t.a1_0:151.2 v.x9_1:153.9 v.a0_0:154.9 v.a0_1:161 v.a0_6:161.1 v.a0_3:161.4 v.a0_5:161.5 v.a0_7:162.5 v.w0:168.8 t.b0_4:170.5 v.a1_1:171.4 v.w1:174.7 v.a0_8:178.3 v.w2:185.4 v.a1_7:190.9 t.n0_0:203.2 v.b1_1!:222.9 t.a1_1:235.3 v.a1_5:235.6 t.b0_0:239.1 t.w0:270.7 t.b1_5:274.8 v.b0_5!:278.8 t.b0_6:280 v.a1_3:282 t.b0_7:310.6 v.b0_3:313.7 x.q0:320 t.b0_2:322 v.b0_0:328.2 v.r0:344.7 v.b0_1:352.1 v.r1:357.6 v.r6!:366.7 t.b1_1:376.7 v.b1_9!:384 v.r5:388.7 v.a1_8:391.2 v.b0_2:396.9 v.f0:397.7 v.r2:406.5 v.b0_6:426.6 v.b1_5!:427.9 t.hb0:431.3 v.b0_9!:435.8 v.b0_8:453 t.b0_3:459 t.f0:459.3 t.b1_3:481.3 v.b1_0:489.9 v.b0_7:496.4 t.r0:496.5 t.b0_5:511 v.b1_3:515 v.n0_1:527.3 v.b1_4:535.7 v.r3:537.7 t.b1_2:538.3 v.n0_e3:543.4 t.b1_4:545.2 v.h0_0:545.3 t.b1_6:545.4 v.b1_2:547.5 v.h0_1:547.5 t.b1_7:550.6 v.n0_e0:551.5 v.r4!:562.8 v.b1_6:572.1 v.b1_7:583.4 v.b1_8:592.9 v.n0_0:599.7 v.p1:626.8 t.n1_0:637.6 v.h4_0:640 v.n0_e5:648 t.r1:650.6 v.p2:666.1 v.h4_1:673.9 v.p3:680.4 v.n0_2!:682.2 v.n0_e1:682.2 v.n0_e2:682.2 v.f1:710.9 v.n1_2!:723.6 t.n0_e5:759.4 v.n1_0:783.2 v.n0_e4:838.6 t.n0_e4:912.3 v.q0!:916.8 v.q1!:998 t.s0:999.3 t.n1_1:1000.9 t.u1:1016.6 t.n0_1:1024.4 t.n0_e0:1024.4 t.n0_e3:1024.7 t.n0_e1:1024.9 t.n0_e2:1025.2 v.s0!:1027.1 t.n1_e5:1038.2 v.n1_1:1054.2 v.n0_o0:1066.8 v.ino0:1082.7 t.n1_e2:1113 v.u1!:1130.4 v.n1_e0:1130.5 v.n1_e5:1158.1 v.ine5:1166.8 t.n1_e0:1171.9 v.in0:1190 t.u0:1195.4 v.n1_e2:1196.5 v.n1_e3:1196.6 v.n1_e4:1197.1 t.j1:1199.5 t.n1_e4:1200.4 v.n1_e1:1214.4 t.n1_e3:1216.7 t.n1_e1:1218.5 t.f1:1244.6 v.n1_o0:1265.9 v.s1:1283.1 v.i0!:1290.2 t.l0:1295.5 t.i0:1299.1 v.u0:1308.4 v.in1:1309.1 t.ine4:1315.1 v.l0:1317.6 t.j0:1326.7 v.j1:1336.8 v.in2:1338.7 t.i1:1347.3 v.ine0:1348.7 v.ine1:1348.7 v.ine2:1361.7 v.ine3:1362.3 v.ine4:1365.1 t.k0:1379.7 v.f2:1385.9 t.ine0:1390.8 t.in0:1394.4 t.ine2:1398 t.ine1:1398.1 t.ine3:1398.2 v.k0:1416.6 v.j0:1455.9 v.j2!:1460.4 v.d0!:1461.4 v.j3:1524.3 v.k1:1530.5 t.k1:1567.9 v.k2:1728 t.ine5:1798.9 t.d0:1898.1 v.k3:1930.2
+"""
+STEP = 13700.0
+
+
+def keys(text):
+    tau, way = {}, {}
+    for w in text.split():
+        name, v = w.split(":")
+        way[name.strip("!")] = int(name[-1] == "!")
+        tau[name.strip("!")] = 10.0 * float(v)
+    return tau, way
+
+
+def part(ops, steps):
+    idx = [i for i, o in enumerate(ops) if o["step"] in steps]
+    at, res = {i: j for j, i in enumerate(idx)}, {"x": -1}
+    num = lambda x: res.setdefault(x, len(res) - 1)
+    s = dict(idx=idx, name=[ops[i]["id"] for i in idx], step=[STEP * ops[i]["step"] for i in idx], lat=[ops[i]["lat"] for i in idx])
+    s["pre"] = [[(at[d], 0.0 if d in ops[i]["soft"] else ops[d]["lat"] + COST["hop"]) for d in sorted(ops[i]["dep"]) if d in at] for i in idx]
+    s["alt"] = [[(num(a[0]), a[3], [num(b) for b in ops[i]["banks"]], a[3] + ops[i]["lat"] + COST["hop"])
+                 for a in ops[i].get("alt", [(ops[i]["eng"], 0, 0, ops[i]["ns"])])] for i in idx]
+    s["res"] = len(res)
+    return s
+
+
+def replay(s, tau, way):
+    pre, name, n = s["pre"], s["name"], len(s["idx"])
+    key = [0.0] * n
+    for i in range(n):
+        x = tau[name[i]] + s["step"][i]
+        for j, d in pre[i]:
+            if key[j] >= x:
+                x = key[j] + 1e-3
+        key[i] = x
+    start, fin, why, kind, prev = [0.0] * n, [0.0] * n, [-1] * n, [0] * n, [-1] * n
+    last, bank, end, final, held = [-1] * s["res"], [{} for _ in range(s["res"])], 0.0, 0, [()] * n
+    for i in sorted(range(n), key=lambda i: key[i]):
+        al = s["alt"][i]
+        e, ns, banks, hold = al[way.get(name[i], 0)] if len(al) > 1 else al[0]
+        t, w, kd = 0.0, -1, 0
+        for j, d in pre[i]:
+            if fin[j] + d > t:
+                t, w = fin[j] + d, j
+        if e >= 0:
+            j = prev[i] = last[e]
+            if j >= 0 and fin[j] >= t:
+                t, w, kd = fin[j], j, 1
+            if banks:
+                held[i] = [(j, f) for b in banks for en, (j, f) in bank[b].items() if en != e]
+                for j, f in held[i]:
+                    if f > t:
+                        t, w, kd = f, j, 2
+                for b in banks:
+                    bank[b][e] = (i, t + hold)
+            last[e] = i
+        start[i], fin[i], why[i], kind[i] = t, t + ns, w, kd
+        if t + ns + s["lat"][i] > end:
+            end, final = t + ns + s["lat"][i], i
+    return end, start, key, why, kind, final, prev, held
+
+
+def improve(s, tau, way, pool, rounds, heat, seed):
+    x = [seed]
+
+    def rnd():
+        x[0] = (x[0] * 6364136223846793005 + 1442695040888963407) % (1 << 64)
+        return (x[0] >> 11) / float(1 << 53)
+    one = lambda c: c[int(rnd() * len(c))]
+    name, step, pre = s["name"], s["step"], s["pre"]
+    names = sorted(set(name) & pool)
+    both = sorted({name[i] for i, a in enumerate(s["alt"]) if len(a) > 1} & pool)
+    cur = replay(s, tau, way)
+    best = (cur[0], dict(tau), dict(way))
+    for n in range(rounds):
+        end, start, key, why, kind, i, prev, held = cur
+        path = []
+        while i >= 0:
+            path.append(i)
+            i = why[i]
+        old, oldway, r = {}, {}, rnd()
+        if r < 0.2:
+            c = [name[i] for i in path if name[i] in both]
+            w = one(c if c and rnd() < 0.6 else both)
+            oldway[w] = way.get(w, 0)
+            way[w] = 1 - oldway[w]
+        elif r < 0.3:
+            w = one(names)
+            old[w] = tau[w]
+            tau[w] += (1 if rnd() < 0.5 else -1) * math.exp(4 + 3.5 * rnd())
+        else:
+            c = [i for i in path if kind[i] and (name[i] in pool or name[why[i]] in pool)]
+            if not c:
+                continue
+            b = one(c)
+            a = why[b]
+            if rnd() < 0.5:
+                for _ in range(one((0, 0, 1, 2, 3))):
+                    a = prev[a] if prev[a] >= 0 else a
+                to, todo, seen = key[a] - 1 - 5 * rnd(), [b], {b}
+                while todo:
+                    for j, d in pre[todo.pop()]:
+                        if key[j] >= to and j not in seen:
+                            seen.add(j)
+                            todo.append(j)
+                if a in seen or len(seen) > 12 or any(name[i] not in pool for i in seen):
+                    continue
+                for m, i in enumerate(sorted(seen, key=lambda i: -key[i])):
+                    old.setdefault(name[i], tau[name[i]])
+                    tau[name[i]] = to - 0.01 * m - step[i]
+            elif name[a] in pool:
+                old[name[a]] = tau[name[a]]
+                tau[name[a]] = key[b] + one((1, 1, 100, 300, 800)) * (0.5 + rnd()) - step[a]
+        new = replay(s, tau, way)
+        if new[0] <= end or rnd() < math.exp((end - new[0]) / (heat * (1 - n / rounds) + 2)):
+            cur = new
+            if new[0] < best[0]:
+                best = (new[0], dict(tau), dict(way))
+        else:
+            tau.update(old)
+            way.update(oldway)
+    tau.update(best[1])
+    way.update(best[2])
+    return best[0]
+
+
+def ordered(rounds):
+    ops = plan()
+    depend(ops)
+    tau, way = keys(ORDER)
+    s = part(ops, (-1, 0))
+    late = [0.0] * len(s["idx"])
+    for i in range(len(late) - 1, -1, -1):
+        late[i] += s["alt"][i][0][1]
+        for j, d in s["pre"][i]:
+            late[j] = max(late[j], late[i] + d)
+    for i, w in enumerate(s["name"]):
+        if w not in tau:
+            tau[w], way[w] = -0.2 * late[i] - (1e5 - i if "load" in w else 0.0), 1
+    for o in ops:
+        if o["id"] not in tau:
+            tau[o["id"]], way[o["id"]] = tau.get(o["id"][1:], 15000.0), way.get(o["id"][1:], 0)
+    ends = [improve(part(ops, (1, 2, 3, 4)), tau, way, {w for w in tau if w[0] not in "pz"}, rounds[0], 60.0, 1),
+            improve(s, tau, way, {w for w in tau if w[0] == "p" and "load" not in w}, rounds[1], 100.0, 2),
+            improve(part(ops, (4, 5)), tau, way, {w for w in tau if w[0] == "z"}, rounds[2], 60.0, 3)]
+    s = part(ops, range(-1, NS))
+    ends.append(improve(s, tau, way, {w for w in tau if "load" not in w}, rounds[3], 20.0, 4))
+    end, start, key, why, kind, final, prev, held = replay(s, tau, way)
+    for i, o in enumerate(ops):
+        if "alt" in o:
+            o["eng"], o["kind"], o["args"], o["ns"] = o["alt"][way.get(o["id"], 0)]
+        o["t0"] = start[i]
+        o["dep"] |= {j for j, f in held[i]}
+    return ops, sorted(range(len(ops)), key=lambda i: key[i]), ends, tau, way
+
+
 _CACHE = {}
 
 
@@ -704,9 +952,7 @@ def rank_program(g, core, T, topo):
     if rank is None:
         return
     if not _CACHE:
-        _CACHE["ops"], tau = prepared()
-        refine(_CACHE["ops"], tau, PAR["rounds"], PAR["seed"])
-        _CACHE["order"] = simulate(_CACHE["ops"], tau, True)[0]
+        _CACHE["ops"], _CACHE["order"] = ordered(PAR["rounds"])[:2]
     ops, order = _CACHE["ops"], _CACHE["order"]
     cores = list(T.cores)
     n = len(cores)
@@ -719,9 +965,8 @@ def rank_program(g, core, T, topo):
             return ap(a[1]).indirect(ap(a[2]))
         if a[0] in ("in", "out"):
             return T[a[1]][:]
-        if a[5] == 1:
-            return T[a[0]][a[1]:a[2], a[3]:a[4]]
-        return T[a[0]][a[1]:a[2], a[3]:a[4]:a[5]]
+        rows = slice(a[1], a[2]) if a[6] == 1 else slice(a[1], a[2], a[6])
+        return T[a[0]][rows, slice(a[3], a[4]) if a[5] == 1 else slice(a[3], a[4], a[5])]
 
     def maskof(es):
         return sum(1 << e for e in es)
@@ -772,11 +1017,7 @@ def rank_program(g, core, T, topo):
                 dst = cores[(rank + d) % n]
                 rid, pid, _ = topo.addr(dst)
                 es = share(core, dst, kind, d)
-                if kind == "c":
-                    land = A("SC_I", 12 * t + 4 * (d - 1), 12 * t + 4 * (d - 1) + 1)
-                else:
-                    land = ("SP_I",) + src[1:]
-                tr.append((rid, pid, es, land))
+                tr.append((rid, pid, es, landing(kind, t, src, d)))
                 totals["sent"] = totals.get("sent", 0) + len(es)
             sem = T.sem["r%s%d" % (kind, t)]
             if len(tr) == 1:
@@ -803,13 +1044,16 @@ def rank_program(g, core, T, topo):
             else:
                 r = q.tensor_scalar(ap(a[0]), ap(a[1]), ap(a[2]), ap(a[3]), a[4], a[5])
         elif k == "scan":
-            r = q.tensor_tensor_scan(ap(a[0]), ap(a[1]), ap(a[2]), 0.0, a[3], a[4])
+            r = q.tensor_tensor_scan(ap(a[0]), ap(a[1]), ap(a[2]), a[5], a[3], a[4])
         elif k == "mset":
             r = q.memset(ap(a[0]), a[1])
         elif k == "red":
             r = q.tensor_reduce(ap(a[0]), ap(a[1]), AxisListType.X, ALU.add, negate=True)
         elif k == "act":
-            r = q.activation(ap(a[0]), ap(a[1]), a[2], bias=ap(a[3]), scale=ap(a[4]))
+            if a[0][0] == "@":
+                r = q.activation(ap(a[0]), ap(a[1]), a[2])
+            else:
+                r = q.activation(ap(a[0]), ap(a[1]), a[2], bias=ap(a[3]), scale=ap(a[4]))
         elif k == "iota":
             if SCRATCH[a[0][0]][2] == I32:
                 r = q.iota(ap(a[0]), a[1], a[2], a[3])
@@ -818,7 +1062,7 @@ def rank_program(g, core, T, topo):
         else:
             its = a[0]
             for m, (x, l, y) in enumerate(its):
-                r = q.matmul(ap(x), ap(l), ap(y), a[1] and m == 0, a[2] and m == len(its) - 1)
+                r = q.matmul(ap(x), ap(l), ap(y), a[1] == "each" or (a[1] and m == 0), a[1] == "each" or (a[2] and m == len(its) - 1))
         if i in needed:
             count[e] += 1
             r.then_inc(T.sem["e" + e], 1)

@@ -13,18 +13,18 @@ SB = {
     "NB": (4096, I32), "QT": (4112, BF), "LH": (16, F32), "SI": (256, I32), "UI": (1536, I32), "CI": (1536, I32),
     "S0F": (256, F32), "U8": (1536, BF), "CB": (1792, BF), "PJ3": (768, F32), "TH": (288, F32), "TH2": (96, F32),
     "PI": (1, I32), "PJ": (4, I32), "PF": (8, F32), "GQ": (144, F32), "IQ": (144, F32), "C16": (48, F32),
-    "IOT": (256, F32), "IOB": (256, F32), "IOX": (288, F32), "TMP": (64, F32), "PK": (128, F32),
+    "IOT": (256, F32), "IOB": (256, F32), "IOX": (288, F32), "TMP": (64, F32), "PK": (256, F32),
     "EWB": (144, BF), "E0B": (144, BF), "BO32": (144, F32), "BOB": (128, BF), "BON": (128, BF), "RM": (16, F32),
     "UH": (16 * 144, F16), "I32W": (144, F32), "IBW": (144, BF),
     "I4": (128, BF), "I16": (128, BF), "I4096": (128, BF), "IMW": (144, BF), "IMH": (128, BF),
     "I16F": (144, F16), "D32": (128, F16), "VJ": (384, BF), "THR": (1, F32), "EW32": (160, F32), "B4": (1160, F32),
     "THB": (256, F32), "GE": (256, F32), "M": (296, F32), "OF": (256, F16), "DG": (128, BF), "TBZ": (128, BF), "TBR": (128, BF),
-    "RS4": (256, F32), "RS48": (48, F32), "C64": (64, BF), "C80": (80, BF), "CIN": (52, BF), "M16": (48, F32), "TBP": (128, BF), "G": (16, BF), "CWB": (16, BF),
+    "RS4": (256, F32), "RS48": (48, F32), "C64": (64, BF), "C80": (96, BF), "CIN": (52, BF), "M16": (48, F32), "TBP": (128, BF), "G": (16, BF), "CWB": (16, BF),
     "CW": (32, F32), "G8": (128, BF), "G832": (128, F32), "E8": (144, BF),
     "X": (4624, BF), "PT": (1160, F32), "TS": (256, F32), "PG": (256, F32), "CMP": (768, BF), "LT": (48, BF), "LT2": (48, BF),
-    "LL": (64, U16), "L": (80, U16), "LS": (16, U16), "SB16": (16, BF), "R": (256, F32), "XG": (768, BF), "C2": (768, BF),
-    "SC": (288, F32), "LW": (18, U16), "NK": (NW, F32), "EQ": (6 * 288, BF), "OU": (288, U16),
-    "WT": (296, F32), "WN": (296, F32), "HT": (296, F32), "HC": (256, F16), "FL": (768, BF), "FG": (48, BF), "DB": (16, BF),
+    "LL": (64, U16), "L": (96, U16), "LS": (16, U16), "SB16": (16, BF), "R": (256, F32), "XG": (768, BF), "C2": (768, BF),
+    "SC": (288, F32), "LW": (18, U16), "NK": (288, F16), "NF": (NW, F32), "EQ": (6 * 288, BF), "OU": (288, U16),
+    "W0": (888, F32), "W1": (888, F32), "GF": (16, BF), "IM16": (128, F16), "P16": (256, F16), "I296": (128, BF), "I592": (128, BF), "HT": (296, F32), "HC": (256, F16), "FL": (768, BF), "FG": (48, BF), "DB": (16, BF),
     "SN": (48, BF), "E": (48, BF), "HF": (296, F32), "WG": (256, F32), "PO": (32, U16), "TT": (2048, F32), "SM": (32, F32), "SL": (2, U16), "SV": (8, F32),
     "SRB": (256, BF), "FW": (16, F16), "YW": (256, F32), "YH": (256, F32),
     "SC_O": (NS * 8, BF), "SC_I": (NS * 24, BF), "SP_O": (NS * 96, F32), "SP_I": (NS * 96, F32),
@@ -39,14 +39,14 @@ SEMAPHORES = (["ev", "es", "et", "eg", "sent"] + ["d%d" % i for i in range(NDMA)
               + ["rc%d" % t for t in range(NS - 1)] + ["r%s%d" % (k, t) for k in "p" for t in range(NS)])
 
 PAR = dict(
-    pieces=[("*", a, a + 32) for a in range(0, 256, 32)] + [("*", 256, 272), ("*", 272, 288)], l1="ssss", wg=False,
-    c1=[(0, 128), (128, 256)], c3=[(0, 128), (128, 256)], c4=[(0, 128), (128, 256)], nk="*", nka="*", hc="*", xg="***", rounds=(8000, 20000, 15000, 5000),
-    bank=dict(sums=[(4, 0), (3, 0), (4, 128), (3, 128), (5, 0), (4, 256), (5, 128), (3, 0), (5, 256), (4, 0)], t=(3, 0),
+    pieces=[("*", a, a + 32) for a in range(0, 192, 32)] + [("*", a, a + 16) for a in (192, 224, 256, 272, 208, 240)], nt=0, slo=False, wide="hhhh", l1="ssss", wg=False, pull=0.2, lag=0, ahead=600.0, any=0.2, soft=False, pool=True,
+    c1=[(0, 128), (128, 256)], cz=[(0, 128), (128, 256)], c2=[(0, 128), (128, 256)], c3=[(0, 128), (128, 256)], c4=[(0, 128), (128, 256)], nk="*", nka="*", hc="*", xg="***", rounds=(4000, 10000, 1000),
+    bank=dict(sums=[(4, 0), (3, 0), (4, 128), (3, 128), (5, 0), (4, 256), (5, 128), (3, 0), (5, 256), (4, 0), (5, 192), (3, 64)], t=(3, 0),
               hb=[(0, 0), (0, 256), (1, 0), (1, 256), (2, 256)], xs=[[(4, 0), (4, 128), (4, 256)], [(5, 0), (5, 128), (5, 256)]],
               v1=[(4, 384), (5, 384)], ge=[(6, 128), (7, 128)], ll=[(6, 0), (7, 0)], hn=[(4, 384), (5, 384)], d=(3, 256), ht=(3, 0),
               of=[(6, 128), (7, 128)], fl=(2, 0), rank=(2, 48), sb=(2, 100), l=(2, 116), fw=(2, 196), cnt=(7, 304), rot=(7, 320),
               fb=(0, 0), ha=(1, 0), hna=(2, 224), ofa=(6, 256)))
-COST = dict(cyc=0.92, pe=0.48, gat=1.56, sca=3.8, hop=165.0, dma=2000.0, rem=3000.0, iss=1100.0, look=60.0)
+COST = dict(cyc=0.92, pe=0.48, gat=1.56, sca=3.8, hop=165.0, dma=2000.0, rem=3000.0, iss=1100.0, first=1500.0, look=60.0)
 
 
 def A(name, c0=0, c1=None, step=1, p0=0, p1=128, ps=1):
@@ -167,7 +167,7 @@ def plan():
 
     def send(kind, t, src, land):
         tok = ("tok%s%d" % (kind, t), 0, 128, 0, 1, 1)
-        add("g", "send", (kind, t, src), [tok], [src], COST["iss"])
+        add("g", "send", (kind, t, src), [tok], [src], COST["iss"] * (1.5 if kind == "c" else 1))
         add("x", "recv", (kind, t), [land], [tok], 0.0, COST["rem"] - COST["iss"])
 
     def K(b, c0, c1, step=1):
@@ -181,15 +181,17 @@ def plan():
     col = lambda n, j: A(n, j, j + 1)
     P_, PG, PR, LWB, SLB, HB = [col("PF", j) for j in range(6)]
     BO, IW, IB, IQ = A("BO32", 16, 144), A("I32W", 16, 144), A("IBW", 16, 144), A("IQ", 16, 144)
-    SRC = A("L", 64, 80)
+    SRC, WL = A("L", 64, 80), A("L", 80, 96)
     IM1 = A("IMW", 16, 144)
 
     at("load")
     mset(A("LH"), 0.0)
-    dma("y", A("SI", p1=8), ("in", "s0"), 1800)
-    dma("y", A("NB"), ("in", "nb"), 8500)
-    dma("y", A("QT", 0, 4096), ("in", "qs"), 12000)
-    for n, s in ((A("CI", p1=8), "coin"), (A("UI", p1=8), "us"), (A("WT", 0, 256), "w0"), (A("LH", 0, 6), "lo"), (A("LH", 8, 14), "hi")):
+    dma("s", A("SI", p1=8), ("in", "s0"), 1800)
+    dma("y", A("NB"), ("in", "nb"), 7000)
+    dma("y", A("QT", 0, 4096), ("in", "qs"), 10000)
+    for n, s in ((A("W1", 0, 256), "w0"), (A("LH", 0, 6), "lo"), (A("LH", 8, 14), "hi")):
+        dma("y", n, ("in", s), 11000)
+    for n, s in ((A("CI", p1=8), "coin"), (A("UI", p1=8), "us")):
         dma("s", n, ("in", s), 2500)
 
     at("c")
@@ -215,7 +217,7 @@ def plan():
     ts(A("I32W"), A("IQ"), P_, ALU.is_equal)
     move("*", A("IBW"), A("I32W"))
     move("*", A("IMW"), A("I32W"), scale=-1.0)
-    for n, c in (("I4096", 4096.0), ("I4", 4.0), ("I16", 16.0), ("IMH", -0.5)):
+    for n, c in (("I4096", 4096.0), ("I4", 4.0), ("I16", 16.0), ("I296", 296.0), ("I592", 592.0), ("IM16", -1.0)):
         move("*", A(n), IW, scale=c)
     ts(A("YW", 0, 160), A("IOT", 0, 160), PG, ALU.subtract, 31.0, ALU.is_equal)
     ts(A("M", 0, 160), A("IOT", 0, 160), PG, ALU.subtract, -97.0, ALU.is_equal)
@@ -224,7 +226,7 @@ def plan():
     move("*", A("E0B"), A("EW32", 16, 160), scale=col("RM", 0))
     mset(A("M", 256, 296), 0.0)
     mset(A("HF", 256, 296), -4096.0)
-    for p in range(16):
+    for p in range(5):
         move("*", A("UH", 144 * p, 144 * p + 144), A("BO32"), scale=col("RM", p))
     ts(col("PF", 6), PR, 15.0, ALU.add)
     ts(col("PF", 7), PR, -1.0, ALU.add)
@@ -234,7 +236,7 @@ def plan():
     ts(A("TMP", 32, 48), c16, col("PF", 7), ALU.is_equal, BIG, ALU.mult)
     tt(A("TMP", 48, 64), A("TMP", 0, 16), A("TMP", 16, 32), ALU.add)
     tt(A("PK", 0, 16), A("TMP", 48, 64), A("TMP", 32, 48), ALU.add)
-    for n in (16, 32, 64):
+    for n in (16, 32, 64, 128)[:3 + (max(b - a for a, b in PAR["c3"]) > 128)]:
         move("*", A("PK", n, 2 * n), A("PK", 0, n))
     ts(LWB, col("RM", 0), -BIG, ALU.mult, 2048.0 - LOWER, ALU.add)
     ts(SLB, col("RM", 0), -BIG, ALU.mult, 0.25 - 64.0 - LOWER, ALU.add)
@@ -262,11 +264,9 @@ def plan():
     move("*", A("YH", 0, 128), IW, scale=1024.0)
     tt(A("TBP"), A("PG", 128, 256), A("YH", 0, 128), ALU.add)
     mset(A("C64", 0, 16), 576.0 - 2304)
-    mset(A("C80", 64, 80), 144.0 - 576)
+    mset(A("C80", 64, 96), 144.0 - 576)
     act(A("IOB"), A("IOT"), ACT.Silu, 64.0)
     ops[-1]["ns"] += 1600.0
-    mset(A("IOX", 0, 256), 208.0 + 111)
-    mset(A("IOX", 256, 288), 64.0 + DEAD)
     move("*", A("I16F"), A("I32W"))
     ts(A("GE", 0, 128), IQ, 1.0, ALU.add, P_, ALU.is_equal)
     ts(col("SV", 4), PR, 0.5, ALU.is_gt)
@@ -282,17 +282,18 @@ def plan():
     ts(col("SV", 5), col("SV", 5), -1.0, ALU.mult, 8.5 / 8, ALU.add)
     tt(A("THR"), col("SV", 5), col("SV", 6), ALU.add)
     mset(A("QT", 4096, 4112), 0.0)
-    mset(A("WT", 256, 296), 0.0)
-    mset(A("WN", 256, 296), 0.0)
+    for n in ("W0", "W1"):
+        for j in range(256, 888, 296):
+            mset(A(n, j, j + 40), 0.0)
     mset(A("HT", 256, 296), -4096.0)
-    mset(A("NK", 256, NW), 0.0)
+    mset(A("NF", 256, NW), 0.0)
     mset(A("X", 4096, 4624), 0.0)
     mset(A("PT", 1024, 1160), 0.0)
     mset(A("TH"), 8.5)
     mset(A("SC_O"), 0.0)
     at("flat")
     iota(A("B4"), [[0, 290], [4, 4]])
-    iota(A("TT"), [[0, 2048]], 208)
+    iota(A("TT", 288, 2048), [[0, 1760]], 208)
 
     at("s")
     move("*", A("S0F", p1=8), A("SI", p1=8), -2048.0)
@@ -320,7 +321,8 @@ def plan():
         ts(lw, A("SC", a + 15, b, 16), LWB, ALU.add, 4095.0, ALU.min)
         nk = A("NK", a, b)
         move(e, nk, IND(A("NB"), lw), -2048.0)
-        mm([(of, IW, nk)], True, False)
+        mm([(of, A("I16F", 16, 144), nk)], True, False)
+        add("g", "sel", (A("NF", a, b), nk), [A("NF", a, b)], [nk], 190 + 2 * (b - a) * COST["cyc"])
         name = tag[0]
         at(name + "e")
         for p in range(t + 1, -1, -1):
@@ -340,24 +342,26 @@ def plan():
             mm([(hn, BO, A("M" if t >= 0 else "HT", a, b))])
             neighbours(t, a, b, lambda p: hn if p == t + 1 else K(B["hb"][p], a, b), K(B["of"][h % 2], 0, b - a), PAR["nk"])
 
-    def lists():
+    def lists(factor):
         at("l")
-        mm([(K(B["l"], 0, 80), IB, A("C80"))] + [(K(B["l"], 16 * j, 16 * j + 16), A("I4") if j < 4 else IB, A("SB16")) for j in range(5)])
-        ts(A("L"), K(B["l"], 0, 80), 576.25, ALU.add)
+        mm([(K(B["l"], 0, 96), IB, A("C80"))] + [(K(B["l"], 16 * j, 16 * j + 16), A("I4") if j < 4 else IB, A("SB16")) for j in range(6)]
+           + [(K(B["l"], 80, 96), A(m), x) for m, x in factor])
+        ts(A("L"), K(B["l"], 0, 96), 576.25, ALU.add)
 
     def steps():
         at("d")
-        move("*", A("OF"), IND(A("NK"), SRC))
+        move("*", A("OF"), IND(A("NF"), SRC))
         mm([(K(B["d"], 0, 256), A("D32"), A("OF"))])
 
     def history():
         move("*", A("HF", 0, 256), IND(A("HT"), SRC))
-        move("*", A("HC"), A("HF", 0, 256))
-        if PAR["wg"]:
-            move("*", A("WG"), IND(A("WT"), SRC), scale=2.0 ** -11)
+        if PAR["pool"]:
+            add("g", "sel", (A("HC"), A("HF", 0, 256)), [A("HC")], [A("HF", 0, 256)], 190 + 512 * COST["cyc"])
+        else:
+            move("*", A("HC"), A("HF", 0, 256))
 
     own(-1)
-    lists()
+    lists([])
     steps()
     at("f")
     history()
@@ -370,38 +374,55 @@ def plan():
                 continue
             at("x%d_" % i)
             move(e, A("X", 16 * a, 16 * b), IND(A("QT"), A("OU", a, b)))
-            k = K(B["sums"][i % len(B["sums"])], 0, 4 * (b - a))
+            k = K(B["sums"][i] if t else (i % 2, 256 + 128 * (i // 2 % 2)), 0, 4 * (b - a))
             mm([(k, IB, A("X", 16 * a + j, 16 * b, 4)) for j in range(4)])
             scan(A("PT", 4 * a, 4 * b), A("RS4", 0, 4 * (b - a)), k, ALU.mult, ALU.add)
-        pt = lambda j, a, b: IND(A("PT"), A("L", 16 * j + a // 16, 16 * j + b // 16))
-        for h, (a, b) in enumerate(PAR["c1"]):
+        pt = lambda j, a, b: IND(A("PT"), A("L", 16 * j + a // 16, 16 * j + b // 16)) if t else A("PT", 4 * a + j, 4 * b, 4)
+        c1 = PAR["cz"] if last else PAR["c1"]
+        for h, (a, b) in enumerate(c1):
             at("a%d_" % h)
             w, th = b - a, K(B["t"], a, b)
-            move("*", A("PG", a, b), pt(3, a, b), scale=2.0 ** -11)
+            if PAR["wide"][3] != "w" or t == 0:
+                move("*", A("PG", a, b), pt(3, a, b), scale=2.0 ** -11)
+            elif h == 0:
+                move("*", A("PG"), pt(3, 0, 256), scale=2.0 ** -11)
+            else:
+                tag[1][(t, "v", tag[0])] = 0
             mm([(th, A("G8", p1=8), A("U8", 256 * t + a, 256 * t + b, p1=8))])
-            tt(th, A("PG", a, b), th, ALU.mult)
-            if "v" in PAR["l1"]:
+            tt(th if "s" in PAR["l1"] else A("TS", a, b), A("PG", a, b), th, ALU.mult)
+            if "v" in PAR["l1"] and "s" in PAR["l1"]:
                 move("*", A("TS", a, b), th)
             for j in range(3):
                 c = A("CMP", 3 * a + w * j, 3 * a + w * j + w)
                 if PAR["l1"][j] == "v":
                     tt(c, pt(j, a, b), A("TS", a, b), ALU.is_gt)
                 else:
-                    pj = A("PJ3", 256 * j + a, 256 * j + b)
-                    move("*", pj, pt(j, a, b))
+                    pj = A("PJ3", 256 * j + a, 256 * j + b) if t else pt(j, a, b)
+                    if t and PAR["wide"][j] == "w" and h == 0:
+                        move("*", A("PJ3", 256 * j, 256 * j + 256), pt(j, 0, 256))
+                    elif t and PAR["wide"][j] != "w":
+                        move("*", pj, pt(j, a, b))
+                    else:
+                        tag[1][(t, "v", tag[0])] += 1
                     tt(c, pj, th, ALU.is_gt)
             v1 = K(B["v1"][h % 2], 0, 3 * w // 16)
             mm([(v1, sel(r), A("CMP", 3 * a + r, 3 * b, 16)) for r in range(16)])
             ts(A("LT", 3 * a // 16, 3 * b // 16), v1, 8.5, ALU.is_lt)
         at("w")
-        if PAR["wg"]:
-            tt(A("WN", 0, 256), pt(3, 0, 256), A("WG"), ALU.mult)
+        wn, wo = "W%d" % (t % 2), "W%d" % (1 - t % 2)
+        WN = A(wn, 0, 256)
+        tt(WN, IND(A(wo, 0, 888 if t else 296), WL), A("PG"), ALU.mult)
+        if PAR["slo"]:
+            act(A("GE", 0, 256), WN, ACT.Sign, col("LH", t), -1.0)
+            act(A("FL", 0, 256), A("GE", 0, 256), ACT.Relu)
+            tag[1][(t, "v", "w")] += 1
         else:
-            tt(A("WN", 0, 256), IND(A("WT"), SRC), A("PG"), ALU.mult)
-        ts(A("FL", 0, 256), A("WN", 0, 256), col("LH", t), ALU.is_lt)
-        ts(A("FL", 256, 512), A("WN", 0, 256), col("LH", 8 + t), ALU.is_gt)
-        ts(A("FL", 512, 768), A("WN", 0, 256), 0.0, ALU.is_equal)
-        either((A("FL", 512, 768), A("WN", 0, 256), ACT.Relu, 1.0, -2.0 ** 85))
+            ts(A("FL", 0, 256), WN, col("LH", t), ALU.is_lt)
+        ts(A("FL", 256, 512), WN, col("LH", 8 + t), ALU.is_gt)
+        ts(A("FL", 512, 768), WN, 0.0, ALU.is_equal)
+        either((A("FL", 512, 768), WN, ACT.Relu, 1.0, -2.0 ** 85))
+        move("*", A(wn, 296, 552), WN, scale=2.0)
+        move("*", A(wn, 592, 848), WN, scale=0.5)
         fl, rk = B["fl"], B["rank"]
         mm([(K(fl, 0, 48), sel(r), A("FL", r, 768, 16)) for r in range(16)])
         at("r")
@@ -415,19 +436,21 @@ def plan():
            + [(K(rk, 0, 16), A("TBZ"), A("FG", j, j + 16)) for j in HOLES])
         ts(A("PO"), K(rk, 0, 32), K(rk, 32, 33), ALU.subtract, 255.0, ALU.add)
         DD = col("SC_O", 8 * t)
-        ts(DD, K(rk, 32, 33), K(rk, 33, 34), ALU.subtract)
+        if not last:
+            ts(DD, K(rk, 32, 33), K(rk, 33, 34), ALU.subtract)
         mm([(K(rk, 36, 52), IB, A("CIN", 36, 52))] + [x for j in HOLES for x in ((K(rk, 36, 52), A("BOB"), A("SN", j, j + 16)),
                                                                                (K(rk, 36, 52), A("TBP"), A("FG", j, j + 16)))])
         ts(A("G"), K(rk, 36, 52), K(rk, 33, 34), ALU.subtract, 0.0, ALU.max)
-        move("*", A("TT", 0, 288), A("IOX"))
+        iota(A("TT", 0, 256), [[0, 256]], 208 + 111)
+        iota(A("TT", 256, 288), [[0, 32]], 64 + DEAD)
         at("p")
         cp(IND(A("TT", 0, 1328), A("PO", 16, 32)), A("IOB"))
         either((IND(A("TT", 0, 1328), A("PO", 16, 32)), A("IOB"), ACT.Silu, 0.0, 1.0))
         scan(A("SM"), A("TT", 256, 288), A("PK", 0, 32), ALU.min, ALU.add, BIG)
         ts(A("SL"), A("SM", 15, 32, 16), SLB, ALU.add, float(DEAD), ALU.min)
         po = 96 * t
-        move("*", A("SP_O", po, po + 32), IND(A("WN"), A("SL")), scale=0.5)
-        for h, (a, b) in enumerate(PAR["c1"]):
+        move("*", A("SP_O", po, po + 32), IND(A(wn, 0, 296), A("SL")), scale=0.5)
+        for h, (a, b) in enumerate(c1):
             at("b%d_" % h)
             w, m, ll = b - a, (b - a) // 16, B["ll"][h % 2]
             lt = lambda j, n=1: A("LT", 3 * a // 16 + j * m, 3 * a // 16 + (j + n) * m)
@@ -436,10 +459,17 @@ def plan():
                + [(K(ll, m * j, m * j + m), A("I16") if j else A("I4"), sb) for j in range(4)], True, False)
             mm([(K(ll, 0, m), IB, lt(i)) for i in range(3)]
                + [(K(ll, m * j, m * (j + n)), A("I4"), lt(i, n)) for j, i, n in ((1, 0, 3), (1, 1, 2), (3, 0, 1), (1, 2, 1), (2, 0, 2))], False)
-            L2 = lambda j: A("LL", a // 4 + m * j, a // 4 + m * j + m)
             ts(A("LL", a // 4, b // 4), K(ll, 0, 4 * m), 2304.25, ALU.add)
+        for h, (a, b) in enumerate(PAR["c2"]):
+            at("g%d_" % h)
+            w = b - a
+            ca, cb = [c for c in c1 if c[0] <= a and b <= c[1]][0]
+            L2 = lambda j: A("LL", (3 * ca + a + j * (cb - ca)) // 16, (3 * ca + b + j * (cb - ca)) // 16)
             if PAR["l1"][3] == "v":
                 tt(A("R", a, b), IND(A("PT"), L2(0)), A("TS", a, b), ALU.subtract)
+            elif PAR["nt"]:
+                move("*", A("P16", a, b), IND(A("PT"), L2(0)), -2048.0)
+                move("*", A("R", a, b), K(B["t"], a, b), 2048.0, -1.0)
             else:
                 move("*", A("PJ3", a, b), IND(A("PT"), L2(0)))
                 tt(A("R", a, b), A("PJ3", a, b), K(B["t"], a, b), ALU.subtract)
@@ -448,33 +478,35 @@ def plan():
                 move(PAR["xg"][i], xg(i), IND(A("X"), L2(i + 1)))
             for i in range(3):
                 k = K(B["xs"][h % 2][i], 0, w)
-                mm([(k, IB, xg(j)) for j in range(i + 1)])
+                mm([(k, IB, xg(j)) for j in range(i + 1)] + [(k, A("IM16"), A("P16", a, b))] * PAR["nt"])
                 tt(A("C2", 3 * a + w * i, 3 * a + w * i + w), k, A("R", a, b), ALU.is_lt)
                 mm([(K(B["ge"][h % 2], 0, w), A("VJ", 128 * (2 - i), 128 * (3 - i)), A("C2", 3 * a + w * i, 3 * a + w * i + w))], i == 0, i == 2)
             move("*", A("THB", a, b), IND(A("B4"), L2(0)), A("THR"))
             for c, d in PAR["c3"]:
                 if a <= c and d <= b:
-                    at("h%d_" % (c // 32))
+                    at("h%d_" % (4 * PAR["c3"].index((c, d))))
                     tt(A("GE", c, d), K(B["ge"][h % 2], c - a, d - a), A("THB", c, d), ALU.is_gt)
                     tt(A("M", c, d), A("GE", c, d), K(B["d"], c, d), ALU.mult)
         at("q")
         move("*", A("SP_O", po + 32, po + 64), IND(A("HF"), A("SL")))
         move("*", A("SP_O", po + 64, po + 96), IND(A("M"), A("SL")))
+        if not last:
+            at("c")
+            send("c", t, A("SC_O", 8 * t, 8 * t + 2), A("SC_I", 24 * t, 24 * t + 24))
+            at("q")
         send("p", t, A("SP_O", po, po + 96), A("SP_I", po, po + 96))
+        if t == 0:
+            ops[-2]["rd"].append(ops[-4]["wr"][0])
+            ops[-4]["ns"] += COST["first"]
         at("u")
         for a, b in PAR["c4"]:
             mm([(K(B["ht"], a, b), A("I16F", 16, 144), A("HC", a, b)), (K(B["ht"], a, b), A("EW32", 30 - t, 158 - t), A("M", a, b))])
             move("*", A("HT", a, b), K(B["ht"], a, b))
         if not last:
-            at("c")
-            send("c", t, A("SC_O", 8 * t, 8 * t + 2), A("SC_I", 24 * t, 24 * t + 24))
             own(t)
         at("f")
         tt(A("DB"), K(fl, 0, 16), A("TH", 48 * t + 32, 48 * t + 48), ALU.is_gt)
-        mm([(K(B["fw"], 0, 16), IB, A("DB")), (K(B["fw"], 0, 16), A("IMH"), HIGH)])
-        ts(A("FW"), K(B["fw"], 0, 16), 1.0, ALU.add)
-        mm([(K(B["fb"], r, 256, 16), uh(r), A("FW")) for r in range(16)], "each")
-        tt(A("WT", 0, 256), A("WN", 0, 256), K(B["fb"], 0, 256), ALU.mult)
+        ts(A("GF"), A("G"), 0.5, ALU.is_gt, -2.0, ALU.mult)
         at("s")
         move("*", A("SRB"), IND(A("TT"), A("PO", 0, 16)), -208.0)
         sb = K(B["sb"], 0, 16)
@@ -482,11 +514,11 @@ def plan():
            + [x for j in HOLES for x in ((sb, A("DG"), A("FG", j, j + 16)), (sb, IM1, A("E", j, j + 16)))]
            + [(sb, sel0(r), A("SRB", r, 256, 16)) for r in range(16)])
         ts(A("SB16"), sb, 144.0, ALU.min)
-        lists()
+        lists([("I592", A("FG", 0, 16)), ("I592", HIGH), ("I296", A("FG", 32, 48)), ("I296", A("DB")), ("I296", A("GF"))])
         at("i")
         mi = A("SP_I", po + 64, po + 96)
-        move("*", A("HA"), A("SP_I", po + 32, po + 64))
         if not last:
+            move("*", A("HA"), A("SP_I", po + 32, po + 64))
             ha = lambda p: K(B["hna"], 0, 32) if p == t + 1 else K(B["ha"], 32 * p, 32 * p + 32)
             mm([(ha(t + 1), A("BO32", 0, 128), mi)])
             mm([(ha(p), uh(p, 16), A("HA")) for p in range(t + 1)], "each")
@@ -495,7 +527,7 @@ def plan():
             steps()
         at("j")
         mm([(K(B["rot"], 0, 32), A("I32W", 0, 128), A("SP_I", po, po + 32))])
-        move("*", A("WT", 256, 288), K(B["rot"], 0, 32))
+        move("*", A(wn, 256, 288), K(B["rot"], 0, 32))
         mm([(K(B["rot"], 32, 64), A("I32W", 0, 128), A("SP_I", po + 32, po + 64)), (K(B["rot"], 32, 64), A("EW32", 14 - t, 142 - t), mi)])
         move("*", A("HT", 256, 288), K(B["rot"], 32, 64))
         if not last:
@@ -513,7 +545,7 @@ def plan():
         else:
             at("y")
             ts(A("YH"), IND(A("HT"), SRC), HB, ALU.add, -1.0, ALU.max)
-            act(A("YW"), IND(A("WT"), SRC))
+            act(A("YW"), IND(A(wn), WL))
             dma("y", ("out", "yh"), A("YH"))
             dma("s", ("out", "yw"), A("YW"))
     return ops
@@ -536,6 +568,7 @@ def depend(ops):
         d = set()
         for a in o["rd"]:
             d.update(j for j, b, w in seen.get(a[0], []) if w and meet(a, b))
+        o["raw"] = set(d) if PAR["soft"] else None
         for a in o["wr"]:
             d.update(j for j, b, w in seen.get(a[0], []) if meet(a, b))
         d.discard(i)
@@ -790,6 +823,15 @@ v.a0_4!:-575.5 v.x2_0!:-530.8 t.x2_0:-484.3 v.x3_0!:-454.3 t.a0_0:-392.8 v.x1_0:
 ORDER = """
 v.a1_6!:-1118.5 v.w3!:-681.9 v.a1_0!:-467.6 t.x8_0:-349.3 g.c0:-297.5 t.a0_1:-281.1 v.x3_0!:-155.5 v.x5_0!:-155.2 v.x1_0:-147.1 v.x2_0!:-110.6 t.x3_0:-91.7 v.x4_0:-79.7 g.q0:-77.2 v.a0_2!:-70.1 v.a1_2!:-69.8 v.x0_0!:-69.6 v.x5_1:-55 t.b0_1:-42.3 v.x3_1:-29.7 v.a1_4!:-23.6 t.x6_0:-23.2 t.b1_0:-12.9 t.hb4:-12 t.x5_0:-3.1 v.a0_4!:1.6 t.x1_0:28.2 t.x2_0:29.4 t.x0_0:29.4 t.x4_0:29.5 v.x7_0:30.1 t.x9_0:31.3 v.x6_0!:31.5 v.x8_0!:32.7 v.x1_1:39.7 x.c0:44.4 v.x2_1:47.2 v.x0_1:48.5 t.x7_0:50.8 v.p0!:57.5 t.hb3:65.4 v.x9_0!:67.3 t.hb1:72.4 t.hb2:79 v.b0_4!:86.1 t.a0_0:111.4 v.x4_1:137.7 v.x6_1:137.8 v.x8_1:147.6 v.x7_1:149.6 t.a1_0:151.2 v.x9_1:153.9 v.a0_0:154.9 v.a0_1:161 v.a0_6:161.1 v.a0_3:161.4 v.a0_5:161.5 v.a0_7:162.5 v.w0:168.8 t.b0_4:170.5 v.a1_1:171.4 v.w1:174.7 v.a0_8:178.3 v.w2:185.4 v.a1_7:190.9 t.n0_0:203.2 v.b1_1!:222.9 t.a1_1:235.3 v.a1_5:235.6 t.b0_0:239.1 t.w0:270.7 t.b1_5:274.8 v.b0_5!:278.8 t.b0_6:280 v.a1_3:282 t.b0_7:310.6 v.b0_3:313.7 x.q0:320 t.b0_2:322 v.b0_0:328.2 v.r0:344.7 v.b0_1:352.1 v.r1:357.6 v.r6!:366.7 t.b1_1:376.7 v.b1_9!:384 v.r5:388.7 v.a1_8:391.2 v.b0_2:396.9 v.f0:397.7 v.r2:406.5 v.b0_6:426.6 v.b1_5!:427.9 t.hb0:431.3 v.b0_9!:435.8 v.b0_8:453 t.b0_3:459 t.f0:459.3 t.b1_3:481.3 v.b1_0:489.9 v.b0_7:496.4 t.r0:496.5 t.b0_5:511 v.b1_3:515 v.n0_1:527.3 v.b1_4:535.7 v.r3:537.7 t.b1_2:538.3 v.n0_e3:543.4 t.b1_4:545.2 v.h0_0:545.3 t.b1_6:545.4 v.b1_2:547.5 v.h0_1:547.5 t.b1_7:550.6 v.n0_e0:551.5 v.r4!:562.8 v.b1_6:572.1 v.b1_7:583.4 v.b1_8:592.9 v.n0_0:599.7 v.p1:626.8 t.n1_0:637.6 v.h4_0:640 v.n0_e5:648 t.r1:650.6 v.p2:666.1 v.h4_1:673.9 v.p3:680.4 v.n0_2!:682.2 v.n0_e1:682.2 v.n0_e2:682.2 v.f1:710.9 v.n1_2!:723.6 t.n0_e5:759.4 v.n1_0:783.2 v.n0_e4:838.6 t.n0_e4:912.3 v.q0!:916.8 v.q1!:998 t.s0:999.3 t.n1_1:1000.9 t.u1:1016.6 t.n0_1:1024.4 t.n0_e0:1024.4 t.n0_e3:1024.7 t.n0_e1:1024.9 t.n0_e2:1025.2 v.s0!:1027.1 t.n1_e5:1038.2 v.n1_1:1054.2 v.n0_o0:1066.8 v.ino0:1082.7 t.n1_e2:1113 v.u1!:1130.4 v.n1_e0:1130.5 v.n1_e5:1158.1 v.ine5:1166.8 t.n1_e0:1171.9 v.in0:1190 t.u0:1195.4 v.n1_e2:1196.5 v.n1_e3:1196.6 v.n1_e4:1197.1 t.j1:1199.5 t.n1_e4:1200.4 v.n1_e1:1214.4 t.n1_e3:1216.7 t.n1_e1:1218.5 t.f1:1244.6 v.n1_o0:1265.9 v.s1:1283.1 v.i0!:1290.2 t.l0:1295.5 t.i0:1299.1 v.u0:1308.4 v.in1:1309.1 t.ine4:1315.1 v.l0:1317.6 t.j0:1326.7 v.j1:1336.8 v.in2:1338.7 t.i1:1347.3 v.ine0:1348.7 v.ine1:1348.7 v.ine2:1361.7 v.ine3:1362.3 v.ine4:1365.1 t.k0:1379.7 v.f2:1385.9 t.ine0:1390.8 t.in0:1394.4 t.ine2:1398 t.ine1:1398.1 t.ine3:1398.2 v.k0:1416.6 v.j0:1455.9 v.j2!:1460.4 v.d0!:1461.4 v.j3:1524.3 v.k1:1530.5 t.k1:1567.9 v.k2:1728 t.ine5:1798.9 t.d0:1898.1 v.k3:1930.2
 """
+ORDER = """
+v.w3!:-1037.8 x.q0:-316.7 v.a0_8:-208.8 v.b0_0:-151.4 v.a0_0:-89.4 x.c0:-84.5 v.x3_0:-43.6 v.x2_0!:-34.3 v.x5_0!:-34 t.x2_0:-26.5 v.x1_0!:-26.5 t.x3_0:-26.4 v.a0_6!:-21.9 v.x4_0:-11.2 t.hb2:3.7 t.x5_0:14.8 v.x7_0:18.6 t.x1_0:21.2 t.x8_0:35.7 g.c0:36.7 v.x0_0!:41.5 t.x4_0:45.1 t.a0_0:65.9 v.x3_1:81.5 v.x6_0!:85.1 v.x5_1:89.3 v.x2_1:89.4 v.a1_0!:94.3 v.x9_0!:95.7 v.x1_1:98.8 t.x0_0:99.7 t.x7_0:128.3 v.x4_1:131.9 v.a0_2!:136.8 t.x6_0:139.9 t.x9_0:145.1 v.x8_0:146.1 v.x0_1:146.4 v.x7_1:165 t.hb4:168.6 t.a1_0:173.1 v.x6_1:174.6 v.x8_1:174.7 v.x9_1:174.7 v.a0_4:174.7 v.a1_6!:175.7 v.a1_2!:176.3 v.a1_4!:176.3 v.a0_1:178.4 t.b1_0:178.7 v.a0_7:185.6 v.a0_3:185.9 v.a0_5:186.5 v.w0:190 v.a1_1:191.5 v.w1:191.6 t.a0_1:196.5 v.w2:198.5 g.q0:203.3 v.g0_2:218.6 g.r0:231.6 t.g0_4:237.3 v.a1_7:238.1 v.g1_4!:253.5 v.a1_5:255.5 t.hb3:265.1 t.g0_2:271.5 g.r1:276.7 t.b0_0:276.7 v.a1_3:281.7 t.b0_1:300.2 t.b1_1:307 t.g1_0:307.7 t.w0:320.6 v.r0:332 t.a1_1:332.7 t.g0_0:360.6 v.g0_4:363.9 v.r1:371.1 v.r2:381.7 v.g0_3!:386.9 v.g0_0!:406.9 v.a1_8:417.1 v.g0_8!:418.6 v.g0_1:421.8 v.g1_3!:431.4 t.r0:433.9 v.g0_6:434.7 v.g0_5:434.8 v.b1_0:449.6 t.g0_3:453.5 t.hb1:477.8 v.p0!:487.6 v.n0_2!:494.3 v.g0_7:510.5 v.n0_0:521.7 t.g0_1:531.7 t.g1_2:532 t.g0_5:543.7 v.g1_2:561.8 v.r3:567.6 t.g1_4:577.8 v.g1_0:582 v.h0_0:583.5 v.g1_1:596.6 v.h0_1:596.9 v.r4!:618.8 v.g1_6:619.4 v.g1_5:631.8 t.g1_3:640.4 t.g1_5:644.7 v.g1_8!:647.9 v.g1_7:654.8 t.n0_0:655.4 t.g1_1:689.5 t.u0:706 v.f0:707 v.q1:712.9 t.f0:740.7 v.p1:744 v.n0_1:751.1 v.h4_0:761.6 v.n1_e5:802 t.hb0:802.2 v.p2:803.5 v.h4_1:816.4 t.r1:862.3 t.n1_0:862.5 v.p3!:893 v.q0!:958.5 v.n0_e0:980.3 v.n0_e1:980.4 v.n0_e3:980.5 v.n1_0:992.6 v.n0_e2:992.9 t.n0_e3:993.9 v.n0_e5:996.9 v.s0!:1013.1 t.n0_1:1031.4 v.n1_1:1051.9 v.n0_e4:1051.9 v.r5:1052 t.u1:1058.7 t.n0_e0:1070.1 v.u1!:1116.5 v.u0!:1126.7 t.n0_e2:1126.8 v.f1:1130.8 g.n1_0:1165.5 t.n1_e5:1168.4 t.n0_e1:1199.5 t.n0_e5:1200.5 v.n1_2:1201 t.n1_e4:1237.6 t.n0_e4:1269.7 v.n0_o0:1269.7 t.s0:1281.8 g.n0_0:1289.1 v.n1_e0:1297 v.n1_e4:1297.2 v.n1_e2:1297.4 t.n1_1:1307.6 v.n1_e1:1311.6 t.l0:1312.1 v.n1_e3:1315 t.n1_e3:1316.1 v.in0:1322.4 t.n1_e2:1323.5 t.n1_e1:1326.6 t.n1_e0:1326.7 t.f1:1335.6 t.j1:1338.5 v.n1_o0:1348.6 v.s1:1349.2 t.i0:1366 t.j0:1369 v.i0:1375.2 v.ine0:1378.9 v.l0:1383.7 v.in1:1384 t.i1:1385 v.j1!:1391 v.in2!:1397.5 v.ine1:1398.7 t.ine4:1401.9 t.in0:1404.4 v.ine2:1421.9 v.ine3:1422 g.in0:1425.5 v.ine4:1429.1 t.k0:1431.9 t.ine3:1459.4 t.ine0:1459.6 t.ine2:1460 t.ine1:1460.1 v.ino0:1468.9 v.j2!:1478.7 v.k0:1501.5 v.ine5:1518.4 t.k1:1522.1 v.f2:1534.8 v.j0:1548.5 v.k1:1551 g.j0:1565 v.d0!:1641.2 t.ine5:1671.3 v.k2:1701.8 v.k3:1791.4 t.d0:1877.5
+"""
+ORDER = """
+x.q0:-1026.2 t.x1_0:-528.6 v.x2_0!:-347 v.x3_0!:-346.6 t.w0:-282.1 t.x8_0:-269.2 g.r0:-244 v.a1_6!:-191.3 v.x4_0!:-99.8 v.x11_0!:-99.7 v.a0_6!:-96.9 t.x9_0:-79.3 t.g0_5:-74.9 v.x1_0:-11.9 g.r1:-0.9 v.a0_4!:10.1 v.w3!:10.5 t.x2_0:13.3 v.x5_0:16.2 v.x6_0:16.4 t.x5_0:29.6 t.a1_1:34 v.a0_2!:70.1 v.a1_0!:71.3 v.x7_0:78.9 t.x11_0:82.3 t.x7_0:86.3 t.x6_0:86.6 t.x3_0:86.9 t.x4_0:87.1 v.x2_1:101.4 v.x0_0!:101.9 t.b1_0:102.7 t.x10_0:106.6 v.x1_1:110.4 v.x5_1:111.6 v.x6_1:113.7 t.a0_0:116.9 v.a0_0:121.4 v.g1_3!:121.9 v.x4_1:122 x.c0:124.6 t.x0_0:125 v.x10_0!:128.3 v.x9_0!:138.9 v.x8_0:139.2 v.x0_1:148 v.x11_1:168.4 v.x3_1:184.3 v.a1_4!:185.7 t.b0_0:187.8 v.x7_1:189.9 v.x8_1:190 t.g0_3:192.1 t.a1_0:195.6 v.x10_1:198.2 v.x9_1:198.2 v.w4!:199.4 v.a1_2!:206.3 v.g0_3:230.8 t.hb2:236.6 t.a0_1:238.3 v.a0_1:242.1 v.a0_5:242.1 v.a0_3:242.6 v.a0_7:244.2 v.a1_1:255.3 v.w0:262.1 t.hb4:270.3 v.a1_7:277 t.b0_1:284.8 t.n0_0:315 v.a0_8:316.1 v.a1_3:321.3 v.a1_5:321.8 v.w1:323.5 v.w2:329 v.b0_0:337.1 v.g0_2!:376.4 v.g0_4:391.3 v.g1_4!:414.3 v.g0_1:421.8 v.a1_8:424.7 t.g0_2:425.1 t.g0_0:425.6 v.r0:433.4 v.g0_0!:434.7 v.g0_8!:446.4 v.r1:450.2 v.w5!:450.3 t.g0_4:453.1 v.r2:461.3 t.b1_1:462.3 t.g1_5:495.9 v.g0_7:509.5 v.g0_6:527 v.b1_0:531.5 v.g0_5:548.6 t.hb3:548.8 v.g1_2:549.2 t.r0:557 t.g0_1:559.4 t.hb1:561.4 t.g1_0:561.6 v.r3:578.5 t.g1_2:595.5 v.g1_0:612.1 v.p0!:618.9 v.h0_0:629.6 t.g1_3:634.4 t.g1_4:657.6 t.r1:663.3 v.g1_1:705.6 v.h0_1:708.8 v.g1_8!:712.5 t.hb0:717.2 v.h4_0:721.7 v.g1_5:737.6 t.n1_e5:740.1 v.g1_6:759.5 v.g1_7:775.5 v.r4!:801.1 v.r5:806.8 v.n0_0:807.9 v.p1:827.4 v.f0:835.5 v.n0_1:844.3 t.g1_1:857.7 t.u0:920.8 g.in0:940.2 v.f1:950 t.n0_e4:994.4 v.p2:994.9 v.h4_1:1000 t.l0:1031.3 t.i1:1033.9 t.n1_e4:1048.5 v.q0:1075.4 t.n1_e1:1075.9 g.q0:1082.3 v.n0_2!:1096.1 t.n1_e0:1113.5 t.n1_0:1115.1 v.p3!:1127.7 v.q1!:1129.7 t.n0_e1:1156.5 t.n0_e2:1164.3 t.j1:1165.4 t.u1:1167.1 t.n0_1:1193.5 v.n1_2:1197.5 g.c0:1202.3 v.n0_e1:1218.8 v.n0_e4:1235.3 v.n0_e2:1235.8 v.n0_e0:1235.9 g.n1_0:1262.8 t.n0_e3:1265.6 v.n1_0:1270.1 t.n0_e0:1271.6 v.n0_e3:1272.1 t.s0:1279.8 v.n1_1:1285.9 v.j1!:1290.2 v.s0!:1302.7 v.u0!:1312.8 v.u1!:1315.6 v.n0_e5:1325.8 v.n0_o0:1333.2 v.n1_e0:1333.6 v.n1_e2:1333.8 t.n1_e2:1334.8 v.n1_e4:1334.9 t.n1_1:1335.7 v.in2!:1335.7 v.n1_e1:1345.8 v.n1_e3:1347.1 t.n1_e3:1356.4 g.n0_0:1356.4 v.n1_e5:1357.9 v.n1_o0:1362.1 t.ine4:1375.6 t.n0_e5:1376.3 v.s1:1377.4 v.ine5:1387.6 t.i0:1392.1 t.j0:1393.2 v.in0:1407.3 v.i0:1415.6 v.l0:1439.2 v.in1:1444.6 t.ine1:1446.8 v.ine1:1451.1 v.ine2:1451.5 v.ine0:1458 v.ine3:1458.4 v.ine4:1462.4 t.in0:1472.7 t.ine0:1472.8 t.ine3:1477.9 t.ine2:1477.9 v.ino0:1490.9 v.j2!:1544.7 g.j0:1545.7 v.j0:1549.1 t.ine5:1551.6 t.k0:1558.2 v.k0:1576.4 v.d0!:1581.6 t.k1:1639 v.k1:1643.7 v.k2:1762.2 t.d0:1927.2 v.k3:2389.2
+"""
+ORDER = """
+x.q0:-578.1 t.b1_0:-295.6 v.g0_0:-284.8 v.a0_6!:-284.3 t.x6_0:-234.2 t.b0_1:-211.9 v.a0_1:-104.8 t.x9_0:-42.8 g.r1:-42.6 x.c0:-5.8 v.x0_0:1.3 v.x11_0!:4.6 v.x1_0!:5.5 v.x4_0!:5.6 v.x2_0!:7.3 v.x7_0!:7.5 v.a1_6!:25.4 t.x1_0:27.3 t.x2_0:29.3 v.x6_0:29.5 v.x5_0:48.2 t.a0_1:62.7 v.a0_0:76.6 t.x8_0:79.8 g.r0:87 t.a1_0:87.6 v.x11_1:113 t.hb2:119.2 t.x4_0:129.3 t.hb3:143.6 v.x3_0!:146.1 v.x1_1:147.5 v.x10_0!:150 t.x5_0:165.8 t.x7_0:166 v.x9_0!:167.9 v.x4_1:171 v.x2_1:178.4 v.x5_1:178.8 v.x6_1:179.8 t.x11_0:182.9 t.x0_0:187.5 t.x3_0:188 t.x10_0:188.2 v.x8_0:191.1 v.a1_0!:199.4 v.a0_4!:200.7 v.x0_1:201 t.hb4:202.4 v.a0_2!:207 v.x7_1:217.1 v.x3_1:220.9 v.x10_1:226.7 v.x8_1:230.4 t.a0_0:234.6 v.a1_8:256.9 v.x9_1:262.7 v.a1_5:269.3 v.a0_3:275.2 v.a0_5:282.3 v.a0_7:288.4 v.a1_1:290.8 v.w0:293.1 v.a1_7:308.7 v.a0_8:313 t.b0_0:330.9 v.a1_2!:331.4 v.a1_4!:334.4 v.a1_3:341.5 v.w1:346.2 v.w2:354.9 v.b0_0:362.8 t.a1_1:374.4 v.g0_2:381.9 t.g1_5:399.2 v.h0_0:409.5 v.w4!:410.2 v.w3!:413.3 v.r0:462.7 v.w5!:473.3 v.g0_1:507.6 v.g0_4!:532.2 v.g0_3!:611.3 t.w0:642 t.b1_1:697.1 v.g0_8!:707.8 v.r1:714.3 v.r2:714.9 v.b1_0:716.9 t.g0_0:728.9 t.g0_4:729.2 t.g0_2:742.1 v.g0_5:748 v.g0_6:748.2 v.g0_7:749.5 t.r0:759.6 t.g0_1:766.5 t.g0_5:780.4 v.g1_2!:786.5 v.g1_3!:792.3 v.r3:796.6 v.g1_0!:826.4 v.g1_4:829.3 t.g0_3:899.2 t.g1_0:899.3 t.g1_2:904.6 t.n0_e3:913 t.r1:920.1 t.g1_4:920.3 t.hb1:927.8 v.n0_0:938.5 v.g1_1:940.5 v.h0_1:959.3 t.g1_3:966.7 v.g1_6:974.2 t.n0_1:977.5 t.n1_1:986.2 v.g1_5:994.4 v.g1_7:997.7 g.q0:999.7 v.p0!:1043.3 t.n0_0:1045 t.hb0:1050.4 v.r4!:1058.5 v.g1_8!:1061.1 t.s0:1089.3 g.c0:1105.2 t.g1_1:1119.9 v.p1:1136.5 t.n0_e4:1146.3 v.n0_1:1158.9 t.u0:1161 t.n1_e0:1169 v.h4_0:1189.3 t.n1_0:1210.9 v.p2:1212 v.r5:1218.2 v.h4_1:1222.2 v.p3:1223.5 v.n0_e5:1230.7 v.n0_2!:1232 v.q0!:1232.7 v.n0_e2:1253.5 v.n0_e0:1253.6 t.n0_e1:1254.9 v.q1!:1256.4 v.n0_e1:1262.9 v.n0_e3:1263 v.n1_0:1276.3 t.u1:1278.7 v.n1_e5:1282.4 v.n0_e4:1294.8 v.n1_1:1296 t.n0_e0:1301.1 t.n0_e2:1301.3 v.s0!:1314.9 v.n1_e4:1332.3 g.n1_0:1333.8 v.n0_o0:1341.4 v.u1!:1343.7 v.f1:1345.3 v.n1_2!:1345.3 t.n1_e4:1346.8 v.n1_e0:1357.2 v.n1_e2:1366.9 v.n1_e1:1367.9 v.n1_e3:1368.1 v.u0!:1374.9 t.n1_e1:1377.5 t.n1_e2:1377.5 t.n1_e3:1377.5 v.n1_o0:1377.5 t.n1_e5:1381.9 v.f0:1388 v.s1:1388.3 t.n0_e5:1388.8 t.l0:1399.1 t.ine2:1413.8 t.i0:1419.7 v.in0:1435.7 v.i0:1441.2 t.j0:1445.2 v.l0:1451.6 v.in1:1451.8 v.j1:1483.2 t.j1:1483.6 v.ino0:1503.2 v.in2:1504.4 v.ine2:1525.7 t.ine4:1525.7 v.ine0:1527.9 v.ine1:1528 g.n0_0:1528.5 t.i1:1533.8 v.ine3:1534.1 v.ine4:1534.9 g.j0:1543.2 t.in0:1552.1 t.ine3:1552.5 t.ine1:1552.8 t.ine0:1552.9 v.ine5:1555.5 g.in0:1561.2 v.j0!:1599.6 t.k0:1604.3 t.k1:1622.6 v.j2!:1623 v.k0:1640.5 t.ine5:1661.6 v.k1:1674.2 v.d0!:2002.2 v.k2:2091.6 t.d0:2118.9 v.k3:2679.1
+"""
 STEP = 13700.0
 
 
@@ -802,52 +844,91 @@ def keys(text):
     return tau, way
 
 
+def unread(ops, i, d):
+    return ops[i]["raw"] is not None and d not in ops[i]["raw"] and all(ops[j]["kind"] not in ("dma", "send", "recv") for j in (i, d))
+
+
 def part(ops, steps):
     idx = [i for i, o in enumerate(ops) if o["step"] in steps]
     at, res = {i: j for j, i in enumerate(idx)}, {"x": -1}
     num = lambda x: res.setdefault(x, len(res) - 1)
     s = dict(idx=idx, name=[ops[i]["id"] for i in idx], step=[STEP * ops[i]["step"] for i in idx], lat=[ops[i]["lat"] for i in idx])
     s["pre"] = [[(at[d], 0.0 if d in ops[i]["soft"] else ops[d]["lat"] + COST["hop"]) for d in sorted(ops[i]["dep"]) if d in at] for i in idx]
-    s["alt"] = [[(num(a[0]), a[3], [num(b) for b in ops[i]["banks"]], a[3] + ops[i]["lat"] + COST["hop"])
+    s["alt"] = [[(num(a[0]), a[3], [num(b) for b in ops[i]["banks"]], a[3] + ops[i]["lat"] + COST["hop"], 0.0)
                  for a in ops[i].get("alt", [(ops[i]["eng"], 0, 0, ops[i]["ns"])])] for i in idx]
+    s["free"] = [{at[d] for d in ops[i]["dep"] if d in at and unread(ops, i, d)} for i in idx]
     s["res"] = len(res)
+    above, used = [], set()
+    for i, p in enumerate(s["pre"]):
+        far = 0
+        for j, d in p:
+            far |= above[j]
+        s["pre"][i] = [(j, d) for j, d in p if not far >> j & 1 or s["lat"][j] > 100]
+        for j, d in p:
+            far |= 1 << j
+            used.add(j)
+        above.append(far)
+    s["ends"] = [i for i in range(len(idx)) if i not in used]
     return s
+
+
+def rest(s, tau, way, pool):
+    end, start, key, why, kind, final, prev, held = replay(s, tau, way)
+    edge = min(key[i] for i, w in enumerate(s["name"]) if w in pool)
+    keep = [i for i in range(len(key)) if key[i] >= edge]
+    at, fin, busy = {i: j for j, i in enumerate(keep)}, {}, {}
+    for i in range(len(key)):
+        if i not in at:
+            e, ns, banks, hold, t = s["alt"][i][way.get(s["name"][i], 0) if len(s["alt"][i]) > 1 else 0]
+            fin[i] = start[i] + ns
+            for r, f in [(e, fin[i])] + [(b, start[i] + hold) for b in banks]:
+                busy[r] = max(busy.get(r, 0.0), f)
+    new = {w: [s[w][i] for i in keep] for w in ("idx", "name", "step", "lat")}
+    new["pre"] = [[(at[j], d) for j, d in s["pre"][i] if j in at] for i in keep]
+    new["alt"] = [[a[:4] + (max([fin[j] + d for j, d in s["pre"][i] if j in fin] + [busy.get(r, 0.0) for r in [a[0]] + a[2] if r >= 0] + [0.0]),)
+                   for a in s["alt"][i]] for i in keep]
+    new.update(free=[set()] * len(keep), res=s["res"], ends=[at[i] for i in s["ends"] if i in at], edge=edge)
+    return new
 
 
 def replay(s, tau, way):
     pre, name, n = s["pre"], s["name"], len(s["idx"])
-    key = [0.0] * n
+    key, eng, free, edge = [0.0] * n, [0] * n, s["free"], s.get("edge", -1e18)
     for i in range(n):
         x = tau[name[i]] + s["step"][i]
+        if x < edge:
+            x = edge
         for j, d in pre[i]:
             if key[j] >= x:
                 x = key[j] + 1e-3
         key[i] = x
     start, fin, why, kind, prev = [0.0] * n, [0.0] * n, [-1] * n, [0] * n, [-1] * n
-    last, bank, end, final, held = [-1] * s["res"], [{} for _ in range(s["res"])], 0.0, 0, [()] * n
-    for i in sorted(range(n), key=lambda i: key[i]):
-        al = s["alt"][i]
-        e, ns, banks, hold = al[way.get(name[i], 0)] if len(al) > 1 else al[0]
-        t, w, kd = 0.0, -1, 0
+    last, bank, other, held, alt = [-1] * s["res"], [(-1, -1.0, -1)] * s["res"], [(-1, -1.0, -1)] * s["res"], [()] * n, s["alt"]
+    for f, i in sorted(zip(key, range(n))):
+        al = alt[i]
+        e, ns, banks, hold, t = al[way.get(name[i], 0)] if len(al) > 1 else al[0]
+        w, kd = -1, 0
+        eng[i] = e
         for j, d in pre[i]:
-            if fin[j] + d > t:
+            if fin[j] + d > t and not (eng[j] == e and j in free[i]):
                 t, w = fin[j] + d, j
         if e >= 0:
             j = prev[i] = last[e]
             if j >= 0 and fin[j] >= t:
                 t, w, kd = fin[j], j, 1
             if banks:
-                held[i] = [(j, f) for b in banks for en, (j, f) in bank[b].items() if en != e]
-                for j, f in held[i]:
+                h = held[i] = [other[b] if bank[b][2] == e else bank[b] for b in banks]
+                for j, f, en in h:
                     if f > t:
                         t, w, kd = f, j, 2
-                for b in banks:
-                    bank[b][e] = (i, t + hold)
+                for b, x in zip(banks, h):
+                    other[b], bank[b] = x, (i, t + hold, e)
             last[e] = i
         start[i], fin[i], why[i], kind[i] = t, t + ns, w, kd
-        if t + ns + s["lat"][i] > end:
-            end, final = t + ns + s["lat"][i], i
-    return end, start, key, why, kind, final, prev, held
+    end, final = max((fin[i] + s["lat"][i], i) for i in s["ends"])
+    if "base" in s:
+        end -= (1 + PAR["pull"]) * fin[s["base"]]
+    return end + PAR["pull"] * sum(fin) / n, start, key, why, kind, final, prev, held
 
 
 def improve(s, tau, way, pool, rounds, heat, seed):
@@ -865,6 +946,8 @@ def improve(s, tau, way, pool, rounds, heat, seed):
     for n in range(rounds):
         end, start, key, why, kind, i, prev, held = cur
         path = []
+        if rnd() < PAR["any"]:
+            i = int(rnd() * len(name))
         while i >= 0:
             path.append(i)
             i = why[i]
@@ -874,6 +957,15 @@ def improve(s, tau, way, pool, rounds, heat, seed):
             w = one(c if c and rnd() < 0.6 else both)
             oldway[w] = way.get(w, 0)
             way[w] = 1 - oldway[w]
+            if r < 0.1:
+                old[w] = tau[w]
+                tau[w] = key[name.index(w)] - step[name.index(w)] + (rnd() - 0.5) * 3000
+            if r < 0.05:
+                c = [u for u in both if way.get(u, 0) == way[w] and u != w and abs(tau[u] - tau[w]) < 3000]
+                if c:
+                    u = one(c)
+                    oldway[u] = way.get(u, 0)
+                    way[u] = 1 - oldway[u]
         elif r < 0.3:
             w = one(names)
             old[w] = tau[w]
@@ -914,6 +1006,10 @@ def improve(s, tau, way, pool, rounds, heat, seed):
     return best[0]
 
 
+WINDOWS = [((-1, 0, 1), (-1, 0), 2.6, 120.0, 13), ((3, 4, 5), (4, 5), 14, 90.0, 6), ((-1, 0, 1, 2), (0, 1), 1.5, 30.0, 4),
+           ((1, 2, 3, 4), (2, 3), 1.5, 30.0, 6)]
+
+
 def ordered(rounds):
     ops = plan()
     depend(ops)
@@ -930,17 +1026,40 @@ def ordered(rounds):
     for o in ops:
         if o["id"] not in tau:
             tau[o["id"]], way[o["id"]] = tau.get(o["id"][1:], 15000.0), way.get(o["id"][1:], 0)
-    ends = [improve(part(ops, (1, 2, 3, 4)), tau, way, {w for w in tau if w[0] not in "pz"}, rounds[0], 60.0, 1),
-            improve(s, tau, way, {w for w in tau if w[0] == "p" and "load" not in w}, rounds[1], 100.0, 2),
-            improve(part(ops, (4, 5)), tau, way, {w for w in tau if w[0] == "z"}, rounds[2], 60.0, 3)]
+    ends = [improve(s, tau, way, {w for w in tau if w[0] == "p" and "load" not in w}, rounds[0], 100.0, 2)]
+    for o in ops:
+        w = "%d%s" % (o["step"] + 1, o["id"])
+        tau[w], way[w], o["id"] = tau[o["id"]], way[o["id"]], w
+        if o["step"] == NS - 1 and w[4] in "abgh" and w[5] in "14" and PAR["lag"]:
+            tau[w] = tau[w[1:5] + "0" + w[6:]] + PAR["lag"]
+        if o["step"] == 0:
+            e, u = w[1:].split(".")
+            if u[0] == "x":
+                m, j = [int(x) for x in u[1:].split("_")]
+                tau[w], way[w] = -4000.0 + 400 * m + (900 if e == "t" else 1300 * j), int(m % 4 != 1)
+            elif u[0] in "abghn" and u[1] == "0":
+                tau[w] -= PAR["ahead"]
+            elif u in ("r4", "c0"):
+                tau[w] = 0.0
+    for steps, mine, n, heat, seed in WINDOWS:
+        pool = {o["id"] for o in ops if o["step"] in mine and "load" not in o["id"]
+                and (o["step"] > mine[0] or o["step"] < 0 or o["id"].split(".")[1][0] in "nslidjku")}
+        s = rest(part(ops, steps), tau, way, pool)
+        for w, x in zip(s["name"], replay(s, tau, way)[2]):
+            tau[w] = x - STEP * (int(w[0]) - 1)
+        ends.append(improve(s, tau, way, pool, int(n * rounds[1]), heat, seed))
+        for w, x in zip(s["name"], replay(s, tau, way)[2]):
+            tau[w] = x - STEP * (int(w[0]) - 1)
     s = part(ops, range(-1, NS))
-    ends.append(improve(s, tau, way, {w for w in tau if "load" not in w}, rounds[3], 20.0, 4))
+    ends.append(improve(s, tau, way, {w for w in tau if "load" not in w}, rounds[2], 15.0, 4))
     end, start, key, why, kind, final, prev, held = replay(s, tau, way)
     for i, o in enumerate(ops):
         if "alt" in o:
             o["eng"], o["kind"], o["args"], o["ns"] = o["alt"][way.get(o["id"], 0)]
         o["t0"] = start[i]
-        o["dep"] |= {j for j, f in held[i]}
+    for i, o in enumerate(ops):
+        o["soft"] |= {j for j in o["dep"] if ops[j]["eng"] == o["eng"] and unread(ops, i, j)}
+        o["dep"] |= {j for j, f, e in held[i] if j >= 0}
     return ops, sorted(range(len(ops)), key=lambda i: key[i]), ends, tau, way
 
 
@@ -978,7 +1097,7 @@ def rank_program(g, core, T, topo):
         es = topo.engines(src, dst)
         if kind == "c":
             k = len(es) // 4
-            return es[k * (d - 1):k * d]
+            return es[:2 * k] if d == 1 else es[k * d:k * (d + 1)]
         return es
 
     needed = set()
@@ -1054,6 +1173,8 @@ def rank_program(g, core, T, topo):
                 r = q.activation(ap(a[0]), ap(a[1]), a[2])
             else:
                 r = q.activation(ap(a[0]), ap(a[1]), a[2], bias=ap(a[3]), scale=ap(a[4]))
+        elif k == "sel":
+            r = q.affine_select(ap(a[0]), ap(a[1]), [[0, width(a[0])]], ALU.is_ge, 0.0, 0, 0)
         elif k == "iota":
             if SCRATCH[a[0][0]][2] == I32:
                 r = q.iota(ap(a[0]), a[1], a[2], a[3])

@@ -1,58 +1,57 @@
-import math
 from concourse.bass import DstId, RemoteDMATransfer
 from concourse.mybir import AluOpType as ALU, AxisListType, ActivationFunctionType as ACT
 
 NS = 6
 F32, BF, F16, I32, U16 = "float32", "bfloat16", "float16", "int32", "uint16"
-DEAD = 288
-NW = 304
-ZR = 1536
+DEAD = 256
+TW = 296
+ZR = 256
 BIG, LOWER = 32768.0, -16384.0
+LOW = 254.0 * 4096
+HALF = 2.0 ** 23 - 0.5
 
 SB = {
     "NB": (4096, I32), "QT": (4112, BF), "LH": (16, F32), "SI": (256, I32), "UI": (1536, I32), "CI": (1536, I32),
-    "S0F": (256, F32), "U8": (1536, BF), "CB": (1792, BF), "PJ3": (768, F32), "TH": (288, F32), "TH2": (96, F32),
-    "PI": (1, I32), "PJ": (4, I32), "PF": (8, F32), "GQ": (144, F32), "IQ": (144, F32), "C16": (48, F32),
-    "IOT": (256, F32), "IOB": (256, F32), "IOX": (288, F32), "TMP": (64, F32), "PK": (256, F32),
-    "EWB": (144, BF), "E0B": (144, BF), "BO32": (144, F32), "BOB": (128, BF), "BON": (128, BF), "RM": (16, F32),
-    "UH": (16 * 144, F16), "I32W": (144, F32), "IBW": (144, BF),
-    "I4": (128, BF), "I16": (128, BF), "I4096": (128, BF), "IMW": (144, BF), "IMH": (128, BF),
-    "I16F": (144, F16), "D32": (128, F16), "VJ": (384, BF), "THR": (1, F32), "EW32": (160, F32), "B4": (1160, F32),
-    "THB": (256, F32), "GE": (256, F32), "M": (296, F32), "OF": (256, F16), "DG": (128, BF), "TBZ": (128, BF), "TBR": (128, BF),
-    "RS4": (256, F32), "RS48": (48, F32), "C64": (64, BF), "C80": (96, BF), "CIN": (52, BF), "M16": (48, F32), "TBP": (128, BF), "G": (16, BF), "CWB": (16, BF),
-    "CW": (32, F32), "G8": (128, BF), "G832": (128, F32), "E8": (144, BF),
-    "X": (4624, BF), "PT": (1160, F32), "TS": (256, F32), "PG": (256, F32), "CMP": (768, BF), "LT": (48, BF), "LT2": (48, BF),
-    "LL": (64, U16), "L": (96, U16), "LS": (16, U16), "SB16": (16, BF), "R": (256, F32), "XG": (768, BF), "C2": (768, BF),
-    "SC": (288, F32), "LW": (18, U16), "NK": (288, F16), "NF": (NW, F32), "EQ": (6 * 288, BF), "OU": (288, U16),
-    "W0": (888, F32), "W1": (888, F32), "GF": (16, BF), "IM16": (128, F16), "P16": (256, F16), "I296": (128, BF), "I592": (128, BF), "HT": (296, F32), "HC": (256, F16), "FL": (768, BF), "FG": (48, BF), "DB": (16, BF),
-    "SN": (48, BF), "E": (48, BF), "HF": (296, F32), "WG": (256, F32), "PO": (32, U16), "TT": (2048, F32), "SM": (32, F32), "SL": (2, U16), "SV": (8, F32),
-    "SRB": (256, BF), "FW": (16, F16), "YW": (256, F32), "YH": (256, F32),
-    "SC_O": (NS * 8, BF), "SC_I": (NS * 24, BF), "SP_O": (NS * 96, F32), "SP_I": (NS * 96, F32),
-    "HA": (32, F16),
+    "S0F": (256, F32), "U8": (1536, BF), "CB": (1536, BF), "TH": (288, F32), "UB": (1576, F32), "UA": (32, F32),
+    "PI": (1, I32), "PJ": (4, I32), "PF": (12, F32), "GQ": (144, F32), "IQ": (144, F32), "C16": (48, F32),
+    "IOT": (256, F32), "IOB": (256, F32), "TMP": (64, F32), "T1": (128, F32), "T2": (128, F32), "PK": (128, F32),
+    "EWB": (144, BF), "E0B": (144, BF), "EW16": (144, F16), "BO32": (144, F32), "BOB": (128, BF), "BO16": (128, F16),
+    "RM": (16, F32), "UH": (5 * 144, F16), "US": (5 * 128, F32), "I32W": (144, F32), "IBW": (144, BF), "IMW": (144, BF),
+    "I16F": (128, F16), "I296": (128, BF), "I592": (128, BF), "R16": (128, F16), "R4096": (128, BF), "DIF": (128, BF),
+    "THR": (1, F32), "DG": (128, BF), "TBZ": (128, BF), "TBR": (128, BF), "RS48": (48, F32), "RSX": (1536, BF),
+    "CIL": (18, F16), "M16": (48, F32), "CWB": (16, BF), "G8": (128, BF), "G832": (128, F32), "E8": (144, BF),
+    "ONE": (TW, BF), "JC": (2, F32),
+    "X": (4608, F16), "CMP": (4608, BF), "Y": (288, F32), "GE": (288, BF), "M": (288, F16), "SC": (320, F32), "LW": (20, U16),
+    "NK": (320, F16), "NKP": (288, F16), "NF": (TW, F32), "NA": (32, F32), "EQ": (6 * 320, BF), "OU": (288, U16),
+    "W": (3 * TW, F32), "WP": (256, F32), "WA": (32, F32), "WB": (32, F32), "HT": (TW, F32), "HC": (288, F16), "HR": (32, F32),
+    "FL": (768, BF), "FG": (48, BF), "DB": (16, BF), "SN": (48, BF), "E": (48, BF), "PO": (32, U16), "TT": (1584, F32),
+    "SM": (32, F32), "SL": (2, U16), "HS": (TW, BF), "H2": (2 * TW, BF), "CU": (TW, F16), "AL": (4, U16), "SV": (8, F32),
+    "SRB": (256, BF), "SB16": (16, BF), "SRC": (16, U16), "WL": (16, U16), "YW": (TW, F32), "YH": (TW, F32),
+    "SC_O": (NS * 8, BF), "SC_I": (NS * 24, BF), "SP_O": (NS * 64, F32), "SP_I": (NS * 64, F32),
 }
 SCRATCH = {k: ("sbuf", [128, v[0]], v[1]) for k, v in SB.items()}
 for _k in range(8):
     SCRATCH["K%d" % _k] = ("psum", [128, 512], F32)
 
-NDMA = 32
+NDMA = 10
 SEMAPHORES = (["ev", "es", "et", "eg", "sent"] + ["d%d" % i for i in range(NDMA)]
-              + ["rc%d" % t for t in range(NS - 1)] + ["r%s%d" % (k, t) for k in "p" for t in range(NS)])
+              + ["rc%d" % t for t in range(NS - 1)] + ["rp%d" % t for t in range(NS)])
 
-PAR = dict(
-    pieces=[("*", a, a + 32) for a in range(0, 192, 32)] + [("*", a, a + 16) for a in (192, 224, 256, 272, 208, 240)], nt=0, slo=False, wide="hhhh", l1="ssss", wg=False, pull=0.2, lag=0, ahead=600.0, any=0.2, soft=False, pool=True,
-    c1=[(0, 128), (128, 256)], cz=[(0, 128), (128, 256)], c2=[(0, 128), (128, 256)], c3=[(0, 128), (128, 256)], c4=[(0, 128), (128, 256)], nk="*", nka="*", hc="*", xg="***", rounds=(4000, 10000, 1000),
-    bank=dict(sums=[(4, 0), (3, 0), (4, 128), (3, 128), (5, 0), (4, 256), (5, 128), (3, 0), (5, 256), (4, 0), (5, 192), (3, 64)], t=(3, 0),
-              hb=[(0, 0), (0, 256), (1, 0), (1, 256), (2, 256)], xs=[[(4, 0), (4, 128), (4, 256)], [(5, 0), (5, 128), (5, 256)]],
-              v1=[(4, 384), (5, 384)], ge=[(6, 128), (7, 128)], ll=[(6, 0), (7, 0)], hn=[(4, 384), (5, 384)], d=(3, 256), ht=(3, 0),
-              of=[(6, 128), (7, 128)], fl=(2, 0), rank=(2, 48), sb=(2, 100), l=(2, 116), fw=(2, 196), cnt=(7, 304), rot=(7, 320),
-              fb=(0, 0), ha=(1, 0), hna=(2, 224), ofa=(6, 256)))
-COST = dict(cyc=0.92, pe=0.48, gat=1.56, sca=3.8, hop=165.0, dma=2000.0, rem=3000.0, iss=1100.0, first=1500.0, look=60.0)
+PIECES = [(a, a + 32) for a in range(0, 192, 32)] + [(a, a + 16) for a in range(192, 288, 16)]
+SUMS, CUT = [(0, 64), (64, 128), (128, 224), (224, 288)], [32, 32, 48, 32]
+NEAR, HIST, LISTS = [(0, 128), (128, 192), (192, 288)], [(0, 128), (128, 224), (224, 256)], [(0, 64), (64, 256)]
+B = dict(p15=[(3, 0), (4, 0), (3, 64), (5, 288)], votes=[(4, 64), (3, 160), (4, 128), (5, 416)],
+         one=[(4, 224), (4, 288), (4, 352), (5, 192)], hn=[(6, 128), (7, 64), (5, 0)], of=[(6, 0), (7, 0), (5, 96)],
+         hb=[[(0, 0), (0, 128), (0, 256), (0, 384), (6, 320)], [(2, 192 + 64 * p) for p in range(5)], [(1, 96 * p) for p in range(5)]],
+         ht=(3, 256), htb=(5, 480), fl=(2, 0), rank=(2, 48), cnt=(2, 140), sb=(3, 224), l=(3, 240), rot=(5, 352), ha=(7, 320),
+         ofa=(6, 256))
+OPEN = (5, 6, 7)
 
 
-def A(name, c0=0, c1=None, step=1, p0=0, p1=128, ps=1):
+def A(name, c0=0, c1=None, step=1, p1=128):
     if c1 is None:
         c1 = SCRATCH[name][1][1]
-    return (name, p0, p1, c0, c1, step, ps)
+    return (name, 0, p1, c0, c1, step, 1)
 
 
 def IND(win, off):
@@ -69,10 +68,6 @@ def is_ap(a):
     return isinstance(a, tuple)
 
 
-def size(a):
-    return {F32: 4, I32: 4}.get(SCRATCH[a[0]][2], 2)
-
-
 def landing(kind, t, src, d):
     if kind == "c":
         return A("SC_I", 24 * t + 8 * (d - 1), 24 * t + 8 * (d - 1) + 2)
@@ -80,12 +75,12 @@ def landing(kind, t, src, d):
 
 
 def plan():
-    ops, now, tag, B = [], [-1], ["", {}], PAR["bank"]
+    ops, now, tag = [], [-1], ["", {}]
 
     def at(name):
         tag[0] = name
 
-    def add(eng, kind, args, outs, ins, ns, lat=0.0):
+    def add(eng, kind, args, outs, ins):
         rd, wr = [], []
         for a in ins:
             if is_ap(a):
@@ -98,43 +93,30 @@ def plan():
                 wr.append(a)
         key = (now[0], eng, tag[0])
         tag[1][key] = tag[1].get(key, -1) + 1
-        name = "%s%s.%s%d" % ({-1: "p", NS - 1: "z"}.get(now[0], ""), eng, tag[0], tag[1][key])
-        ops.append(dict(step=now[0], eng=eng, kind=kind, args=args, rd=rd, wr=wr, ns=ns, lat=lat, id=name))
+        name = "%d%s%s%d" % (now[0] + 1, "" if eng == "v" else eng.upper(), tag[0], tag[1][key])
+        ops.append(dict(step=now[0], eng=eng, kind=kind, args=args, rd=rd, wr=wr, id=name))
         return ops[-1]
 
-    def vcost(out, ins, k=1.0):
-        n = width(out)
-        if out[0] == "@":
-            return 50 + n * COST["sca"] * COST["cyc"]
-        if ins[0][0] == "@":
-            return 55 + n * COST["gat"] * COST["cyc"]
-        if k == 1.0 and all(size(a) == 2 for a in [out] + ins):
-            k = 0.5
-        return max(64, n * k) * COST["cyc"]
-
     def cp(out, in_):
-        add("v", "cp", (out, in_), [out], [in_], vcost(out, [in_]))
+        add("v", "cp", (out, in_), [out], [in_])
 
     def tt(out, a, b, op):
-        k = 2.0 if a[0][0] != "K" and b[0][0] != "K" else 1.001
-        add("v", "tt", (out, a, b, op), [out], [a, b], vcost(out, [a, b], k))
+        add("v", "tt", (out, a, b, op), [out], [a, b])
 
     def ts(out, a, s1, op0, s2=None, op1=None):
-        add("v", "ts", (out, a, s1, s2, op0, op1), [out], [a, s1, s2], vcost(out, [a]))
+        add("v", "ts", (out, a, s1, s2, op0, op1), [out], [a, s1, s2])
 
     def scan(out, d0, d1, op0, op1, first=0.0):
-        add("v", "scan", (out, d0, d1, op0, op1, first), [out], [d0, d1], vcost(out, [d0, d1]))
+        add("v", "scan", (out, d0, d1, op0, op1, first), [out], [d0, d1])
 
     def mset(out, c):
-        add("v", "mset", (out, c), [out], [], max(64, width(out) * size(out) / 4) * COST["cyc"])
+        add("v", "mset", (out, c), [out], [])
 
-    def act(out, in_, func=ACT.Identity, bias=0.0, scale=1.0):
-        add("s", "act", (out, in_, func, bias, scale), [out], [in_, bias, scale], vcost(out, [in_], 1.001) + 15)
+    def act(out, in_, func, bias=0.0, scale=1.0, total=None):
+        sums = [total] if total else []
+        add("s", "act", (out, in_, func, bias, scale) + tuple(sums), [out] + sums, [in_, bias, scale])
 
-    def move(e, out, in_, bias=0.0, scale=1.0):
-        if e == "s":
-            act(out, in_, bias=bias, scale=scale)
-            return
+    def move(out, in_, bias=0.0, scale=1.0):
         if bias == 0.0 and scale == 1.0:
             cp(out, in_)
         elif scale == 1.0:
@@ -143,56 +125,51 @@ def plan():
             ts(out, in_, scale, ALU.mult)
         else:
             ts(out, in_, scale, ALU.mult, bias, ALU.add)
-        if e == "*":
-            either((out, in_, ACT.Identity, bias, scale))
-
-    def either(args):
-        o = ops[-1]
-        o["alt"] = [(o["eng"], o["kind"], o["args"], o["ns"]), ("s", "act", args, vcost(args[0], [args[1]], 1.001) + 15)]
+        ops[-1]["alt"] = (out, in_, ACT.Identity, bias, scale)
 
     def iota(out, pat, base=0, ch=0):
-        add("g", "iota", (out, pat, base, ch), [out], [], 130 + 2 * width(out) * COST["cyc"])
+        add("g", "iota", (out, pat, base, ch), [out], [])
+
+    def fill(out, c):
+        iota(out, [[0, width(out)]], c)
 
     def mm(items, start=True, stop=True):
-        ns = sum(max(64, width(r)) * (4 if size(r) == 4 else 1) * COST["pe"] for o, l, r in items)
-        tok = ("grp" + items[0][0][0], 0, 128, 0, 1, 1)
-        op = add("t", "mm", (items, start, stop), [o for o, l, r in items], [x for o, l, r in items for x in (l, r)], ns, 40.0)
-        if tok[0] in ("grpK6", "grpK7"):
-            op["wr"].append(tok)
-        else:
-            assert start and stop
+        op = add("t", "mm", (items, start, stop), [o for o, l, r in items], [x for o, l, r in items for x in (l, r)])
+        if int(items[0][0][0][1]) in OPEN:
+            op["wr"].append(("grp" + items[0][0][0], 0, 128, 0, 1, 1, 1))
 
-    def dma(eng, out, in_, ns=COST["dma"]):
-        add(eng, "dma", (out, in_), [out] if out[0] != "out" else [], [in_] if in_[0] != "in" else [], 60.0, ns)
+    def dma(eng, out, in_):
+        add(eng, "dma", (out, in_), [out] if out[0] != "out" else [], [in_] if in_[0] != "in" else [])
 
     def send(kind, t, src, land):
-        tok = ("tok%s%d" % (kind, t), 0, 128, 0, 1, 1)
-        add("g", "send", (kind, t, src), [tok], [src], COST["iss"] * (1.5 if kind == "c" else 1))
-        add("x", "recv", (kind, t), [land], [tok], 0.0, COST["rem"] - COST["iss"])
+        tok = ("tok%s%d" % (kind, t), 0, 128, 0, 1, 1, 1)
+        add("g", "send", (kind, t, src), [tok], [src])
+        add("x", "recv", (kind, t), [land], [tok])
 
-    def K(b, c0, c1, step=1):
+    def K(b, c0, c1):
         if is_ap(b):
             b, c0, c1 = b[0], b[1] + c0, b[1] + c1
-        return A("K%d" % b, c0, c1, step)
+        return A("K%d" % b, c0, c1)
 
     sel = lambda r: A("EWB", 15 - r, 143 - r)
     sel0 = lambda r: A("E0B", 15 - r, 143 - r)
-    uh = lambda r, turn=0: A("UH", 144 * r + 16 - turn, 144 * r + 144 - turn)
+    uh = lambda r: A("UH", 144 * r + 16, 144 * r + 144)
     col = lambda n, j: A(n, j, j + 1)
-    P_, PG, PR, LWB, SLB, HB = [col("PF", j) for j in range(6)]
+    P_, PG, PR, LWB, SLB, HB, NX, SD = [col("PF", j) for j in (0, 1, 2, 3, 4, 5, 8, 10)]
     BO, IW, IB, IQ = A("BO32", 16, 144), A("I32W", 16, 144), A("IBW", 16, 144), A("IQ", 16, 144)
-    SRC, WL = A("L", 64, 80), A("L", 80, 96)
-    IM1 = A("IMW", 16, 144)
+    SRC, WL, IM1 = A("SRC"), A("WL"), A("IMW", 16, 144)
+    ha = lambda p: K(B["ha"], 32 * p, 32 * p + 32)
+    al = lambda t: A("AL", 2 * (t % 2), 2 * (t % 2) + 2)
 
     at("load")
     mset(A("LH"), 0.0)
-    dma("s", A("SI", p1=8), ("in", "s0"), 1800)
-    dma("y", A("NB"), ("in", "nb"), 7000)
-    dma("y", A("QT", 0, 4096), ("in", "qs"), 10000)
-    for n, s in ((A("W1", 0, 256), "w0"), (A("LH", 0, 6), "lo"), (A("LH", 8, 14), "hi")):
-        dma("y", n, ("in", s), 11000)
-    for n, s in ((A("CI", p1=8), "coin"), (A("UI", p1=8), "us")):
-        dma("s", n, ("in", s), 2500)
+    dma("s", A("SI", p1=8), ("in", "s0"))
+    dma("y", A("NB"), ("in", "nb"))
+    dma("y", A("QT", 0, 4096), ("in", "qs"))
+    for n, s in ((A("YW", 0, 256), "w0"), (A("LH", 0, 6), "lo"), (A("LH", 8, 14), "hi")):
+        dma("y", n, ("in", s))
+    for n, s in ((A("UI", p1=8), "us"), (A("CI", p1=8), "coin")):
+        dma("s", n, ("in", s))
 
     at("c")
     iota(A("PI"), [[0, 1]], 0, 1)
@@ -201,33 +178,27 @@ def plan():
     iota(A("C16"), [[0, 3], [1, 16]])
     iota(A("M16", 0, 32), [[704, 2], [16, 16]], -144)
     iota(A("M16", 32, 48), [[16, 16]], -144)
-    iota(A("C64", 16, 64), [[-1, 3], [0, 16]], 3)
-    iota(A("C80", 0, 64), [[1, 4], [0, 16]])
     mset(A("GQ", 0, 16), 112.0)
-    move("*", IQ, A("IOT", 0, 128))
-    move("*", A("IQ", 0, 16), A("IOT", 112, 128))
+    move(IQ, A("IOT", 0, 128))
+    move(A("IQ", 0, 16), A("IOT", 112, 128))
     ts(col("PJ", 0), A("PI"), 112, ALU.bitwise_and)
     ts(col("PJ", 1), A("PI"), 15, ALU.bitwise_and)
     cp(P_, A("PI"))
     cp(A("PF", 1, 3), A("PJ", 0, 2))
     ts(A("BO32"), A("GQ"), PG, ALU.is_equal)
-    move("*", A("BOB"), BO)
-    move("*", A("BON"), BO, scale=-1.0)
+    move(A("BOB"), BO)
     ts(A("RM"), A("IOT", 0, 16), PR, ALU.is_equal)
     ts(A("I32W"), A("IQ"), P_, ALU.is_equal)
-    move("*", A("IBW"), A("I32W"))
-    move("*", A("IMW"), A("I32W"), scale=-1.0)
-    for n, c in (("I4096", 4096.0), ("I4", 4.0), ("I16", 16.0), ("I296", 296.0), ("I592", 592.0), ("IM16", -1.0)):
-        move("*", A(n), IW, scale=c)
-    ts(A("YW", 0, 160), A("IOT", 0, 160), PG, ALU.subtract, 31.0, ALU.is_equal)
-    ts(A("M", 0, 160), A("IOT", 0, 160), PG, ALU.subtract, -97.0, ALU.is_equal)
-    tt(A("EW32"), A("YW", 0, 160), A("M", 0, 160), ALU.add)
-    move("*", A("EWB"), A("EW32", 16, 160))
-    move("*", A("E0B"), A("EW32", 16, 160), scale=col("RM", 0))
-    mset(A("M", 256, 296), 0.0)
-    mset(A("HF", 256, 296), -4096.0)
+    move(A("IBW"), A("I32W"))
+    move(A("IMW"), A("I32W"), scale=-1.0)
+    for n, c in (("I16F", 1.0), ("I296", 296.0), ("I592", 592.0)):
+        move(A(n), IW, scale=c)
+    ts(A("EWB"), A("IOT", 0, 144), PG, ALU.subtract, 15.0, ALU.is_equal)
+    move(A("EW16"), A("EWB"))
+    move(A("BO16"), BO)
+    move(A("E0B"), A("EWB"), scale=col("RM", 0))
     for p in range(5):
-        move("*", A("UH", 144 * p, 144 * p + 144), A("BO32"), scale=col("RM", p))
+        move(A("UH", 144 * p, 144 * p + 144), A("BO32"), scale=col("RM", p))
     ts(col("PF", 6), PR, 15.0, ALU.add)
     ts(col("PF", 7), PR, -1.0, ALU.add)
     c16 = A("C16", 0, 16)
@@ -236,330 +207,270 @@ def plan():
     ts(A("TMP", 32, 48), c16, col("PF", 7), ALU.is_equal, BIG, ALU.mult)
     tt(A("TMP", 48, 64), A("TMP", 0, 16), A("TMP", 16, 32), ALU.add)
     tt(A("PK", 0, 16), A("TMP", 48, 64), A("TMP", 32, 48), ALU.add)
-    for n in (16, 32, 64, 128)[:3 + (max(b - a for a, b in PAR["c3"]) > 128)]:
-        move("*", A("PK", n, 2 * n), A("PK", 0, n))
+    for n in (16, 32, 64):
+        move(A("PK", n, 2 * n), A("PK", 0, n))
     ts(LWB, col("RM", 0), -BIG, ALU.mult, 2048.0 - LOWER, ALU.add)
     ts(SLB, col("RM", 0), -BIG, ALU.mult, 0.25 - 64.0 - LOWER, ALU.add)
     ts(HB, PR, 6.5, ALU.is_lt, 2049.0, ALU.mult)
     ts(HB, HB, -1.0, ALU.add)
-    mset(A("RS4"), 1.0)
-    mset(A("RS4", 0, 256, 4), 0.0)
     ts(A("RS48"), A("C16"), 0.5, ALU.is_gt)
     ts(A("SV", 3, 4, p1=8), A("PF", 0, 1, p1=8), 16.0, ALU.mult)
     ts(A("G832", p1=8), A("GQ", 16, 144, p1=8), A("SV", 3, 4, p1=8), ALU.is_equal)
-    move("*", A("G8", p1=8), A("G832", p1=8), scale=8.0)
+    move(A("G8", p1=8), A("G832", p1=8))
     ts(A("E8", p1=8), A("IOT", 0, 144, p1=8), -15.0, ALU.add, A("SV", 3, 4, p1=8), ALU.is_equal)
-    ts(A("PG", 0, 128), IQ, P_, ALU.is_lt, -1.0, ALU.mult)
-    tt(A("PG", 128, 256), A("PG", 0, 128), BO, ALU.mult)
-    move("*", A("YW", 0, 128), IW, scale=-float(ZR))
-    tt(A("TBZ"), A("PG", 128, 256), A("YW", 0, 128), ALU.add)
+    ts(NX, col("RM", 15), -16.0, ALU.mult, P_, ALU.add)
+    ts(A("R16"), A("IOT", 0, 128), -1.0, ALU.add, NX, ALU.is_equal)
+    move(A("R4096"), A("R16"), scale=4096.0)
+    ts(SD, col("RM", 0), -0.5, ALU.add)
+    move(A("T1"), A("R16"), scale=SD)
+    move(A("T2"), IW, scale=0.5)
+    tt(A("DIF"), A("T1"), A("T2"), ALU.add)
+    thr = 16 * LOW + 8.5 * 4096
+    ts(A("THR"), col("RM", 0), thr + 1.0, ALU.mult, -thr, ALU.add)
+    ts(A("GE", 0, 128), IQ, P_, ALU.is_lt, -1.0, ALU.mult)
+    tt(A("GE", 128, 256), A("GE", 0, 128), BO, ALU.mult)
+    move(A("Y", 0, 128), IW, scale=float(ZR))
+    tt(A("TBZ"), A("GE", 128, 256), A("Y", 0, 128), ALU.add)
     ts(A("DG"), IW, PR, ALU.mult, -1.0, ALU.mult)
-    tt(A("TBR"), A("PG", 128, 256), A("DG"), ALU.add)
-    move("*", A("CW", 0, 16), A("M16", 0, 16), PR)
-    move("*", A("CWB"), A("CW", 0, 16))
-    mset(A("CIN", 0, 16), float(ZR))
-    mset(A("CIN", 16, 32), 704.0)
-    mset(A("CIN", 32, 36), 0.0)
-    mset(A("CIN", 36, 52), -1024.0)
-    move("*", A("YH", 0, 128), IW, scale=1024.0)
-    tt(A("TBP"), A("PG", 128, 256), A("YH", 0, 128), ALU.add)
-    mset(A("C64", 0, 16), 576.0 - 2304)
-    mset(A("C80", 64, 96), 144.0 - 576)
+    tt(A("TBR"), A("GE", 128, 256), A("DG"), ALU.add)
+    move(A("CWB"), A("M16", 0, 16), PR)
+    move(A("CIL", 0, 16), A("CWB"), 704.0)
+    mset(A("CIL", 16, 18), 0.0)
     act(A("IOB"), A("IOT"), ACT.Silu, 64.0)
-    ops[-1]["ns"] += 1600.0
-    move("*", A("I16F"), A("I32W"))
-    ts(A("GE", 0, 128), IQ, 1.0, ALU.add, P_, ALU.is_equal)
-    ts(col("SV", 4), PR, 0.5, ALU.is_gt)
-    move("*", A("GE", 128, 256), A("GE", 0, 128), scale=col("SV", 4))
-    tt(A("D32"), IW, A("GE", 128, 256), ALU.subtract)
-    mset(A("VJ"), 0.0)
-    for j in range(3):
-        move("*", A("VJ", 129 * j, 128 * j + 128, 4), A("BOB", j, 128, 4), scale=0.125)
-    ts(col("PJ", 2), A("PI"), 12, ALU.bitwise_and)
-    ts(col("PJ", 3), A("PI"), 3, ALU.bitwise_and)
-    cp(A("SV", 5, 7), A("PJ", 2, 4))
-    ts(col("SV", 6), col("SV", 6), 3.0, ALU.is_equal, -2.0, ALU.mult)
-    ts(col("SV", 5), col("SV", 5), -1.0, ALU.mult, 8.5 / 8, ALU.add)
-    tt(A("THR"), col("SV", 5), col("SV", 6), ALU.add)
     mset(A("QT", 4096, 4112), 0.0)
-    for n in ("W0", "W1"):
-        for j in range(256, 888, 296):
-            mset(A(n, j, j + 40), 0.0)
-    mset(A("HT", 256, 296), -4096.0)
-    mset(A("NF", 256, NW), 0.0)
-    mset(A("X", 4096, 4624), 0.0)
-    mset(A("PT", 1024, 1160), 0.0)
-    mset(A("TH"), 8.5)
+    for j in range(256, 888, TW):
+        mset(A("W", j, j + 40), 0.0)
+    mset(A("HT", 256, TW), -4096.0)
+    mset(A("NF", 256, TW), 2048.0)
+    for p in range(5):
+        move(A("US", 128 * p, 128 * p + 128), A("BO32", 0, 128), scale=col("RM", p + 1))
+    mset(A("UB", 1536, 1576), 0.0)
     mset(A("SC_O"), 0.0)
+    at("d")
+    ts(A("JC"), A("IOT", 0, 32, 16), PR, ALU.add, -1.0, ALU.mult)
+    ts(A("JC"), A("JC"), -0.5, ALU.add)
+    mset(A("ONE"), 1.0)
+    mset(A("HS", 256, 264), -1.0)
+    mset(A("HS", 264, TW), 1.0)
     at("flat")
-    iota(A("B4"), [[0, 290], [4, 4]])
-    iota(A("TT", 288, 2048), [[0, 1760]], 208)
+    iota(A("RSX"), [[0, 96], [8192, 16]], int(LOW))
+    fill(A("TH"), 9)
+    fill(A("TT", 0, ZR), 208)
 
     at("s")
-    move("*", A("S0F", p1=8), A("SI", p1=8), -2048.0)
-    mm([(K(0, 0, 256), A("G832", p1=8), A("S0F", p1=8))])
-    move("*", A("HT", 0, 256), K(0, 0, 256), scale=col("RM", 0))
+    move(A("S0F", p1=8), A("SI", p1=8), -2048.0)
+    k0 = K(0, 0, 256)
+    mm([(k0, A("G832", p1=8), A("S0F", p1=8))])
+    move(A("HC", 0, 256), k0, scale=col("RM", 0))
+    ts(K(0, 256, 512), k0, -2048.5, ALU.is_gt, 2.0 ** -11, ALU.mult)
+    tt(A("WP"), A("YW", 0, 256), K(0, 256, 512), ALU.mult)
+    add("v", "red", (col("SV", 2), K(0, 256, 512)), [col("SV", 2)], [K(0, 256, 512)])
+    ts(col("SC_O", 1), col("SV", 2), -2048.0, ALU.mult, -256.0, ALU.add)
+    at("u")
+    for j in range(0, 1536, 256):
+        move(A("U8", j, j + 256, p1=8), A("UI", j, j + 256, p1=8))
+        k = K(3 + j // 256 % 2, 256, 512)
+        mm([(k, A("G8", p1=8), A("U8", j, j + 256, p1=8))])
+        move(A("UB", j, j + 256), k, scale=-(1 + 2.0 ** -21) / 256)
     for j in range(0, 1536, 512):
-        move("*", A("U8", j, j + 512, p1=8), A("UI", j, j + 512, p1=8))
-        move("*", A("CB", j, j + 512, p1=8), A("CI", j, j + 512, p1=8))
-    ts(A("CB", 1536, 1792, p1=8), A("S0F", p1=8), -2048.5, ALU.is_lt)
-    mm([(K(7, 0, 112), A("E8", 15 - r, 143 - r, p1=8), A("CB", r, 1792, 16, p1=8)) for r in range(16)])
+        move(A("CB", j, j + 512, p1=8), A("CI", j, j + 512, p1=8))
+    mm([(K(5, 0, 96), A("E8", 15 - r, 143 - r, p1=8), A("CB", r, 1536, 16, p1=8)) for r in range(16)])
     for t in range(NS):
-        move("*", A("TH", 48 * t, 48 * t + 16), K(7, 16 * t, 16 * t + 16), 8.5, 100.0)
-        move("*", A("TH", 48 * t + 32, 48 * t + 48), K(7, 16 * t, 16 * t + 16), 108.5, -100.0)
-    move("*", A("DB"), K(7, 96, 112))
-    move("*", A("CW", 16, 32), K(7, 96, 112), scale=1024.0)
-    tt(A("CW", 16, 32), A("CW", 16, 32), A("CW", 0, 16), ALU.add)
-    ts(A("SB16"), A("CW", 16, 32), 144.0, ALU.min)
-    mm([(K(7, 128, 144), A("BOB"), A("DB"))])
-    add("v", "red", (col("SV", 2), K(7, 128, 144)), [col("SV", 2)], [K(7, 128, 144)], 64 * COST["cyc"])
-    cp(col("SC_O", 1), col("SV", 2))
+        move(A("TH", 48 * t, 48 * t + 16), K(5, 16 * t, 16 * t + 16), 9.0, 100.0)
+        move(A("TH", 48 * t + 32, 48 * t + 48), K(5, 16 * t, 16 * t + 16), 109.0, -100.0)
 
-    def neighbours(t, a, b, hb, of, e):
+    def neighbours(t, a, b, hb, of, out):
+        lw, nk = A("LW", a // 16, b // 16), A("NK", a, b)
         scan(A("SC", a, b), hb(t + 1), A("PK", 0, b - a), ALU.min, ALU.add, BIG)
-        lw = A("LW", a // 16, b // 16)
         ts(lw, A("SC", a + 15, b, 16), LWB, ALU.add, 4095.0, ALU.min)
-        nk = A("NK", a, b)
-        move(e, nk, IND(A("NB"), lw), -2048.0)
-        mm([(of, A("I16F", 16, 144), nk)], True, False)
-        add("g", "sel", (A("NF", a, b), nk), [A("NF", a, b)], [nk], 190 + 2 * (b - a) * COST["cyc"])
+        move(nk, IND(A("NB"), lw), -2048.0)
+        mm([(K(of, 0, b - a), A("R16"), nk)], True, False)
         name = tag[0]
         at(name + "e")
         for p in range(t + 1, -1, -1):
-            eq = A("EQ", 288 * p + a, 288 * p + b)
+            eq = A("EQ", 320 * p + a, 320 * p + b)
             tt(eq, nk, hb(p), ALU.is_equal)
-            mm([(of, A("I4096"), eq)], False, p == 0)
+            mm([(K(of, 0, b - a), A("R4096"), eq)], False, p == 0)
         at(name + "o")
-        ts(A("OU", a, b), of, 2048.0, ALU.add, 4096.0, ALU.min)
+        if out is not None:
+            ts(A("OU", out, out + b - a), K(of, 0, b - a), 2048.0, ALU.add, 4096.0, ALU.min)
+            move(A("NKP", out, out + b - a), K(of, 0, b - a))
+        else:
+            move(A("NF", a, min(b, 256)), K(of, 0, min(b, 256) - a))
+            if b > 256:
+                move(A("NA"), K(of, 256 - a, b - a))
+                cp(IND(A("NF"), al(t - 1)), A("NA"))
 
     def own(t):
-        at("hb")
-        for p in range(t + 1):
-            mm([(K(B["hb"][p], 0, 256), uh(p), A("HC"))])
-        for h, (a, b) in enumerate(PAR["c3"]):
-            at("n%d_" % h)
-            hn = K(B["hn"][h % 2], 0, b - a)
-            mm([(hn, BO, A("M" if t >= 0 else "HT", a, b))])
-            neighbours(t, a, b, lambda p: hn if p == t + 1 else K(B["hb"][p], a, b), K(B["of"][h % 2], 0, b - a), PAR["nk"])
-
-    def lists(factor):
-        at("l")
-        mm([(K(B["l"], 0, 96), IB, A("C80"))] + [(K(B["l"], 16 * j, 16 * j + 16), A("I4") if j < 4 else IB, A("SB16")) for j in range(6)]
-           + [(K(B["l"], 80, 96), A(m), x) for m, x in factor])
-        ts(A("L"), K(B["l"], 0, 96), 576.25, ALU.add)
-
-    def steps():
-        at("d")
-        move("*", A("OF"), IND(A("NF"), SRC))
-        mm([(K(B["d"], 0, 256), A("D32"), A("OF"))])
-
-    def history():
-        move("*", A("HF", 0, 256), IND(A("HT"), SRC))
-        if PAR["pool"]:
-            add("g", "sel", (A("HC"), A("HF", 0, 256)), [A("HC")], [A("HF", 0, 256)], 190 + 512 * COST["cyc"])
-        else:
-            move("*", A("HC"), A("HF", 0, 256))
+        for h, (a, b) in enumerate(NEAR):
+            b = b if t > 0 else min(b, 256)
+            hb = lambda p: K(B["hb"][h][p], 0, b - a)
+            at("hb%d" % h)
+            for p in range(t + 1):
+                mm([(hb(p), uh(p), A("HC", a, b))])
+            at("n%d" % h)
+            hn = K(B["hn"][h], 0, b - a) if t >= 0 else K(0, a, b)
+            if t >= 0:
+                mm([(hn, A("BO16"), A("M", a, b))])
+            neighbours(t, a, b, lambda p: hn if p == t + 1 else hb(p), B["of"][h], a if t < 0 else None)
 
     own(-1)
-    lists([])
-    steps()
-    at("f")
-    history()
 
     for t in range(NS):
         last = t == NS - 1
         now[0] = t
-        for i, (e, a, b) in enumerate(PAR["pieces"]):
-            if a >= 256 and t == 0:
-                continue
-            at("x%d_" % i)
-            move(e, A("X", 16 * a, 16 * b), IND(A("QT"), A("OU", a, b)))
-            k = K(B["sums"][i] if t else (i % 2, 256 + 128 * (i // 2 % 2)), 0, 4 * (b - a))
-            mm([(k, IB, A("X", 16 * a + j, 16 * b, 4)) for j in range(4)])
-            scan(A("PT", 4 * a, 4 * b), A("RS4", 0, 4 * (b - a)), k, ALU.mult, ALU.add)
-        pt = lambda j, a, b: IND(A("PT"), A("L", 16 * j + a // 16, 16 * j + b // 16)) if t else A("PT", 4 * a + j, 4 * b, 4)
-        c1 = PAR["cz"] if last else PAR["c1"]
-        for h, (a, b) in enumerate(c1):
-            at("a%d_" % h)
-            w, th = b - a, K(B["t"], a, b)
-            if PAR["wide"][3] != "w" or t == 0:
-                move("*", A("PG", a, b), pt(3, a, b), scale=2.0 ** -11)
-            elif h == 0:
-                move("*", A("PG"), pt(3, 0, 256), scale=2.0 ** -11)
-            else:
-                tag[1][(t, "v", tag[0])] = 0
-            mm([(th, A("G8", p1=8), A("U8", 256 * t + a, 256 * t + b, p1=8))])
-            tt(th if "s" in PAR["l1"] else A("TS", a, b), A("PG", a, b), th, ALU.mult)
-            if "v" in PAR["l1"] and "s" in PAR["l1"]:
-                move("*", A("TS", a, b), th)
-            for j in range(3):
-                c = A("CMP", 3 * a + w * j, 3 * a + w * j + w)
-                if PAR["l1"][j] == "v":
-                    tt(c, pt(j, a, b), A("TS", a, b), ALU.is_gt)
-                else:
-                    pj = A("PJ3", 256 * j + a, 256 * j + b) if t else pt(j, a, b)
-                    if t and PAR["wide"][j] == "w" and h == 0:
-                        move("*", A("PJ3", 256 * j, 256 * j + 256), pt(j, 0, 256))
-                    elif t and PAR["wide"][j] != "w":
-                        move("*", pj, pt(j, a, b))
-                    else:
-                        tag[1][(t, "v", tag[0])] += 1
-                    tt(c, pj, th, ALU.is_gt)
-            v1 = K(B["v1"][h % 2], 0, 3 * w // 16)
-            mm([(v1, sel(r), A("CMP", 3 * a + r, 3 * b, 16)) for r in range(16)])
-            ts(A("LT", 3 * a // 16, 3 * b // 16), v1, 8.5, ALU.is_lt)
+        for i, (a, b) in enumerate(PIECES):
+            if a < 256 or t:
+                at("x%d" % i)
+                move(A("X", 16 * a, 16 * b), IND(A("QT"), A("OU", a, b)))
+        for i, (a, b) in enumerate(SUMS):
+            b = b if t else min(b, 256)
+            c = min(b, 256)
+            p15, votes, one = B["p15"][i], K(B["votes"][i], 0, b - a), K(B["one"][i], 0, b - a)
+            at("a%d" % i)
+            mm([(K(p15, 0, b - a), A("I16F"), A("X", 16 * a + j, 16 * b, 16)) for j in range(16)])
+            at("a%dw" % i)
+            tt(A("W", a, c), A("WP", a, c), K(p15, 0, c - a), ALU.mult)
+            tt(A("Y", a, c), A("UB", 256 * t + a, 256 * t + c), K(p15, 0, c - a), ALU.mult)
+            if c < b:
+                at("b")
+                tt(A("WB"), A("WA"), K(p15, c - a, b - a), ALU.mult)
+                cp(IND(A("W", 0, TW), al(t - 1)), A("WB"))
+                tt(A("Y", c, b), A("UA"), K(p15, c - a, b - a), ALU.mult)
+            at("a%dz" % i)
+            ts(A("X", 16 * a, 16 * b, 16), A("Y", a, b), -HALF, ALU.add, 2.0 ** 23 + 2048, ALU.add)
+            at("a%dc" % i)
+            for d in range(a, b, CUT[i]):
+                e = min(d + CUT[i], b)
+                scan(A("CMP", 16 * d, 16 * e), A("RSX", 0, 16 * (e - d)), A("X", 16 * d, 16 * e), ALU.min, ALU.add, 2 * LOW)
+                at("a%ds" % i)
+            at("a%dc" % i)
+            mm([(votes, sel(s), A("CMP", 16 * a + s, 16 * b, 16)) for s in range(1, 16)])
+            act(A("GE", a, b), votes, ACT.Sign, A("THR"))
+            mm([(one, A("DIF"), A("GE", a, b))])
+            tt(A("M", a, b), A("NKP", a, b), one, ALU.mult)
         at("w")
-        wn, wo = "W%d" % (t % 2), "W%d" % (1 - t % 2)
-        WN = A(wn, 0, 256)
-        tt(WN, IND(A(wo, 0, 888 if t else 296), WL), A("PG"), ALU.mult)
-        if PAR["slo"]:
-            act(A("GE", 0, 256), WN, ACT.Sign, col("LH", t), -1.0)
-            act(A("FL", 0, 256), A("GE", 0, 256), ACT.Relu)
-            tag[1][(t, "v", "w")] += 1
-        else:
-            ts(A("FL", 0, 256), WN, col("LH", t), ALU.is_lt)
+        WN = A("W", 0, 256)
+        ts(A("FL", 0, 256), WN, col("LH", t), ALU.is_lt)
         ts(A("FL", 256, 512), WN, col("LH", 8 + t), ALU.is_gt)
         ts(A("FL", 512, 768), WN, 0.0, ALU.is_equal)
-        either((A("FL", 512, 768), WN, ACT.Relu, 1.0, -2.0 ** 85))
-        move("*", A(wn, 296, 552), WN, scale=2.0)
-        move("*", A(wn, 592, 848), WN, scale=0.5)
+        ops[-1]["alt"] = (A("FL", 512, 768), WN, ACT.Relu, 1.0, -2.0 ** 85)
+        move(A("W", TW, TW + 256), WN, scale=2.0)
+        move(A("W", 2 * TW, 2 * TW + 256), WN, scale=0.5)
         fl, rk = B["fl"], B["rank"]
         mm([(K(fl, 0, 48), sel(r), A("FL", r, 768, 16)) for r in range(16)])
         at("r")
-        tt(A("FG"), K(fl, 0, 48), A("TH", 48 * t, 48 * t + 48), ALU.is_gt)
+        tt(A("FG"), K(fl, 0, 48), A("TH", 48 * t, 48 * t + 48), ALU.is_ge)
         HIGH, HOLES = A("FG", 16, 32), (0, 32)
         scan(A("SN"), A("RS48"), A("FG"), ALU.mult, ALU.add)
         tt(A("E"), A("FG"), A("M16"), ALU.mult)
-        mm([(K(rk, 0, 36), IB, A("CIN", 0, 36)), (K(rk, 16, 32), IB, A("CWB")), (K(rk, 16, 32), A("TBR"), HIGH),
-            (K(rk, 16, 32), IM1, A("E", 16, 32)), (K(rk, 0, 32), A("BOB"), A("SN", 0, 32)), (K(rk, 0, 16), A("BOB"), A("SN", 32, 48)),
-            (K(rk, 32, 34), A("BOB"), A("SN", 15, 32, 16)), (K(rk, 32, 33), A("BOB"), col("SN", 47))]
-           + [(K(rk, 0, 16), A("TBZ"), A("FG", j, j + 16)) for j in HOLES])
-        ts(A("PO"), K(rk, 0, 32), K(rk, 32, 33), ALU.subtract, 255.0, ALU.add)
+        k = K(rk, 16, 32)
+        mm([(K(rk, 16, 34), A("I16F"), A("CIL")), (k, A("TBR"), HIGH), (k, IM1, A("E", 16, 32)), (k, A("BOB"), A("SN", 16, 32)),
+            (K(rk, 32, 34), A("BOB"), A("SN", 15, 32, 16)), (K(rk, 32, 33), A("BOB"), col("SN", 47))])
+        ts(A("PO", 16, 32), k, K(rk, 32, 33), ALU.subtract, 255.0, ALU.add)
         DD = col("SC_O", 8 * t)
         if not last:
             ts(DD, K(rk, 32, 33), K(rk, 33, 34), ALU.subtract)
-        mm([(K(rk, 36, 52), IB, A("CIN", 36, 52))] + [x for j in HOLES for x in ((K(rk, 36, 52), A("BOB"), A("SN", j, j + 16)),
-                                                                               (K(rk, 36, 52), A("TBP"), A("FG", j, j + 16)))])
-        ts(A("G"), K(rk, 36, 52), K(rk, 33, 34), ALU.subtract, 0.0, ALU.max)
-        iota(A("TT", 0, 256), [[0, 256]], 208 + 111)
-        iota(A("TT", 256, 288), [[0, 32]], 64 + DEAD)
+        at("h")
+        k = K(rk, 0, 16)
+        mm([x for j in HOLES for x in ((k, A("BOB"), A("SN", j, j + 16)), (k, A("TBZ"), A("FG", j, j + 16)))])
+        ts(A("PO", 0, 16), k, K(rk, 32, 33), ALU.subtract, 255.0, ALU.add)
+        at("r")
+        fill(A("TT", ZR, ZR + 256), 208 + 112)
+        fill(A("TT", ZR + 256, ZR + 288), 64 + DEAD)
         at("p")
-        cp(IND(A("TT", 0, 1328), A("PO", 16, 32)), A("IOB"))
-        either((IND(A("TT", 0, 1328), A("PO", 16, 32)), A("IOB"), ACT.Silu, 0.0, 1.0))
-        scan(A("SM"), A("TT", 256, 288), A("PK", 0, 32), ALU.min, ALU.add, BIG)
-        ts(A("SL"), A("SM", 15, 32, 16), SLB, ALU.add, float(DEAD), ALU.min)
-        po = 96 * t
-        move("*", A("SP_O", po, po + 32), IND(A(wn, 0, 296), A("SL")), scale=0.5)
-        for h, (a, b) in enumerate(c1):
-            at("b%d_" % h)
-            w, m, ll = b - a, (b - a) // 16, B["ll"][h % 2]
-            lt = lambda j, n=1: A("LT", 3 * a // 16 + j * m, 3 * a // 16 + (j + n) * m)
-            sb = A("SB16", a // 16, b // 16)
-            mm([(K(ll, 0, 4 * m), IB, A("C64", 0, 64, 16 // m))]
-               + [(K(ll, m * j, m * j + m), A("I16") if j else A("I4"), sb) for j in range(4)], True, False)
-            mm([(K(ll, 0, m), IB, lt(i)) for i in range(3)]
-               + [(K(ll, m * j, m * (j + n)), A("I4"), lt(i, n)) for j, i, n in ((1, 0, 3), (1, 1, 2), (3, 0, 1), (1, 2, 1), (2, 0, 2))], False)
-            ts(A("LL", a // 4, b // 4), K(ll, 0, 4 * m), 2304.25, ALU.add)
-        for h, (a, b) in enumerate(PAR["c2"]):
-            at("g%d_" % h)
-            w = b - a
-            ca, cb = [c for c in c1 if c[0] <= a and b <= c[1]][0]
-            L2 = lambda j: A("LL", (3 * ca + a + j * (cb - ca)) // 16, (3 * ca + b + j * (cb - ca)) // 16)
-            if PAR["l1"][3] == "v":
-                tt(A("R", a, b), IND(A("PT"), L2(0)), A("TS", a, b), ALU.subtract)
-            elif PAR["nt"]:
-                move("*", A("P16", a, b), IND(A("PT"), L2(0)), -2048.0)
-                move("*", A("R", a, b), K(B["t"], a, b), 2048.0, -1.0)
-            else:
-                move("*", A("PJ3", a, b), IND(A("PT"), L2(0)))
-                tt(A("R", a, b), A("PJ3", a, b), K(B["t"], a, b), ALU.subtract)
-            xg = lambda i: A("XG", 256 * i + a, 256 * i + b)
-            for i in range(3):
-                move(PAR["xg"][i], xg(i), IND(A("X"), L2(i + 1)))
-            for i in range(3):
-                k = K(B["xs"][h % 2][i], 0, w)
-                mm([(k, IB, xg(j)) for j in range(i + 1)] + [(k, A("IM16"), A("P16", a, b))] * PAR["nt"])
-                tt(A("C2", 3 * a + w * i, 3 * a + w * i + w), k, A("R", a, b), ALU.is_lt)
-                mm([(K(B["ge"][h % 2], 0, w), A("VJ", 128 * (2 - i), 128 * (3 - i)), A("C2", 3 * a + w * i, 3 * a + w * i + w))], i == 0, i == 2)
-            move("*", A("THB", a, b), IND(A("B4"), L2(0)), A("THR"))
-            for c, d in PAR["c3"]:
-                if a <= c and d <= b:
-                    at("h%d_" % (4 * PAR["c3"].index((c, d))))
-                    tt(A("GE", c, d), K(B["ge"][h % 2], c - a, d - a), A("THB", c, d), ALU.is_gt)
-                    tt(A("M", c, d), A("GE", c, d), K(B["d"], c, d), ALU.mult)
-        at("q")
-        move("*", A("SP_O", po + 32, po + 64), IND(A("HF"), A("SL")))
-        move("*", A("SP_O", po + 64, po + 96), IND(A("M"), A("SL")))
-        if not last:
-            at("c")
-            send("c", t, A("SC_O", 8 * t, 8 * t + 2), A("SC_I", 24 * t, 24 * t + 24))
-            at("q")
-        send("p", t, A("SP_O", po, po + 96), A("SP_I", po, po + 96))
-        if t == 0:
-            ops[-2]["rd"].append(ops[-4]["wr"][0])
-            ops[-4]["ns"] += COST["first"]
+        inverse = IND(A("TT", ZR, ZR + 1328), A("PO", 16, 32))
+        cp(inverse, A("IOB"))
+        ops[-1]["alt"] = (inverse, A("IOB"), ACT.Silu, 0.0, 1.0)
+        scan(A("SM"), A("TT", ZR + 256, ZR + 288), A("PK", 0, 32), ALU.min, ALU.add, BIG)
+        ts(A("SL"), A("SM", 15, 32, 16), SLB, ALU.add)
         at("u")
-        for a, b in PAR["c4"]:
-            mm([(K(B["ht"], a, b), A("I16F", 16, 144), A("HC", a, b)), (K(B["ht"], a, b), A("EW32", 30 - t, 158 - t), A("M", a, b))])
-            move("*", A("HT", a, b), K(B["ht"], a, b))
+        for a, b in HIST + [(256, 288)] * (t > 0):
+            k = K(B["ht"], a, b) if a < 256 else K(B["htb"], 0, 32)
+            mm([(k, A("I16F"), A("HC", a, b)), (k, A("EW16", 14 - t, 142 - t), A("M", a, b))])
+            move(A("HT", a, b) if a < 256 else A("HR"), k)
+        if t:
+            cp(IND(A("HT"), al(t - 1)), A("HR"))
+        at("p")
+        po = 64 * t
+        move(A("SP_O", po, po + 32), IND(A("W", 0, TW), A("SL")), scale=0.5 if last else 2.0 ** -12)
+        at("q")
+        move(A("SP_O", po + 32, po + 64), IND(A("HT"), A("SL")))
+        for kind in ("p" if last else "pc" if t else "cp"):
+            at("q" if kind == "p" else "c")
+            if kind == "c":
+                send("c", t, A("SC_O", 8 * t, 8 * t + 2), A("SC_I", 24 * t, 24 * t + 24))
+            else:
+                send("p", t, A("SP_O", po, po + 64), A("SP_I", po, po + 64))
         if not last:
+            ops[-2]["rd"].append(ops[-4]["wr"][0])
             own(t)
-        at("f")
-        tt(A("DB"), K(fl, 0, 16), A("TH", 48 * t + 32, 48 * t + 48), ALU.is_gt)
-        ts(A("GF"), A("G"), 0.5, ALU.is_gt, -2.0, ALU.mult)
         at("s")
-        move("*", A("SRB"), IND(A("TT"), A("PO", 0, 16)), -208.0)
+        tt(A("DB"), K(fl, 0, 16), A("TH", 48 * t + 32, 48 * t + 48), ALU.is_ge)
+        move(A("SRB"), IND(A("TT", 0, ZR + 256), A("PO", 0, 16)), -208.0)
         sb = K(B["sb"], 0, 16)
-        mm([(sb, IB, A("CWB")), (sb, IB, A("G"))]
-           + [x for j in HOLES for x in ((sb, A("DG"), A("FG", j, j + 16)), (sb, IM1, A("E", j, j + 16)))]
+        mm([(sb, IB, A("CWB"))] + [x for j in HOLES for x in ((sb, A("DG"), A("FG", j, j + 16)), (sb, IM1, A("E", j, j + 16)))]
            + [(sb, sel0(r), A("SRB", r, 256, 16)) for r in range(16)])
-        ts(A("SB16"), sb, 144.0, ALU.min)
-        lists([("I592", A("FG", 0, 16)), ("I592", HIGH), ("I296", A("FG", 32, 48)), ("I296", A("DB")), ("I296", A("GF"))])
-        at("i")
-        mi = A("SP_I", po + 64, po + 96)
+        ts(SRC, sb, 144.25, ALU.add)
+        move(A("SB16"), sb)
+        k = K(B["l"], 0, 16)
+        mm([(k, IB, A("SB16")), (k, A("I592"), A("FG", 0, 16)), (k, A("I592"), HIGH), (k, A("I296"), A("FG", 32, 48)), (k, A("I296"), A("DB"))])
+        ts(WL, k, 144.25, ALU.add)
+        at("v")
+        act(A("HS", 0, 256), A("SRB"), ACT.Sign, -111.5)
+        scan(A("CU"), A("ONE"), A("HS"), ALU.add, ALU.add)
+        for j in range(2):
+            act(A("H2", TW * j, TW * j + TW), A("CU"), ACT.Sign, col("JC", j), 0.5, col("SV", 6 + j))
+        ts(al(t), A("SV", 6, 8), -0.5, ALU.mult, TW / 2 + 0.25, ALU.add)
+        hi = A("SP_I", po + 32, po + 64)
         if not last:
-            move("*", A("HA"), A("SP_I", po + 32, po + 64))
-            ha = lambda p: K(B["hna"], 0, 32) if p == t + 1 else K(B["ha"], 32 * p, 32 * p + 32)
-            mm([(ha(t + 1), A("BO32", 0, 128), mi)])
-            mm([(ha(p), uh(p, 16), A("HA")) for p in range(t + 1)], "each")
+            at("l")
+            for a, b in LISTS:
+                move(A("NKP", a, b), IND(A("NF"), A("SRC", a // 16, b // 16)))
+            at("o")
+            for a, b in LISTS:
+                ts(A("OU", a, b), A("NKP", a, b), 2048.0, ALU.add, 4096.0, ALU.min)
+            at("f")
+            move(A("WP"), IND(A("W"), WL), scale=2.0 ** -11)
+            move(A("HC", 0, 256), IND(A("HT"), SRC))
+            move(A("UA"), IND(A("UB", 256 * t + 256, 256 * t + 256 + TW), al(t)))
+            at("i")
+            mm([(ha(t + 1), A("US", 128 * t, 128 * t + 128), hi)])
+            mm([(K(B["rot"], 32, 64), A("I32W", 0, 128), hi)])
+            move(A("HC", 256, 288), K(B["rot"], 32, 64))
+            mm([(ha(p), uh(p), A("HC", 256, 288)) for p in range(t + 1)], "each")
             at("in")
-            neighbours(t, 256, 288, ha, K(B["ofa"], 0, 32), PAR["nka"])
-            steps()
+            neighbours(t, 288, 320, ha, B["ofa"], 256)
+        else:
+            at("y")
+            ts(A("YH", 0, 256), IND(A("HT"), SRC), HB, ALU.add, -1.0, ALU.max)
+            move(A("YW", 0, 256), IND(A("W"), WL))
         at("j")
         mm([(K(B["rot"], 0, 32), A("I32W", 0, 128), A("SP_I", po, po + 32))])
-        move("*", A(wn, 256, 288), K(B["rot"], 0, 32))
-        mm([(K(B["rot"], 32, 64), A("I32W", 0, 128), A("SP_I", po + 32, po + 64)), (K(B["rot"], 32, 64), A("EW32", 14 - t, 142 - t), mi)])
-        move("*", A("HT", 256, 288), K(B["rot"], 32, 64))
+        move(A("WA"), K(B["rot"], 0, 32))
         if not last:
-            history()
             at("k")
             cn = B["cnt"]
             got = [A("SC_O", 8 * t, 8 * t + 2)] + [A("SC_I", 24 * t + 8 * j, 24 * t + 8 * j + 2) for j in range(3)]
             mm([(K(cn, 0, 1), IM1, A(x[0], x[3] + j, x[3] + j + 1)) for x in got for j in range(2)])
             ts(col("SV", 0), K(cn, 0, 1), 0.5, ALU.is_gt, 1.0, ALU.add)
-            ts(A("LH", 0, 14), A("LH", 0, 14), col("SV", 0), ALU.mult)
+            move(A("LH", 0, 14), A("LH", 0, 14), scale=col("SV", 0))
             if t < NS - 2:
                 mm([(K(cn, 1, 2), A("IMW", 0, 128), col("SC_I", 24 * t))])
                 ts(col("SV", 1), K(cn, 1, 2), 0.0, ALU.max, 32.0, ALU.min)
                 ts(col("SC_O", 8 * t + 9), col("SV", 1), DD, ALU.subtract, 0.0, ALU.min)
         else:
-            at("y")
-            ts(A("YH"), IND(A("HT"), SRC), HB, ALU.add, -1.0, ALU.max)
-            act(A("YW"), IND(A(wn), WL))
-            dma("y", ("out", "yh"), A("YH"))
-            dma("s", ("out", "yw"), A("YW"))
+            mm([(ha(0), A("I32W", 0, 128), hi)])
+            ts(A("HR"), ha(0), HB, ALU.add, -1.0, ALU.max)
+            cp(IND(A("YW"), al(t)), A("WA"))
+            cp(IND(A("YH"), al(t)), A("HR"))
+            dma("s", ("out", "yw"), A("YW", 0, 256))
+            dma("y", ("out", "yh"), A("YH", 0, 256))
     return ops
 
 
 def meet(a, b):
     return a[0] == b[0] and a[1] < b[2] and b[1] < a[2] and a[3] < b[4] and b[3] < a[4]
-
-
-def whole(a):
-    return a[5] == 1 and (len(a) < 7 or a[6] == 1)
-
-
-BIAS = {"py.load0": 2e6, "py.load1": 1e6}
 
 
 def depend(ops):
@@ -568,499 +479,51 @@ def depend(ops):
         d = set()
         for a in o["rd"]:
             d.update(j for j, b, w in seen.get(a[0], []) if w and meet(a, b))
-        o["raw"] = set(d) if PAR["soft"] else None
         for a in o["wr"]:
             d.update(j for j, b, w in seen.get(a[0], []) if meet(a, b))
         d.discard(i)
         o["dep"] = d
         o["soft"] = {j for j in d if ops[j]["kind"] == o["kind"]} if o["kind"] in ("mm", "send") else set()
-        o["hard"] = sorted(d - o["soft"])
         for a in o["wr"]:
-            keep = [e for e in seen.get(a[0], []) if not (whole(a) and a[1] <= e[1][1] and e[1][2] <= a[2] and a[3] <= e[1][3] and e[1][4] <= a[4] and e[0] != i)]
-            seen[a[0]] = keep + [(i, a, True)]
+            over = lambda b: a[5] == 1 and b[2] <= a[2] and a[3] <= b[3] and b[4] <= a[4]
+            seen[a[0]] = [e for e in seen.get(a[0], []) if e[0] == i or not over(e[1])] + [(i, a, True)]
         for a in o["rd"]:
             seen.setdefault(a[0], []).append((i, a, False))
         o["banks"] = sorted({a[0] for a in o["rd"] + o["wr"] if a[0][0] == "K"})
 
 
-def schedule(ops):
-    n = len(ops)
-    depend(ops)
-    users = [[] for _ in range(n)]
-    for i, o in enumerate(ops):
-        for j in o["dep"]:
-            users[j].append(i)
-    hop = COST["hop"]
-    prio = [0.0] * n
-    for i in range(n - 1, -1, -1):
-        prio[i] = ops[i]["ns"] + max([prio[u] + (0.0 if i in ops[u]["soft"] else hop + ops[i]["lat"]) for u in users[i]], default=ops[i]["lat"])
-    for i, o in enumerate(ops):
-        prio[i] += BIAS.get(o["id"], 0.0)
-    left = [len(o["dep"]) for o in ops]
-    done = [0.0] * n
-    free, bank = {}, {}
-    cand = [i for i in range(n) if left[i] == 0]
-
-    def ready(i):
-        o = ops[i]
-        r = max([0.0 if j in o["soft"] else done[j] + hop for j in o["dep"]], default=0.0)
-        for b in o["banks"]:
-            if b in bank and ops[bank[b]]["eng"] != o["eng"]:
-                r = max(r, done[bank[b]] + hop)
-        return max(r, free.get(o["eng"], 0.0))
-    while cand:
-        st = {i: ready(i) for i in cand}
-        first = min(cand, key=lambda i: (st[i], -prio[i]))
-        e = ops[first]["eng"]
-        mine = [i for i in cand if ops[i]["eng"] == e]
-        now = [i for i in mine if st[i] <= st[first] + 1e-6]
-        pick = max(now, key=lambda i: prio[i])
-        if e not in "xy":
-            while True:
-                b = [i for i in mine if prio[i] > prio[pick] + ops[pick]["ns"] and st[i] < st[pick] + ops[pick]["ns"] - COST["look"]]
-                if not b:
-                    break
-                lim = min(st[i] for i in b)
-                fit = [i for i in now if st[i] + ops[i]["ns"] <= lim + COST["look"]]
-                if fit:
-                    pick = max(fit, key=lambda i: prio[i])
-                    break
-                pick = min(b, key=lambda i: (st[i], -prio[i]))
-        o = ops[pick]
-        for b in o["banks"]:
-            bank[b] = pick
-        o["t0"] = st[pick]
-        free[o["eng"]] = st[pick] + o["ns"]
-        done[pick] = st[pick] + o["ns"] + o["lat"]
-        cand.remove(pick)
-        for u in users[pick]:
-            left[u] -= 1
-            if left[u] == 0:
-                cand.append(u)
-    return max(done)
-
-
-PERIOD = 13000.0
-
-
-def simulate(ops, tau, fix=False):
-    hop = COST["hop"]
-    seq, key = {}, []
-    for i, o in enumerate(ops):
-        k = tau[o["id"]] + PERIOD * o["step"]
-        for j in o["dep"]:
-            if j < i and key[j] > k:
-                k = key[j]
-        key.append(k)
-        seq.setdefault(o["eng"], []).append((k, i))
-    qs = [[i for k, i in sorted(v)] for v in seq.values()]
-    pos, free, done, bank, order = [0] * len(qs), [0.0] * len(qs), [-1.0] * len(ops), {}, []
-    rdy = [None] * len(qs)
-    for _ in range(len(ops)):
-        best, bs = -1, 1e18
-        for q in range(len(qs)):
-            if pos[q] == len(qs[q]):
-                continue
-            o = ops[qs[q][pos[q]]]
-            r = rdy[q]
-            if r is None:
-                r = free[q]
-                for j in o["hard"]:
-                    d = done[j]
-                    if d < 0:
-                        r = None
-                        break
-                    if d + hop > r:
-                        r = d + hop
-                if r is None or any(done[j] < 0 for j in o["soft"]):
-                    continue
-                rdy[q] = r
-            for b in o["banks"]:
-                if b in bank and bank[b][0] != q and done[bank[b][1]] + hop > r:
-                    r = done[bank[b][1]] + hop
-            if r < bs:
-                best, bs = q, r
-        if best < 0:
-            return None, 1e18
-        i = qs[best][pos[best]]
-        o = ops[i]
-        for b in o["banks"]:
-            if fix and b in bank and bank[b][0] != best:
-                o["dep"].add(bank[b][1])
-            bank[b] = (best, i)
-        o["t0"] = bs
-        free[best] = bs + o["ns"]
-        done[i] = bs + o["ns"] + o["lat"]
-        pos[best] += 1
-        rdy[best] = None
-        order.append(i)
-    return order, max(done)
-
-
-def prepared():
-    ops = plan()
-    schedule(ops)
-    sent = {o["step"]: o["t0"] for o in ops if o["kind"] == "send" and o["args"][0] == "p"}
-    sent[-1] = sent[0] - PERIOD
-    tau = {}
-    for s in (3, 4, 5, 2, 1, 0, -1):
-        for o in ops:
-            if o["step"] == s:
-                tau.setdefault(o["id"], o["t0"] - sent[s])
-    return ops, tau
-
-
-def refine(ops, tau, rounds, seed=12345):
-    st = sorted(k for k in tau if k[0] != "p")
-    pr = sorted(k for k in tau if k[0] == "p" and "load" not in k)
-    x = [seed]
-
-    def rnd():
-        x[0] = (x[0] * 6364136223846793005 + 1442695040888963407) % (1 << 64)
-        return (x[0] >> 11) / float(1 << 53)
-    best = simulate(ops, tau)[1]
-    for _ in range(rounds):
-        pool = pr if rnd() < 0.12 else st
-        old = {}
-        for _k in range(2 if rnd() < 0.3 else 1):
-            k = pool[int(rnd() * len(pool))]
-            old.setdefault(k, tau[k])
-            tau[k] += (1 if rnd() < 0.5 else -1) * math.exp(4 + rnd() * (3.6 if pool is st else 4.5))
-        v = simulate(ops, tau)[1]
-        if v <= best + 5:
-            best = v
-        else:
-            tau.update(old)
-    return best
-
-
-def place(ops, key, before, after, back, lean, way):
-    n, hop = len(ops), COST["hop"]
-    left = [len(b) for b in before]
-    pend = sorted((key[i], i) for i in range(n) if left[i] == 0)
-    start, early, lines = [0.0] * n, [0.0] * n, {}
-    while pend:
-        i = pend.pop(0)[1]
-        o = ops[i]
-        tail = o["lat"] + hop
-        pick = None
-        for w, (e, ns) in enumerate([(a[0], a[3]) for a in o["alt"]] if "alt" in o else [(o["eng"], o["ns"])]):
-            t = early[i] if early[i] or not back else o["lat"]
-            need = ([] if e == "x" else [(e, 0.0, ns)]) + [(b, -tail if back else 0.0, ns if back else ns + tail) for b in o["banks"]]
-            moved = True
-            while moved:
-                moved = False
-                for r, lo, hi in need:
-                    for s, f, who in reversed(lines.get(r, ())):
-                        if f <= t + lo + 0.01:
-                            break
-                        if s + 0.01 < t + hi and (who != e or r == e):
-                            t, moved = f - lo, True
-            v = t + ns + (lean[i] if w == 0 else 0.0)
-            if pick is None or v < pick[0]:
-                pick = (v, t, ns, e, need, w)
-        v, t, ns, e, need, way[i] = pick
-        start[i], o["ns"] = t, ns
-        for r, lo, hi in need:
-            line = lines.setdefault(r, [])
-            k = len(line)
-            while k and line[k - 1][1] > t + hi:
-                k -= 1
-            line.insert(k, (t + lo, t + hi, e))
-        for u, d in after[i]:
-            if t + ns + d > early[u]:
-                early[u] = t + ns + d
-            left[u] -= 1
-            if left[u] == 0:
-                k, v = len(pend), (key[u], u)
-                while k and pend[k - 1] > v:
-                    k -= 1
-                pend.insert(k, v)
-    return start
-
-
-def arrange(ops, rounds, seed):
-    depend(ops)
-    n, x = len(ops), [seed]
-
-    def rnd():
-        x[0] = (x[0] * 6364136223846793005 + 1442695040888963407) % (1 << 64)
-        return (x[0] >> 11) / float(1 << 53)
-    pre, post = [[] for _ in ops], [[] for _ in ops]
-    for i, o in enumerate(ops):
-        for j in o["dep"]:
-            d = 0.0 if j in o["soft"] else ops[j]["lat"] + COST["hop"]
-            pre[i].append((j, d))
-            post[j].append((i, d))
-    best, keep = 1e18, [float(i) for i in range(n)]
-    key, lean, way = keep, [PAR["lean"]] * n, [0] * n
-    good = lean
-    for r in range(rounds):
-        f = place(ops, key, pre, post, False, lean, way)
-        v = max(f[i] + ops[i]["ns"] + ops[i]["lat"] for i in range(n))
-        if v < best:
-            best, keep, ways, good = v, f, list(way), lean
-        if r % 3 == 2:
-            amp = 50.0 + 700.0 * rnd()
-            lo = best * rnd()
-            f = [s + amp * rnd() if lo < s < lo + PAR["span"] else s for s in keep]
-            lean = [(3 * rnd() - 1) * PAR["lean"] if lo < keep[i] < lo + PAR["span"] and rnd() < 0.3 else good[i] for i in range(n)]
-        b = place(ops, [-(f[i] + ops[i]["ns"]) for i in range(n)], post, pre, True, lean, way)
-        key = [-(b[i] + ops[i]["ns"]) - BIAS.get(ops[i]["id"], 0.0) for i in range(n)]
-    for i, o in enumerate(ops):
-        o["id"] = i
-        if "alt" in o:
-            o["eng"], o["kind"], o["args"], o["ns"] = o["alt"][ways[i]]
-    return {i: keep[i] - PERIOD * ops[i]["step"] for i in range(n)}, best
-
-
 ORDER = """
-v.a0_4!:-439 v.x1_0:-414 t.x2_0:-389 t.x1_0:-319 v.x4_0:-317 v.x3_0!:-303 v.x2_0!:-302 t.a0_0:-301 t.x5_0:-246 v.x2_1:-222 t.x0_0:-218 t.x3_0:-162 t.x8_0:-157 v.x3_1:-150 v.x1_1:-150 v.x7_0:-123 t.x6_0:-120 t.x4_0:-63 v.a0_0:-55 v.x0_0!:-46 v.x6_0!:-46 v.x5_0!:-41 t.x7_0:-27 v.x6_1:-16 v.x4_1:-15 v.b0_0:-14 v.x8_0!:-14 v.x0_1:23 v.x5_1:31 v.a0_2!:33 v.p0!:35 v.w1:51 v.a1_0!:57 v.x7_1:58 t.a1_0:60 t.hb2:60 v.x8_1:61 t.r0:64 v.a1_2!:66 t.hb4:72 t.hb3:73 t.a0_1:96 v.a0_1:112 t.hb0:113 v.a0_6:130 v.a0_3:134 t.b0_0:134 v.a0_7:134 v.a0_5:134 v.w0:135 v.p3!:136 v.a1_6!:154 v.a1_4!:161 v.w3!:176 v.b0_3!:178 v.a0_8:181 t.hb1:192 v.w2:193 v.a1_1:194 t.b0_1:194 v.a1_7:198 v.b1_4!:201 v.a1_3:207 x.c0:207 t.b1_0:218 v.b0_1!:226 v.b0_6:243 v.r6!:245 v.a1_5:246 t.w0:253 t.b0_2:253 g.c0:258 v.q2:260 v.b0_4!:263 t.n1_0:273 v.b0_9:276 v.b0_2:288 v.r1:289 t.a1_1:292 v.r0:295 v.a1_8:295 v.b0_5!:303 v.b1_9!:310 t.b1_4:322 v.f0:331 t.b0_4:348 t.b0_6:349 v.r3:357 t.b0_7:357 t.b1_1:365 v.b0_8:368 t.f0:369 t.b0_3:378 t.b0_5:383 v.b0_7:388 v.b1_0:388 v.r2:391 v.b1_3:411 v.b1_5!:417 t.b1_7:423 v.h0_0:433 v.h4_1:434 v.h0_1:438 t.n0_1:445 v.r5:461 x.p0:468 v.b1_1:477 v.r4:483 t.b1_2:488 v.b1_2:492 v.n0_0:496 t.n0_0:510 t.b1_6:526 t.n0_e2:538 t.q0:550 v.b1_6:573 v.n0_1:574 v.b1_7:574 v.b1_8:578 t.b1_5:578 t.b1_3:578 v.n0_2:581 v.h4_0:593 v.q0!:599 v.p1:600 v.p2:615 v.n0_e2:615 v.n0_e0:615 v.s0!:616 g.p0:620 t.n0_e5:625 t.k1:636 v.n0_o0:667 v.n0_e1:668 v.n0_e3:669 v.n1_0:670 t.q1:683 x.q0:685 v.n0_e4:694 v.n1_1:694 t.n0_e1:694 t.n0_e0:695 t.n0_e3:698 v.q1!:698 t.n0_e4:701 t.s0:711 v.n1_2!:776 v.n1_e2:776 v.n0_e5:799 t.n1_e3:807 t.n1_1:818 v.n1_e1:853 v.n1_e4:853 v.n1_e0:854 t.n1_e5:881 v.n1_e5:882 v.n1_e3:884 g.q0:915 t.n1_e4:919 t.n1_e2:929 v.f1:934 t.n1_e0:936 v.in0:939 v.s1:941 t.n1_e1:955 t.f1:960 v.n1_o0:965 v.f2:1000 t.l0:1000 t.j0:1006 t.ine5:1086 v.ino0:1109 t.ine4:1110 t.i0:1113 v.i0:1113 t.i1:1120 v.ine0:1129 v.l0:1147 v.in1:1148 t.k0:1158 v.ine5:1169 t.ine0:1177 t.j1:1179 v.in2:1193 v.ine2:1193 v.ine4:1193 v.ine1:1194 v.ine3:1194 t.in0:1242 t.ine3:1243 t.ine2:1243 t.ine1:1244 v.j1!:1406 v.j0!:1418 v.j2!:1424 v.k0:1424 v.k1:1444 v.d0!:1491 t.d0:1508 v.k2:1553 v.k3:1641
+0Yload0 0Yload1 0Yload2 0load0 0Yload3 0Yload4 0Sload0 0Sload1 0Sload2 0Gc0 0c61 0Gc3 0c73 0c3 0Gc2 0c4 0c5 0c0 0c6 0c40 0c60 0c26 0c25 0c27 0Gc1 0c1! 0c9 0c28 0c62 0c29 0Gc4 0c65 0c35 0c30 0Gflat1 0c16 0c44 0c41 0c19! 0c31 0c45 0c39 0s0! 0c32 0c52 0Gflat0 0c46! 0c33 0c43 0c42! 0Ts0 0c7 0c2! 0c34! 0d4 0u13! 0u14 0c36 0u12! 0n00 0n10 0n20 0c47 0s2 0u0! 0c51 0c10 0Tu6 0c48! 0c66 0s4 0u8! 0c17 0c13! 0c53 0u2! 0n21 0Tu0 0n01 0u4 0u10! 0Tu1 0u16 0u6! 0c8 1Gr0 0d2 0Sc0 0n11 0c56 0d0 0s5 0c58 0d3 0Gc5 0u26 0u15 0Gflat2 0c57 0u1 0c14 1Gr1 0s1 0Tu2 0u21 0u3 0d1 0Tu3 0u19! 0n12 0c59! 0n22! 0c54! 0u5! 0n02 0c15! 0c21! 0n1e0 0u18 0n2e0 0n0e0 0Tn10 0Tn20 0c37 0Tn1e0 0Tn2e0 0c20 0c68 0Tn00 0Tn0e0 0c22! 0c64 0c18! 0Tu4 0c38 0u22 1Thb00 0c11! 1Thb20 1Thb10 0u25 0c63 0n2o0 0n2o1 0c69 0n0o1! 0c12! 0u23 0c70 0c55 0c24! 0c49! 0u17 0n0o0 0c23 0n1o1 0n1o0 0c50 0c67! 0u7! 0Tu5 0u20! 0c72 0u9! 0u24!
+1x70 1x60! 1x50! 1x40 1x10 1x00! 1x30 1Ta20 1x20! 1Ta00 1x80 1x90! 1Ta10 0s3 0c71! 1a0w1 1a2w1 1Ta30 1a0w0 1a0z0 1a1w1 1a2w0 1a1w0 1a0s0 1a3w0 0u11! 1w2! 1w0 1w1 1w3! 1a3w1 1a1z0 1a0c0 1Tw0 1w4! 1a1c0 1a1s0 1Ta0c0 1r0 1s0 1a2z0 1r2 1Ta1c0 1r1 1a2s0 1Sa0c0 1Tr0 1a2c0 1Ta0c1 1Sa1c0 1a3z0 1r3 1Ta1c1 1r4 1Ta2c0 1a3c0 1p0! 1Gc0 1Ta3c0 1a1c1 1a0c1 1Sa2c0 1Tn00 1p1 1Th0 1Sa3c0 1n00 1Ta2c1 1h0 1Ta3c1 1Tu0 1a2c1 1s1! 1a3c1 1n01 1p2 1Tu1 1Tu2 1n02 1Tn10 1Tn20 1u2! 1p3 1u1! 1n10 1u0! 1n20 1Tn01 1n0e1 1Sv0 1n11 1n21 1Ts0 1q0 1n12! 1n22 1n0e0 1n1e1 1n1e0 1Gq0 1n2e0 1n2e1 1Tn0e0 1Xc0 1v0 1Tn0e1 1s2 1Tn11 1Tn1e0 1Tn1e1 1s3 1Tn21 1Tn2e0 1Tn2e1 1n0o0 1Sv1 1n1o0 1Ts1 1n2o0 1l0! 1l1 1Sv2 2Gr0 1o0 1Xq0 1s4 1o1
+2x00! 2x10 2Gr1 2x60! 2x70 2Ta00 2x20 2x30! 2a0w1 2x40! 2x50 2Ta10 1Ti0 1Ti1 1f0! 2a0z0 2a1w1 1in0 2Ta20 2a1z0 2a0s0 1i0! 1in1 2a0c0 1in2! 2a1s0 1Ti2 2x80! 1Tj0 1Tk1 1Tk0 1ine0 1ine1 2a2w1 1Tin0 2a1c0 2x90! 1Tine0 1Tine1 2Ta0c0 1v1 1ino0 2a0w0 2a2z0 1j0! 1f2! 2x110 2Ta1c0 2x100! 2a1w0 2a2s0 2a2c0 2Sa0c0 2Ta30 2Sa1c0 1f1! 2Ta0c1 2a2w0 2Ta1c1 1ino1! 1k0 1k2 2Ta2c0 2a3w0 2b0 1k1! 2a3w1 2b2 2b1 2a3z0 2w0 2w2! 2Thb11 2Thb10 2Thb21 2Thb20 2Thb00 2Thb01 2w3! 2a1c1 2a0c1 2w1 2Sa2c0 2Tu0 2a3c0 2w4! 2Tn00 2Tw0 2a3s0 2u0! 2n00 1k3 2Ta2c1 2Ta3c0 2n01 2r0 2a2c1 2n02! 2r1 2r2 2Tn10 2Tu1 2Sa3c0 2n0e0 2Tr0 2n10 2u1 2Ta3c1 2n0e2 2Tn01 2Tn0e0 2r3 2a3c1 2n11 2p0! 2Tu3 2n12 2Tn20 2Th0 2n0e1 2Tu2 2n20 2Tn11 2u3 2n1e2 2Tn0e1 2n1e1 2Tn0e2 2n21 2n1e0 2u2 2h0 2n22 2Tn1e0 2Tn1e1 2Tn1e2 2p1 2s1! 2u4 2p2 3Gr1 2n2e0 2n2e1 2q0! 2p3 2Tn21 2n2e2 2Tn2e0 2Sv0 2Tn2e1 2s0 2r4 2Gq0 2Tn2e2 2n0o0! 2Ts0 2v0 2n2o0! 2n2o1! 2n1o0 2Sv1 2n2o2 2Sv2 2s2 2s3 2Gc0 2l0 2l1! 2Ts1 2Xq0 2o0 2s4 2o1
+3x10! 3x00 3x30! 3x20 3Gr0 3Ta00 2Xc0 2f0! 3x40 3Ta10 3x60! 2Ti0 2Ti1 2v1 3x70! 3a0w1 2in0 3a0z0 2i0 2in1 3a1w1 3x50! 2Ti2 2Tj0 2in2 3a1z0 2Tin0 2ine0 2ine1 2ine2 2j0 2Tine0 3a0s0 2Tine1 2Tine2 3x90! 3a0c0 3Ta20 2ino0 3a1w0 3x80! 3a1s0 3x110 3x100! 3Ta0c0 3a2w1 3a2w0 3a0w0 2f2! 3a2z0 2f1! 3a1c0 3Ta30 3a2s0 3Sa0c0 2Tk0 3a2c0 3Ta0c1 3Ta1c0 3a3w0 3b0 2k0 3b1 3Ta2c0 2k1! 3a3w1 3b2 3Sa1c0 3w0 3w2! 3w1 3w4! 3Ta1c1 2Tk1 3Thb11 3Thb22 3a3z0 3w3! 3Thb00 3Thb12 3Thb10 3a1c1 3Tw0 3a0c1 3a3s0 3Sa2c0 3a3c0 3Tn00 3Ta2c1 3Tu0 3r0 3Ta3c0 2k2 2ino1! 3a2c1 3r1 3u0! 3r2 3n00 3Tn10 3Tr0 3n01 3Sa3c0 3Thb01 3n10 3Thb21 2k3 3n02! 3r3 3Ta3c1 3Thb20 3n11 3Th0 3p0! 3a3c1 3n12 3n0e3 3Tu3 3Tn20 3n0e0 3Tu1 3Tu2 3h0 3Thb02 3n20 3Tn01 3n1e0 3Tn0e0 3n1e1 3u2 3n21 3Tn11 3n0e1 3Tn1e0 3Tn1e1 3u3! 3u1 3n22! 3n0e2 3Tn0e1 3p1 3s1! 3u4 3Tn0e2 3p2 4Gr1 3Tn0e3 3n2e0 3n2e1 3p3 3q0! 3Tn21 3n1e3 3Tn2e0 3n2e2 3Tn2e1 3Sv0 3n1e2 3n2e3 3Gq0 3r4 3Tn2e2 3s0 3Tn1e2 3Tn1e3 3Tn2e3 3Ts0 3v0 3n0o0 3n2o0! 3n1o0 3Sv1 3n2o1 3Sv2 3n2o2 3Gc0 3s2 3s3 3Xq0 3l0 3l1! 3Ts1 3o0 3s4 3o1
+4x00! 4x10 4x30! 4Gr0 4x20 3Xc0 4Ta00 4x70! 4x50 4x60! 3Ti0 3Ti1 4Ta10 3in0 4x40! 4a0w1 3i0 3in1 4a0z0 3Ti2 3in2 3Tj0 3v1 4a1w1 3Tin0 3ine0 3ine1 4x80! 3ine2 3ine3 3Tine0 3j0 3Tine1 4a1z0 3Tine2 4a0s0 3Tine3 4Ta20 4x90! 4a1s0 3ino0 4a0c0 3f0! 4x110 4Ta0c0 4x100! 4a2w1 4a1c0 4a2z0 3f2! 4a0w0 3f1! 4a2w0 4Ta30 4a1w0 4a2s0 3ino1! 4Sa0c0 4a2c0 3Tk0 4Ta0c1 4Ta1c0 4a3w0 4b0 3k0 4a3w1 4b2 4b1 3k1! 4Ta2c0 4a3z0 4Sa1c0 4w0 4w2! 4w1 4w4! 4Ta1c1 4a3c0 4Thb11 3Tk1 4Thb12 4Thb23 4Tw0 4a0c1 4a1c1 4a3s0 4Sa2c0 4w3! 4Thb03 4Tn00 4Ta2c1 4Ta3c0 4r0 3k2 4a2c1 4r1 4r2 4n00 4Tu0 4Tn10 4Tr0 4Thb01 4n01 4Thb00 4Sa3c0 4Ta3c1 4n10 3k3 4n02! 4Thb02 4r3 4u0 4a3c1 4Thb13 4n11 4p0! 4Tu1 4Tu2 4Tu3 4n0e0 4n0e1 4n0e2 4Tn20 4Th0 4u1 4n20 4Tn01 4Thb22 4Tn0e0 4Tn0e1 4Tn0e2 4u3 4u2 4h0 4n21 4Thb20 4n0e4 4n12! 4Thb10 4u4 4n22! 4p1 4n0e3 4s1! 4n1e2 5Gr1 4p2 4n1e3 4n2e0 4Tn11 4n1e0 4p3 4Thb21 4q0! 4Gq0 4Tn0e3 4Tn1e0 4Sv0 4Tn0e4 4n1e1 4n2e1 4n2e2 4n2e3 4Tn21 4Tn2e0 4Tn1e1 4Tn1e2 4n2e4 4Tn2e1 4Tn2e2 4n1e4 4Tn2e3 4s0 4Tn1e3 4Tn2e4 4n2o1! 4Tn1e4 4Ts0 4r4 4v0 4n1o0 4n0o0! 4n2o0 4n2o2 4Sv2 4Gc0 4Sv1 4s2 4s3 4Ts1 4l0 4l1! 4Xq0 4v1 4o0 4s4 4o1
+5x00! 5x10 5Gr0 5x60! 5x30 4Xc0 5Ta00 5x20! 5x40 4Ti0 5x70! 4Ti1 5Ta10 4in0 5x50! 5a0w1 4i0 4in1 4f2 4Ti2 4in2 5a0z0 5a1w1 4Tin0 4ine0 4Tj0 4ine1 4ine2 4f0! 4ine3 4Tine0 4ine4 4Tine1 5a0s0 4Tine2 4Tine3 4Tine4 5Ta20 5a1z0 5x90! 5a0c0 5a1w0 4ino0 5a1s0 5x80! 5x100 5Ta0c0 5x110! 5a2w1 4j0 5a0w0 5a2w0 4ino1! 5a2z0 5Sa0c0 5a1c0 4f1! 5Ta30 5a2c0 4Tk0 5a2s0 5Ta0c1 5Ta1c0 5b0 5a3w0 4k0 5b2 5b1 4k1! 5Ta2c0 5a3w1 5Sa1c0 5w0 5w2! 5w1 5w3! 5Ta1c1 5Thb12 5a3z0 5Thb22 5Thb23 4Tk1 5Tw0 5a0c1 5a1c1 5a3s0 5Sa2c0 5a3c0 5w4! 5Tu0 5Thb04 5Tn00 5r0 5Ta2c1 4k2 5Ta3c0 5u0! 5r2 5r1 5n00 5a2c1 5Tr0 4k3 5n01 5Thb20 5Sa3c0 5Thb03 5Thb21 5Thb24 5n02! 5Tn10 5r3 5Ta3c1 5Thb00 5Th0 5n10 5a3c1 5Tu1 5n0e5 5n0e0 5Tu2 5Tu3 5h0 5n0e1 5Tn20 5Thb01 5p0! 5Thb02 5n11 5u1 5n20 5Tn01 5u3! 5u2 5n0e3 5n21 5Thb13 5n12! 5Thb11 5Thb14 5n0e2 5Thb10 5Tn0e0 5p1 5n22! 5u4 5p2 6Gr1 5Tn0e1 5Tn0e2 5n1e2 5n1e1 5n1e3 5Tn0e3 5Tn11 5p3 5q0! 5Tn21 5s1! 5Gq0 5n1e0 5Tn1e0 5n0e4 5n2e0 5n1e5 5n2e2 5n2e1 5Tn0e4 5Tn0e5 5n2e4 5Tn2e0 5Tn1e1 5n1e4 5n2e3 5Tn2e1 5n2e5 5Sv0 5Tn2e2 5Tn1e2 5Tn1e3 5Tn1e4 5s0 5Tn1e5 5r4 5Tn2e3 5Tn2e4 5Tn2e5 5v0 5Ts0 5n1o0! 5Sv1 5n2o1 5n2o0 5n0o0 5Xq0 5Gc0 5n2o2 5Sv2 5s2 5s3 5l0 5l1! 5v1 5Ts1 5o0 5f2! 5s4 5o1
+6x10! 6x00 6Gr0 5Xc0 6x70! 6x30 6Ta00 6x20! 5Ti0 6x50 5Ti1 6x40! 6Ta10 5in0 6a0w1 5i0 5in1 6a0z0 5Ti2 6x60! 5in2 6a0c0 5Tin0 5Tj0 5ine2 5ine0 6x90! 5ine1 5ine3 5ine4 5Tine0 5ine5 5Tine1 6a1w1 5Tine2 5Tine3 5j0 5Tine4 6a0s0 5f0! 5Tine5 6Ta20 6a1z0 5ino0 6x80 6x100! 6a1s0 6Ta0c0 6x110! 6a2w1 6a1c0 6a2z0 5f1! 6a0w0 6a2w0 6Ta30 6a1w0 6a2c0 5ino1! 6Sa0c0 6a2s0 5Tk0 6Ta1c0 6b0 6a3w0 6b2 5k0 6a3w1 6b1 5k1! 6Ta2c0 6a3z0 6w2! 6w0 6Sa1c0 6w1 6Ta0c1 6a3s0 6Ta1c1 6Tw0 6a3c0 6Sa2c0 6w4! 6a0c1 6a1c1 6w3! 6Ta3c0 6r0 6s0 6r1 6Tu0 6r2 6Ta2c1 6Sa3c0 6Tr0 6u0! 6a2c1 6Ta3c1 6Tu1 6r3 6a3c1 6Th0 6p0! 6Tu2 6Tu3 6h0 6u1 6u3 6u2 6u4 6p1 6s1! 6p2 6p3 6q0! 6Ts0 6Sv0 6Gq0 6v0 6Sv2 6s2 6s3 6Sv1 6y0 6Ts1 6Xq0 6s4 6v1 6y1! 6Tj1 6Tj0 6j1 6j0 6j3 6j2 6Yj0 6Sj0
 """
-ORDER = """
-v.a0_4!:-575.5 v.x2_0!:-530.8 t.x2_0:-484.3 v.x3_0!:-454.3 t.a0_0:-392.8 v.x1_0:-354 v.x6_0!:-351.6 v.x0_0!:-351 t.x1_0:-312.7 v.x2_1:-312.5 v.x4_0:-303.9 t.x3_0:-295.8 v.w3!:-283.9 v.w1:-278.5 t.x4_0:-210.9 t.r0:-163 v.a1_6!:-152.2 v.b0_0:-107 v.a1_0!:-105.2 v.b0_6:-80.1 v.x1_1:-76.7 v.x3_1:-76.4 t.x5_0:-55.8 v.p0!:-47.8 t.a0_1:-29.2 t.x6_0:-17.7 v.a0_2!:-12.3 t.x0_0:-6.2 t.a1_0:14.4 v.x5_0!:16.2 v.x7_0:18.2 t.hb3:22.1 t.x7_0:24.2 t.f0:24.5 t.x8_0:31.8 v.x6_1:31.9 v.x4_1:32 x.c0:34.9 v.x8_0!:43.6 v.x5_1:49.4 v.a0_0:49.7 v.x0_1:52 v.x7_1:52.5 v.x8_1:52.5 v.a0_6:52.5 v.a0_1:71.1 t.hb4:78 t.hb2:84.4 t.b1_0:105.4 t.hb0:115 v.h0_1:115.7 t.b0_0:119.3 v.a1_4!:122.1 v.a1_2!:123.6 v.a0_5:129.2 v.a0_7:129.5 v.a0_3:130.3 v.w0:135 v.a0_8:154.9 t.n0_0:164.5 g.c0:173.8 v.b1_5!:185.7 t.hb1:186.5 v.w2:193 v.a1_1:194 t.b0_1:194 v.b0_3!:198.4 v.a1_5:202.7 v.r1:209.9 v.a1_7:213.4 v.b0_1!:224.6 v.a1_3:234.2 t.w0:235.3 v.b0_4!:239.8 t.b0_2:241 t.b0_7:254.2 t.a1_1:264.1 t.b0_6:267.3 v.b0_9:275.7 v.b0_2:294.3 t.b1_5:301.4 v.r0:302.1 v.a1_8:303.7 t.b0_4:305.2 v.r3:306.3 t.b1_7:309.7 v.b0_5!:314.3 t.b1_1:317.1 t.b1_2:325.2 v.r6!:340.3 v.f0:358.6 t.b0_5:361.9 v.b0_8:377.3 v.b1_2:379.7 v.b0_7:387.3 v.b1_4!:392.5 v.b1_0:395.5 t.b0_3:401.2 t.b1_3:407 v.r2:410.1 t.n1_0:413.9 t.q1:457.3 v.r5!:467.2 x.p0:468 v.b1_3:468.8 v.b1_9!:475.2 t.b1_4:477.3 v.h0_0:483 v.b1_1:484.4 v.h4_1:498.6 v.r4:511.8 v.n0_0:516.6 t.b1_6:524.4 t.n0_e5:525 t.q0:553.1 v.s0!:555.3 t.n0_1:572.9 v.b1_6:573.3 v.b1_7:573.5 v.n0_1:574.7 v.b1_8:578 g.q0:580.8 v.n0_2:581 v.h4_0:581.1 x.q0:586 v.p1:596.6 v.n0_e1:612.5 v.n0_e4:614.5 v.q2:617.1 g.p0:620 v.n0_e0:632.1 v.q1!:646.4 v.p2:672.2 v.n0_e2:673.4 v.n0_e3:678.8 v.n1_0:682.1 v.q0!:699.4 t.n0_e4:700 v.p3!:712.1 v.n0_e5:724.8 t.n0_e0:824.2 t.n0_e1:824.2 t.n0_e2:824.2 v.n0_o0:824.2 v.n1_1:824.5 t.n1_e4:835.8 t.n0_e3:836 t.n1_1:849.3 t.s0:853 v.n1_2:872.1 t.n1_e0:900.4 t.n1_e1:911.7 v.n1_e3:947.6 v.n1_e4:948 v.n1_e2:960.3 t.n1_e2:975.4 v.n1_e1:981.3 v.s1:996.4 v.f1:1002.8 t.n1_e3:1011.4 v.n1_e0:1015.5 v.n1_o0:1037.4 t.f1:1037.8 v.ino0:1044.6 t.l0:1047.1 v.in0:1069.1 t.n1_e5:1092.9 v.f2:1106.5 v.n1_e5:1108.3 t.i0:1121.7 v.i0:1122.5 t.j0:1123.2 t.ine4:1128.5 t.i1:1144.4 t.ine1:1167.3 v.in1:1176 t.j1:1179 v.l0:1179 t.in0:1232.6 v.in2:1241.9 v.j1!:1259.2 v.ine0:1275.9 v.ine1:1276 v.ine2:1276.1 v.ine3:1277 v.ine4:1277.1 t.ine0:1315 t.ine3:1327.4 t.ine2:1330.6 v.ine5:1373.8 t.ine5:1373.8 t.k0:1374 v.j2!:1415.7 v.k0:1419.9 v.j0:1422.4 t.k1:1454.3 v.d0!:1463.8 v.k1:1466.8 t.d0:1512.7 v.k2:1536.5 v.k3:1682
-"""
-ORDER = """
-v.a1_6!:-1118.5 v.w3!:-681.9 v.a1_0!:-467.6 t.x8_0:-349.3 g.c0:-297.5 t.a0_1:-281.1 v.x3_0!:-155.5 v.x5_0!:-155.2 v.x1_0:-147.1 v.x2_0!:-110.6 t.x3_0:-91.7 v.x4_0:-79.7 g.q0:-77.2 v.a0_2!:-70.1 v.a1_2!:-69.8 v.x0_0!:-69.6 v.x5_1:-55 t.b0_1:-42.3 v.x3_1:-29.7 v.a1_4!:-23.6 t.x6_0:-23.2 t.b1_0:-12.9 t.hb4:-12 t.x5_0:-3.1 v.a0_4!:1.6 t.x1_0:28.2 t.x2_0:29.4 t.x0_0:29.4 t.x4_0:29.5 v.x7_0:30.1 t.x9_0:31.3 v.x6_0!:31.5 v.x8_0!:32.7 v.x1_1:39.7 x.c0:44.4 v.x2_1:47.2 v.x0_1:48.5 t.x7_0:50.8 v.p0!:57.5 t.hb3:65.4 v.x9_0!:67.3 t.hb1:72.4 t.hb2:79 v.b0_4!:86.1 t.a0_0:111.4 v.x4_1:137.7 v.x6_1:137.8 v.x8_1:147.6 v.x7_1:149.6 t.a1_0:151.2 v.x9_1:153.9 v.a0_0:154.9 v.a0_1:161 v.a0_6:161.1 v.a0_3:161.4 v.a0_5:161.5 v.a0_7:162.5 v.w0:168.8 t.b0_4:170.5 v.a1_1:171.4 v.w1:174.7 v.a0_8:178.3 v.w2:185.4 v.a1_7:190.9 t.n0_0:203.2 v.b1_1!:222.9 t.a1_1:235.3 v.a1_5:235.6 t.b0_0:239.1 t.w0:270.7 t.b1_5:274.8 v.b0_5!:278.8 t.b0_6:280 v.a1_3:282 t.b0_7:310.6 v.b0_3:313.7 x.q0:320 t.b0_2:322 v.b0_0:328.2 v.r0:344.7 v.b0_1:352.1 v.r1:357.6 v.r6!:366.7 t.b1_1:376.7 v.b1_9!:384 v.r5:388.7 v.a1_8:391.2 v.b0_2:396.9 v.f0:397.7 v.r2:406.5 v.b0_6:426.6 v.b1_5!:427.9 t.hb0:431.3 v.b0_9!:435.8 v.b0_8:453 t.b0_3:459 t.f0:459.3 t.b1_3:481.3 v.b1_0:489.9 v.b0_7:496.4 t.r0:496.5 t.b0_5:511 v.b1_3:515 v.n0_1:527.3 v.b1_4:535.7 v.r3:537.7 t.b1_2:538.3 v.n0_e3:543.4 t.b1_4:545.2 v.h0_0:545.3 t.b1_6:545.4 v.b1_2:547.5 v.h0_1:547.5 t.b1_7:550.6 v.n0_e0:551.5 v.r4!:562.8 v.b1_6:572.1 v.b1_7:583.4 v.b1_8:592.9 v.n0_0:599.7 v.p1:626.8 t.n1_0:637.6 v.h4_0:640 v.n0_e5:648 t.r1:650.6 v.p2:666.1 v.h4_1:673.9 v.p3:680.4 v.n0_2!:682.2 v.n0_e1:682.2 v.n0_e2:682.2 v.f1:710.9 v.n1_2!:723.6 t.n0_e5:759.4 v.n1_0:783.2 v.n0_e4:838.6 t.n0_e4:912.3 v.q0!:916.8 v.q1!:998 t.s0:999.3 t.n1_1:1000.9 t.u1:1016.6 t.n0_1:1024.4 t.n0_e0:1024.4 t.n0_e3:1024.7 t.n0_e1:1024.9 t.n0_e2:1025.2 v.s0!:1027.1 t.n1_e5:1038.2 v.n1_1:1054.2 v.n0_o0:1066.8 v.ino0:1082.7 t.n1_e2:1113 v.u1!:1130.4 v.n1_e0:1130.5 v.n1_e5:1158.1 v.ine5:1166.8 t.n1_e0:1171.9 v.in0:1190 t.u0:1195.4 v.n1_e2:1196.5 v.n1_e3:1196.6 v.n1_e4:1197.1 t.j1:1199.5 t.n1_e4:1200.4 v.n1_e1:1214.4 t.n1_e3:1216.7 t.n1_e1:1218.5 t.f1:1244.6 v.n1_o0:1265.9 v.s1:1283.1 v.i0!:1290.2 t.l0:1295.5 t.i0:1299.1 v.u0:1308.4 v.in1:1309.1 t.ine4:1315.1 v.l0:1317.6 t.j0:1326.7 v.j1:1336.8 v.in2:1338.7 t.i1:1347.3 v.ine0:1348.7 v.ine1:1348.7 v.ine2:1361.7 v.ine3:1362.3 v.ine4:1365.1 t.k0:1379.7 v.f2:1385.9 t.ine0:1390.8 t.in0:1394.4 t.ine2:1398 t.ine1:1398.1 t.ine3:1398.2 v.k0:1416.6 v.j0:1455.9 v.j2!:1460.4 v.d0!:1461.4 v.j3:1524.3 v.k1:1530.5 t.k1:1567.9 v.k2:1728 t.ine5:1798.9 t.d0:1898.1 v.k3:1930.2
-"""
-ORDER = """
-v.w3!:-1037.8 x.q0:-316.7 v.a0_8:-208.8 v.b0_0:-151.4 v.a0_0:-89.4 x.c0:-84.5 v.x3_0:-43.6 v.x2_0!:-34.3 v.x5_0!:-34 t.x2_0:-26.5 v.x1_0!:-26.5 t.x3_0:-26.4 v.a0_6!:-21.9 v.x4_0:-11.2 t.hb2:3.7 t.x5_0:14.8 v.x7_0:18.6 t.x1_0:21.2 t.x8_0:35.7 g.c0:36.7 v.x0_0!:41.5 t.x4_0:45.1 t.a0_0:65.9 v.x3_1:81.5 v.x6_0!:85.1 v.x5_1:89.3 v.x2_1:89.4 v.a1_0!:94.3 v.x9_0!:95.7 v.x1_1:98.8 t.x0_0:99.7 t.x7_0:128.3 v.x4_1:131.9 v.a0_2!:136.8 t.x6_0:139.9 t.x9_0:145.1 v.x8_0:146.1 v.x0_1:146.4 v.x7_1:165 t.hb4:168.6 t.a1_0:173.1 v.x6_1:174.6 v.x8_1:174.7 v.x9_1:174.7 v.a0_4:174.7 v.a1_6!:175.7 v.a1_2!:176.3 v.a1_4!:176.3 v.a0_1:178.4 t.b1_0:178.7 v.a0_7:185.6 v.a0_3:185.9 v.a0_5:186.5 v.w0:190 v.a1_1:191.5 v.w1:191.6 t.a0_1:196.5 v.w2:198.5 g.q0:203.3 v.g0_2:218.6 g.r0:231.6 t.g0_4:237.3 v.a1_7:238.1 v.g1_4!:253.5 v.a1_5:255.5 t.hb3:265.1 t.g0_2:271.5 g.r1:276.7 t.b0_0:276.7 v.a1_3:281.7 t.b0_1:300.2 t.b1_1:307 t.g1_0:307.7 t.w0:320.6 v.r0:332 t.a1_1:332.7 t.g0_0:360.6 v.g0_4:363.9 v.r1:371.1 v.r2:381.7 v.g0_3!:386.9 v.g0_0!:406.9 v.a1_8:417.1 v.g0_8!:418.6 v.g0_1:421.8 v.g1_3!:431.4 t.r0:433.9 v.g0_6:434.7 v.g0_5:434.8 v.b1_0:449.6 t.g0_3:453.5 t.hb1:477.8 v.p0!:487.6 v.n0_2!:494.3 v.g0_7:510.5 v.n0_0:521.7 t.g0_1:531.7 t.g1_2:532 t.g0_5:543.7 v.g1_2:561.8 v.r3:567.6 t.g1_4:577.8 v.g1_0:582 v.h0_0:583.5 v.g1_1:596.6 v.h0_1:596.9 v.r4!:618.8 v.g1_6:619.4 v.g1_5:631.8 t.g1_3:640.4 t.g1_5:644.7 v.g1_8!:647.9 v.g1_7:654.8 t.n0_0:655.4 t.g1_1:689.5 t.u0:706 v.f0:707 v.q1:712.9 t.f0:740.7 v.p1:744 v.n0_1:751.1 v.h4_0:761.6 v.n1_e5:802 t.hb0:802.2 v.p2:803.5 v.h4_1:816.4 t.r1:862.3 t.n1_0:862.5 v.p3!:893 v.q0!:958.5 v.n0_e0:980.3 v.n0_e1:980.4 v.n0_e3:980.5 v.n1_0:992.6 v.n0_e2:992.9 t.n0_e3:993.9 v.n0_e5:996.9 v.s0!:1013.1 t.n0_1:1031.4 v.n1_1:1051.9 v.n0_e4:1051.9 v.r5:1052 t.u1:1058.7 t.n0_e0:1070.1 v.u1!:1116.5 v.u0!:1126.7 t.n0_e2:1126.8 v.f1:1130.8 g.n1_0:1165.5 t.n1_e5:1168.4 t.n0_e1:1199.5 t.n0_e5:1200.5 v.n1_2:1201 t.n1_e4:1237.6 t.n0_e4:1269.7 v.n0_o0:1269.7 t.s0:1281.8 g.n0_0:1289.1 v.n1_e0:1297 v.n1_e4:1297.2 v.n1_e2:1297.4 t.n1_1:1307.6 v.n1_e1:1311.6 t.l0:1312.1 v.n1_e3:1315 t.n1_e3:1316.1 v.in0:1322.4 t.n1_e2:1323.5 t.n1_e1:1326.6 t.n1_e0:1326.7 t.f1:1335.6 t.j1:1338.5 v.n1_o0:1348.6 v.s1:1349.2 t.i0:1366 t.j0:1369 v.i0:1375.2 v.ine0:1378.9 v.l0:1383.7 v.in1:1384 t.i1:1385 v.j1!:1391 v.in2!:1397.5 v.ine1:1398.7 t.ine4:1401.9 t.in0:1404.4 v.ine2:1421.9 v.ine3:1422 g.in0:1425.5 v.ine4:1429.1 t.k0:1431.9 t.ine3:1459.4 t.ine0:1459.6 t.ine2:1460 t.ine1:1460.1 v.ino0:1468.9 v.j2!:1478.7 v.k0:1501.5 v.ine5:1518.4 t.k1:1522.1 v.f2:1534.8 v.j0:1548.5 v.k1:1551 g.j0:1565 v.d0!:1641.2 t.ine5:1671.3 v.k2:1701.8 v.k3:1791.4 t.d0:1877.5
-"""
-ORDER = """
-x.q0:-1026.2 t.x1_0:-528.6 v.x2_0!:-347 v.x3_0!:-346.6 t.w0:-282.1 t.x8_0:-269.2 g.r0:-244 v.a1_6!:-191.3 v.x4_0!:-99.8 v.x11_0!:-99.7 v.a0_6!:-96.9 t.x9_0:-79.3 t.g0_5:-74.9 v.x1_0:-11.9 g.r1:-0.9 v.a0_4!:10.1 v.w3!:10.5 t.x2_0:13.3 v.x5_0:16.2 v.x6_0:16.4 t.x5_0:29.6 t.a1_1:34 v.a0_2!:70.1 v.a1_0!:71.3 v.x7_0:78.9 t.x11_0:82.3 t.x7_0:86.3 t.x6_0:86.6 t.x3_0:86.9 t.x4_0:87.1 v.x2_1:101.4 v.x0_0!:101.9 t.b1_0:102.7 t.x10_0:106.6 v.x1_1:110.4 v.x5_1:111.6 v.x6_1:113.7 t.a0_0:116.9 v.a0_0:121.4 v.g1_3!:121.9 v.x4_1:122 x.c0:124.6 t.x0_0:125 v.x10_0!:128.3 v.x9_0!:138.9 v.x8_0:139.2 v.x0_1:148 v.x11_1:168.4 v.x3_1:184.3 v.a1_4!:185.7 t.b0_0:187.8 v.x7_1:189.9 v.x8_1:190 t.g0_3:192.1 t.a1_0:195.6 v.x10_1:198.2 v.x9_1:198.2 v.w4!:199.4 v.a1_2!:206.3 v.g0_3:230.8 t.hb2:236.6 t.a0_1:238.3 v.a0_1:242.1 v.a0_5:242.1 v.a0_3:242.6 v.a0_7:244.2 v.a1_1:255.3 v.w0:262.1 t.hb4:270.3 v.a1_7:277 t.b0_1:284.8 t.n0_0:315 v.a0_8:316.1 v.a1_3:321.3 v.a1_5:321.8 v.w1:323.5 v.w2:329 v.b0_0:337.1 v.g0_2!:376.4 v.g0_4:391.3 v.g1_4!:414.3 v.g0_1:421.8 v.a1_8:424.7 t.g0_2:425.1 t.g0_0:425.6 v.r0:433.4 v.g0_0!:434.7 v.g0_8!:446.4 v.r1:450.2 v.w5!:450.3 t.g0_4:453.1 v.r2:461.3 t.b1_1:462.3 t.g1_5:495.9 v.g0_7:509.5 v.g0_6:527 v.b1_0:531.5 v.g0_5:548.6 t.hb3:548.8 v.g1_2:549.2 t.r0:557 t.g0_1:559.4 t.hb1:561.4 t.g1_0:561.6 v.r3:578.5 t.g1_2:595.5 v.g1_0:612.1 v.p0!:618.9 v.h0_0:629.6 t.g1_3:634.4 t.g1_4:657.6 t.r1:663.3 v.g1_1:705.6 v.h0_1:708.8 v.g1_8!:712.5 t.hb0:717.2 v.h4_0:721.7 v.g1_5:737.6 t.n1_e5:740.1 v.g1_6:759.5 v.g1_7:775.5 v.r4!:801.1 v.r5:806.8 v.n0_0:807.9 v.p1:827.4 v.f0:835.5 v.n0_1:844.3 t.g1_1:857.7 t.u0:920.8 g.in0:940.2 v.f1:950 t.n0_e4:994.4 v.p2:994.9 v.h4_1:1000 t.l0:1031.3 t.i1:1033.9 t.n1_e4:1048.5 v.q0:1075.4 t.n1_e1:1075.9 g.q0:1082.3 v.n0_2!:1096.1 t.n1_e0:1113.5 t.n1_0:1115.1 v.p3!:1127.7 v.q1!:1129.7 t.n0_e1:1156.5 t.n0_e2:1164.3 t.j1:1165.4 t.u1:1167.1 t.n0_1:1193.5 v.n1_2:1197.5 g.c0:1202.3 v.n0_e1:1218.8 v.n0_e4:1235.3 v.n0_e2:1235.8 v.n0_e0:1235.9 g.n1_0:1262.8 t.n0_e3:1265.6 v.n1_0:1270.1 t.n0_e0:1271.6 v.n0_e3:1272.1 t.s0:1279.8 v.n1_1:1285.9 v.j1!:1290.2 v.s0!:1302.7 v.u0!:1312.8 v.u1!:1315.6 v.n0_e5:1325.8 v.n0_o0:1333.2 v.n1_e0:1333.6 v.n1_e2:1333.8 t.n1_e2:1334.8 v.n1_e4:1334.9 t.n1_1:1335.7 v.in2!:1335.7 v.n1_e1:1345.8 v.n1_e3:1347.1 t.n1_e3:1356.4 g.n0_0:1356.4 v.n1_e5:1357.9 v.n1_o0:1362.1 t.ine4:1375.6 t.n0_e5:1376.3 v.s1:1377.4 v.ine5:1387.6 t.i0:1392.1 t.j0:1393.2 v.in0:1407.3 v.i0:1415.6 v.l0:1439.2 v.in1:1444.6 t.ine1:1446.8 v.ine1:1451.1 v.ine2:1451.5 v.ine0:1458 v.ine3:1458.4 v.ine4:1462.4 t.in0:1472.7 t.ine0:1472.8 t.ine3:1477.9 t.ine2:1477.9 v.ino0:1490.9 v.j2!:1544.7 g.j0:1545.7 v.j0:1549.1 t.ine5:1551.6 t.k0:1558.2 v.k0:1576.4 v.d0!:1581.6 t.k1:1639 v.k1:1643.7 v.k2:1762.2 t.d0:1927.2 v.k3:2389.2
-"""
-ORDER = """
-x.q0:-578.1 t.b1_0:-295.6 v.g0_0:-284.8 v.a0_6!:-284.3 t.x6_0:-234.2 t.b0_1:-211.9 v.a0_1:-104.8 t.x9_0:-42.8 g.r1:-42.6 x.c0:-5.8 v.x0_0:1.3 v.x11_0!:4.6 v.x1_0!:5.5 v.x4_0!:5.6 v.x2_0!:7.3 v.x7_0!:7.5 v.a1_6!:25.4 t.x1_0:27.3 t.x2_0:29.3 v.x6_0:29.5 v.x5_0:48.2 t.a0_1:62.7 v.a0_0:76.6 t.x8_0:79.8 g.r0:87 t.a1_0:87.6 v.x11_1:113 t.hb2:119.2 t.x4_0:129.3 t.hb3:143.6 v.x3_0!:146.1 v.x1_1:147.5 v.x10_0!:150 t.x5_0:165.8 t.x7_0:166 v.x9_0!:167.9 v.x4_1:171 v.x2_1:178.4 v.x5_1:178.8 v.x6_1:179.8 t.x11_0:182.9 t.x0_0:187.5 t.x3_0:188 t.x10_0:188.2 v.x8_0:191.1 v.a1_0!:199.4 v.a0_4!:200.7 v.x0_1:201 t.hb4:202.4 v.a0_2!:207 v.x7_1:217.1 v.x3_1:220.9 v.x10_1:226.7 v.x8_1:230.4 t.a0_0:234.6 v.a1_8:256.9 v.x9_1:262.7 v.a1_5:269.3 v.a0_3:275.2 v.a0_5:282.3 v.a0_7:288.4 v.a1_1:290.8 v.w0:293.1 v.a1_7:308.7 v.a0_8:313 t.b0_0:330.9 v.a1_2!:331.4 v.a1_4!:334.4 v.a1_3:341.5 v.w1:346.2 v.w2:354.9 v.b0_0:362.8 t.a1_1:374.4 v.g0_2:381.9 t.g1_5:399.2 v.h0_0:409.5 v.w4!:410.2 v.w3!:413.3 v.r0:462.7 v.w5!:473.3 v.g0_1:507.6 v.g0_4!:532.2 v.g0_3!:611.3 t.w0:642 t.b1_1:697.1 v.g0_8!:707.8 v.r1:714.3 v.r2:714.9 v.b1_0:716.9 t.g0_0:728.9 t.g0_4:729.2 t.g0_2:742.1 v.g0_5:748 v.g0_6:748.2 v.g0_7:749.5 t.r0:759.6 t.g0_1:766.5 t.g0_5:780.4 v.g1_2!:786.5 v.g1_3!:792.3 v.r3:796.6 v.g1_0!:826.4 v.g1_4:829.3 t.g0_3:899.2 t.g1_0:899.3 t.g1_2:904.6 t.n0_e3:913 t.r1:920.1 t.g1_4:920.3 t.hb1:927.8 v.n0_0:938.5 v.g1_1:940.5 v.h0_1:959.3 t.g1_3:966.7 v.g1_6:974.2 t.n0_1:977.5 t.n1_1:986.2 v.g1_5:994.4 v.g1_7:997.7 g.q0:999.7 v.p0!:1043.3 t.n0_0:1045 t.hb0:1050.4 v.r4!:1058.5 v.g1_8!:1061.1 t.s0:1089.3 g.c0:1105.2 t.g1_1:1119.9 v.p1:1136.5 t.n0_e4:1146.3 v.n0_1:1158.9 t.u0:1161 t.n1_e0:1169 v.h4_0:1189.3 t.n1_0:1210.9 v.p2:1212 v.r5:1218.2 v.h4_1:1222.2 v.p3:1223.5 v.n0_e5:1230.7 v.n0_2!:1232 v.q0!:1232.7 v.n0_e2:1253.5 v.n0_e0:1253.6 t.n0_e1:1254.9 v.q1!:1256.4 v.n0_e1:1262.9 v.n0_e3:1263 v.n1_0:1276.3 t.u1:1278.7 v.n1_e5:1282.4 v.n0_e4:1294.8 v.n1_1:1296 t.n0_e0:1301.1 t.n0_e2:1301.3 v.s0!:1314.9 v.n1_e4:1332.3 g.n1_0:1333.8 v.n0_o0:1341.4 v.u1!:1343.7 v.f1:1345.3 v.n1_2!:1345.3 t.n1_e4:1346.8 v.n1_e0:1357.2 v.n1_e2:1366.9 v.n1_e1:1367.9 v.n1_e3:1368.1 v.u0!:1374.9 t.n1_e1:1377.5 t.n1_e2:1377.5 t.n1_e3:1377.5 v.n1_o0:1377.5 t.n1_e5:1381.9 v.f0:1388 v.s1:1388.3 t.n0_e5:1388.8 t.l0:1399.1 t.ine2:1413.8 t.i0:1419.7 v.in0:1435.7 v.i0:1441.2 t.j0:1445.2 v.l0:1451.6 v.in1:1451.8 v.j1:1483.2 t.j1:1483.6 v.ino0:1503.2 v.in2:1504.4 v.ine2:1525.7 t.ine4:1525.7 v.ine0:1527.9 v.ine1:1528 g.n0_0:1528.5 t.i1:1533.8 v.ine3:1534.1 v.ine4:1534.9 g.j0:1543.2 t.in0:1552.1 t.ine3:1552.5 t.ine1:1552.8 t.ine0:1552.9 v.ine5:1555.5 g.in0:1561.2 v.j0!:1599.6 t.k0:1604.3 t.k1:1622.6 v.j2!:1623 v.k0:1640.5 t.ine5:1661.6 v.k1:1674.2 v.d0!:2002.2 v.k2:2091.6 t.d0:2118.9 v.k3:2679.1
-"""
-STEP = 13700.0
 
 
-def keys(text):
-    tau, way = {}, {}
-    for w in text.split():
-        name, v = w.split(":")
-        way[name.strip("!")] = int(name[-1] == "!")
-        tau[name.strip("!")] = 10.0 * float(v)
-    return tau, way
-
-
-def unread(ops, i, d):
-    return ops[i]["raw"] is not None and d not in ops[i]["raw"] and all(ops[j]["kind"] not in ("dma", "send", "recv") for j in (i, d))
-
-
-def part(ops, steps):
-    idx = [i for i, o in enumerate(ops) if o["step"] in steps]
-    at, res = {i: j for j, i in enumerate(idx)}, {"x": -1}
-    num = lambda x: res.setdefault(x, len(res) - 1)
-    s = dict(idx=idx, name=[ops[i]["id"] for i in idx], step=[STEP * ops[i]["step"] for i in idx], lat=[ops[i]["lat"] for i in idx])
-    s["pre"] = [[(at[d], 0.0 if d in ops[i]["soft"] else ops[d]["lat"] + COST["hop"]) for d in sorted(ops[i]["dep"]) if d in at] for i in idx]
-    s["alt"] = [[(num(a[0]), a[3], [num(b) for b in ops[i]["banks"]], a[3] + ops[i]["lat"] + COST["hop"], 0.0)
-                 for a in ops[i].get("alt", [(ops[i]["eng"], 0, 0, ops[i]["ns"])])] for i in idx]
-    s["free"] = [{at[d] for d in ops[i]["dep"] if d in at and unread(ops, i, d)} for i in idx]
-    s["res"] = len(res)
-    above, used = [], set()
-    for i, p in enumerate(s["pre"]):
-        far = 0
-        for j, d in p:
-            far |= above[j]
-        s["pre"][i] = [(j, d) for j, d in p if not far >> j & 1 or s["lat"][j] > 100]
-        for j, d in p:
-            far |= 1 << j
-            used.add(j)
-        above.append(far)
-    s["ends"] = [i for i in range(len(idx)) if i not in used]
-    return s
-
-
-def rest(s, tau, way, pool):
-    end, start, key, why, kind, final, prev, held = replay(s, tau, way)
-    edge = min(key[i] for i, w in enumerate(s["name"]) if w in pool)
-    keep = [i for i in range(len(key)) if key[i] >= edge]
-    at, fin, busy = {i: j for j, i in enumerate(keep)}, {}, {}
-    for i in range(len(key)):
-        if i not in at:
-            e, ns, banks, hold, t = s["alt"][i][way.get(s["name"][i], 0) if len(s["alt"][i]) > 1 else 0]
-            fin[i] = start[i] + ns
-            for r, f in [(e, fin[i])] + [(b, start[i] + hold) for b in banks]:
-                busy[r] = max(busy.get(r, 0.0), f)
-    new = {w: [s[w][i] for i in keep] for w in ("idx", "name", "step", "lat")}
-    new["pre"] = [[(at[j], d) for j, d in s["pre"][i] if j in at] for i in keep]
-    new["alt"] = [[a[:4] + (max([fin[j] + d for j, d in s["pre"][i] if j in fin] + [busy.get(r, 0.0) for r in [a[0]] + a[2] if r >= 0] + [0.0]),)
-                   for a in s["alt"][i]] for i in keep]
-    new.update(free=[set()] * len(keep), res=s["res"], ends=[at[i] for i in s["ends"] if i in at], edge=edge)
-    return new
-
-
-def replay(s, tau, way):
-    pre, name, n = s["pre"], s["name"], len(s["idx"])
-    key, eng, free, edge = [0.0] * n, [0] * n, s["free"], s.get("edge", -1e18)
-    for i in range(n):
-        x = tau[name[i]] + s["step"][i]
-        if x < edge:
-            x = edge
-        for j, d in pre[i]:
-            if key[j] >= x:
-                x = key[j] + 1e-3
-        key[i] = x
-    start, fin, why, kind, prev = [0.0] * n, [0.0] * n, [-1] * n, [0] * n, [-1] * n
-    last, bank, other, held, alt = [-1] * s["res"], [(-1, -1.0, -1)] * s["res"], [(-1, -1.0, -1)] * s["res"], [()] * n, s["alt"]
-    for f, i in sorted(zip(key, range(n))):
-        al = alt[i]
-        e, ns, banks, hold, t = al[way.get(name[i], 0)] if len(al) > 1 else al[0]
-        w, kd = -1, 0
-        eng[i] = e
-        for j, d in pre[i]:
-            if fin[j] + d > t and not (eng[j] == e and j in free[i]):
-                t, w = fin[j] + d, j
-        if e >= 0:
-            j = prev[i] = last[e]
-            if j >= 0 and fin[j] >= t:
-                t, w, kd = fin[j], j, 1
-            if banks:
-                h = held[i] = [other[b] if bank[b][2] == e else bank[b] for b in banks]
-                for j, f, en in h:
-                    if f > t:
-                        t, w, kd = f, j, 2
-                for b, x in zip(banks, h):
-                    other[b], bank[b] = x, (i, t + hold, e)
-            last[e] = i
-        start[i], fin[i], why[i], kind[i] = t, t + ns, w, kd
-    end, final = max((fin[i] + s["lat"][i], i) for i in s["ends"])
-    if "base" in s:
-        end -= (1 + PAR["pull"]) * fin[s["base"]]
-    return end + PAR["pull"] * sum(fin) / n, start, key, why, kind, final, prev, held
-
-
-def improve(s, tau, way, pool, rounds, heat, seed):
-    x = [seed]
-
-    def rnd():
-        x[0] = (x[0] * 6364136223846793005 + 1442695040888963407) % (1 << 64)
-        return (x[0] >> 11) / float(1 << 53)
-    one = lambda c: c[int(rnd() * len(c))]
-    name, step, pre = s["name"], s["step"], s["pre"]
-    names = sorted(set(name) & pool)
-    both = sorted({name[i] for i, a in enumerate(s["alt"]) if len(a) > 1} & pool)
-    cur = replay(s, tau, way)
-    best = (cur[0], dict(tau), dict(way))
-    for n in range(rounds):
-        end, start, key, why, kind, i, prev, held = cur
-        path = []
-        if rnd() < PAR["any"]:
-            i = int(rnd() * len(name))
-        while i >= 0:
-            path.append(i)
-            i = why[i]
-        old, oldway, r = {}, {}, rnd()
-        if r < 0.2:
-            c = [name[i] for i in path if name[i] in both]
-            w = one(c if c and rnd() < 0.6 else both)
-            oldway[w] = way.get(w, 0)
-            way[w] = 1 - oldway[w]
-            if r < 0.1:
-                old[w] = tau[w]
-                tau[w] = key[name.index(w)] - step[name.index(w)] + (rnd() - 0.5) * 3000
-            if r < 0.05:
-                c = [u for u in both if way.get(u, 0) == way[w] and u != w and abs(tau[u] - tau[w]) < 3000]
-                if c:
-                    u = one(c)
-                    oldway[u] = way.get(u, 0)
-                    way[u] = 1 - oldway[u]
-        elif r < 0.3:
-            w = one(names)
-            old[w] = tau[w]
-            tau[w] += (1 if rnd() < 0.5 else -1) * math.exp(4 + 3.5 * rnd())
-        else:
-            c = [i for i in path if kind[i] and (name[i] in pool or name[why[i]] in pool)]
-            if not c:
-                continue
-            b = one(c)
-            a = why[b]
-            if rnd() < 0.5:
-                for _ in range(one((0, 0, 1, 2, 3))):
-                    a = prev[a] if prev[a] >= 0 else a
-                to, todo, seen = key[a] - 1 - 5 * rnd(), [b], {b}
-                while todo:
-                    for j, d in pre[todo.pop()]:
-                        if key[j] >= to and j not in seen:
-                            seen.add(j)
-                            todo.append(j)
-                if a in seen or len(seen) > 12 or any(name[i] not in pool for i in seen):
-                    continue
-                for m, i in enumerate(sorted(seen, key=lambda i: -key[i])):
-                    old.setdefault(name[i], tau[name[i]])
-                    tau[name[i]] = to - 0.01 * m - step[i]
-            elif name[a] in pool:
-                old[name[a]] = tau[name[a]]
-                tau[name[a]] = key[b] + one((1, 1, 100, 300, 800)) * (0.5 + rnd()) - step[a]
-        new = replay(s, tau, way)
-        if new[0] <= end or rnd() < math.exp((end - new[0]) / (heat * (1 - n / rounds) + 2)):
-            cur = new
-            if new[0] < best[0]:
-                best = (new[0], dict(tau), dict(way))
-        else:
-            tau.update(old)
-            way.update(oldway)
-    tau.update(best[1])
-    way.update(best[2])
-    return best[0]
-
-
-WINDOWS = [((-1, 0, 1), (-1, 0), 2.6, 120.0, 13), ((3, 4, 5), (4, 5), 14, 90.0, 6), ((-1, 0, 1, 2), (0, 1), 1.5, 30.0, 4),
-           ((1, 2, 3, 4), (2, 3), 1.5, 30.0, 6)]
-
-
-def ordered(rounds):
+def ordered():
     ops = plan()
     depend(ops)
-    tau, way = keys(ORDER)
-    s = part(ops, (-1, 0))
-    late = [0.0] * len(s["idx"])
-    for i in range(len(late) - 1, -1, -1):
-        late[i] += s["alt"][i][0][1]
-        for j, d in s["pre"][i]:
-            late[j] = max(late[j], late[i] + d)
-    for i, w in enumerate(s["name"]):
-        if w not in tau:
-            tau[w], way[w] = -0.2 * late[i] - (1e5 - i if "load" in w else 0.0), 1
-    for o in ops:
-        if o["id"] not in tau:
-            tau[o["id"]], way[o["id"]] = tau.get(o["id"][1:], 15000.0), way.get(o["id"][1:], 0)
-    ends = [improve(s, tau, way, {w for w in tau if w[0] == "p" and "load" not in w}, rounds[0], 100.0, 2)]
-    for o in ops:
-        w = "%d%s" % (o["step"] + 1, o["id"])
-        tau[w], way[w], o["id"] = tau[o["id"]], way[o["id"]], w
-        if o["step"] == NS - 1 and w[4] in "abgh" and w[5] in "14" and PAR["lag"]:
-            tau[w] = tau[w[1:5] + "0" + w[6:]] + PAR["lag"]
-        if o["step"] == 0:
-            e, u = w[1:].split(".")
-            if u[0] == "x":
-                m, j = [int(x) for x in u[1:].split("_")]
-                tau[w], way[w] = -4000.0 + 400 * m + (900 if e == "t" else 1300 * j), int(m % 4 != 1)
-            elif u[0] in "abghn" and u[1] == "0":
-                tau[w] -= PAR["ahead"]
-            elif u in ("r4", "c0"):
-                tau[w] = 0.0
-    for steps, mine, n, heat, seed in WINDOWS:
-        pool = {o["id"] for o in ops if o["step"] in mine and "load" not in o["id"]
-                and (o["step"] > mine[0] or o["step"] < 0 or o["id"].split(".")[1][0] in "nslidjku")}
-        s = rest(part(ops, steps), tau, way, pool)
-        for w, x in zip(s["name"], replay(s, tau, way)[2]):
-            tau[w] = x - STEP * (int(w[0]) - 1)
-        ends.append(improve(s, tau, way, pool, int(n * rounds[1]), heat, seed))
-        for w, x in zip(s["name"], replay(s, tau, way)[2]):
-            tau[w] = x - STEP * (int(w[0]) - 1)
-    s = part(ops, range(-1, NS))
-    ends.append(improve(s, tau, way, {w for w in tau if "load" not in w}, rounds[2], 15.0, 4))
-    end, start, key, why, kind, final, prev, held = replay(s, tau, way)
-    for i, o in enumerate(ops):
-        if "alt" in o:
-            o["eng"], o["kind"], o["args"], o["ns"] = o["alt"][way.get(o["id"], 0)]
-        o["t0"] = start[i]
-    for i, o in enumerate(ops):
-        o["soft"] |= {j for j in o["dep"] if ops[j]["eng"] == o["eng"] and unread(ops, i, j)}
-        o["dep"] |= {j for j, f, e in held[i] if j >= 0}
-    return ops, sorted(range(len(ops)), key=lambda i: key[i]), ends, tau, way
+    at = {o["id"]: i for i, o in enumerate(ops)}
+    order = [at[w.strip("!")] for w in ORDER.split()]
+    assert sorted(order) == list(range(len(ops)))
+    last, other, done = {}, {}, set()
+    for n, (i, w) in enumerate(zip(order, ORDER.split())):
+        o = ops[i]
+        assert o["dep"] <= done
+        done.add(i)
+        o["pos"] = n
+        if w[-1] == "!":
+            o["eng"], o["kind"], o["args"] = "s", "act", o["alt"]
+        for b in o["banks"]:
+            if b in last and ops[last[b]]["eng"] != o["eng"]:
+                other[b] = last[b]
+            if b in other:
+                o["dep"].add(other[b])
+            last[b] = i
+    return ops, order
 
 
 _CACHE = {}
@@ -1071,7 +534,7 @@ def rank_program(g, core, T, topo):
     if rank is None:
         return
     if not _CACHE:
-        _CACHE["ops"], _CACHE["order"] = ordered(PAR["rounds"])[:2]
+        _CACHE["ops"], _CACHE["order"] = ordered()
     ops, order = _CACHE["ops"], _CACHE["order"]
     cores = list(T.cores)
     n = len(cores)
@@ -1084,8 +547,7 @@ def rank_program(g, core, T, topo):
             return ap(a[1]).indirect(ap(a[2]))
         if a[0] in ("in", "out"):
             return T[a[1]][:]
-        rows = slice(a[1], a[2]) if a[6] == 1 else slice(a[1], a[2], a[6])
-        return T[a[0]][rows, slice(a[3], a[4]) if a[5] == 1 else slice(a[3], a[4], a[5])]
+        return T[a[0]][slice(a[1], a[2]), slice(a[3], a[4]) if a[5] == 1 else slice(a[3], a[4], a[5])]
 
     def maskof(es):
         return sum(1 << e for e in es)
@@ -1121,7 +583,7 @@ def rank_program(g, core, T, topo):
             s, v = mark[j]
             if v > want.get(s, (0, 0))[0]:
                 want[s] = (v, j)
-        for s, (v, j) in sorted(want.items(), key=lambda x: -ops[x[1][1]]["t0"]):
+        for s, (v, j) in sorted(want.items(), key=lambda x: -ops[x[1][1]]["pos"]):
             if kn.get(s, 0) < v:
                 q.wait_ge(T.sem[s], v)
                 kn[s] = v
@@ -1171,10 +633,10 @@ def rank_program(g, core, T, topo):
         elif k == "act":
             if a[0][0] == "@":
                 r = q.activation(ap(a[0]), ap(a[1]), a[2])
+            elif len(a) > 5:
+                r = q.activation(ap(a[0]), ap(a[1]), a[2], bias=ap(a[3]), scale=ap(a[4]), accum_out=ap(a[5]))
             else:
                 r = q.activation(ap(a[0]), ap(a[1]), a[2], bias=ap(a[3]), scale=ap(a[4]))
-        elif k == "sel":
-            r = q.affine_select(ap(a[0]), ap(a[1]), [[0, width(a[0])]], ALU.is_ge, 0.0, 0, 0)
         elif k == "iota":
             if SCRATCH[a[0][0]][2] == I32:
                 r = q.iota(ap(a[0]), a[1], a[2], a[3])

@@ -3,7 +3,7 @@ from concourse.mybir import AluOpType as ALU, AxisListType, ActivationFunctionTy
 
 NS = 6
 F32, BF, F16, I32, U16 = "float32", "bfloat16", "float16", "int32", "uint16"
-DEAD = 256
+DEAD = 288
 TW = 296
 ZR = 256
 BIG, LOWER = 32768.0, -16384.0
@@ -14,19 +14,20 @@ SB = {
     "NB": (4096, I32), "QT": (4112, BF), "LH": (16, F32), "SI": (256, I32), "UI": (1536, I32), "CI": (1536, I32),
     "S0F": (256, F32), "U8": (1536, BF), "CB": (1536, BF), "TH": (288, F32), "UB": (1576, F32), "UA": (32, F32),
     "PI": (1, I32), "PJ": (4, I32), "PF": (12, F32), "GQ": (144, F32), "IQ": (144, F32), "C16": (48, F32),
-    "IOT": (256, F32), "IOB": (256, F32), "TMP": (64, F32), "T1": (128, F32), "T2": (128, F32), "PK": (128, F32),
-    "EWB": (144, BF), "E0B": (144, BF), "EW16": (144, F16), "BO32": (144, F32), "BOB": (128, BF), "BO16": (128, F16),
+    "IOT": (256, F32), "IA": (32, F32), "TMP": (64, F32), "T1": (128, F32), "T2": (128, F32), "PK": (256, F32), "PKE": (2, F32),
+    "EWB": (144, BF), "E0B": (144, F16), "EW16": (144, F16), "BO32": (144, F32), "BOB": (128, BF), "BO16": (128, F16),
     "RM": (16, F32), "UH": (5 * 144, F16), "US": (5 * 128, F32), "I32W": (144, F32), "IBW": (144, BF), "IMW": (144, BF),
+    "IR16": (128, F16), "EWR": (128, F16),
     "I16F": (128, F16), "I296": (128, BF), "I592": (128, BF), "R16": (128, F16), "R4096": (128, BF), "DIF": (128, BF),
     "THR": (1, F32), "DG": (128, BF), "TBZ": (128, BF), "TBR": (128, BF), "RS48": (48, F32), "RSX": (1536, BF),
-    "CIL": (18, F16), "M16": (48, F32), "CWB": (16, BF), "G8": (128, BF), "G832": (128, F32), "E8": (144, BF),
-    "ONE": (TW, BF), "JC": (2, F32),
+    "CIL": (18, F16), "G8": (128, BF), "G832": (128, F32), "E8": (144, BF), "ONE": (DEAD, BF), "JC": (2, F32),
     "X": (4608, F16), "CMP": (4608, BF), "Y": (288, F32), "GE": (288, BF), "M": (288, F16), "SC": (320, F32), "LW": (20, U16),
-    "NK": (320, F16), "NKP": (288, F16), "NF": (TW, F32), "NA": (32, F32), "EQ": (6 * 320, BF), "OU": (288, U16),
-    "W": (3 * TW, F32), "WP": (256, F32), "WA": (32, F32), "WB": (32, F32), "HT": (TW, F32), "HC": (288, F16), "HR": (32, F32),
-    "FL": (768, BF), "FG": (48, BF), "DB": (16, BF), "SN": (48, BF), "E": (48, BF), "PO": (32, U16), "TT": (1584, F32),
-    "SM": (32, F32), "SL": (2, U16), "HS": (TW, BF), "H2": (2 * TW, BF), "CU": (TW, F16), "AL": (4, U16), "SV": (8, F32),
-    "SRB": (256, BF), "SB16": (16, BF), "SRC": (16, U16), "WL": (16, U16), "YW": (TW, F32), "YH": (TW, F32),
+    "NK": (320, F16), "NKP": (288, F16), "NF": (TW, F32), "EQ": (6 * 320, BF), "OU": (288, U16), "HR": (TW, F32), "WR": (TW, F32),
+    "W": (3 * TW, F32), "WP": (256, F32), "WA": (32, F32), "WB": (32, F32), "HT": (TW, F32), "HC": (288, F16),
+    "FL0": (384, BF), "FL1": (384, BF), "FG": (48, BF), "DB": (16, BF), "SN": (48, BF), "E": (48, BF), "M16": (48, BF),
+    "PO": (32, U16), "TT": (1584, F32), "IOB": (DEAD, F32), "CBH": (256, F16), "PKD": (256, F16), "SD": (256, F16),
+    "SM": (32, F32), "SL": (2, U16), "HS": (DEAD, BF), "H2": (2 * DEAD, BF), "CU": (DEAD, F16), "AL": (4, U16), "SV": (8, F32),
+    "SRB": (256, BF), "SRC": (16, U16), "WL": (16, U16), "YW": (TW, F32), "YH": (TW, F32),
     "SC_O": (NS * 8, BF), "SC_I": (NS * 24, BF), "SP_O": (NS * 64, F32), "SP_I": (NS * 64, F32),
 }
 SCRATCH = {k: ("sbuf", [128, v[0]], v[1]) for k, v in SB.items()}
@@ -39,13 +40,26 @@ SEMAPHORES = (["ev", "es", "et", "eg", "sent"] + ["d%d" % i for i in range(NDMA)
 
 PIECES = [(a, a + 32) for a in range(0, 192, 32)] + [(a, a + 16) for a in range(192, 288, 16)]
 SUMS, CUT = [(0, 64), (64, 128), (128, 224), (224, 288)], [32, 32, 48, 32]
-NEAR, HIST, LISTS = [(0, 128), (128, 192), (192, 288)], [(0, 128), (128, 224), (224, 256)], [(0, 64), (64, 256)]
-B = dict(p15=[(3, 0), (4, 0), (3, 64), (5, 288)], votes=[(4, 64), (3, 160), (4, 128), (5, 416)],
-         one=[(4, 224), (4, 288), (4, 352), (5, 192)], hn=[(6, 128), (7, 64), (5, 0)], of=[(6, 0), (7, 0), (5, 96)],
-         hb=[[(0, 0), (0, 128), (0, 256), (0, 384), (6, 320)], [(2, 192 + 64 * p) for p in range(5)], [(1, 96 * p) for p in range(5)]],
-         ht=(3, 256), htb=(5, 480), fl=(2, 0), rank=(2, 48), cnt=(2, 140), sb=(3, 224), l=(3, 240), rot=(5, 352), ha=(7, 320),
-         ofa=(6, 256))
-OPEN = (5, 6, 7)
+NEAR, HIST, LISTS = [(0, 128), (128, 192), (192, 288)], [(0, 128), (128, 224), (224, 288)], [(0, 64), (64, 256)]
+BANKS = ["hb00 hb01 hb02 hb03", "hb20 hb21 hb22 hb23 hb24", "fl rank col cnt hb10 hb11 hb12 hb13 hb14",
+         "p150 p152 votes1 sb l ht0 ht1", "p151 votes0 votes2 one0 one1 one2", "hn2 of2 one3 p153 rotw roth votes3",
+         "of0 hn0 ofa hb04 ht2 hw", "of1 hn1 ha"]
+
+
+def places():
+    wide = dict(fl=48, rank=34, cnt=2, sb=16, l=16, rotw=32, roth=32, hw=32, ha=160, ofa=32, col=16)
+    for names, pieces in ((("p15", "votes", "one"), SUMS), (("hn", "of"), NEAR), (("ht",), HIST)):
+        wide.update({n + str(i): b - a for n in names for i, (a, b) in enumerate(pieces)})
+    wide.update({"hb%d%d" % (i, p): b - a for i, (a, b) in enumerate(NEAR) for p in range(NS - 1)})
+    at = {}
+    for bank, names in enumerate(BANKS):
+        c = 0
+        for n in names.split():
+            at[n] = (bank, c, wide[n])
+            c += wide[n]
+        assert c <= 512
+    assert sorted(at) == sorted(wide)
+    return at
 
 
 def A(name, c0=0, c1=None, step=1, p1=128):
@@ -75,7 +89,7 @@ def landing(kind, t, src, d):
 
 
 def plan():
-    ops, now, tag = [], [-1], ["", {}]
+    ops, now, tag, B = [], [-1], ["", {}], places()
 
     def at(name):
         tag[0] = name
@@ -127,6 +141,10 @@ def plan():
             ts(out, in_, scale, ALU.mult, bias, ALU.add)
         ops[-1]["alt"] = (out, in_, ACT.Identity, bias, scale)
 
+    def scatter(win, off, in_):
+        cp(IND(win, off), in_)
+        ops[-1]["alt"] = (IND(win, off), in_, ACT.Silu, 0.0, 1.0)
+
     def iota(out, pat, base=0, ch=0):
         add("g", "iota", (out, pat, base, ch), [out], [])
 
@@ -134,9 +152,7 @@ def plan():
         iota(out, [[0, width(out)]], c)
 
     def mm(items, start=True, stop=True):
-        op = add("t", "mm", (items, start, stop), [o for o, l, r in items], [x for o, l, r in items for x in (l, r)])
-        if int(items[0][0][0][1]) in OPEN:
-            op["wr"].append(("grp" + items[0][0][0], 0, 128, 0, 1, 1, 1))
+        add("t", "mm", (items, start, stop), [o for o, l, r in items], [x for o, l, r in items for x in (l, r)])
 
     def dma(eng, out, in_):
         add(eng, "dma", (out, in_), [out] if out[0] != "out" else [], [in_] if in_[0] != "in" else [])
@@ -176,8 +192,8 @@ def plan():
     iota(A("GQ", 16, 144), [[16, 8], [0, 16]])
     iota(A("IOT"), [[1, 256]])
     iota(A("C16"), [[0, 3], [1, 16]])
-    iota(A("M16", 0, 32), [[704, 2], [16, 16]], -144)
-    iota(A("M16", 32, 48), [[16, 16]], -144)
+    iota(A("T2", 0, 16), [[16, 16]], -144)
+    iota(A("M16", 16, 32), [[16, 16]], 560)
     mset(A("GQ", 0, 16), 112.0)
     move(IQ, A("IOT", 0, 128))
     move(A("IQ", 0, 16), A("IOT", 112, 128))
@@ -185,6 +201,10 @@ def plan():
     ts(col("PJ", 1), A("PI"), 15, ALU.bitwise_and)
     cp(P_, A("PI"))
     cp(A("PF", 1, 3), A("PJ", 0, 2))
+    at("cw")
+    move(A("M16", 0, 16), A("T2", 0, 16), PR)
+    move(A("IA"), A("IOT", 0, 32), 320.0)
+    at("c")
     ts(A("BO32"), A("GQ"), PG, ALU.is_equal)
     move(A("BOB"), BO)
     ts(A("RM"), A("IOT", 0, 16), PR, ALU.is_equal)
@@ -207,8 +227,10 @@ def plan():
     ts(A("TMP", 32, 48), c16, col("PF", 7), ALU.is_equal, BIG, ALU.mult)
     tt(A("TMP", 48, 64), A("TMP", 0, 16), A("TMP", 16, 32), ALU.add)
     tt(A("PK", 0, 16), A("TMP", 48, 64), A("TMP", 32, 48), ALU.add)
-    for n in (16, 32, 64):
+    at("pk")
+    for n in (16, 32, 64, 128):
         move(A("PK", n, 2 * n), A("PK", 0, n))
+    at("c")
     ts(LWB, col("RM", 0), -BIG, ALU.mult, 2048.0 - LOWER, ALU.add)
     ts(SLB, col("RM", 0), -BIG, ALU.mult, 0.25 - 64.0 - LOWER, ALU.add)
     ts(HB, PR, 6.5, ALU.is_lt, 2049.0, ALU.mult)
@@ -233,10 +255,10 @@ def plan():
     tt(A("TBZ"), A("GE", 128, 256), A("Y", 0, 128), ALU.add)
     ts(A("DG"), IW, PR, ALU.mult, -1.0, ALU.mult)
     tt(A("TBR"), A("GE", 128, 256), A("DG"), ALU.add)
-    move(A("CWB"), A("M16", 0, 16), PR)
-    move(A("CIL", 0, 16), A("CWB"), 704.0)
+    move(A("M16", 32, 48), A("M16", 0, 16))
+    move(A("CIL", 0, 16), A("M16", 0, 16), 704.0)
     mset(A("CIL", 16, 18), 0.0)
-    act(A("IOB"), A("IOT"), ACT.Silu, 64.0)
+    act(A("IOB", 0, 256), A("IOT"), ACT.Silu, 64.0)
     mset(A("QT", 4096, 4112), 0.0)
     for j in range(256, 888, TW):
         mset(A("W", j, j + 40), 0.0)
@@ -250,8 +272,17 @@ def plan():
     ts(A("JC"), A("IOT", 0, 32, 16), PR, ALU.add, -1.0, ALU.mult)
     ts(A("JC"), A("JC"), -0.5, ALU.add)
     mset(A("ONE"), 1.0)
-    mset(A("HS", 256, 264), -1.0)
-    mset(A("HS", 264, TW), 1.0)
+    at("e")
+    move(A("PKD"), A("PK"), scale=1.0 / 32)
+    move(col("PKE", 0), col("PK", 15), scale=1.0 / 32)
+    ts(col("PKE", 1), col("RM", 0), -BIG / 32, ALU.mult, 144.25 - LOWER / 32, ALU.add)
+    at("d2")
+    mset(A("HS", 256, DEAD), 1.0)
+    at("z")
+    move(A("IR16"), A("I32W", 0, 128))
+    ts(A("EWR"), A("IQ", 0, 128), PG, ALU.subtract, float(NS), ALU.is_equal)
+    mset(A("HR", DEAD, TW), -1.0)
+    mset(A("WR", DEAD, TW), 0.0)
     at("flat")
     iota(A("RSX"), [[0, 96], [8192, 16]], int(LOW))
     fill(A("TH"), 9)
@@ -296,23 +327,22 @@ def plan():
             ts(A("OU", out, out + b - a), K(of, 0, b - a), 2048.0, ALU.add, 4096.0, ALU.min)
             move(A("NKP", out, out + b - a), K(of, 0, b - a))
         else:
-            move(A("NF", a, min(b, 256)), K(of, 0, min(b, 256) - a))
-            if b > 256:
-                move(A("NA"), K(of, 256 - a, b - a))
-                cp(IND(A("NF"), al(t - 1)), A("NA"))
+            move(A("NF", a, b), K(of, 0, b - a))
 
     def own(t):
         for h, (a, b) in enumerate(NEAR):
             b = b if t > 0 else min(b, 256)
-            hb = lambda p: K(B["hb"][h][p], 0, b - a)
+            if a == b:
+                continue
+            hb = lambda p: K(B["hb%d%d" % (h, p)], 0, b - a)
             at("hb%d" % h)
             for p in range(t + 1):
                 mm([(hb(p), uh(p), A("HC", a, b))])
             at("n%d" % h)
-            hn = K(B["hn"][h], 0, b - a) if t >= 0 else K(0, a, b)
+            hn = K(B["hn%d" % h], 0, b - a) if t >= 0 else K(0, a, b)
             if t >= 0:
                 mm([(hn, A("BO16"), A("M", a, b))])
-            neighbours(t, a, b, lambda p: hn if p == t + 1 else hb(p), B["of"][h], a if t < 0 else None)
+            neighbours(t, a, b, lambda p: hn if p == t + 1 else hb(p), B["of%d" % h], a if t < 0 else None)
 
     own(-1)
 
@@ -326,17 +356,21 @@ def plan():
         for i, (a, b) in enumerate(SUMS):
             b = b if t else min(b, 256)
             c = min(b, 256)
-            p15, votes, one = B["p15"][i], K(B["votes"][i], 0, b - a), K(B["one"][i], 0, b - a)
+            if a == b:
+                continue
+            p15, votes, one = B["p15%d" % i], K(B["votes%d" % i], 0, b - a), K(B["one%d" % i], 0, b - a)
             at("a%d" % i)
             mm([(K(p15, 0, b - a), A("I16F"), A("X", 16 * a + j, 16 * b, 16)) for j in range(16)])
             at("a%dw" % i)
-            tt(A("W", a, c), A("WP", a, c), K(p15, 0, c - a), ALU.mult)
-            tt(A("Y", a, c), A("UB", 256 * t + a, 256 * t + c), K(p15, 0, c - a), ALU.mult)
+            if a < c:
+                tt(A("W", a, c), A("WP", a, c), K(p15, 0, c - a), ALU.mult)
+                tt(A("Y", a, c), A("UB", 256 * t + a, 256 * t + c), K(p15, 0, c - a), ALU.mult)
             if c < b:
                 at("b")
                 tt(A("WB"), A("WA"), K(p15, c - a, b - a), ALU.mult)
-                cp(IND(A("W", 0, TW), al(t - 1)), A("WB"))
+                cp(IND(A("W", 0, DEAD), al(t - 1)), A("WB"))
                 tt(A("Y", c, b), A("UA"), K(p15, c - a, b - a), ALU.mult)
+                move(A("W", 256, DEAD), A("WB"))
             at("a%dz" % i)
             ts(A("X", 16 * a, 16 * b, 16), A("Y", a, b), -HALF, ALU.add, 2.0 ** 23 + 2048, ALU.add)
             at("a%dc" % i)
@@ -349,16 +383,18 @@ def plan():
             act(A("GE", a, b), votes, ACT.Sign, A("THR"))
             mm([(one, A("DIF"), A("GE", a, b))])
             tt(A("M", a, b), A("NKP", a, b), one, ALU.mult)
-        at("w")
-        WN = A("W", 0, 256)
-        ts(A("FL", 0, 256), WN, col("LH", t), ALU.is_lt)
-        ts(A("FL", 256, 512), WN, col("LH", 8 + t), ALU.is_gt)
-        ts(A("FL", 512, 768), WN, 0.0, ALU.is_equal)
-        ops[-1]["alt"] = (A("FL", 512, 768), WN, ACT.Relu, 1.0, -2.0 ** 85)
-        move(A("W", TW, TW + 256), WN, scale=2.0)
-        move(A("W", 2 * TW, 2 * TW + 256), WN, scale=0.5)
         fl, rk = B["fl"], B["rank"]
-        mm([(K(fl, 0, 48), sel(r), A("FL", r, 768, 16)) for r in range(16)])
+        for h in range(2):
+            at("w" + "eo"[h])
+            ts(A("FL%d" % h, 0, 128), A("W", h, 256, 2), col("LH", t), ALU.is_lt)
+            ts(A("FL%d" % h, 128, 256), A("W", h, 256, 2), col("LH", 8 + t), ALU.is_gt)
+            ts(A("FL%d" % h, 256, 384), A("W", h, 256, 2), 0.0, ALU.is_equal)
+            ops[-1]["alt"] = (A("FL%d" % h, 256, 384), A("W", h, 256, 2), ACT.Relu, 1.0, -2.0 ** 85)
+            mm([(K(fl, 0, 48), sel(2 * r + h), A("FL%d" % h, r, 384, 8)) for r in range(8)], h == 0, h == 1)
+        at("wt")
+        c = DEAD if t else 256
+        move(A("W", TW, TW + c), A("W", 0, c), scale=2.0)
+        move(A("W", 2 * TW, 2 * TW + c), A("W", 0, c), scale=0.5)
         at("r")
         tt(A("FG"), K(fl, 0, 48), A("TH", 48 * t, 48 * t + 48), ALU.is_ge)
         HIGH, HOLES = A("FG", 16, 32), (0, 32)
@@ -376,26 +412,33 @@ def plan():
         mm([x for j in HOLES for x in ((k, A("BOB"), A("SN", j, j + 16)), (k, A("TBZ"), A("FG", j, j + 16)))])
         ts(A("PO", 0, 16), k, K(rk, 32, 33), ALU.subtract, 255.0, ALU.add)
         at("r")
-        fill(A("TT", ZR, ZR + 256), 208 + 112)
-        fill(A("TT", ZR + 256, ZR + 288), 64 + DEAD)
+        fill(A("TT", ZR, ZR + 288), 64 + DEAD)
         at("p")
-        inverse = IND(A("TT", ZR, ZR + 1328), A("PO", 16, 32))
-        cp(inverse, A("IOB"))
-        ops[-1]["alt"] = (inverse, A("IOB"), ACT.Silu, 0.0, 1.0)
+        scatter(A("TT", ZR, ZR + 1328), A("PO", 16, 32), A("IOB", 0, 256))
         scan(A("SM"), A("TT", ZR + 256, ZR + 288), A("PK", 0, 32), ALU.min, ALU.add, BIG)
-        ts(A("SL"), A("SM", 15, 32, 16), SLB, ALU.add)
+        if last:
+            mm([(K(B["hw"], 0, 2), A("I32W", 0, 128), A("SM", 15, 32, 16))])
+        ts(A("SL"), K(B["hw"], 0, 2) if last else A("SM", 15, 32, 16), SLB, ALU.add)
         at("u")
-        for a, b in HIST + [(256, 288)] * (t > 0):
-            k = K(B["ht"], a, b) if a < 256 else K(B["htb"], 0, 32)
+        for i, (a, b) in enumerate(HIST):
+            b = b if t else min(b, 256)
+            if a == b:
+                continue
+            k = K(B["ht%d" % i], 0, b - a)
             mm([(k, A("I16F"), A("HC", a, b)), (k, A("EW16", 14 - t, 142 - t), A("M", a, b))])
-            move(A("HT", a, b) if a < 256 else A("HR"), k)
-        if t:
-            cp(IND(A("HT"), al(t - 1)), A("HR"))
+            move(A("HT", a, b), k)
+        if last:
+            at("z")
+            for a, b in HIST:
+                mm([(K(0, a, b), A("IR16"), A("HC", a, b)), (K(0, a, b), A("EWR"), A("M", a, b))])
+                ts(A("HR", a, b), K(0, a, b), HB, ALU.add, -1.0, ALU.max)
+            mm([(K(1, 0, DEAD), A("I32W", 0, 128), A("W", 0, DEAD))])
+            move(A("WR", 0, DEAD), K(1, 0, DEAD), scale=0.5)
         at("p")
         po = 64 * t
-        move(A("SP_O", po, po + 32), IND(A("W", 0, TW), A("SL")), scale=0.5 if last else 2.0 ** -12)
+        move(A("SP_O", po, po + 32), IND(A("WR") if last else A("W", 0, TW), A("SL")), scale=1.0 if last else 2.0 ** -12)
         at("q")
-        move(A("SP_O", po + 32, po + 64), IND(A("HT"), A("SL")))
+        move(A("SP_O", po + 32, po + 64), IND(A("HR" if last else "HT"), A("SL")))
         for kind in ("p" if last else "pc" if t else "cp"):
             at("q" if kind == "p" else "c")
             if kind == "c":
@@ -407,47 +450,58 @@ def plan():
             own(t)
         at("s")
         tt(A("DB"), K(fl, 0, 16), A("TH", 48 * t + 32, 48 * t + 48), ALU.is_ge)
-        move(A("SRB"), IND(A("TT", 0, ZR + 256), A("PO", 0, 16)), -208.0)
         sb = K(B["sb"], 0, 16)
-        mm([(sb, IB, A("CWB"))] + [x for j in HOLES for x in ((sb, A("DG"), A("FG", j, j + 16)), (sb, IM1, A("E", j, j + 16)))]
-           + [(sb, sel0(r), A("SRB", r, 256, 16)) for r in range(16)])
-        ts(SRC, sb, 144.25, ALU.add)
-        move(A("SB16"), sb)
+        mm([(sb, IB, A("M16", 0, 16))] + [(sb, IM1, A("E", j, j + 16)) for j in HOLES])
+        at("sp")
+        move(A("PKD", 15, 256, 16), sb, col("PKE", 0))
+        for i, (a, b) in enumerate(LISTS):
+            at("s%d" % i)
+            move(A("SRB", a, b), IND(A("TT", 0, ZR + 256), A("PO", a // 16, b // 16)), -208.0)
+            scan(A("SD", a, b), A("SRB", a, b), A("PKD", a, b), ALU.min, ALU.add, BIG / 32)
+            ts(A("SRC", a // 16, b // 16), A("SD", a + 15, b, 16), col("PKE", 1), ALU.add)
+        at("sw")
         k = K(B["l"], 0, 16)
-        mm([(k, IB, A("SB16")), (k, A("I592"), A("FG", 0, 16)), (k, A("I592"), HIGH), (k, A("I296"), A("FG", 32, 48)), (k, A("I296"), A("DB"))])
-        ts(WL, k, 144.25, ALU.add)
+        mm([(k, A("I592"), A("FG", 0, 16)), (k, A("I592"), HIGH), (k, A("I296"), A("FG", 32, 48)), (k, A("I296"), A("DB")),
+            (k, A("I16F"), A("SD", 15, 256, 16))])
+        ts(WL, k, col("PKE", 1), ALU.add)
         at("v")
-        act(A("HS", 0, 256), A("SRB"), ACT.Sign, -111.5)
+        act(A("HS", 0, 256), A("SRB"), ACT.Sign, 144.5 - DEAD)
         scan(A("CU"), A("ONE"), A("HS"), ALU.add, ALU.add)
         for j in range(2):
-            act(A("H2", TW * j, TW * j + TW), A("CU"), ACT.Sign, col("JC", j), 0.5, col("SV", 6 + j))
-        ts(al(t), A("SV", 6, 8), -0.5, ALU.mult, TW / 2 + 0.25, ALU.add)
+            act(A("H2", DEAD * j, DEAD * j + DEAD), A("CU"), ACT.Sign, col("JC", j), 0.5, col("SV", 6 + j))
+        ts(al(t), A("SV", 6, 8), -0.5, ALU.mult, DEAD / 2 + 0.25, ALU.add)
         hi = A("SP_I", po + 32, po + 64)
         if not last:
-            at("l")
-            for a, b in LISTS:
-                move(A("NKP", a, b), IND(A("NF"), A("SRC", a // 16, b // 16)))
-            at("o")
-            for a, b in LISTS:
-                ts(A("OU", a, b), A("NKP", a, b), 2048.0, ALU.add, 4096.0, ALU.min)
+            at("g")
+            iota(A("IOB"), [[1, DEAD]], 64)
+            scatter(A("IOB"), al(t), A("IA"))
+            add("g", "gcp", (A("CBH"), A("IOB", 0, 256)), [A("CBH")], [A("IOB", 0, 256)])
+            k = K(B["col"], 0, 16)
+            mm([(k, sel0(r), A("CBH", r, 256, 16)) for r in range(16)])
+            for j in HOLES:
+                move(A("M16", j, j + 16), k, -208.0)
+            for i, (a, b) in enumerate(LISTS):
+                at("l%d" % i)
+                ts(A("OU", a, b), IND(A("NF"), A("SRC", a // 16, b // 16)), 2048.0, ALU.add, 4096.0, ALU.min)
+                ts(A("NKP", a, b), A("OU", a, b), -2048.0, ALU.add)
             at("f")
             move(A("WP"), IND(A("W"), WL), scale=2.0 ** -11)
             move(A("HC", 0, 256), IND(A("HT"), SRC))
             move(A("UA"), IND(A("UB", 256 * t + 256, 256 * t + 256 + TW), al(t)))
             at("i")
-            mm([(ha(t + 1), A("US", 128 * t, 128 * t + 128), hi)])
-            mm([(K(B["rot"], 32, 64), A("I32W", 0, 128), hi)])
-            move(A("HC", 256, 288), K(B["rot"], 32, 64))
-            mm([(ha(p), uh(p), A("HC", 256, 288)) for p in range(t + 1)], "each")
+            mm([(K(B["hw"], 0, 32), A("US", 128 * t, 128 * t + 128), hi)])
+            mm([(K(B["roth"], 0, 32), A("I32W", 0, 128), hi)])
+            move(A("HC", 256, 288), K(B["roth"], 0, 32))
+            mm([(ha(p), uh(p), A("HC", 256, 288)) for p in range(t + 1)])
             at("in")
-            neighbours(t, 288, 320, ha, B["ofa"], 256)
+            neighbours(t, 288, 320, lambda p: K(B["hw"], 0, 32) if p == t + 1 else ha(p), B["ofa"], 256)
+            at("j")
+            mm([(K(B["rotw"], 0, 32), A("I32W", 0, 128), A("SP_I", po, po + 32))])
+            move(A("WA"), K(B["rotw"], 0, 32))
         else:
             at("y")
             ts(A("YH", 0, 256), IND(A("HT"), SRC), HB, ALU.add, -1.0, ALU.max)
             move(A("YW", 0, 256), IND(A("W"), WL))
-        at("j")
-        mm([(K(B["rot"], 0, 32), A("I32W", 0, 128), A("SP_I", po, po + 32))])
-        move(A("WA"), K(B["rot"], 0, 32))
         if not last:
             at("k")
             cn = B["cnt"]
@@ -460,10 +514,9 @@ def plan():
                 ts(col("SV", 1), K(cn, 1, 2), 0.0, ALU.max, 32.0, ALU.min)
                 ts(col("SC_O", 8 * t + 9), col("SV", 1), DD, ALU.subtract, 0.0, ALU.min)
         else:
-            mm([(ha(0), A("I32W", 0, 128), hi)])
-            ts(A("HR"), ha(0), HB, ALU.add, -1.0, ALU.max)
-            cp(IND(A("YW"), al(t)), A("WA"))
-            cp(IND(A("YH"), al(t)), A("HR"))
+            at("j")
+            cp(IND(A("YW"), al(t)), A("SP_I", po, po + 32))
+            cp(IND(A("YH"), al(t)), hi)
             dma("s", ("out", "yw"), A("YW", 0, 256))
             dma("y", ("out", "yh"), A("YH", 0, 256))
     return ops
@@ -493,13 +546,13 @@ def depend(ops):
 
 
 ORDER = """
-0Yload0 0Yload1 0Yload2 0load0 0Yload3 0Yload4 0Sload0 0Sload1 0Sload2 0Gc0 0c61 0Gc3 0c73 0c3 0Gc2 0c4 0c5 0c0 0c6 0c40 0c60 0c26 0c25 0c27 0Gc1 0c1! 0c9 0c28 0c62 0c29 0Gc4 0c65 0c35 0c30 0Gflat1 0c16 0c44 0c41 0c19! 0c31 0c45 0c39 0s0! 0c32 0c52 0Gflat0 0c46! 0c33 0c43 0c42! 0Ts0 0c7 0c2! 0c34! 0d4 0u13! 0u14 0c36 0u12! 0n00 0n10 0n20 0c47 0s2 0u0! 0c51 0c10 0Tu6 0c48! 0c66 0s4 0u8! 0c17 0c13! 0c53 0u2! 0n21 0Tu0 0n01 0u4 0u10! 0Tu1 0u16 0u6! 0c8 1Gr0 0d2 0Sc0 0n11 0c56 0d0 0s5 0c58 0d3 0Gc5 0u26 0u15 0Gflat2 0c57 0u1 0c14 1Gr1 0s1 0Tu2 0u21 0u3 0d1 0Tu3 0u19! 0n12 0c59! 0n22! 0c54! 0u5! 0n02 0c15! 0c21! 0n1e0 0u18 0n2e0 0n0e0 0Tn10 0Tn20 0c37 0Tn1e0 0Tn2e0 0c20 0c68 0Tn00 0Tn0e0 0c22! 0c64 0c18! 0Tu4 0c38 0u22 1Thb00 0c11! 1Thb20 1Thb10 0u25 0c63 0n2o0 0n2o1 0c69 0n0o1! 0c12! 0u23 0c70 0c55 0c24! 0c49! 0u17 0n0o0 0c23 0n1o1 0n1o0 0c50 0c67! 0u7! 0Tu5 0u20! 0c72 0u9! 0u24!
-1x70 1x60! 1x50! 1x40 1x10 1x00! 1x30 1Ta20 1x20! 1Ta00 1x80 1x90! 1Ta10 0s3 0c71! 1a0w1 1a2w1 1Ta30 1a0w0 1a0z0 1a1w1 1a2w0 1a1w0 1a0s0 1a3w0 0u11! 1w2! 1w0 1w1 1w3! 1a3w1 1a1z0 1a0c0 1Tw0 1w4! 1a1c0 1a1s0 1Ta0c0 1r0 1s0 1a2z0 1r2 1Ta1c0 1r1 1a2s0 1Sa0c0 1Tr0 1a2c0 1Ta0c1 1Sa1c0 1a3z0 1r3 1Ta1c1 1r4 1Ta2c0 1a3c0 1p0! 1Gc0 1Ta3c0 1a1c1 1a0c1 1Sa2c0 1Tn00 1p1 1Th0 1Sa3c0 1n00 1Ta2c1 1h0 1Ta3c1 1Tu0 1a2c1 1s1! 1a3c1 1n01 1p2 1Tu1 1Tu2 1n02 1Tn10 1Tn20 1u2! 1p3 1u1! 1n10 1u0! 1n20 1Tn01 1n0e1 1Sv0 1n11 1n21 1Ts0 1q0 1n12! 1n22 1n0e0 1n1e1 1n1e0 1Gq0 1n2e0 1n2e1 1Tn0e0 1Xc0 1v0 1Tn0e1 1s2 1Tn11 1Tn1e0 1Tn1e1 1s3 1Tn21 1Tn2e0 1Tn2e1 1n0o0 1Sv1 1n1o0 1Ts1 1n2o0 1l0! 1l1 1Sv2 2Gr0 1o0 1Xq0 1s4 1o1
-2x00! 2x10 2Gr1 2x60! 2x70 2Ta00 2x20 2x30! 2a0w1 2x40! 2x50 2Ta10 1Ti0 1Ti1 1f0! 2a0z0 2a1w1 1in0 2Ta20 2a1z0 2a0s0 1i0! 1in1 2a0c0 1in2! 2a1s0 1Ti2 2x80! 1Tj0 1Tk1 1Tk0 1ine0 1ine1 2a2w1 1Tin0 2a1c0 2x90! 1Tine0 1Tine1 2Ta0c0 1v1 1ino0 2a0w0 2a2z0 1j0! 1f2! 2x110 2Ta1c0 2x100! 2a1w0 2a2s0 2a2c0 2Sa0c0 2Ta30 2Sa1c0 1f1! 2Ta0c1 2a2w0 2Ta1c1 1ino1! 1k0 1k2 2Ta2c0 2a3w0 2b0 1k1! 2a3w1 2b2 2b1 2a3z0 2w0 2w2! 2Thb11 2Thb10 2Thb21 2Thb20 2Thb00 2Thb01 2w3! 2a1c1 2a0c1 2w1 2Sa2c0 2Tu0 2a3c0 2w4! 2Tn00 2Tw0 2a3s0 2u0! 2n00 1k3 2Ta2c1 2Ta3c0 2n01 2r0 2a2c1 2n02! 2r1 2r2 2Tn10 2Tu1 2Sa3c0 2n0e0 2Tr0 2n10 2u1 2Ta3c1 2n0e2 2Tn01 2Tn0e0 2r3 2a3c1 2n11 2p0! 2Tu3 2n12 2Tn20 2Th0 2n0e1 2Tu2 2n20 2Tn11 2u3 2n1e2 2Tn0e1 2n1e1 2Tn0e2 2n21 2n1e0 2u2 2h0 2n22 2Tn1e0 2Tn1e1 2Tn1e2 2p1 2s1! 2u4 2p2 3Gr1 2n2e0 2n2e1 2q0! 2p3 2Tn21 2n2e2 2Tn2e0 2Sv0 2Tn2e1 2s0 2r4 2Gq0 2Tn2e2 2n0o0! 2Ts0 2v0 2n2o0! 2n2o1! 2n1o0 2Sv1 2n2o2 2Sv2 2s2 2s3 2Gc0 2l0 2l1! 2Ts1 2Xq0 2o0 2s4 2o1
-3x10! 3x00 3x30! 3x20 3Gr0 3Ta00 2Xc0 2f0! 3x40 3Ta10 3x60! 2Ti0 2Ti1 2v1 3x70! 3a0w1 2in0 3a0z0 2i0 2in1 3a1w1 3x50! 2Ti2 2Tj0 2in2 3a1z0 2Tin0 2ine0 2ine1 2ine2 2j0 2Tine0 3a0s0 2Tine1 2Tine2 3x90! 3a0c0 3Ta20 2ino0 3a1w0 3x80! 3a1s0 3x110 3x100! 3Ta0c0 3a2w1 3a2w0 3a0w0 2f2! 3a2z0 2f1! 3a1c0 3Ta30 3a2s0 3Sa0c0 2Tk0 3a2c0 3Ta0c1 3Ta1c0 3a3w0 3b0 2k0 3b1 3Ta2c0 2k1! 3a3w1 3b2 3Sa1c0 3w0 3w2! 3w1 3w4! 3Ta1c1 2Tk1 3Thb11 3Thb22 3a3z0 3w3! 3Thb00 3Thb12 3Thb10 3a1c1 3Tw0 3a0c1 3a3s0 3Sa2c0 3a3c0 3Tn00 3Ta2c1 3Tu0 3r0 3Ta3c0 2k2 2ino1! 3a2c1 3r1 3u0! 3r2 3n00 3Tn10 3Tr0 3n01 3Sa3c0 3Thb01 3n10 3Thb21 2k3 3n02! 3r3 3Ta3c1 3Thb20 3n11 3Th0 3p0! 3a3c1 3n12 3n0e3 3Tu3 3Tn20 3n0e0 3Tu1 3Tu2 3h0 3Thb02 3n20 3Tn01 3n1e0 3Tn0e0 3n1e1 3u2 3n21 3Tn11 3n0e1 3Tn1e0 3Tn1e1 3u3! 3u1 3n22! 3n0e2 3Tn0e1 3p1 3s1! 3u4 3Tn0e2 3p2 4Gr1 3Tn0e3 3n2e0 3n2e1 3p3 3q0! 3Tn21 3n1e3 3Tn2e0 3n2e2 3Tn2e1 3Sv0 3n1e2 3n2e3 3Gq0 3r4 3Tn2e2 3s0 3Tn1e2 3Tn1e3 3Tn2e3 3Ts0 3v0 3n0o0 3n2o0! 3n1o0 3Sv1 3n2o1 3Sv2 3n2o2 3Gc0 3s2 3s3 3Xq0 3l0 3l1! 3Ts1 3o0 3s4 3o1
-4x00! 4x10 4x30! 4Gr0 4x20 3Xc0 4Ta00 4x70! 4x50 4x60! 3Ti0 3Ti1 4Ta10 3in0 4x40! 4a0w1 3i0 3in1 4a0z0 3Ti2 3in2 3Tj0 3v1 4a1w1 3Tin0 3ine0 3ine1 4x80! 3ine2 3ine3 3Tine0 3j0 3Tine1 4a1z0 3Tine2 4a0s0 3Tine3 4Ta20 4x90! 4a1s0 3ino0 4a0c0 3f0! 4x110 4Ta0c0 4x100! 4a2w1 4a1c0 4a2z0 3f2! 4a0w0 3f1! 4a2w0 4Ta30 4a1w0 4a2s0 3ino1! 4Sa0c0 4a2c0 3Tk0 4Ta0c1 4Ta1c0 4a3w0 4b0 3k0 4a3w1 4b2 4b1 3k1! 4Ta2c0 4a3z0 4Sa1c0 4w0 4w2! 4w1 4w4! 4Ta1c1 4a3c0 4Thb11 3Tk1 4Thb12 4Thb23 4Tw0 4a0c1 4a1c1 4a3s0 4Sa2c0 4w3! 4Thb03 4Tn00 4Ta2c1 4Ta3c0 4r0 3k2 4a2c1 4r1 4r2 4n00 4Tu0 4Tn10 4Tr0 4Thb01 4n01 4Thb00 4Sa3c0 4Ta3c1 4n10 3k3 4n02! 4Thb02 4r3 4u0 4a3c1 4Thb13 4n11 4p0! 4Tu1 4Tu2 4Tu3 4n0e0 4n0e1 4n0e2 4Tn20 4Th0 4u1 4n20 4Tn01 4Thb22 4Tn0e0 4Tn0e1 4Tn0e2 4u3 4u2 4h0 4n21 4Thb20 4n0e4 4n12! 4Thb10 4u4 4n22! 4p1 4n0e3 4s1! 4n1e2 5Gr1 4p2 4n1e3 4n2e0 4Tn11 4n1e0 4p3 4Thb21 4q0! 4Gq0 4Tn0e3 4Tn1e0 4Sv0 4Tn0e4 4n1e1 4n2e1 4n2e2 4n2e3 4Tn21 4Tn2e0 4Tn1e1 4Tn1e2 4n2e4 4Tn2e1 4Tn2e2 4n1e4 4Tn2e3 4s0 4Tn1e3 4Tn2e4 4n2o1! 4Tn1e4 4Ts0 4r4 4v0 4n1o0 4n0o0! 4n2o0 4n2o2 4Sv2 4Gc0 4Sv1 4s2 4s3 4Ts1 4l0 4l1! 4Xq0 4v1 4o0 4s4 4o1
-5x00! 5x10 5Gr0 5x60! 5x30 4Xc0 5Ta00 5x20! 5x40 4Ti0 5x70! 4Ti1 5Ta10 4in0 5x50! 5a0w1 4i0 4in1 4f2 4Ti2 4in2 5a0z0 5a1w1 4Tin0 4ine0 4Tj0 4ine1 4ine2 4f0! 4ine3 4Tine0 4ine4 4Tine1 5a0s0 4Tine2 4Tine3 4Tine4 5Ta20 5a1z0 5x90! 5a0c0 5a1w0 4ino0 5a1s0 5x80! 5x100 5Ta0c0 5x110! 5a2w1 4j0 5a0w0 5a2w0 4ino1! 5a2z0 5Sa0c0 5a1c0 4f1! 5Ta30 5a2c0 4Tk0 5a2s0 5Ta0c1 5Ta1c0 5b0 5a3w0 4k0 5b2 5b1 4k1! 5Ta2c0 5a3w1 5Sa1c0 5w0 5w2! 5w1 5w3! 5Ta1c1 5Thb12 5a3z0 5Thb22 5Thb23 4Tk1 5Tw0 5a0c1 5a1c1 5a3s0 5Sa2c0 5a3c0 5w4! 5Tu0 5Thb04 5Tn00 5r0 5Ta2c1 4k2 5Ta3c0 5u0! 5r2 5r1 5n00 5a2c1 5Tr0 4k3 5n01 5Thb20 5Sa3c0 5Thb03 5Thb21 5Thb24 5n02! 5Tn10 5r3 5Ta3c1 5Thb00 5Th0 5n10 5a3c1 5Tu1 5n0e5 5n0e0 5Tu2 5Tu3 5h0 5n0e1 5Tn20 5Thb01 5p0! 5Thb02 5n11 5u1 5n20 5Tn01 5u3! 5u2 5n0e3 5n21 5Thb13 5n12! 5Thb11 5Thb14 5n0e2 5Thb10 5Tn0e0 5p1 5n22! 5u4 5p2 6Gr1 5Tn0e1 5Tn0e2 5n1e2 5n1e1 5n1e3 5Tn0e3 5Tn11 5p3 5q0! 5Tn21 5s1! 5Gq0 5n1e0 5Tn1e0 5n0e4 5n2e0 5n1e5 5n2e2 5n2e1 5Tn0e4 5Tn0e5 5n2e4 5Tn2e0 5Tn1e1 5n1e4 5n2e3 5Tn2e1 5n2e5 5Sv0 5Tn2e2 5Tn1e2 5Tn1e3 5Tn1e4 5s0 5Tn1e5 5r4 5Tn2e3 5Tn2e4 5Tn2e5 5v0 5Ts0 5n1o0! 5Sv1 5n2o1 5n2o0 5n0o0 5Xq0 5Gc0 5n2o2 5Sv2 5s2 5s3 5l0 5l1! 5v1 5Ts1 5o0 5f2! 5s4 5o1
-6x10! 6x00 6Gr0 5Xc0 6x70! 6x30 6Ta00 6x20! 5Ti0 6x50 5Ti1 6x40! 6Ta10 5in0 6a0w1 5i0 5in1 6a0z0 5Ti2 6x60! 5in2 6a0c0 5Tin0 5Tj0 5ine2 5ine0 6x90! 5ine1 5ine3 5ine4 5Tine0 5ine5 5Tine1 6a1w1 5Tine2 5Tine3 5j0 5Tine4 6a0s0 5f0! 5Tine5 6Ta20 6a1z0 5ino0 6x80 6x100! 6a1s0 6Ta0c0 6x110! 6a2w1 6a1c0 6a2z0 5f1! 6a0w0 6a2w0 6Ta30 6a1w0 6a2c0 5ino1! 6Sa0c0 6a2s0 5Tk0 6Ta1c0 6b0 6a3w0 6b2 5k0 6a3w1 6b1 5k1! 6Ta2c0 6a3z0 6w2! 6w0 6Sa1c0 6w1 6Ta0c1 6a3s0 6Ta1c1 6Tw0 6a3c0 6Sa2c0 6w4! 6a0c1 6a1c1 6w3! 6Ta3c0 6r0 6s0 6r1 6Tu0 6r2 6Ta2c1 6Sa3c0 6Tr0 6u0! 6a2c1 6Ta3c1 6Tu1 6r3 6a3c1 6Th0 6p0! 6Tu2 6Tu3 6h0 6u1 6u3 6u2 6u4 6p1 6s1! 6p2 6p3 6q0! 6Ts0 6Sv0 6Gq0 6v0 6Sv2 6s2 6s3 6Sv1 6y0 6Ts1 6Xq0 6s4 6v1 6y1! 6Tj1 6Tj0 6j1 6j0 6j3 6j2 6Yj0 6Sj0
+0c70 0Yload0 0Sload0 0Gc0 0Sload2 0Yload1 0c57 0Sload1 0Yload2 0c69 0Gc2 0c4 0c5 0c3 0c0 0Gc3 0c6 0load0 0c37 0c2! 0Gc1 0c1! 0c25 0c9 0Yload4 0Yload3 0c26 0c62 0d0 0Gflat1 0c41 0c27 0s0 0u13! 0c38 0c40 0Gc4 0c28 0c36 0Ts0 0Gflat2 0c29 0u14! 0c10 0c7 0c30 0c44 0c51 0u12! 0c49 0Gflat0 0c13 0c31 0s2 0u4! 0u8 0Tu6 0cw0! 0pk0! 0u2! 0c63 0pk1 0c39! 0c61 0c59 0u0! 0z3 0s4 0Tu1 0pk2! 0cw1 0d20 0Sc0 0c42 0Tu0 0n00 0u23 0c32 0c48 0n20 0c16 0n01 0u26 0e1 0z1 0c53 0c50 0n10 0e2 0Gc5 1Gr0 0u6! 0pk3! 0u18! 0c56! 0u21! 0u1! 0u16! 0c46! 0c45! 0n02 0c54 0z2 0d2 0Tn00 0Tu2 0n11 0n21 0c58 0c8 0n12! 0n22 0u3! 0n0e0 0c43 0c47 0u19! 0u17! 0u10! 0Tn0e0 0n2e0 0n1e0 0c52 0Tn20 0z0! 0Tn10 0c65! 0Tn1e0 0n0o0 0Tn2e0 0u5! 0Tu3 0s5 0n1o0 0c60 0n2o0 0u7! 0c33 0Tu5 0Tu4
+1x40 1x60! 1x50! 1x70 1x10 1x00! 1Ta20 1x30 1x20! 1Ta00 1x80 1x90! 1Ta10 1a0w1 0s3 0u24! 0c19! 0c21! 1a2w1 1Ta30 1a0z0 0c24! 1a2w0 0c67! 1a0w0 0c20! 1a0s0 0s1! 1a1w0 1a1w1 1a0c0 0c15! 0c66! 1a3w0 1a2z0 1a1z0 1Ta0c0 1we2! 1we1 0c12! 1we0 1wo0 0u15! 0n1o1! 1wo1 1wo2! 1Thb10 1Twe0 1a1s0 0u9! 1a1c0 1Two0 0c55! 0c11! 1a2s0 0n2o1! 0c64! 1Ta1c0 0u20! 1Sa0c0 1r0 0u11! 0c34 1a3w1 0c17! 1r1 1r2 0c14! 1a2c0 1Ta0c1 1Sa1c0 1Tr0 0u22! 1wt0! 0n0o1 1a3z0 1Ta1c1 0c23! 1Ta2c0 1r3 1r4 1a3c0 1p0! 1Gc0 0d1 0c18 0c22 1Ta3c0 1a0c1 1a1c1 0c35 1wt1 1Th0 1Tn00 1Thb20 1Sa2c0 1Tu0 1Sa3c0 0e0! 1h0 1n00 1Ta2c1 1Ta3c1 1Ts0 1p1 1s0 1s10! 1Thb00 1a2c1 1a3c1 1n01 1sp0! 1p2 1s00 1Tn10 1Tn20 1Tu2 1n02! 1Tu1 1n10 2Gr0 1n20 1s11 1u2! 1n11 1n21 0u25! 1s01 1u0! 1n0e0 1n12! 1n22 1u1! 1n0e1 1Tn01 1Sv0 1Tn0e0 1n1e0 1n2e0 1q0! 1n1e1 1Tn0e1 1n2e1 1p3! 1s02 1Tn11 1Tn1e0 1v0 1Tn21 1Tn2e0 1Tn1e1 1Tn2e1 1Tsw0 1n0o0 1Gq0 1n1o0! 1n2o0 1Sv2 1s12 1Gg0 1sw0 1l00 1Sv1 1l10 1Xc0
+2x00! 2x10 2x30! 2x20 1Xq0 2Ta00 2x70! 2x60 2Ta10 2x40! 2a0w1 2x50 1Ti1 1Ti0 1Tk0 1i0! 1f0! 1in0 2a0z0 1v1 2a1w1 1Ti2 2Ta20 1in1 2a0c0 1g0! 2a0s0 1in2! 2x90! 1Gg1 2a1z0 1l11 1ine0 1ine1 2Ta0c0 1k0 2a1s0 2x80! 2a2w1 2a1c0 1Tin0 1Tine0 1Tine1 1Tj0 1k1! 1Tg0 1ino0 2a2w0 1j0! 2a2z0 2x100! 2x110 1Tk1 2Ta1c0 2a1w0 2a2s0 2Ta30 2Sa1c0 2a2c0 2Sa0c0 1g1! 1f2! 1f1! 2a0w0 2Ta2c0 2a3w0 2b0 2a3w1 0c68! 2b2 2b1 1l01 2a3z0 2Ta0c1 2Ta1c1 2Thb10 2we2! 2we0 2Thb20 2wo2! 2we1 2b3! 2wo1 2wo0 2Twe0 2wt1! 2a1c1 2a0c1 2a3s0 2Two0 2Sa2c0 2a3c0 2wt0! 2Tu0 2Ta2c1 2Tn00 1g2 2r0 2Ta3c0 2u0! 2a2c1 1k2 2r1 2r2 2n00 2Sa3c0 2Tn10 2Tr0 2n01 1ino1! 2n10 2Ts0 1k3 2Ta3c1 2Thb01 2n02! 2Thb21 2r3 2Tu1 2n11 2Thb00 2r4 2a3c1 2p0! 2n12 2Thb11 2n0e0 2Tn20 2Th0 2n0e1 2n20 2Tu2 2n1e0 2n1e1 2h0 2n21 2n0e2 2u2! 2u1! 2n1e2 2n22 2Gg0 2s10! 2Tn01 2Tn0e0 2p1 2Tn11 2s00 2Tn1e0 2Tn0e1 2Tn1e1 2Tn1e2 2sp0! 2Tn0e2 2n2e0 2p2 2n2e1 2Sv0 2n2e2 2Tn21 2Tn2e0 2p3 2q0! 2Tn2e1 2s11 2Tn2e2 2s01 2n0o0! 2v0 2n1o0! 2Gq0 2s12 2s02 2n2o0! 2Sv1 2s0 2Gc0 2l00 2Tsw0 2Sv2 2l10
+3x10! 3x00 3x50! 3x30 2Xq0 3Ta00 2Ti0 3x70! 2v1 2Ti1 3x20 2Tj0 2g0! 3x60! 2Xc0 2Gg1 2l11 2in0 3a0w1 3x40! 2sw0 3Ta10 2in1 2i0 3Gr0 2in2 2Ti2 3a0z0 2j0 2Tg0 2f0! 3a1w1 2ine0 2ine1 2ine2 3a1z0 3a0s0 2Tin0 2Tine0 2Tine1 3x80! 2Tine2 3Ta20 3a1s0 3a1w0 2ino0 3x90! 3a0c0 3x110 2Tk0 3x100! 3Ta0c0 3a2w1 3a1c0 2f2! 3a2z0 3Ta30 3a2w0 3a0w0 2k0 3Sa0c0 3a2s0 2k1! 3Ta1c0 2f1! 3a2c0 3Ta0c1 3b0 3a3w0 3b2 3a3w1 3Ta2c0 3Sa1c0 2g2! 3b1 2l01 2ino1 3a3z0 3we2! 3we0 3we1 2g1! 3Ta1c1 3b3! 3Thb01 3wo1 3wo2! 3wo0 2Tk1 3Twe0 3wt0! 3a1c1 3a0c1 3a3s0 3Two0 3Sa2c0 3a3c0 3wt1! 3Tn00 3Tu0 3Ta2c1 3r0 2k2 3Ta3c0 3n00 3a2c1 3r2 3r1 3u0 3Tn10 3n01 3Tr0 3Sa3c0 3Thb20 3n02! 3n10 3Ta3c1 3Thb00 3r3 3Ts0 3n11 3Thb22 3a3c1 3p0! 3Thb10 3Thb12 3n12 3Tu1 3n0e2 3Tn20 3Tu2 3n0e3 3Thb11 3Th0 3n1e0 3Thb21 3n20 3Thb02 3n0e0 3Tn11 3Tn1e0 3h0 3n21 3u1! 3u2 3n0e1 3n1e1 3Gg0 3n22! 3p1 3n1e3 3s00 3s10! 3Tn1e1 3n1e2 3p2 3sp0 3n2e0 3n2e1 3Tn1e2 3Tn01 3p3! 3q0 3Tn0e0 3Tn0e1 3n2e2 3Tn0e2 3Sv0 3n2e3 3Tn21 3Tn0e3 3s01 3Tn2e0 3Gq0 3s0 3Tn1e3 3Tn2e1 3s11 3Tn2e2 3Tn2e3 3v0 4Gr0 3n1o0! 3Tsw0 3n0o0 3n2o0! 3s02 2k3 3Sv1 3s12 3r4 3l00 3Sv2 3l10 3Gc0
+4x00! 4x10 3Xq0 4x30! 3v1 4x20 4Ta00 3Ti0 4x60! 3Ti1 3g0 4a0w1 4Ta10 3l11 3in0 4x40! 3sw0 3Gg1 3i0 4a0z0 3in1 4x50 3Ti2 3Tj0 3Xc0 3in2! 4x70! 3Tg0 3ine0 3ine1 3ine2 3ine3 3f0! 4a1w1 3Tin0 3j0 3Tine0 3Tine1 4a0s0 3Tine2 3Tine3 4Ta20 4a1z0 4a0c0 4x90! 3ino0 4a1s0 4x80! 4x110 4Ta0c0 4x100! 4a2w1 3Tk0 4a1c0 4a2z0 3f1! 4a0w0 4a2w0 4a1w0 4Ta30 4a2c0 3f2! 4Sa0c0 4a2s0 3ino1! 4Ta1c0 4b0 4a3w0 3k0 4Ta0c1 4a3w1 4Ta2c0 4b2 4b1 3g1! 3k1! 3l01 3g2! 4a3z0 4Sa1c0 4we2! 4we0 4b3! 4we1 4Ta1c1 4Thb03 4wo2! 4Thb10 4wo1 3Tk1 4Thb12 4wo0 4Twe0 4a0c1 4a1c1 4a3s0 4Two0 4Sa2c0 4a3c0 4Thb00 4Tn00 4Tu0 4Ta2c1 4r0 3k2 4Ta3c0 4n00 4u0! 4r2 4r1 4wt1! 4n01 4a2c1 3k3 4Tr0 4n02 4Sa3c0 4Tn10 4Ts0 4Thb02 4Ta3c1 4r3 4Thb22 4n10 4Thb01 4n0e0 4sp0! 4Th0 4p0! 4a3c1 4n11 4Thb21 4n0e4 4Thb11 4Thb23 4n0e3 4Tn20 4Thb13 4n12 4Tu2 4Tn01 4Tu1 4Thb20 4n20 4s0 4Tn11 4n1e2 4n1e1 4n21 4u1! 4h0 4u2! 4n0e1 4p1 4Gg0 4n22! 4n0e2 4n1e0 4n1e3 4s10! 4p2 4s00 4Tn1e0 4Tn1e1 4n2e1 4Tn0e0 4Tn1e2 4n2e0 4p3! 4Tn0e1 4Tn1e3 4n2e2 4Tn0e2 4q0! 4Tn0e3 4n1e4 4Tn0e4 4n2e3 4Sv0 4Tn21 4n2e4 4Tn2e0 4Tn2e1 4s11 4Tn2e2 4Gq0 4wt0! 4Tn1e4 4r4 4Tn2e3 4s01 4Tn2e4 4v0 4Gc0 4n1o0! 4s02 4Tsw0 4n0o0! 4n2o0 4s12 4Sv2 4l00 4Sv1 5Gr0 4l10
+5x00! 5x10 4Xq0 5x60! 4v1 5x30 5Ta00 5x20! 4Ti0 4Ti1 4g0 4Xc0 5a0w1 4sw0 4in0 5x70! 4l11 4Gg1 4i0 5a0z0 5Ta10 4in1 5x40 4in2! 5x50! 4Tj0 4Ti2 4Tg0 4ine0 5a1w1 4ine1 4ine3 4ine2 4ine4 4Tin0 5a1z0 4f0! 4Tine0 4Tine1 5a0c0 4Tine2 4Tine3 4Tine4 5Ta20 5a0s0 5x90! 4ino0 4j0 5a1w0 5a1c0 5x80! 5x100 4Tk0 4Tk1 5Ta0c0 5x110! 5a2w1 5a1s0 5a2z0 4f1! 4l01 5a0w0 5a2w0 5Ta30 5a2c0 4f2! 4g1! 5a2s0 5Sa0c0 5Ta1c0 5b0 5a3w0 4k0 5b2 5Ta2c0 5a3w1 5b1 4k1! 4g2! 5a3z0 5Sa1c0 4ino1! 5we2! 5we0 5wo2! 5we1 5Ta0c1 5Ta1c1 5Thb24 5wo0 5b3! 5Thb14 5Thb11 5Thb03 5wo1 5Twe0 5a0c1 5wt0! 5a1c1 5a3c0 5Two0 5Sa2c0 5a3s0 5wt1! 5Tn00 5Tu0 5Ta2c1 5r0 5n00 5Ta3c0 4k2 5u0! 5r2 5r1 5n01 4k3 5a2c1 5Tr0 5n02 5Sa3c0 5Tn10 5Thb04 5Ts0 5Thb00 5r3 5Ta3c1 5Thb01 5n10 5Thb02 5n0e0 5n0e1 5p0! 5Thb12 5Thb23 5a3c1 5Th0 5n0e3 5n0e4 5Tn20 5n11 5Thb13 5Thb21 5n0e5 5Tu2 5Thb22 5Tn01 5Tn0e0 5n20 5Tu1 5h0 5Thb20 5s0 5r4 5n12! 5n21 5n0e2 5u2! 5Thb10 5Gg0 5p1 5u1! 5n22 5s00! 5Tn0e1 5s10! 5p2 5Tn0e2 5n1e2 5Tn0e3 5n1e0 5Tn0e4 5n1e1 5n2e0 5p3! 5n2e2 5Tn11 5n2e1 5Tn1e0 5q0! 5Tn1e1 5Tn1e2 5n2e3 5Tn21 5sp0! 5n2e4 5Tn2e0 5Sv0 5n1e3 5Tn2e1 5n2e5 5Tn2e2 5Gq0 5Tn2e3 5n1e4 5Tn0e5 5n1e5 5Tn2e4 5s01 5Tn1e3 5Tn2e5 5v0 5Tn1e4 6Gr0 5Tn1e5 5n0o0! 5s11 5s02 5n2o0! 5Sv2 5n1o0 5Tsw0 5s12 5Sv1 5l00 5Gc0 5l10
+6x10! 5sw0 6x00 5Xq0 5f0! 5v1 6x30 6Ta00 6x20! 5Ti0 5Ti1 5g0 5l11 6x40! 5in0 6a0w1 5i0 5Gg1 6a0w0 6Ta10 5in1 5Xc0 6x50 5Ti2 5in2! 6x70! 5Tg0 5ine0 6a0z0 5ine1 5ine2 6x60! 5ine3 5ine4 5ine5 5Tin0 5Tine0 6a1w1 5Tj0 6a0s0 5Tine1 5Tine2 5Tine3 5Tine4 5Tine5 6x90! 6a1w0 6a0c0 6Ta20 5ino0 5j0 6a1z0 6x80 6x110! 5Tk0 6a1c0 6x100! 6Ta0c0 6a2w1 6a1s0 6a2z0 6a2w0 6Ta30 5k0 6a2c0 6Sa0c0 5ino1! 5f2! 5k1! 6Ta1c0 5g2! 6a2s0 5g1! 6b0 6a3w0 6a3w1 6b2 6Ta2c0 6b1 6a3z0 6wo2! 6we1 6we2! 6we0 6Ta0c1 6wo1 6wo0 6Twe0 6a3s0 6Sa2c0 6Sa1c0 6b3! 5f1! 6Two0 6a3c0 6Ta1c1 6Ta2c1 6wt0! 6Ta3c0 6r0 6s0 6a2c1 6wt1! 6r2 6r1 5l01 6Tr0 6Sa3c0 6a0c1 6Ts0 6Ta3c1 6Tz3 6r3 6sp0! 6a3c1 6a1c1 6p0! 6Tz2 6Th0 6Tz0 6Tz1 6Tu1 6h0 6z3! 6p1 6s00! 6z2 6z0 6s10! 6z1 6Tp0 6Tu0 6p2 6u1 6q0 6Tu2 6p3! 6s01 6Sv0 6Gq0 6u0! 6s02 6s11 6v0 6u2 6Tsw0 6s12 6Sv1 6sw0 6Sv2 6y0 6y1! 6v1 6Xq0 6j1 6j0 6Yj0 6Sj0
 """
 
 
@@ -509,12 +562,15 @@ def ordered():
     at = {o["id"]: i for i, o in enumerate(ops)}
     order = [at[w.strip("!")] for w in ORDER.split()]
     assert sorted(order) == list(range(len(ops)))
-    last, other, done = {}, {}, set()
+    last, other, done, opened = {}, {}, set(), set()
     for n, (i, w) in enumerate(zip(order, ORDER.split())):
         o = ops[i]
         assert o["dep"] <= done
         done.add(i)
         o["pos"] = n
+        if o["kind"] == "mm":
+            assert not (o["args"][1] and o["banks"][0] in opened)
+            (opened.discard if o["args"][2] else opened.add)(o["banks"][0])
         if w[-1] == "!":
             o["eng"], o["kind"], o["args"] = "s", "act", o["alt"]
         for b in o["banks"]:
@@ -637,6 +693,8 @@ def rank_program(g, core, T, topo):
                 r = q.activation(ap(a[0]), ap(a[1]), a[2], bias=ap(a[3]), scale=ap(a[4]), accum_out=ap(a[5]))
             else:
                 r = q.activation(ap(a[0]), ap(a[1]), a[2], bias=ap(a[3]), scale=ap(a[4]))
+        elif k == "gcp":
+            r = q.affine_select(ap(a[0]), ap(a[1]), [[0, width(a[0])]], ALU.is_ge, 0.0, 0, 0)
         elif k == "iota":
             if SCRATCH[a[0][0]][2] == I32:
                 r = q.iota(ap(a[0]), a[1], a[2], a[3])

@@ -6,6 +6,7 @@ F32, BF, F16, I32, U16 = "float32", "bfloat16", "float16", "int32", "uint16"
 DEAD = 288
 TW = 296
 ZR = 256
+NONE = 2 ** 18
 BIG, LOWER = 32768.0, -16384.0
 LOW = 254.0 * 4096
 HALF = 2.0 ** 23 - 0.5
@@ -17,17 +18,17 @@ SB = {
     "IOT": (256, F32), "IA": (32, F32), "TMP": (64, F32), "T1": (128, F32), "T2": (128, F32), "PK": (256, F32), "PKE": (2, F32),
     "EWB": (144, BF), "E0B": (144, F16), "EW16": (144, F16), "BO32": (144, F32), "BOB": (128, BF), "BO16": (128, F16),
     "RM": (16, F32), "UH": (5 * 144, F16), "US": (5 * 128, F32), "I32W": (144, F32), "IBW": (144, BF), "IMW": (144, BF),
-    "IR16": (128, F16), "EWR": (128, F16),
+    "IR16": (128, F16), "EWR": (128, F16), "DIT": (128, F16), "EW32": (144, F32), "EWR32": (128, F32), "M32": (64, F32),
     "I16F": (128, F16), "I296": (128, BF), "I592": (128, BF), "R16": (128, F16), "R4096": (128, BF), "DIF": (128, BF),
     "THR": (1, F32), "DG": (128, BF), "TBZ": (128, BF), "TBR": (128, BF), "RS48": (48, F32), "RSX": (1536, BF),
-    "CIL": (18, F16), "G8": (128, BF), "G832": (128, F32), "E8": (144, BF), "ONE": (DEAD, BF), "JC": (2, F32),
+    "CIL": (18, F16), "G8": (128, BF), "G832": (128, F32), "E8": (144, BF), "ZERO": (DEAD, BF), "JC": (2, F32),
     "X": (4608, F16), "CMP": (4608, BF), "Y": (288, F32), "GE": (288, BF), "M": (288, F16), "SC": (320, F32), "LW": (20, U16),
     "NK": (320, F16), "NKP": (288, F16), "NF": (TW, F32), "EQ": (6 * 320, BF), "OU": (288, U16), "HR": (TW, F32), "WR": (TW, F32),
     "W": (3 * TW, F32), "WP": (256, F32), "WA": (32, F32), "WB": (32, F32), "HT": (TW, F32), "HC": (288, F16),
-    "FL0": (384, BF), "FL1": (384, BF), "FG": (48, BF), "DB": (16, BF), "SN": (48, BF), "E": (48, BF), "M16": (48, BF),
+    "FL": (768, BF), "FG": (48, BF), "DB": (16, BF), "SN": (48, BF), "E": (48, BF), "M16": (48, BF),
     "PO": (32, U16), "TT": (1584, F32), "IOB": (DEAD, F32), "CBH": (256, F16), "PKD": (256, F16), "SD": (256, F16),
-    "SM": (32, F32), "SL": (2, U16), "HS": (DEAD, BF), "H2": (2 * DEAD, BF), "CU": (DEAD, F16), "AL": (4, U16), "SV": (8, F32),
-    "SRB": (256, BF), "SRC": (16, U16), "WL": (16, U16), "YW": (TW, F32), "YH": (TW, F32),
+    "SM": (32, F32), "SL": (2, U16), "H2": (2 * DEAD, BF), "CU": (DEAD, BF), "AL": (8, U16), "SV": (8, F32),
+    "SRB": (DEAD, BF), "SRC": (16, U16), "WL": (16, U16), "YY": (2 * TW, F32),
     "SC_O": (NS * 8, BF), "SC_I": (NS * 24, BF), "SP_O": (NS * 64, F32), "SP_I": (NS * 64, F32),
 }
 SCRATCH = {k: ("sbuf", [128, v[0]], v[1]) for k, v in SB.items()}
@@ -41,9 +42,13 @@ SEMAPHORES = (["ev", "es", "et", "eg", "sent"] + ["d%d" % i for i in range(NDMA)
 PIECES = [(a, a + 32) for a in range(0, 192, 32)] + [(a, a + 16) for a in range(192, 288, 16)]
 SUMS, CUT = [(0, 64), (64, 128), (128, 224), (224, 288)], [32, 32, 48, 32]
 NEAR, HIST, LISTS = [(0, 128), (128, 192), (192, 288)], [(0, 128), (128, 224), (224, 288)], [(0, 64), (64, 256)]
-BANKS = ["hb00 hb01 hb02 hb03", "hb20 hb21 hb22 hb23 hb24", "fl rank col cnt hb10 hb11 hb12 hb13 hb14",
-         "p150 p152 votes1 sb l ht0 ht1", "p151 votes0 votes2 one0 one1 one2", "hn2 of2 one3 p153 rotw roth votes3",
-         "of0 hn0 ofa hb04 ht2 hw", "of1 hn1 ha"]
+BANKS = ["hb00 hb01 hb03 votes1 rotw", "hb20 hb22 hb23 p153 hw hb21", "fl rank col cnt hb10 hb11 hb12 hb13 hb24",
+         "hb14 p152 sb ht0 ht1 one0", "hb04 p150 l votes2 one2 hn1", "hn2 of2 one3 votes3 ha", "roth votes0 of0 hn0 ofa",
+         "hb02 p151 one1 ht2 of1"]
+
+
+FIRST = [(0, 64), (64, 128), (128, 192), (192, 256)]
+FQ = 4
 
 
 def places():
@@ -148,6 +153,9 @@ def plan():
     def iota(out, pat, base=0, ch=0):
         add("g", "iota", (out, pat, base, ch), [out], [])
 
+    def side(out, in_, c=None, first=0):
+        add("g", "side", (out, in_, c, first), [out], [in_])
+
     def fill(out, c):
         iota(out, [[0, width(out)]], c)
 
@@ -175,16 +183,12 @@ def plan():
     BO, IW, IB, IQ = A("BO32", 16, 144), A("I32W", 16, 144), A("IBW", 16, 144), A("IQ", 16, 144)
     SRC, WL, IM1 = A("SRC"), A("WL"), A("IMW", 16, 144)
     ha = lambda p: K(B["ha"], 32 * p, 32 * p + 32)
-    al = lambda t: A("AL", 2 * (t % 2), 2 * (t % 2) + 2)
+    al = lambda t: A("AL", 2 * (t % 3), 2 * (t % 3) + 2)
 
     at("load")
     mset(A("LH"), 0.0)
-    dma("s", A("SI", p1=8), ("in", "s0"))
     dma("y", A("NB"), ("in", "nb"))
-    dma("y", A("QT", 0, 4096), ("in", "qs"))
-    for n, s in ((A("YW", 0, 256), "w0"), (A("LH", 0, 6), "lo"), (A("LH", 8, 14), "hi")):
-        dma("y", n, ("in", s))
-    for n, s in ((A("UI", p1=8), "us"), (A("CI", p1=8), "coin")):
+    for n, s in ((A("SI", p1=8), "s0"), (A("UI", p1=8), "us"), (A("CI", p1=8), "coin"), (A("QT", 0, 4096), "qs"), (A("LH", 8, 14), "hi")):
         dma("s", n, ("in", s))
 
     at("c")
@@ -206,16 +210,17 @@ def plan():
     move(A("IA"), A("IOT", 0, 32), 320.0)
     at("c")
     ts(A("BO32"), A("GQ"), PG, ALU.is_equal)
-    move(A("BOB"), BO)
+    side(A("BOB"), BO)
     ts(A("RM"), A("IOT", 0, 16), PR, ALU.is_equal)
     ts(A("I32W"), A("IQ"), P_, ALU.is_equal)
-    move(A("IBW"), A("I32W"))
-    move(A("IMW"), A("I32W"), scale=-1.0)
-    for n, c in (("I16F", 1.0), ("I296", 296.0), ("I592", 592.0)):
-        move(A(n), IW, scale=c)
+    mset(A("ZERO"), 0.0)
+    for n, c in ((IB, 1.0), (IM1, -1.0), (A("I296"), 296.0), (A("I592"), 592.0)):
+        side(n, A("ZERO", 0, 128), c)
+    side(A("IMW", 0, 16), A("ZERO", 0, 16), -1.0, 112)
+    move(A("I16F"), IW)
     ts(A("EWB"), A("IOT", 0, 144), PG, ALU.subtract, 15.0, ALU.is_equal)
-    move(A("EW16"), A("EWB"))
-    move(A("BO16"), BO)
+    side(A("EW16"), A("EWB"))
+    side(A("BO16"), BO)
     move(A("E0B"), A("EWB"), scale=col("RM", 0))
     for p in range(5):
         move(A("UH", 144 * p, 144 * p + 144), A("BO32"), scale=col("RM", p))
@@ -264,25 +269,33 @@ def plan():
         mset(A("W", j, j + 40), 0.0)
     mset(A("HT", 256, TW), -4096.0)
     mset(A("NF", 256, TW), 2048.0)
-    for p in range(5):
-        move(A("US", 128 * p, 128 * p + 128), A("BO32", 0, 128), scale=col("RM", p + 1))
+    for p in range(4):
+        side(A("US", 128 * p, 128 * p + 128), A("UH", 144 * p + 144, 144 * p + 272))
+    move(A("US", 512, 640), A("BO32", 0, 128), scale=col("RM", 5))
     mset(A("UB", 1536, 1576), 0.0)
     mset(A("SC_O"), 0.0)
     at("d")
     ts(A("JC"), A("IOT", 0, 32, 16), PR, ALU.add, -1.0, ALU.mult)
     ts(A("JC"), A("JC"), -0.5, ALU.add)
-    mset(A("ONE"), 1.0)
     at("e")
     move(A("PKD"), A("PK"), scale=1.0 / 32)
     move(col("PKE", 0), col("PK", 15), scale=1.0 / 32)
     ts(col("PKE", 1), col("RM", 0), -BIG / 32, ALU.mult, 144.25 - LOWER / 32, ALU.add)
     at("d2")
-    mset(A("HS", 256, DEAD), 1.0)
+    mset(A("SRB", 256, DEAD), float(NONE))
     at("z")
-    move(A("IR16"), A("I32W", 0, 128))
+    side(A("IR16"), A("I32W", 0, 128))
     ts(A("EWR"), A("IQ", 0, 128), PG, ALU.subtract, float(NS), ALU.is_equal)
     mset(A("HR", DEAD, TW), -1.0)
     mset(A("WR", DEAD, TW), 0.0)
+    at("zz")
+    side(A("EW32"), A("EWB"))
+    side(A("EWR32"), A("EWR"))
+    ts(col("PF", 9), col("RM", 0), 16.0, ALU.mult, P_, ALU.add)
+    ts(A("Y", 128, 256), A("IOT", 0, 128), 1.0, ALU.add, col("PF", 9), ALU.is_equal)
+    ts(col("PF", 11), col("RM", 1), -0.5, ALU.add)
+    move(A("T1"), A("Y", 128, 256), scale=col("PF", 11))
+    tt(A("DIT"), A("T1"), A("T2"), ALU.add)
     at("flat")
     iota(A("RSX"), [[0, 96], [8192, 16]], int(LOW))
     fill(A("TH"), 9)
@@ -293,10 +306,10 @@ def plan():
     k0 = K(0, 0, 256)
     mm([(k0, A("G832", p1=8), A("S0F", p1=8))])
     move(A("HC", 0, 256), k0, scale=col("RM", 0))
-    ts(K(0, 256, 512), k0, -2048.5, ALU.is_gt, 2.0 ** -11, ALU.mult)
-    tt(A("WP"), A("YW", 0, 256), K(0, 256, 512), ALU.mult)
-    add("v", "red", (col("SV", 2), K(0, 256, 512)), [col("SV", 2)], [K(0, 256, 512)])
-    ts(col("SC_O", 1), col("SV", 2), -2048.0, ALU.mult, -256.0, ALU.add)
+    dead = A("EQ", 320, 576)
+    ts(dead, k0, -2048.5, ALU.is_lt)
+    add("v", "red", (col("SV", 2), dead), [col("SV", 2)], [dead])
+    move(col("SC_O", 1), col("SV", 2))
     at("u")
     for j in range(0, 1536, 256):
         move(A("U8", j, j + 256, p1=8), A("UI", j, j + 256, p1=8))
@@ -315,7 +328,7 @@ def plan():
         scan(A("SC", a, b), hb(t + 1), A("PK", 0, b - a), ALU.min, ALU.add, BIG)
         ts(lw, A("SC", a + 15, b, 16), LWB, ALU.add, 4095.0, ALU.min)
         move(nk, IND(A("NB"), lw), -2048.0)
-        mm([(K(of, 0, b - a), A("R16"), nk)], True, False)
+        mm([(K(of, 0, b - a), A("R4096"), A("EQ", 320 + a, 320 + b))] * (t < 0 and a < 256) + [(K(of, 0, b - a), A("R16"), nk)], True, False)
         name = tag[0]
         at(name + "e")
         for p in range(t + 1, -1, -1):
@@ -329,6 +342,11 @@ def plan():
         else:
             move(A("NF", a, b), K(of, 0, b - a))
 
+    def chosen(k, a, b, l16, l32):
+        late = (SUMS if now[0] else FIRST)[-1][0]
+        c = max(a, min(b, late))
+        return [(K(k, 0, c - a), l16, A("M", a, c))] * (a < c) + [(K(k, c - a, b - a), l32, A("M32", c - late, b - late))] * (c < b)
+
     def own(t):
         for h, (a, b) in enumerate(NEAR):
             b = b if t > 0 else min(b, 256)
@@ -341,10 +359,15 @@ def plan():
             at("n%d" % h)
             hn = K(B["hn%d" % h], 0, b - a) if t >= 0 else K(0, a, b)
             if t >= 0:
-                mm([(hn, A("BO16"), A("M", a, b))])
+                mm(chosen(B["hn%d" % h], a, b, A("BO16"), BO))
             neighbours(t, a, b, lambda p: hn if p == t + 1 else hb(p), B["of%d" % h], a if t < 0 else None)
 
     own(-1)
+    at("late")
+    dma("y", A("WP"), ("in", "w0"))
+    ops[-1]["rd"].append(A("OU", 0, 16))
+    dma("y", A("LH", 0, 6), ("in", "lo"))
+    move(A("LH", 0, 9, 8), A("LH", 0, 9, 8), scale=2048.0)
 
     for t in range(NS):
         last = t == NS - 1
@@ -353,11 +376,8 @@ def plan():
             if a < 256 or t:
                 at("x%d" % i)
                 move(A("X", 16 * a, 16 * b), IND(A("QT"), A("OU", a, b)))
-        for i, (a, b) in enumerate(SUMS):
-            b = b if t else min(b, 256)
+        for i, (a, b) in enumerate(SUMS if t else FIRST):
             c = min(b, 256)
-            if a == b:
-                continue
             p15, votes, one = B["p15%d" % i], K(B["votes%d" % i], 0, b - a), K(B["one%d" % i], 0, b - a)
             at("a%d" % i)
             mm([(K(p15, 0, b - a), A("I16F"), A("X", 16 * a + j, 16 * b, 16)) for j in range(16)])
@@ -381,16 +401,22 @@ def plan():
             at("a%dc" % i)
             mm([(votes, sel(s), A("CMP", 16 * a + s, 16 * b, 16)) for s in range(1, 16)])
             act(A("GE", a, b), votes, ACT.Sign, A("THR"))
-            mm([(one, A("DIF"), A("GE", a, b))])
-            tt(A("M", a, b), A("NKP", a, b), one, ALU.mult)
+            if i < len(SUMS) - 1:
+                mm([(one, A("DIF"), A("GE", a, b))])
+                tt(A("M", a, b), A("NKP", a, b), one, ALU.mult)
+            else:
+                mm([(one, A("DIT"), A("NKP", a, b))])
+                tt(A("M32", 0, b - a), A("GE", a, b), one, ALU.mult)
         fl, rk = B["fl"], B["rank"]
-        for h in range(2):
-            at("w" + "eo"[h])
-            ts(A("FL%d" % h, 0, 128), A("W", h, 256, 2), col("LH", t), ALU.is_lt)
-            ts(A("FL%d" % h, 128, 256), A("W", h, 256, 2), col("LH", 8 + t), ALU.is_gt)
-            ts(A("FL%d" % h, 256, 384), A("W", h, 256, 2), 0.0, ALU.is_equal)
-            ops[-1]["alt"] = (A("FL%d" % h, 256, 384), A("W", h, 256, 2), ACT.Relu, 1.0, -2.0 ** 85)
-            mm([(K(fl, 0, 48), sel(2 * r + h), A("FL%d" % h, r, 384, 8)) for r in range(8)], h == 0, h == 1)
+        for h in range(FQ):
+            at("w" + "eoab"[h])
+            n = 256 // FQ
+            f = lambda j: A("FL", n * (3 * h + j), n * (3 * h + j + 1))
+            ts(f(0), A("W", h, 256, FQ), col("LH", t), ALU.is_lt)
+            ts(f(1), A("W", h, 256, FQ), col("LH", 8 + t), ALU.is_gt)
+            ts(f(2), A("W", h, 256, FQ), 0.0, ALU.is_equal)
+            ops[-1]["alt"] = (f(2), A("W", h, 256, FQ), ACT.Relu, 1.0, -2.0 ** 85)
+            mm([(K(fl, 0, 48), sel(FQ * r + h), A("FL", 3 * n * h + r, 3 * n * (h + 1), 16 // FQ)) for r in range(16 // FQ)], h == 0, h == FQ - 1)
         at("wt")
         c = DEAD if t else 256
         move(A("W", TW, TW + c), A("W", 0, c), scale=2.0)
@@ -401,8 +427,11 @@ def plan():
         scan(A("SN"), A("RS48"), A("FG"), ALU.mult, ALU.add)
         tt(A("E"), A("FG"), A("M16"), ALU.mult)
         k = K(rk, 16, 32)
-        mm([(K(rk, 16, 34), A("I16F"), A("CIL")), (k, A("TBR"), HIGH), (k, IM1, A("E", 16, 32)), (k, A("BOB"), A("SN", 16, 32)),
-            (K(rk, 32, 34), A("BOB"), A("SN", 15, 32, 16)), (K(rk, 32, 33), A("BOB"), col("SN", 47))])
+        at("ra")
+        mm([(K(rk, 16, 34), A("I16F"), A("CIL")), (k, A("TBR"), HIGH)], True, False)
+        at("r")
+        mm([(k, IM1, A("E", 16, 32)), (k, A("BOB"), A("SN", 16, 32)),
+            (K(rk, 32, 34), A("BOB"), A("SN", 15, 32, 16)), (K(rk, 32, 33), A("BOB"), col("SN", 47))], False, True)
         ts(A("PO", 16, 32), k, K(rk, 32, 33), ALU.subtract, 255.0, ALU.add)
         DD = col("SC_O", 8 * t)
         if not last:
@@ -412,7 +441,9 @@ def plan():
         mm([x for j in HOLES for x in ((k, A("BOB"), A("SN", j, j + 16)), (k, A("TBZ"), A("FG", j, j + 16)))])
         ts(A("PO", 0, 16), k, K(rk, 32, 33), ALU.subtract, 255.0, ALU.add)
         at("r")
-        fill(A("TT", ZR, ZR + 288), 64 + DEAD)
+        at("r")
+        fill(A("TT", ZR, ZR + 256), 208 + NONE)
+        fill(A("TT", ZR + 256, ZR + 288), 64 + DEAD)
         at("p")
         scatter(A("TT", ZR, ZR + 1328), A("PO", 16, 32), A("IOB", 0, 256))
         scan(A("SM"), A("TT", ZR + 256, ZR + 288), A("PK", 0, 32), ALU.min, ALU.add, BIG)
@@ -425,18 +456,18 @@ def plan():
             if a == b:
                 continue
             k = K(B["ht%d" % i], 0, b - a)
-            mm([(k, A("I16F"), A("HC", a, b)), (k, A("EW16", 14 - t, 142 - t), A("M", a, b))])
+            mm([(k, A("I16F"), A("HC", a, b))] + chosen(B["ht%d" % i], a, b, A("EW16", 14 - t, 142 - t), A("EW32", 14 - t, 142 - t)))
             move(A("HT", a, b), k)
         if last:
             at("z")
             for a, b in HIST:
-                mm([(K(0, a, b), A("IR16"), A("HC", a, b)), (K(0, a, b), A("EWR"), A("M", a, b))])
+                mm([(K(0, a, b), A("IR16"), A("HC", a, b))] + chosen((0, a), a, b, A("EWR"), A("EWR32")))
                 ts(A("HR", a, b), K(0, a, b), HB, ALU.add, -1.0, ALU.max)
             mm([(K(1, 0, DEAD), A("I32W", 0, 128), A("W", 0, DEAD))])
             move(A("WR", 0, DEAD), K(1, 0, DEAD), scale=0.5)
         at("p")
         po = 64 * t
-        move(A("SP_O", po, po + 32), IND(A("WR") if last else A("W", 0, TW), A("SL")), scale=1.0 if last else 2.0 ** -12)
+        move(A("SP_O", po, po + 32), IND(A("WR") if last else A("W", 0, TW), A("SL")), scale=1.0 if last else 2.0 ** (-12 if t else -23))
         at("q")
         move(A("SP_O", po + 32, po + 64), IND(A("HR" if last else "HT"), A("SL")))
         for kind in ("p" if last else "pc" if t else "cp"):
@@ -458,24 +489,24 @@ def plan():
             at("s%d" % i)
             move(A("SRB", a, b), IND(A("TT", 0, ZR + 256), A("PO", a // 16, b // 16)), -208.0)
             scan(A("SD", a, b), A("SRB", a, b), A("PKD", a, b), ALU.min, ALU.add, BIG / 32)
-            ts(A("SRC", a // 16, b // 16), A("SD", a + 15, b, 16), col("PKE", 1), ALU.add)
+            ts(A("SRC", a // 16, b // 16), A("SD", a + 15, b, 16), col("PKE", 1), ALU.add, float(DEAD), ALU.min)
         at("sw")
         k = K(B["l"], 0, 16)
         mm([(k, A("I592"), A("FG", 0, 16)), (k, A("I592"), HIGH), (k, A("I296"), A("FG", 32, 48)), (k, A("I296"), A("DB")),
             (k, A("I16F"), A("SD", 15, 256, 16))])
-        ts(WL, k, col("PKE", 1), ALU.add)
+        ts(WL, k, col("PKE", 1), ALU.add, 2.0 * TW + DEAD, ALU.min)
         at("v")
-        act(A("HS", 0, 256), A("SRB"), ACT.Sign, 144.5 - DEAD)
-        scan(A("CU"), A("ONE"), A("HS"), ALU.add, ALU.add)
+        scan(A("CU"), A("SRB"), A("ZERO"), ALU.add, ALU.add)
+        at("vs")
         for j in range(2):
-            act(A("H2", DEAD * j, DEAD * j + DEAD), A("CU"), ACT.Sign, col("JC", j), 0.5, col("SV", 6 + j))
+            act(A("H2", DEAD * j, DEAD * j + DEAD), A("CU"), ACT.Sign, col("JC", j), 1.0 / NONE, col("SV", 6 + j))
         ts(al(t), A("SV", 6, 8), -0.5, ALU.mult, DEAD / 2 + 0.25, ALU.add)
         hi = A("SP_I", po + 32, po + 64)
         if not last:
             at("g")
             iota(A("IOB"), [[1, DEAD]], 64)
             scatter(A("IOB"), al(t), A("IA"))
-            add("g", "gcp", (A("CBH"), A("IOB", 0, 256)), [A("CBH")], [A("IOB", 0, 256)])
+            side(A("CBH"), A("IOB", 0, 256))
             k = K(B["col"], 0, 16)
             mm([(k, sel0(r), A("CBH", r, 256, 16)) for r in range(16)])
             for j in HOLES:
@@ -485,7 +516,7 @@ def plan():
                 ts(A("OU", a, b), IND(A("NF"), A("SRC", a // 16, b // 16)), 2048.0, ALU.add, 4096.0, ALU.min)
                 ts(A("NKP", a, b), A("OU", a, b), -2048.0, ALU.add)
             at("f")
-            move(A("WP"), IND(A("W"), WL), scale=2.0 ** -11)
+            move(A("WP"), IND(A("W"), WL), scale=2.0 ** (-11 if t else -22))
             move(A("HC", 0, 256), IND(A("HT"), SRC))
             move(A("UA"), IND(A("UB", 256 * t + 256, 256 * t + 256 + TW), al(t)))
             at("i")
@@ -500,8 +531,8 @@ def plan():
             move(A("WA"), K(B["rotw"], 0, 32))
         else:
             at("y")
-            ts(A("YH", 0, 256), IND(A("HT"), SRC), HB, ALU.add, -1.0, ALU.max)
-            move(A("YW", 0, 256), IND(A("W"), WL))
+            ts(A("YY", TW, TW + 256), IND(A("HT"), SRC), HB, ALU.add, -1.0, ALU.max)
+            move(A("YY", 0, 256), IND(A("W"), WL))
         if not last:
             at("k")
             cn = B["cnt"]
@@ -515,10 +546,10 @@ def plan():
                 ts(col("SC_O", 8 * t + 9), col("SV", 1), DD, ALU.subtract, 0.0, ALU.min)
         else:
             at("j")
-            cp(IND(A("YW"), al(t)), A("SP_I", po, po + 32))
-            cp(IND(A("YH"), al(t)), hi)
-            dma("s", ("out", "yw"), A("YW", 0, 256))
-            dma("y", ("out", "yh"), A("YH", 0, 256))
+            ts(A("AL", 6, 8), A("SV", 6, 8), -0.5, ALU.mult, DEAD / 2 + 0.25 + TW, ALU.add)
+            cp(IND(A("YY"), A("AL", 4, 8)), A("SP_I", po, po + 64))
+            dma("s", ("out", "yw"), A("YY", 0, 256))
+            dma("y", ("out", "yh"), A("YY", TW, TW + 256))
     return ops
 
 
@@ -546,13 +577,13 @@ def depend(ops):
 
 
 ORDER = """
-0c70 0Yload0 0Sload0 0Gc0 0Sload2 0Yload1 0c57 0Sload1 0Yload2 0c69 0Gc2 0c4 0c5 0c3 0c0 0Gc3 0c6 0load0 0c37 0c2! 0Gc1 0c1! 0c25 0c9 0Yload4 0Yload3 0c26 0c62 0d0 0Gflat1 0c41 0c27 0s0 0u13! 0c38 0c40 0Gc4 0c28 0c36 0Ts0 0Gflat2 0c29 0u14! 0c10 0c7 0c30 0c44 0c51 0u12! 0c49 0Gflat0 0c13 0c31 0s2 0u4! 0u8 0Tu6 0cw0! 0pk0! 0u2! 0c63 0pk1 0c39! 0c61 0c59 0u0! 0z3 0s4 0Tu1 0pk2! 0cw1 0d20 0Sc0 0c42 0Tu0 0n00 0u23 0c32 0c48 0n20 0c16 0n01 0u26 0e1 0z1 0c53 0c50 0n10 0e2 0Gc5 1Gr0 0u6! 0pk3! 0u18! 0c56! 0u21! 0u1! 0u16! 0c46! 0c45! 0n02 0c54 0z2 0d2 0Tn00 0Tu2 0n11 0n21 0c58 0c8 0n12! 0n22 0u3! 0n0e0 0c43 0c47 0u19! 0u17! 0u10! 0Tn0e0 0n2e0 0n1e0 0c52 0Tn20 0z0! 0Tn10 0c65! 0Tn1e0 0n0o0 0Tn2e0 0u5! 0Tu3 0s5 0n1o0 0c60 0n2o0 0u7! 0c33 0Tu5 0Tu4
-1x40 1x60! 1x50! 1x70 1x10 1x00! 1Ta20 1x30 1x20! 1Ta00 1x80 1x90! 1Ta10 1a0w1 0s3 0u24! 0c19! 0c21! 1a2w1 1Ta30 1a0z0 0c24! 1a2w0 0c67! 1a0w0 0c20! 1a0s0 0s1! 1a1w0 1a1w1 1a0c0 0c15! 0c66! 1a3w0 1a2z0 1a1z0 1Ta0c0 1we2! 1we1 0c12! 1we0 1wo0 0u15! 0n1o1! 1wo1 1wo2! 1Thb10 1Twe0 1a1s0 0u9! 1a1c0 1Two0 0c55! 0c11! 1a2s0 0n2o1! 0c64! 1Ta1c0 0u20! 1Sa0c0 1r0 0u11! 0c34 1a3w1 0c17! 1r1 1r2 0c14! 1a2c0 1Ta0c1 1Sa1c0 1Tr0 0u22! 1wt0! 0n0o1 1a3z0 1Ta1c1 0c23! 1Ta2c0 1r3 1r4 1a3c0 1p0! 1Gc0 0d1 0c18 0c22 1Ta3c0 1a0c1 1a1c1 0c35 1wt1 1Th0 1Tn00 1Thb20 1Sa2c0 1Tu0 1Sa3c0 0e0! 1h0 1n00 1Ta2c1 1Ta3c1 1Ts0 1p1 1s0 1s10! 1Thb00 1a2c1 1a3c1 1n01 1sp0! 1p2 1s00 1Tn10 1Tn20 1Tu2 1n02! 1Tu1 1n10 2Gr0 1n20 1s11 1u2! 1n11 1n21 0u25! 1s01 1u0! 1n0e0 1n12! 1n22 1u1! 1n0e1 1Tn01 1Sv0 1Tn0e0 1n1e0 1n2e0 1q0! 1n1e1 1Tn0e1 1n2e1 1p3! 1s02 1Tn11 1Tn1e0 1v0 1Tn21 1Tn2e0 1Tn1e1 1Tn2e1 1Tsw0 1n0o0 1Gq0 1n1o0! 1n2o0 1Sv2 1s12 1Gg0 1sw0 1l00 1Sv1 1l10 1Xc0
-2x00! 2x10 2x30! 2x20 1Xq0 2Ta00 2x70! 2x60 2Ta10 2x40! 2a0w1 2x50 1Ti1 1Ti0 1Tk0 1i0! 1f0! 1in0 2a0z0 1v1 2a1w1 1Ti2 2Ta20 1in1 2a0c0 1g0! 2a0s0 1in2! 2x90! 1Gg1 2a1z0 1l11 1ine0 1ine1 2Ta0c0 1k0 2a1s0 2x80! 2a2w1 2a1c0 1Tin0 1Tine0 1Tine1 1Tj0 1k1! 1Tg0 1ino0 2a2w0 1j0! 2a2z0 2x100! 2x110 1Tk1 2Ta1c0 2a1w0 2a2s0 2Ta30 2Sa1c0 2a2c0 2Sa0c0 1g1! 1f2! 1f1! 2a0w0 2Ta2c0 2a3w0 2b0 2a3w1 0c68! 2b2 2b1 1l01 2a3z0 2Ta0c1 2Ta1c1 2Thb10 2we2! 2we0 2Thb20 2wo2! 2we1 2b3! 2wo1 2wo0 2Twe0 2wt1! 2a1c1 2a0c1 2a3s0 2Two0 2Sa2c0 2a3c0 2wt0! 2Tu0 2Ta2c1 2Tn00 1g2 2r0 2Ta3c0 2u0! 2a2c1 1k2 2r1 2r2 2n00 2Sa3c0 2Tn10 2Tr0 2n01 1ino1! 2n10 2Ts0 1k3 2Ta3c1 2Thb01 2n02! 2Thb21 2r3 2Tu1 2n11 2Thb00 2r4 2a3c1 2p0! 2n12 2Thb11 2n0e0 2Tn20 2Th0 2n0e1 2n20 2Tu2 2n1e0 2n1e1 2h0 2n21 2n0e2 2u2! 2u1! 2n1e2 2n22 2Gg0 2s10! 2Tn01 2Tn0e0 2p1 2Tn11 2s00 2Tn1e0 2Tn0e1 2Tn1e1 2Tn1e2 2sp0! 2Tn0e2 2n2e0 2p2 2n2e1 2Sv0 2n2e2 2Tn21 2Tn2e0 2p3 2q0! 2Tn2e1 2s11 2Tn2e2 2s01 2n0o0! 2v0 2n1o0! 2Gq0 2s12 2s02 2n2o0! 2Sv1 2s0 2Gc0 2l00 2Tsw0 2Sv2 2l10
-3x10! 3x00 3x50! 3x30 2Xq0 3Ta00 2Ti0 3x70! 2v1 2Ti1 3x20 2Tj0 2g0! 3x60! 2Xc0 2Gg1 2l11 2in0 3a0w1 3x40! 2sw0 3Ta10 2in1 2i0 3Gr0 2in2 2Ti2 3a0z0 2j0 2Tg0 2f0! 3a1w1 2ine0 2ine1 2ine2 3a1z0 3a0s0 2Tin0 2Tine0 2Tine1 3x80! 2Tine2 3Ta20 3a1s0 3a1w0 2ino0 3x90! 3a0c0 3x110 2Tk0 3x100! 3Ta0c0 3a2w1 3a1c0 2f2! 3a2z0 3Ta30 3a2w0 3a0w0 2k0 3Sa0c0 3a2s0 2k1! 3Ta1c0 2f1! 3a2c0 3Ta0c1 3b0 3a3w0 3b2 3a3w1 3Ta2c0 3Sa1c0 2g2! 3b1 2l01 2ino1 3a3z0 3we2! 3we0 3we1 2g1! 3Ta1c1 3b3! 3Thb01 3wo1 3wo2! 3wo0 2Tk1 3Twe0 3wt0! 3a1c1 3a0c1 3a3s0 3Two0 3Sa2c0 3a3c0 3wt1! 3Tn00 3Tu0 3Ta2c1 3r0 2k2 3Ta3c0 3n00 3a2c1 3r2 3r1 3u0 3Tn10 3n01 3Tr0 3Sa3c0 3Thb20 3n02! 3n10 3Ta3c1 3Thb00 3r3 3Ts0 3n11 3Thb22 3a3c1 3p0! 3Thb10 3Thb12 3n12 3Tu1 3n0e2 3Tn20 3Tu2 3n0e3 3Thb11 3Th0 3n1e0 3Thb21 3n20 3Thb02 3n0e0 3Tn11 3Tn1e0 3h0 3n21 3u1! 3u2 3n0e1 3n1e1 3Gg0 3n22! 3p1 3n1e3 3s00 3s10! 3Tn1e1 3n1e2 3p2 3sp0 3n2e0 3n2e1 3Tn1e2 3Tn01 3p3! 3q0 3Tn0e0 3Tn0e1 3n2e2 3Tn0e2 3Sv0 3n2e3 3Tn21 3Tn0e3 3s01 3Tn2e0 3Gq0 3s0 3Tn1e3 3Tn2e1 3s11 3Tn2e2 3Tn2e3 3v0 4Gr0 3n1o0! 3Tsw0 3n0o0 3n2o0! 3s02 2k3 3Sv1 3s12 3r4 3l00 3Sv2 3l10 3Gc0
-4x00! 4x10 3Xq0 4x30! 3v1 4x20 4Ta00 3Ti0 4x60! 3Ti1 3g0 4a0w1 4Ta10 3l11 3in0 4x40! 3sw0 3Gg1 3i0 4a0z0 3in1 4x50 3Ti2 3Tj0 3Xc0 3in2! 4x70! 3Tg0 3ine0 3ine1 3ine2 3ine3 3f0! 4a1w1 3Tin0 3j0 3Tine0 3Tine1 4a0s0 3Tine2 3Tine3 4Ta20 4a1z0 4a0c0 4x90! 3ino0 4a1s0 4x80! 4x110 4Ta0c0 4x100! 4a2w1 3Tk0 4a1c0 4a2z0 3f1! 4a0w0 4a2w0 4a1w0 4Ta30 4a2c0 3f2! 4Sa0c0 4a2s0 3ino1! 4Ta1c0 4b0 4a3w0 3k0 4Ta0c1 4a3w1 4Ta2c0 4b2 4b1 3g1! 3k1! 3l01 3g2! 4a3z0 4Sa1c0 4we2! 4we0 4b3! 4we1 4Ta1c1 4Thb03 4wo2! 4Thb10 4wo1 3Tk1 4Thb12 4wo0 4Twe0 4a0c1 4a1c1 4a3s0 4Two0 4Sa2c0 4a3c0 4Thb00 4Tn00 4Tu0 4Ta2c1 4r0 3k2 4Ta3c0 4n00 4u0! 4r2 4r1 4wt1! 4n01 4a2c1 3k3 4Tr0 4n02 4Sa3c0 4Tn10 4Ts0 4Thb02 4Ta3c1 4r3 4Thb22 4n10 4Thb01 4n0e0 4sp0! 4Th0 4p0! 4a3c1 4n11 4Thb21 4n0e4 4Thb11 4Thb23 4n0e3 4Tn20 4Thb13 4n12 4Tu2 4Tn01 4Tu1 4Thb20 4n20 4s0 4Tn11 4n1e2 4n1e1 4n21 4u1! 4h0 4u2! 4n0e1 4p1 4Gg0 4n22! 4n0e2 4n1e0 4n1e3 4s10! 4p2 4s00 4Tn1e0 4Tn1e1 4n2e1 4Tn0e0 4Tn1e2 4n2e0 4p3! 4Tn0e1 4Tn1e3 4n2e2 4Tn0e2 4q0! 4Tn0e3 4n1e4 4Tn0e4 4n2e3 4Sv0 4Tn21 4n2e4 4Tn2e0 4Tn2e1 4s11 4Tn2e2 4Gq0 4wt0! 4Tn1e4 4r4 4Tn2e3 4s01 4Tn2e4 4v0 4Gc0 4n1o0! 4s02 4Tsw0 4n0o0! 4n2o0 4s12 4Sv2 4l00 4Sv1 5Gr0 4l10
-5x00! 5x10 4Xq0 5x60! 4v1 5x30 5Ta00 5x20! 4Ti0 4Ti1 4g0 4Xc0 5a0w1 4sw0 4in0 5x70! 4l11 4Gg1 4i0 5a0z0 5Ta10 4in1 5x40 4in2! 5x50! 4Tj0 4Ti2 4Tg0 4ine0 5a1w1 4ine1 4ine3 4ine2 4ine4 4Tin0 5a1z0 4f0! 4Tine0 4Tine1 5a0c0 4Tine2 4Tine3 4Tine4 5Ta20 5a0s0 5x90! 4ino0 4j0 5a1w0 5a1c0 5x80! 5x100 4Tk0 4Tk1 5Ta0c0 5x110! 5a2w1 5a1s0 5a2z0 4f1! 4l01 5a0w0 5a2w0 5Ta30 5a2c0 4f2! 4g1! 5a2s0 5Sa0c0 5Ta1c0 5b0 5a3w0 4k0 5b2 5Ta2c0 5a3w1 5b1 4k1! 4g2! 5a3z0 5Sa1c0 4ino1! 5we2! 5we0 5wo2! 5we1 5Ta0c1 5Ta1c1 5Thb24 5wo0 5b3! 5Thb14 5Thb11 5Thb03 5wo1 5Twe0 5a0c1 5wt0! 5a1c1 5a3c0 5Two0 5Sa2c0 5a3s0 5wt1! 5Tn00 5Tu0 5Ta2c1 5r0 5n00 5Ta3c0 4k2 5u0! 5r2 5r1 5n01 4k3 5a2c1 5Tr0 5n02 5Sa3c0 5Tn10 5Thb04 5Ts0 5Thb00 5r3 5Ta3c1 5Thb01 5n10 5Thb02 5n0e0 5n0e1 5p0! 5Thb12 5Thb23 5a3c1 5Th0 5n0e3 5n0e4 5Tn20 5n11 5Thb13 5Thb21 5n0e5 5Tu2 5Thb22 5Tn01 5Tn0e0 5n20 5Tu1 5h0 5Thb20 5s0 5r4 5n12! 5n21 5n0e2 5u2! 5Thb10 5Gg0 5p1 5u1! 5n22 5s00! 5Tn0e1 5s10! 5p2 5Tn0e2 5n1e2 5Tn0e3 5n1e0 5Tn0e4 5n1e1 5n2e0 5p3! 5n2e2 5Tn11 5n2e1 5Tn1e0 5q0! 5Tn1e1 5Tn1e2 5n2e3 5Tn21 5sp0! 5n2e4 5Tn2e0 5Sv0 5n1e3 5Tn2e1 5n2e5 5Tn2e2 5Gq0 5Tn2e3 5n1e4 5Tn0e5 5n1e5 5Tn2e4 5s01 5Tn1e3 5Tn2e5 5v0 5Tn1e4 6Gr0 5Tn1e5 5n0o0! 5s11 5s02 5n2o0! 5Sv2 5n1o0 5Tsw0 5s12 5Sv1 5l00 5Gc0 5l10
-6x10! 5sw0 6x00 5Xq0 5f0! 5v1 6x30 6Ta00 6x20! 5Ti0 5Ti1 5g0 5l11 6x40! 5in0 6a0w1 5i0 5Gg1 6a0w0 6Ta10 5in1 5Xc0 6x50 5Ti2 5in2! 6x70! 5Tg0 5ine0 6a0z0 5ine1 5ine2 6x60! 5ine3 5ine4 5ine5 5Tin0 5Tine0 6a1w1 5Tj0 6a0s0 5Tine1 5Tine2 5Tine3 5Tine4 5Tine5 6x90! 6a1w0 6a0c0 6Ta20 5ino0 5j0 6a1z0 6x80 6x110! 5Tk0 6a1c0 6x100! 6Ta0c0 6a2w1 6a1s0 6a2z0 6a2w0 6Ta30 5k0 6a2c0 6Sa0c0 5ino1! 5f2! 5k1! 6Ta1c0 5g2! 6a2s0 5g1! 6b0 6a3w0 6a3w1 6b2 6Ta2c0 6b1 6a3z0 6wo2! 6we1 6we2! 6we0 6Ta0c1 6wo1 6wo0 6Twe0 6a3s0 6Sa2c0 6Sa1c0 6b3! 5f1! 6Two0 6a3c0 6Ta1c1 6Ta2c1 6wt0! 6Ta3c0 6r0 6s0 6a2c1 6wt1! 6r2 6r1 5l01 6Tr0 6Sa3c0 6a0c1 6Ts0 6Ta3c1 6Tz3 6r3 6sp0! 6a3c1 6a1c1 6p0! 6Tz2 6Th0 6Tz0 6Tz1 6Tu1 6h0 6z3! 6p1 6s00! 6z2 6z0 6s10! 6z1 6Tp0 6Tu0 6p2 6u1 6q0 6Tu2 6p3! 6s01 6Sv0 6Gq0 6u0! 6s02 6s11 6v0 6u2 6Tsw0 6s12 6Sv1 6sw0 6Sv2 6y0 6y1! 6v1 6Xq0 6j1 6j0 6Yj0 6Sj0
+0c0 0Sload0 0Yload0 0Gc0 0Sload1 0c55 0Sload2 0Sload3 0c52 0Gc2 0c3 0c10 0c4 0c6 0Gc1 0c1! 0c12 0Sc0 0c20 0c2 0Gc4 0c5 0c8 0c7 0Gc3 0c19 0c9 0Gc10 0c14 0c22 0c21 0c23 0Gflat0 0c15 0c24 0c56 0c60 0c26 0c25 0cw0! 0c30 0s0! 0c28 0c35 0c27 0pk0! 0c43 0cw1! 0c16! 0c13 0c31 0c18! 0c38 0c34 0c32 0c36 0Ts0 0c29 0c39 0u4! 0pk1! 0c40! 0pk2! 0u0! 0pk3 0z0 0c17! 0c54 0u2! 0c47 0zz0 0Gc8 0n00 0c49! 0c33! 0c59 0c11 0c58! 0Tu0 0n10 0u10! 0Gc15 0s2 0Tu1 0c37 0zz1 0Gc11 0n20 0c44 0Gc16 0u13! 0zz2 0n11 0n01 0d0 0n21 0Gzz1 0c57 0c42 0c45! 0load0 0c48 0u14! 0u3 0Gc5 0Gc13 0u6 0c41 0Gflat1 0n12! 0n02 0c50! 0Sload4 0z1 0Tn10 0n22! 0n1e0 0c46 0u1! 0Tn1e0 0n0e0 0Gc9 0e0! 0s3 0Tu2 0Tn20 0u8! 0Tn00 0n2e0 0Gflat2 0n1o0 0Tn0e0 0zz3! 0Tn2e0 0Tu3 0u12! 0zz4 0d20 0Gc17 0n0o0 0u5! 0n2o0 0e1 0Ylate0 0c53 0Ylate1 0Tu6 0s1! 0c51 1Gr0 0Gz0 0Gc14
+1x40! 1x50 1Gr1 0Gc6 0Gc12 1x10 1x00! 1Ta20 0Gzz0 1x30 1x20! 1Ta00 0Gc7 1x70 1x90! 1Ta10 1a0w1 1x60! 1x80 1Thb00 1a0w0 0u19! 1a0z0 1Ta30 1a2w1 0u7! 1a1w0 1a1w1 1a0c0 0u16! 0late0! 0u26! 1a0s0 0Tu5 0u18! 1a2w0 1a3w0 1Ta0c0 1a2z0 1a1z0 1we2! 1we1 0u15! 1we0 1wa2! 1wo0 1wo2! 1wo1 0s4! 1wa1 1Thb10 1wb2! 1Twe0 1wa0 0u22! 1wb0 1Two0 0u20! 1wb1 0n1o1! 1a1s0 1Twa0 1Sa0c0 0u24! 1Twb0 0u17! 0u11! 1a1c0 0Tu4 0n2o1! 1a2s0 0u21! 1Ta1c0 1r0 1wt1! 1a3w1 1r2 1r1 0u9! 1a2c0 1Tra0 1Tr0 1wt0! 1Thb20 1Ta0c1 1Ts0 1a3z0 0u23! 1r3 1Ta2c0 0n0o1! 1r4 1a3c0 1Sa1c0 1p0! 1Gc0 1a3s0 1Ta3c1 1Ta1c1 1Th0 0d1 1a1c1 1Ta3c0 0z2 1s0 1a0c1 1sp0 1Sa2c0 1h0 1Gg0 1p1 1Tn00 0e2 1s00! 1Ta2c1 1Tu0 1Sa3c0 1n00 1s10! 1a2c1 1a3c1 1n01 1Tn10 1s01 1Tn20 1p2 1n02! 1Tu2 1n10 1s11 1n20 1u0! 1n11 0u25 1u2! 1n21 1Tu1 1n12! 1n0e0 1n22! 1n0e1 1Tn11 1n1e1 1Tn01 1Tn0e0 1n1e0 1u1! 1Tn0e1 1n2e0 1p3! 1n2e1 1Tn1e0 1v0 1Tn1e1 1q0! 1Tn21 1Tn2e0 1Tn2e1 1n0o0! 1Tsw0 1s02 1n1o0 1Gq0 1Svs0 1n2o0 1s12 1sw0 1l00 1Svs1 2Gr1 1l10
+2x00! 2x10 2x30! 2x20 2Ta00 2x70! 2x60 1Xq0 2Ta10 1Xc0 2x40! 2a0w1 2x50 1Ti1 1Tj0 1Ti0 1Tk0 1i0! 1f0! 2a0z0 1vs0 1Ti2 2Ta20 1in0 2a1w1 2a0c0 1g0! 1in1 2a0s0 1Gg1 1in2! 2x80! 2a0w0 2a1z0 2Ta0c0 2a1w0 1k0 1ine1 1ine0 2x90! 2a1s0 2Gr0 1Tin0 1Tine0 1Tine1 1Tg0 2a2w1 2a1c0 1ino0 2a2w0 2Ta1c0 2a2z0 2x100! 2x110 2Ta30 2Sa0c0 1f2! 2a2s0 2Sa1c0 1j0! 1f1! 2a2c0 2Ta1c1 1Tk1 1l01 2Ta0c1 1l11 1g2! 2Ta2c0 1ino1! 2b0 1k1! 2a3w0 1g1! 2b2 2a0c1 2a3w1 2b1 2a3z0 2a1c1 2wo2! 2Thb11 2Ta3c1 2we2! 2Thb01 2we0 2we1 2wa2! 2Tn00 2wo1 2Thb10 2wb2! 2wo0 2Twe0 2Sa2c0 2wa1 2wa0 2b3! 2Two0 2wb1 2wb0 2Twa0 2wt1! 2a3s0 2a3c0 2Twb0 2Ta2c1 2Tu0 2r0 2u0! 1k2 2Ta3c0 2a2c1 2wt0! 2Tra0 2r2 2r1 2n00 2Tn10 2Tr0 2n01 1k3 2Sa3c0 2n10 2Ts0 2n02! 2Tu1 2r3 2Thb00 2a3c1 2n11 2p0! 2r4 2Tn20 2u1 2n12 2Th0 2n0e0 2Tu2 2n0e2 2Tn11 2Tn01 2n20 2Tn0e0 2n1e2 2Thb20 2Thb21 2n1e0 2sp0! 2h0 2n21 2Gg0 2u2 2n0e1 2n22! 2n1e1 2p1 2s10! 2Tn0e1 2s00 2Tn0e2 2Tn1e0 2Tn1e1 2p2 2Tn1e2 2n2e0 2n2e1 2q0! 2n2e2 2Tn21 2p3! 2Tn2e0 2s0 2Tn2e1 2n1o0! 2s01 2n0o0! 2Tn2e2 2v0 2Gq0 2s02 2s11 2Svs1 2n2o0 2Gc0 2s12 2l00 2Svs0 2l10
+3x10! 3x00 3x30! 2vs0 3x20 3Ta00 2Xq0 2Tsw0 3x50! 2Ti0 2g0 2Ti1 3x40 2Tj0 2Gg1 3Ta10 3x70! 2in0 3a0w1 3Gr1 2i0! 2sw0 3x60! 2in1 3a0z0 2Ti2 3Gr0 2l01 2Tg0 2in2 3a0s0 2f0! 2Xc0 2ine1 2ine0 2Tin0 2ine2 3x80! 3a1w1 2Tine0 3a0c0 2Tine1 2Tine2 3Ta20 3a1z0 3x90! 3a1w0 2ino0 3a1s0 3x100! 3x110 3Ta0c0 3a2w1 3a1c0 2Tk0 3Sa0c0 3a2z0 2j0! 3Ta30 3a2w0 3a0w0 2g2! 3a2c0 2f2! 2f1! 3Ta1c0 3a2s0 2ino1! 3b0 3Ta0c1 3a3w0 3Ta2c0 2k0 3b2 3a3w1 2k1! 3b1 2g1! 3Sa1c0 2l11 3a0c1 3we2! 3a3z0 3wo2! 3we1 3wa2! 2Tk1 3we0 3wb2! 3Thb10 3Ta1c1 3wo0 3wo1 3Sa2c0 3Twe0 3wa1 3b3! 3wa0 3Two0 3wb1 3wb0 3wt0! 3Twa0 3a3c0 3Twb0 3Ta2c1 3a1c1 3Ta3c1 3a3s0 3Tn00 3Tu0 3r0 2k2 3Ta3c0 3a2c1 3u0! 3r1 3r2 3wt1! 3n00 2k3 3Tn10 3Tra0 3n01 3Tr0 3Sa3c0 3n10 3Thb21 3n02! 3Thb01 3Ts0 3r3 3Thb00 3n11 3Thb02 3a3c1 3Th0 3p0! 3sp0 3n12 3Tn20 3n0e0 3Tu2 3n0e3 3Tu1 3h0 3n1e3 3n20 3n0e2 3Thb12 3Thb11 3u1! 3Thb22 3Tn01 3u2 3Tn0e0 3n21 3Thb20 3n0e1 3n22! 3n1e0 3n1e1 3Tn11 3p1 3Tn0e1 3s10! 3Tn0e2 3s00 3Tn0e3 4Gr1 3Tn1e0 3n1e2 3Tn1e1 3p2 3n2e0 3Tn1e2 3Tn1e3 3n2e1 3q0! 3n2e2 3Tn21 3p3! 3Tn2e0 3n2e3 3Tn2e1 3n0o0! 3s01 3Tn2e2 3Gq0 3n1o0! 3v0 3Tn2e3 3s11 3s02 3Svs1 3r4 3n2o0 3s12 3Gc0 3s0 3Svs0 3l00 3Tsw0 3l10
+4x00! 3vs0 3Gg0 4x10 4x60! 3l11 4x20 4Ta00 4x30! 3Xq0 3Ti0 3Ti1 3g0 4x50! 4a0w1 4Ta10 3l01 3Gg1 3in0 4a0z0 3i0 3sw0 3in1 4x40 3Tj0 3in2! 3Ti2 4x70! 4Gr0 3Tg0 4x90! 3ine0 3Xc0 3ine1 3ine2 3ine3 3Tin0 3Tine0 3Tine1 4a1w1 3Tine2 4x80! 4a0s0 3Tine3 4Ta20 4a1z0 4a0c0 3f0! 3ino0 4a1s0 4x100! 4Ta0c0 4x110 3f2! 4a2w1 3Tk0 3j0! 4a1c0 4Sa0c0 3Tk1 4Ta30 4a2z0 3g1! 4a0w0 3ino1! 4a2w0 3g2! 4a1w0 4a2s0 4Ta1c0 4a2c0 4Ta0c1 4a3w0 4b0 4Ta2c0 3k0 4a3w1 4b2 3k1! 4b1 4Sa1c0 4a3z0 4a0c1 4we2! 4we1 4wb2! 4we0 4wo2! 4wo0 4Ta3c1 4wa2! 4Ta1c1 4wo1 4b3! 4Twe0 4wb0 3f1! 4wa0 4Two0 4wa1 4wb1 4a3s0 4Twa0 4Sa2c0 4Twb0 4wt1! 4a1c1 4a3c0 4Tn00 4Tu0 4wt0! 4r0 4Ta2c1 3k2 4Ta3c0 4n00 4u0! 4r1 4r2 4n01 4a2c1 4Tra0 3k3 4Tr0 4n02 4Sa3c0 4Thb01 4Tn10 4Thb00 4Thb02 4r3 4Thb22 4a3c1 4Ts0 4n0e0 4p0! 4Thb20 4Thb10 4Thb12 4n10 4Tn20 4n0e2 4Tu1 4n0e4 4Thb11 4Th0 4n11 4n0e3 4Tu2 4n20 4Thb13 4Thb23 4n12 4Thb03 4Tn01 4u2! 4sp0 4Thb21 4Gg0 4n21 4u1 4Tn11 4Tn0e0 4h0 4n22! 4n1e2 4n0e1 4s00! 4p1 4n1e0 4s10! 4Tn0e1 4n1e4 4Tn0e2 4n1e1 4Tn0e3 4p2 4Tn0e4 4n1e3 4Tn1e0 4Tn1e1 4n2e0 4Tn1e2 4p3! 4n2e1 4Tn1e3 4Tn1e4 4q0! 4n2e2 4Tn21 4Tn2e0 4n0o0! 4n2e3 4Tn2e1 4Gq0 4n1o0! 4n2e4 4Tn2e2 4s01 4Tn2e3 4v0 4Tn2e4 4s11 4s02 4Svs1 4s0 4n2o0 4r4 4Tsw0 4s12 4Svs0 4l00 4Gc0 4l10
+5x00! 5x10 5x70! 4vs0 5x30 5Ta00 5x20! 4Xq0 4Ti0 4Ti1 4g0 4Tj0 5a0w1 5x60! 4in0 4Gg1 5Ta10 4i0 5a0z0 4in1 5x40 4in2! 5x50! 4Ti2 5Gr0 4Tg0 4ine0 4ine1 5a1w1 4ine3 5x80! 4ine2 4ine4 4Tin0 4Tine0 5Gr1 4Tine1 4sw0 4Xc0 4Tine2 5a1z0 4Tine3 4Tine4 5a0c0 5Ta20 5x90! 5a0s0 4f0! 4ino0 5a1c0 4Tk1 4Tk0 5x100 5x110! 5Ta0c0 5a2w1 4f2! 5a1s0 4j0! 5Ta30 4k0 5a2z0 5a0w0 4g1! 5a1w0 4f1! 5a2w0 5a2s0 5Ta1c0 4g2! 4k1! 5Sa0c0 5a2c0 4ino1! 5Ta0c1 5Sa1c0 4l01 5b0 5Ta2c0 5a3w0 5b2 5a3w1 5b1 4l11 5a3z0 5wa2! 5we1 5wb2! 5wb0 5we0 5we2! 5Ta1c1 5wo2! 5Thb24 5wo1 5Thb12 5b3! 5Thb11 5Twe0 5wo0 5wb1 5wt0! 5wa0 5Two0 5wa1 5a0c1 5a1c1 5Twa0 5Sa2c0 5a3c0 5Twb0 5Tn00 5a3s0 5Tu0 5Ta2c1 5Thb04 5r0 5Ta3c1 5u0! 5n00 5Ta3c0 4k2 5r2 5r1 5n01 5a2c1 5Tra0 4k3 5Tr0 5n02 5Sa3c0 5r3 5Tn10 5Thb01 5wt1! 5Thb02 5Tu1 5n10 5Tn01 5a3c1 5Thb14 5p0! 5Th0 5n0e4 5Tn20 5n11 5n0e3 5Thb00 5Thb03 5n0e0 5Ts0 5n12 5Tu2 5h0 5Tn0e0 5n20 5Thb22 5n0e1 5u2! 5u1! 5n1e4 5n21 5n1e0 5Thb10 5n0e2 5Thb13 5Thb20 5Thb21 5n22! 5Tn11 5n0e5 5Tn0e1 5Thb23 5p1 5Tn0e2 5s10! 5Tn0e3 5sp0 5Tn0e4 5n1e1 6Gr1 5Tn0e5 5n1e2 5Tn1e0 5p2 5n2e0 5s00! 5n2e1 5q0! 5n2e3 5Tn21 5Tn2e0 5p3! 5n2e2 5Tn1e1 5Tn2e1 5n0o0! 5n2e4 5Gq0 5n2e5 5Tn2e2 5Tn2e3 5n1e3 5Tn1e2 5Tn2e4 5n1e5 5Tn2e5 5s01 5Tn1e3 5v0 5Tn1e4 5Tn1e5 6Gr0 5n2o0! 5s11 5s02 5Svs1 5n1o0 5r4 5s12 5l00 5Svs0 5s0 5Gc0 5l10 5Tsw0
+6x10! 6x00 5Gg0 6x20! 5vs0 6x30 6Ta00 5Xq0 6x40! 5Ti0 5Ti1 5g0 6Ta10 6a0w1 5sw0 5Gg1 5in0 6a0z0 5i0 5in1 6x60! 6x50 5Tj0 5Ti2 5in2! 6x70! 5Tg0 5ine1 5ine0 5f0! 5ine3 5ine2 5ine4 5Tin0 5Tine0 5Tine1 5ine5 5Tine2 5Xc0 6a0c0 5Tine3 5Tine4 5Tine5 6x90! 6Ta20 6a1w1 6a0s0 5ino0 6a1z0 6x80 6x110! 5Tk0 6a1c0 6Ta0c0 6x100! 6a2w1 6a1w0 6a0w0 5j0! 6a2w0 5g2! 6Ta30 5f2! 6a2z0 6a1s0 5f1! 6a2c0 6Ta1c0 6Sa0c0 5k0 6a2s0 5g1! 5k1! 6b0 6a3w0 6Ta2c0 6b2 6a3w1 6b1 6a3z0 6we0 6we2! 6we1 6wb2! 6wo0 6wo2! 6wo1 6wa2! 6Twe0 6wa0 6Sa1c0 6wa1 6b3! 6Two0 6wb0 6Sa2c0 6wb1 5ino1! 6Twa0 6a3c0 6wt1! 6Twb0 6Ta0c1 6a3s0 6Ta2c1 6Ta1c1 6wt0! 5l01 6r0 6Ta3c0 6r2 6r1 5l11 6Tra0 6Tr0 6Sa3c0 6Tz3 6r3 6a0c1 6s0 6p0! 6a2c1 6a1c1 6Ta3c1 6Tz1 6Ts0 6a3c1 6Th0 6z3 6Tz2 6Tz0 6h0 6sp0! 6p1 6s10! 6z0 6Tp0 6z1 6Tu2 6s00! 6z2 6Tu1 6p2 6s11 6Tu0 6p3! 6q0 6s01 6u2! 6v0 6u1! 6Gq0 6Tsw0 6s12 6s02 6Svs0 6sw0 6u0! 6Svs1 6y0 6y1! 6vs0 6j0 6Xq0 6j1 6Yj0 6Sj0
 """
 
 
@@ -693,8 +724,11 @@ def rank_program(g, core, T, topo):
                 r = q.activation(ap(a[0]), ap(a[1]), a[2], bias=ap(a[3]), scale=ap(a[4]), accum_out=ap(a[5]))
             else:
                 r = q.activation(ap(a[0]), ap(a[1]), a[2], bias=ap(a[3]), scale=ap(a[4]))
-        elif k == "gcp":
-            r = q.affine_select(ap(a[0]), ap(a[1]), [[0, width(a[0])]], ALU.is_ge, 0.0, 0, 0)
+        elif k == "side":
+            if a[2] is None:
+                r = q.affine_select(ap(a[0]), ap(a[1]), [[0, width(a[0])]], ALU.is_ge, 0.0, 0, 0)
+            else:
+                r = q.affine_select(ap(a[0]), ap(a[1]), [[-1, width(a[0])]], ALU.not_equal, a[2], -a[3], 1)
         elif k == "iota":
             if SCRATCH[a[0][0]][2] == I32:
                 r = q.iota(ap(a[0]), a[1], a[2], a[3])

from concourse.bass import DstId, RemoteDMATransfer
from concourse.mybir import AluOpType as ALU, AxisListType, ActivationFunctionType as ACT

NS = 6
F32, BF, F16, I32, U16 = "float32", "bfloat16", "float16", "int32", "uint16"
DEAD = 288
TW = 296
ZR = 256
NONE = 2 ** 18
BIG, LOWER = 32768.0, -16384.0
LOW = 254.0 * 4096
HALF = 2.0 ** 23 - 0.5

SB = {
    "NB": (4096, I32), "QT": (4112, BF), "LH": (16, F32), "SI": (256, I32), "UI": (1536, I32), "CI": (1536, I32),
    "S0F": (256, F32), "U8": (1536, BF), "CB": (1536, BF), "TH": (288, F32), "UB": (1576, F32), "UA": (32, F32),
    "PI": (1, I32), "PJ": (4, I32), "PF": (12, F32), "GQ": (144, F32), "IQ": (144, F32), "C16": (48, F32),
    "IOT": (256, F32), "IA": (32, F32), "TMP": (64, F32), "T1": (128, F32), "T2": (128, F32), "PK": (256, F32), "PKE": (2, F32),
    "EWB": (144, BF), "E0B": (144, F16), "EW16": (144, F16), "BO32": (144, F32), "BOB": (128, BF), "BO16": (128, F16),
    "RM": (16, F32), "UH": (5 * 144, F16), "US": (5 * 128, F32), "I32W": (144, F32), "IBW": (144, BF), "IMW": (144, BF),
    "IR16": (128, F16), "EWR": (128, F16), "DIT": (128, F16), "EW32": (144, F32), "EWR32": (128, F32), "M32": (64, F32),
    "I16F": (128, F16), "I296": (128, BF), "I592": (128, BF), "R16": (128, F16), "R4096": (128, BF), "DIF": (128, BF),
    "THR": (1, F32), "DG": (128, BF), "TBZ": (128, BF), "TBR": (128, BF), "RS48": (48, F32), "RSX": (1536, BF),
    "CIL": (18, F16), "G8": (128, BF), "G832": (128, F32), "E8": (144, BF), "ZERO": (DEAD, BF), "JC": (2, F32),
    "X": (4608, F16), "CMP": (4608, BF), "Y": (288, F32), "GE": (288, BF), "M": (288, F16), "SC": (320, F32), "LW": (20, U16),
    "NK": (320, F16), "NKP": (288, F16), "NF": (TW, F32), "EQ": (6 * 320, BF), "OU": (288, U16), "HR": (TW, F32), "WR": (TW, F32),
    "W": (3 * TW, F32), "WP": (256, F32), "WA": (32, F32), "WB": (32, F32), "HT": (TW, F32), "HC": (288, F16),
    "FL": (768, BF), "FG": (48, BF), "DB": (16, BF), "SN": (48, BF), "E": (48, BF), "M16": (48, BF),
    "PO": (32, U16), "TT": (1584, F32), "IOB": (DEAD, F32), "CBH": (256, F16), "PKD": (256, F16), "SD": (256, F16),
    "SM": (32, F32), "SL": (2, U16), "H2": (2 * DEAD, BF), "CU": (DEAD, BF), "AL": (8, U16), "SV": (8, F32),
    "SRB": (DEAD, BF), "SRC": (16, U16), "WL": (16, U16), "YY": (2 * TW, F32),
    "SC_O": (NS * 8, BF), "SC_I": (NS * 24, BF), "SP_O": (NS * 64, F32), "SP_I": (NS * 64, F32),
}
SCRATCH = {k: ("sbuf", [128, v[0]], v[1]) for k, v in SB.items()}
for _k in range(8):
    SCRATCH["K%d" % _k] = ("psum", [128, 512], F32)

NDMA = 10
SEMAPHORES = (["ev", "es", "et", "eg", "sent"] + ["d%d" % i for i in range(NDMA)]
              + ["rc%d" % t for t in range(NS - 1)] + ["rp%d" % t for t in range(NS)])

PIECES = [(a, a + 32) for a in range(0, 192, 32)] + [(a, a + 16) for a in range(192, 288, 16)]
SUMS, CUT = [(0, 64), (64, 128), (128, 224), (224, 288)], [32, 32, 48, 32]
NEAR, HIST, LISTS = [(0, 128), (128, 192), (192, 288)], [(0, 128), (128, 224), (224, 288)], [(0, 64), (64, 256)]
BANKS = ["hb00 hb01 hb03 votes1 rotw", "hb20 hb22 hb23 p153 hw hb21", "fl rank col cnt hb10 hb11 hb12 hb13 hb24",
         "hb14 p152 sb ht0 ht1 one0", "hb04 p150 l votes2 one2 hn1", "hn2 of2 one3 votes3 ha", "roth votes0 of0 hn0 ofa",
         "hb02 p151 one1 ht2 of1"]


FIRST = [(0, 64), (64, 128), (128, 192), (192, 256)]
FQ = 4


def places():
    wide = dict(fl=48, rank=34, cnt=2, sb=16, l=16, rotw=32, roth=32, hw=32, ha=160, ofa=32, col=16)
    for names, pieces in ((("p15", "votes", "one"), SUMS), (("hn", "of"), NEAR), (("ht",), HIST)):
        wide.update({n + str(i): b - a for n in names for i, (a, b) in enumerate(pieces)})
    wide.update({"hb%d%d" % (i, p): b - a for i, (a, b) in enumerate(NEAR) for p in range(NS - 1)})
    at = {}
    for bank, names in enumerate(BANKS):
        c = 0
        for n in names.split():
            at[n] = (bank, c, wide[n])
            c += wide[n]
        assert c <= 512
    assert sorted(at) == sorted(wide)
    return at


def A(name, c0=0, c1=None, step=1, p1=128):
    if c1 is None:
        c1 = SCRATCH[name][1][1]
    return (name, 0, p1, c0, c1, step, 1)


def IND(win, off):
    return ("@", win, off)


def width(a):
    if a[0] == "@":
        return 16 * width(a[2])
    return (a[4] - a[3] + a[5] - 1) // a[5]


def is_ap(a):
    return isinstance(a, tuple)


def landing(kind, t, src, d):
    if kind == "c":
        return A("SC_I", 24 * t + 8 * (d - 1), 24 * t + 8 * (d - 1) + 2)
    return (src[0][:3] + "I",) + src[1:]


def plan():
    ops, now, tag, B = [], [-1], ["", {}], places()

    def at(name):
        tag[0] = name

    def add(eng, kind, args, outs, ins):
        rd, wr = [], []
        for a in ins:
            if is_ap(a):
                rd += [a[1], a[2]] if a[0] == "@" else [a]
        for a in outs:
            if a[0] == "@":
                wr.append(a[1])
                rd.append(a[2])
            else:
                wr.append(a)
        key = (now[0], eng, tag[0])
        tag[1][key] = tag[1].get(key, -1) + 1
        name = "%d%s%s%d" % (now[0] + 1, "" if eng == "v" else eng.upper(), tag[0], tag[1][key])
        ops.append(dict(step=now[0], eng=eng, kind=kind, args=args, rd=rd, wr=wr, id=name))
        return ops[-1]

    def cp(out, in_):
        add("v", "cp", (out, in_), [out], [in_])

    def tt(out, a, b, op):
        add("v", "tt", (out, a, b, op), [out], [a, b])

    def ts(out, a, s1, op0, s2=None, op1=None):
        add("v", "ts", (out, a, s1, s2, op0, op1), [out], [a, s1, s2])

    def scan(out, d0, d1, op0, op1, first=0.0):
        add("v", "scan", (out, d0, d1, op0, op1, first), [out], [d0, d1])

    def mset(out, c):
        add("v", "mset", (out, c), [out], [])

    def act(out, in_, func, bias=0.0, scale=1.0, total=None):
        sums = [total] if total else []
        add("s", "act", (out, in_, func, bias, scale) + tuple(sums), [out] + sums, [in_, bias, scale])

    def move(out, in_, bias=0.0, scale=1.0):
        if bias == 0.0 and scale == 1.0:
            cp(out, in_)
        elif scale == 1.0:
            ts(out, in_, bias, ALU.add)
        elif bias == 0.0:
            ts(out, in_, scale, ALU.mult)
        else:
            ts(out, in_, scale, ALU.mult, bias, ALU.add)
        ops[-1]["alt"] = (out, in_, ACT.Identity, bias, scale)

    def scatter(win, off, in_):
        cp(IND(win, off), in_)
        ops[-1]["alt"] = (IND(win, off), in_, ACT.Silu, 0.0, 1.0)

    def iota(out, pat, base=0, ch=0):
        add("g", "iota", (out, pat, base, ch), [out], [])

    def side(out, in_, c=None, first=0):
        add("g", "side", (out, in_, c, first), [out], [in_])

    def fill(out, c):
        iota(out, [[0, width(out)]], c)

    def mm(items, start=True, stop=True):
        add("t", "mm", (items, start, stop), [o for o, l, r in items], [x for o, l, r in items for x in (l, r)])

    def dma(eng, out, in_):
        add(eng, "dma", (out, in_), [out] if out[0] != "out" else [], [in_] if in_[0] != "in" else [])

    def send(kind, t, src, land):
        tok = ("tok%s%d" % (kind, t), 0, 128, 0, 1, 1, 1)
        add("g", "send", (kind, t, src), [tok], [src])
        add("x", "recv", (kind, t), [land], [tok])

    def K(b, c0, c1):
        if is_ap(b):
            b, c0, c1 = b[0], b[1] + c0, b[1] + c1
        return A("K%d" % b, c0, c1)

    sel = lambda r: A("EWB", 15 - r, 143 - r)
    sel0 = lambda r: A("E0B", 15 - r, 143 - r)
    uh = lambda r: A("UH", 144 * r + 16, 144 * r + 144)
    col = lambda n, j: A(n, j, j + 1)
    P_, PG, PR, LWB, SLB, HB, NX, SD = [col("PF", j) for j in (0, 1, 2, 3, 4, 5, 8, 10)]
    BO, IW, IB, IQ = A("BO32", 16, 144), A("I32W", 16, 144), A("IBW", 16, 144), A("IQ", 16, 144)
    SRC, WL, IM1 = A("SRC"), A("WL"), A("IMW", 16, 144)
    ha = lambda p: K(B["ha"], 32 * p, 32 * p + 32)
    al = lambda t: A("AL", 2 * (t % 3), 2 * (t % 3) + 2)

    at("load")
    mset(A("LH"), 0.0)
    dma("y", A("NB"), ("in", "nb"))
    for n, s in ((A("SI", p1=8), "s0"), (A("UI", p1=8), "us"), (A("CI", p1=8), "coin"), (A("QT", 0, 4096), "qs"), (A("LH", 8, 14), "hi")):
        dma("s", n, ("in", s))

    at("c")
    iota(A("PI"), [[0, 1]], 0, 1)
    iota(A("GQ", 16, 144), [[16, 8], [0, 16]])
    iota(A("IOT"), [[1, 256]])
    iota(A("C16"), [[0, 3], [1, 16]])
    iota(A("T2", 0, 16), [[16, 16]], -144)
    iota(A("M16", 16, 32), [[16, 16]], 560)
    mset(A("GQ", 0, 16), 112.0)
    move(IQ, A("IOT", 0, 128))
    move(A("IQ", 0, 16), A("IOT", 112, 128))
    ts(col("PJ", 0), A("PI"), 112, ALU.bitwise_and)
    ts(col("PJ", 1), A("PI"), 15, ALU.bitwise_and)
    cp(P_, A("PI"))
    cp(A("PF", 1, 3), A("PJ", 0, 2))
    at("cw")
    move(A("M16", 0, 16), A("T2", 0, 16), PR)
    move(A("IA"), A("IOT", 0, 32), 320.0)
    at("c")
    ts(A("BO32"), A("GQ"), PG, ALU.is_equal)
    side(A("BOB"), BO)
    ts(A("RM"), A("IOT", 0, 16), PR, ALU.is_equal)
    ts(A("I32W"), A("IQ"), P_, ALU.is_equal)
    mset(A("ZERO"), 0.0)
    for n, c in ((IB, 1.0), (IM1, -1.0), (A("I296"), 296.0), (A("I592"), 592.0)):
        side(n, A("ZERO", 0, 128), c)
    side(A("IMW", 0, 16), A("ZERO", 0, 16), -1.0, 112)
    move(A("I16F"), IW)
    ts(A("EWB"), A("IOT", 0, 144), PG, ALU.subtract, 15.0, ALU.is_equal)
    side(A("EW16"), A("EWB"))
    side(A("BO16"), BO)
    move(A("E0B"), A("EWB"), scale=col("RM", 0))
    for p in range(5):
        move(A("UH", 144 * p, 144 * p + 144), A("BO32"), scale=col("RM", p))
    ts(col("PF", 6), PR, 15.0, ALU.add)
    ts(col("PF", 7), PR, -1.0, ALU.add)
    c16 = A("C16", 0, 16)
    ts(A("TMP", 0, 16), c16, PR, ALU.is_equal, LOWER, ALU.mult)
    ts(A("TMP", 16, 32), c16, col("PF", 6), ALU.is_equal, BIG, ALU.mult)
    ts(A("TMP", 32, 48), c16, col("PF", 7), ALU.is_equal, BIG, ALU.mult)
    tt(A("TMP", 48, 64), A("TMP", 0, 16), A("TMP", 16, 32), ALU.add)
    tt(A("PK", 0, 16), A("TMP", 48, 64), A("TMP", 32, 48), ALU.add)
    at("pk")
    for n in (16, 32, 64, 128):
        move(A("PK", n, 2 * n), A("PK", 0, n))
    at("c")
    ts(LWB, col("RM", 0), -BIG, ALU.mult, 2048.0 - LOWER, ALU.add)
    ts(SLB, col("RM", 0), -BIG, ALU.mult, 0.25 - 64.0 - LOWER, ALU.add)
    ts(HB, PR, 6.5, ALU.is_lt, 2049.0, ALU.mult)
    ts(HB, HB, -1.0, ALU.add)
    ts(A("RS48"), A("C16"), 0.5, ALU.is_gt)
    ts(A("SV", 3, 4, p1=8), A("PF", 0, 1, p1=8), 16.0, ALU.mult)
    ts(A("G832", p1=8), A("GQ", 16, 144, p1=8), A("SV", 3, 4, p1=8), ALU.is_equal)
    move(A("G8", p1=8), A("G832", p1=8))
    ts(A("E8", p1=8), A("IOT", 0, 144, p1=8), -15.0, ALU.add, A("SV", 3, 4, p1=8), ALU.is_equal)
    ts(NX, col("RM", 15), -16.0, ALU.mult, P_, ALU.add)
    ts(A("R16"), A("IOT", 0, 128), -1.0, ALU.add, NX, ALU.is_equal)
    move(A("R4096"), A("R16"), scale=4096.0)
    ts(SD, col("RM", 0), -0.5, ALU.add)
    move(A("T1"), A("R16"), scale=SD)
    move(A("T2"), IW, scale=0.5)
    tt(A("DIF"), A("T1"), A("T2"), ALU.add)
    thr = 16 * LOW + 8.5 * 4096
    ts(A("THR"), col("RM", 0), thr + 1.0, ALU.mult, -thr, ALU.add)
    ts(A("GE", 0, 128), IQ, P_, ALU.is_lt, -1.0, ALU.mult)
    tt(A("GE", 128, 256), A("GE", 0, 128), BO, ALU.mult)
    move(A("Y", 0, 128), IW, scale=float(ZR))
    tt(A("TBZ"), A("GE", 128, 256), A("Y", 0, 128), ALU.add)
    ts(A("DG"), IW, PR, ALU.mult, -1.0, ALU.mult)
    tt(A("TBR"), A("GE", 128, 256), A("DG"), ALU.add)
    move(A("M16", 32, 48), A("M16", 0, 16))
    move(A("CIL", 0, 16), A("M16", 0, 16), 704.0)
    mset(A("CIL", 16, 18), 0.0)
    act(A("IOB", 0, 256), A("IOT"), ACT.Silu, 64.0)
    mset(A("QT", 4096, 4112), 0.0)
    for j in range(256, 888, TW):
        mset(A("W", j, j + 40), 0.0)
    mset(A("HT", 256, TW), -4096.0)
    mset(A("NF", 256, TW), 2048.0)
    for p in range(4):
        side(A("US", 128 * p, 128 * p + 128), A("UH", 144 * p + 144, 144 * p + 272))
    move(A("US", 512, 640), A("BO32", 0, 128), scale=col("RM", 5))
    mset(A("UB", 1536, 1576), 0.0)
    mset(A("SC_O"), 0.0)
    at("d")
    ts(A("JC"), A("IOT", 0, 32, 16), PR, ALU.add, -1.0, ALU.mult)
    ts(A("JC"), A("JC"), -0.5, ALU.add)
    at("e")
    move(A("PKD"), A("PK"), scale=1.0 / 32)
    move(col("PKE", 0), col("PK", 15), scale=1.0 / 32)
    ts(col("PKE", 1), col("RM", 0), -BIG / 32, ALU.mult, 144.25 - LOWER / 32, ALU.add)
    at("d2")
    mset(A("SRB", 256, DEAD), float(NONE))
    at("z")
    side(A("IR16"), A("I32W", 0, 128))
    ts(A("EWR"), A("IQ", 0, 128), PG, ALU.subtract, float(NS), ALU.is_equal)
    mset(A("HR", DEAD, TW), -1.0)
    mset(A("WR", DEAD, TW), 0.0)
    at("zz")
    side(A("EW32"), A("EWB"))
    side(A("EWR32"), A("EWR"))
    ts(col("PF", 9), col("RM", 0), 16.0, ALU.mult, P_, ALU.add)
    ts(A("Y", 128, 256), A("IOT", 0, 128), 1.0, ALU.add, col("PF", 9), ALU.is_equal)
    ts(col("PF", 11), col("RM", 1), -0.5, ALU.add)
    move(A("T1"), A("Y", 128, 256), scale=col("PF", 11))
    tt(A("DIT"), A("T1"), A("T2"), ALU.add)
    at("flat")
    iota(A("RSX"), [[0, 96], [8192, 16]], int(LOW))
    fill(A("TH"), 9)
    fill(A("TT", 0, ZR), 208)

    at("s")
    move(A("S0F", p1=8), A("SI", p1=8), -2048.0)
    k0 = K(0, 0, 256)
    mm([(k0, A("G832", p1=8), A("S0F", p1=8))])
    move(A("HC", 0, 256), k0, scale=col("RM", 0))
    dead = A("EQ", 320, 576)
    ts(dead, k0, -2048.5, ALU.is_lt)
    add("v", "red", (col("SV", 2), dead), [col("SV", 2)], [dead])
    move(col("SC_O", 1), col("SV", 2))
    at("u")
    for j in range(0, 1536, 256):
        move(A("U8", j, j + 256, p1=8), A("UI", j, j + 256, p1=8))
        k = K(3 + j // 256 % 2, 256, 512)
        mm([(k, A("G8", p1=8), A("U8", j, j + 256, p1=8))])
        move(A("UB", j, j + 256), k, scale=-(1 + 2.0 ** -21) / 256)
    for j in range(0, 1536, 512):
        move(A("CB", j, j + 512, p1=8), A("CI", j, j + 512, p1=8))
    mm([(K(5, 0, 96), A("E8", 15 - r, 143 - r, p1=8), A("CB", r, 1536, 16, p1=8)) for r in range(16)])
    for t in range(NS):
        move(A("TH", 48 * t, 48 * t + 16), K(5, 16 * t, 16 * t + 16), 9.0, 100.0)
        move(A("TH", 48 * t + 32, 48 * t + 48), K(5, 16 * t, 16 * t + 16), 109.0, -100.0)

    def neighbours(t, a, b, hb, of, out):
        lw, nk = A("LW", a // 16, b // 16), A("NK", a, b)
        scan(A("SC", a, b), hb(t + 1), A("PK", 0, b - a), ALU.min, ALU.add, BIG)
        ts(lw, A("SC", a + 15, b, 16), LWB, ALU.add, 4095.0, ALU.min)
        move(nk, IND(A("NB"), lw), -2048.0)
        mm([(K(of, 0, b - a), A("R4096"), A("EQ", 320 + a, 320 + b))] * (t < 0 and a < 256) + [(K(of, 0, b - a), A("R16"), nk)], True, False)
        name = tag[0]
        at(name + "e")
        for p in range(t + 1, -1, -1):
            eq = A("EQ", 320 * p + a, 320 * p + b)
            tt(eq, nk, hb(p), ALU.is_equal)
            mm([(K(of, 0, b - a), A("R4096"), eq)], False, p == 0)
        at(name + "o")
        if out is not None:
            ts(A("OU", out, out + b - a), K(of, 0, b - a), 2048.0, ALU.add, 4096.0, ALU.min)
            move(A("NKP", out, out + b - a), K(of, 0, b - a))
        else:
            move(A("NF", a, b), K(of, 0, b - a))

    def chosen(k, a, b, l16, l32):
        late = (SUMS if now[0] else FIRST)[-1][0]
        c = max(a, min(b, late))
        return [(K(k, 0, c - a), l16, A("M", a, c))] * (a < c) + [(K(k, c - a, b - a), l32, A("M32", c - late, b - late))] * (c < b)

    def own(t):
        for h, (a, b) in enumerate(NEAR):
            b = b if t > 0 else min(b, 256)
            if a == b:
                continue
            hb = lambda p: K(B["hb%d%d" % (h, p)], 0, b - a)
            at("hb%d" % h)
            for p in range(t + 1):
                mm([(hb(p), uh(p), A("HC", a, b))])
            at("n%d" % h)
            hn = K(B["hn%d" % h], 0, b - a) if t >= 0 else K(0, a, b)
            if t >= 0:
                mm(chosen(B["hn%d" % h], a, b, A("BO16"), BO))
            neighbours(t, a, b, lambda p: hn if p == t + 1 else hb(p), B["of%d" % h], a if t < 0 else None)

    own(-1)
    at("late")
    dma("y", A("WP"), ("in", "w0"))
    ops[-1]["rd"].append(A("OU", 0, 16))
    dma("y", A("LH", 0, 6), ("in", "lo"))
    move(A("LH", 0, 9, 8), A("LH", 0, 9, 8), scale=2048.0)

    for t in range(NS):
        last = t == NS - 1
        now[0] = t
        for i, (a, b) in enumerate(PIECES):
            if a < 256 or t:
                at("x%d" % i)
                move(A("X", 16 * a, 16 * b), IND(A("QT"), A("OU", a, b)))
        for i, (a, b) in enumerate(SUMS if t else FIRST):
            c = min(b, 256)
            p15, votes, one = B["p15%d" % i], K(B["votes%d" % i], 0, b - a), K(B["one%d" % i], 0, b - a)
            at("a%d" % i)
            mm([(K(p15, 0, b - a), A("I16F"), A("X", 16 * a + j, 16 * b, 16)) for j in range(16)])
            at("a%dw" % i)
            if a < c:
                tt(A("W", a, c), A("WP", a, c), K(p15, 0, c - a), ALU.mult)
                tt(A("Y", a, c), A("UB", 256 * t + a, 256 * t + c), K(p15, 0, c - a), ALU.mult)
            if c < b:
                at("b")
                tt(A("WB"), A("WA"), K(p15, c - a, b - a), ALU.mult)
                cp(IND(A("W", 0, DEAD), al(t - 1)), A("WB"))
                tt(A("Y", c, b), A("UA"), K(p15, c - a, b - a), ALU.mult)
                move(A("W", 256, DEAD), A("WB"))
            at("a%dz" % i)
            ts(A("X", 16 * a, 16 * b, 16), A("Y", a, b), -HALF, ALU.add, 2.0 ** 23 + 2048, ALU.add)
            at("a%dc" % i)
            for d in range(a, b, CUT[i]):
                e = min(d + CUT[i], b)
                scan(A("CMP", 16 * d, 16 * e), A("RSX", 0, 16 * (e - d)), A("X", 16 * d, 16 * e), ALU.min, ALU.add, 2 * LOW)
                at("a%ds" % i)
            at("a%dc" % i)
            mm([(votes, sel(s), A("CMP", 16 * a + s, 16 * b, 16)) for s in range(1, 16)])
            act(A("GE", a, b), votes, ACT.Sign, A("THR"))
            if i < len(SUMS) - 1:
                mm([(one, A("DIF"), A("GE", a, b))])
                tt(A("M", a, b), A("NKP", a, b), one, ALU.mult)
            else:
                mm([(one, A("DIT"), A("NKP", a, b))])
                tt(A("M32", 0, b - a), A("GE", a, b), one, ALU.mult)
        fl, rk = B["fl"], B["rank"]
        for h in range(FQ):
            at("w" + "eoab"[h])
            n = 256 // FQ
            f = lambda j: A("FL", n * (3 * h + j), n * (3 * h + j + 1))
            ts(f(0), A("W", h, 256, FQ), col("LH", t), ALU.is_lt)
            ts(f(1), A("W", h, 256, FQ), col("LH", 8 + t), ALU.is_gt)
            ts(f(2), A("W", h, 256, FQ), 0.0, ALU.is_equal)
            ops[-1]["alt"] = (f(2), A("W", h, 256, FQ), ACT.Relu, 1.0, -2.0 ** 85)
            mm([(K(fl, 0, 48), sel(FQ * r + h), A("FL", 3 * n * h + r, 3 * n * (h + 1), 16 // FQ)) for r in range(16 // FQ)], h == 0, h == FQ - 1)
        at("wt")
        c = DEAD if t else 256
        move(A("W", TW, TW + c), A("W", 0, c), scale=2.0)
        move(A("W", 2 * TW, 2 * TW + c), A("W", 0, c), scale=0.5)
        at("r")
        tt(A("FG"), K(fl, 0, 48), A("TH", 48 * t, 48 * t + 48), ALU.is_ge)
        HIGH, HOLES = A("FG", 16, 32), (0, 32)
        scan(A("SN"), A("RS48"), A("FG"), ALU.mult, ALU.add)
        tt(A("E"), A("FG"), A("M16"), ALU.mult)
        k = K(rk, 16, 32)
        at("ra")
        mm([(K(rk, 16, 34), A("I16F"), A("CIL")), (k, A("TBR"), HIGH)], True, False)
        at("r")
        mm([(k, IM1, A("E", 16, 32)), (k, A("BOB"), A("SN", 16, 32)),
            (K(rk, 32, 34), A("BOB"), A("SN", 15, 32, 16)), (K(rk, 32, 33), A("BOB"), col("SN", 47))], False, True)
        ts(A("PO", 16, 32), k, K(rk, 32, 33), ALU.subtract, 255.0, ALU.add)
        DD = col("SC_O", 8 * t)
        if not last:
            ts(DD, K(rk, 32, 33), K(rk, 33, 34), ALU.subtract)
        at("h")
        k = K(rk, 0, 16)
        mm([x for j in HOLES for x in ((k, A("BOB"), A("SN", j, j + 16)), (k, A("TBZ"), A("FG", j, j + 16)))])
        ts(A("PO", 0, 16), k, K(rk, 32, 33), ALU.subtract, 255.0, ALU.add)
        at("r")
        at("r")
        fill(A("TT", ZR, ZR + 256), 208 + NONE)
        fill(A("TT", ZR + 256, ZR + 288), 64 + DEAD)
        at("p")
        scatter(A("TT", ZR, ZR + 1328), A("PO", 16, 32), A("IOB", 0, 256))
        scan(A("SM"), A("TT", ZR + 256, ZR + 288), A("PK", 0, 32), ALU.min, ALU.add, BIG)
        if last:
            mm([(K(B["hw"], 0, 2), A("I32W", 0, 128), A("SM", 15, 32, 16))])
        ts(A("SL"), K(B["hw"], 0, 2) if last else A("SM", 15, 32, 16), SLB, ALU.add)
        at("u")
        for i, (a, b) in enumerate(HIST):
            b = b if t else min(b, 256)
            if a == b:
                continue
            k = K(B["ht%d" % i], 0, b - a)
            mm([(k, A("I16F"), A("HC", a, b))] + chosen(B["ht%d" % i], a, b, A("EW16", 14 - t, 142 - t), A("EW32", 14 - t, 142 - t)))
            move(A("HT", a, b), k)
        if last:
            at("z")
            for a, b in HIST:
                mm([(K(0, a, b), A("IR16"), A("HC", a, b))] + chosen((0, a), a, b, A("EWR"), A("EWR32")))
                ts(A("HR", a, b), K(0, a, b), HB, ALU.add, -1.0, ALU.max)
            mm([(K(1, 0, DEAD), A("I32W", 0, 128), A("W", 0, DEAD))])
            move(A("WR", 0, DEAD), K(1, 0, DEAD), scale=0.5)
        at("p")
        po = 64 * t
        move(A("SP_O", po, po + 32), IND(A("WR") if last else A("W", 0, TW), A("SL")), scale=1.0 if last else 2.0 ** (-12 if t else -23))
        at("q")
        move(A("SP_O", po + 32, po + 64), IND(A("HR" if last else "HT"), A("SL")))
        for kind in ("p" if last else "pc" if t else "cp"):
            at("q" if kind == "p" else "c")
            if kind == "c":
                send("c", t, A("SC_O", 8 * t, 8 * t + 2), A("SC_I", 24 * t, 24 * t + 24))
            else:
                send("p", t, A("SP_O", po, po + 64), A("SP_I", po, po + 64))
        if not last:
            ops[-2]["rd"].append(ops[-4]["wr"][0])
            own(t)
        at("s")
        tt(A("DB"), K(fl, 0, 16), A("TH", 48 * t + 32, 48 * t + 48), ALU.is_ge)
        sb = K(B["sb"], 0, 16)
        mm([(sb, IB, A("M16", 0, 16))] + [(sb, IM1, A("E", j, j + 16)) for j in HOLES])
        at("sp")
        move(A("PKD", 15, 256, 16), sb, col("PKE", 0))
        for i, (a, b) in enumerate(LISTS):
            at("s%d" % i)
            move(A("SRB", a, b), IND(A("TT", 0, ZR + 256), A("PO", a // 16, b // 16)), -208.0)
            scan(A("SD", a, b), A("SRB", a, b), A("PKD", a, b), ALU.min, ALU.add, BIG / 32)
            ts(A("SRC", a // 16, b // 16), A("SD", a + 15, b, 16), col("PKE", 1), ALU.add, float(DEAD), ALU.min)
        at("sw")
        k = K(B["l"], 0, 16)
        mm([(k, A("I592"), A("FG", 0, 16)), (k, A("I592"), HIGH), (k, A("I296"), A("FG", 32, 48)), (k, A("I296"), A("DB")),
            (k, A("I16F"), A("SD", 15, 256, 16))])
        ts(WL, k, col("PKE", 1), ALU.add, 2.0 * TW + DEAD, ALU.min)
        at("v")
        scan(A("CU"), A("SRB"), A("ZERO"), ALU.add, ALU.add)
        at("vs")
        for j in range(2):
            act(A("H2", DEAD * j, DEAD * j + DEAD), A("CU"), ACT.Sign, col("JC", j), 1.0 / NONE, col("SV", 6 + j))
        ts(al(t), A("SV", 6, 8), -0.5, ALU.mult, DEAD / 2 + 0.25, ALU.add)
        hi = A("SP_I", po + 32, po + 64)
        if not last:
            at("g")
            iota(A("IOB"), [[1, DEAD]], 64)
            scatter(A("IOB"), al(t), A("IA"))
            side(A("CBH"), A("IOB", 0, 256))
            k = K(B["col"], 0, 16)
            mm([(k, sel0(r), A("CBH", r, 256, 16)) for r in range(16)])
            for j in HOLES:
                move(A("M16", j, j + 16), k, -208.0)
            for i, (a, b) in enumerate(LISTS):
                at("l%d" % i)
                ts(A("OU", a, b), IND(A("NF"), A("SRC", a // 16, b // 16)), 2048.0, ALU.add, 4096.0, ALU.min)
                ts(A("NKP", a, b), A("OU", a, b), -2048.0, ALU.add)
            at("f")
            move(A("WP"), IND(A("W"), WL), scale=2.0 ** (-11 if t else -22))
            move(A("HC", 0, 256), IND(A("HT"), SRC))
            move(A("UA"), IND(A("UB", 256 * t + 256, 256 * t + 256 + TW), al(t)))
            at("i")
            mm([(K(B["hw"], 0, 32), A("US", 128 * t, 128 * t + 128), hi)])
            mm([(K(B["roth"], 0, 32), A("I32W", 0, 128), hi)])
            move(A("HC", 256, 288), K(B["roth"], 0, 32))
            mm([(ha(p), uh(p), A("HC", 256, 288)) for p in range(t + 1)])
            at("in")
            neighbours(t, 288, 320, lambda p: K(B["hw"], 0, 32) if p == t + 1 else ha(p), B["ofa"], 256)
            at("j")
            mm([(K(B["rotw"], 0, 32), A("I32W", 0, 128), A("SP_I", po, po + 32))])
            move(A("WA"), K(B["rotw"], 0, 32))
        else:
            at("y")
            ts(A("YY", TW, TW + 256), IND(A("HT"), SRC), HB, ALU.add, -1.0, ALU.max)
            move(A("YY", 0, 256), IND(A("W"), WL))
        if not last:
            at("k")
            cn = B["cnt"]
            got = [A("SC_O", 8 * t, 8 * t + 2)] + [A("SC_I", 24 * t + 8 * j, 24 * t + 8 * j + 2) for j in range(3)]
            mm([(K(cn, 0, 1), IM1, A(x[0], x[3] + j, x[3] + j + 1)) for x in got for j in range(2)])
            ts(col("SV", 0), K(cn, 0, 1), 0.5, ALU.is_gt, 1.0, ALU.add)
            move(A("LH", 0, 14), A("LH", 0, 14), scale=col("SV", 0))
            if t < NS - 2:
                mm([(K(cn, 1, 2), A("IMW", 0, 128), col("SC_I", 24 * t))])
                ts(col("SV", 1), K(cn, 1, 2), 0.0, ALU.max, 32.0, ALU.min)
                ts(col("SC_O", 8 * t + 9), col("SV", 1), DD, ALU.subtract, 0.0, ALU.min)
        else:
            at("j")
            ts(A("AL", 6, 8), A("SV", 6, 8), -0.5, ALU.mult, DEAD / 2 + 0.25 + TW, ALU.add)
            cp(IND(A("YY"), A("AL", 4, 8)), A("SP_I", po, po + 64))
            dma("s", ("out", "yw"), A("YY", 0, 256))
            dma("y", ("out", "yh"), A("YY", TW, TW + 256))
    return ops


def meet(a, b):
    return a[0] == b[0] and a[1] < b[2] and b[1] < a[2] and a[3] < b[4] and b[3] < a[4]


def depend(ops):
    seen = {}
    for i, o in enumerate(ops):
        d = set()
        for a in o["rd"]:
            d.update(j for j, b, w in seen.get(a[0], []) if w and meet(a, b))
        for a in o["wr"]:
            d.update(j for j, b, w in seen.get(a[0], []) if meet(a, b))
        d.discard(i)
        o["dep"] = d
        o["soft"] = {j for j in d if ops[j]["kind"] == o["kind"]} if o["kind"] in ("mm", "send") else set()
        for a in o["wr"]:
            over = lambda b: a[5] == 1 and b[2] <= a[2] and a[3] <= b[3] and b[4] <= a[4]
            seen[a[0]] = [e for e in seen.get(a[0], []) if e[0] == i or not over(e[1])] + [(i, a, True)]
        for a in o["rd"]:
            seen.setdefault(a[0], []).append((i, a, False))
        o["banks"] = sorted({a[0] for a in o["rd"] + o["wr"] if a[0][0] == "K"})


ORDER = """
0c0 0Sload0 0Yload0 0Gc0 0Sload1 0c55 0Sload2 0Sload3 0c52 0Gc2 0c3 0c10 0c4 0c6 0Gc1 0c1! 0c12 0Sc0 0c20 0c2 0Gc4 0c5 0c8 0c7 0Gc3 0c19 0c9 0Gc10 0c14 0c22 0c21 0c23 0Gflat0 0c15 0c24 0c56 0c60 0c26 0c25 0cw0! 0c30 0s0! 0c28 0c35 0c27 0pk0! 0c43 0cw1! 0c16! 0c13 0c31 0c18! 0c38 0c34 0c32 0c36 0Ts0 0c29 0c39 0u4! 0pk1! 0c40! 0pk2! 0u0! 0pk3 0z0 0c17! 0c54 0u2! 0c47 0zz0 0Gc8 0n00 0c49! 0c33! 0c59 0c11 0c58! 0Tu0 0n10 0u10! 0Gc15 0s2 0Tu1 0c37 0zz1 0Gc11 0n20 0c44 0Gc16 0u13! 0zz2 0n11 0n01 0d0 0n21 0Gzz1 0c57 0c42 0c45! 0load0 0c48 0u14! 0u3 0Gc5 0Gc13 0u6 0c41 0Gflat1 0n12! 0n02 0c50! 0Sload4 0z1 0Tn10 0n22! 0n1e0 0c46 0u1! 0Tn1e0 0n0e0 0Gc9 0e0! 0s3 0Tu2 0Tn20 0u8! 0Tn00 0n2e0 0Gflat2 0n1o0 0Tn0e0 0zz3! 0Tn2e0 0Tu3 0u12! 0zz4 0d20 0Gc17 0n0o0 0u5! 0n2o0 0e1 0Ylate0 0c53 0Ylate1 0Tu6 0s1! 0c51 1Gr0 0Gz0 0Gc14
1x40! 1x50 1Gr1 0Gc6 0Gc12 1x10 1x00! 1Ta20 0Gzz0 1x30 1x20! 1Ta00 0Gc7 1x70 1x90! 1Ta10 1a0w1 1x60! 1x80 1Thb00 1a0w0 0u19! 1a0z0 1Ta30 1a2w1 0u7! 1a1w0 1a1w1 1a0c0 0u16! 0late0! 0u26! 1a0s0 0Tu5 0u18! 1a2w0 1a3w0 1Ta0c0 1a2z0 1a1z0 1we2! 1we1 0u15! 1we0 1wa2! 1wo0 1wo2! 1wo1 0s4! 1wa1 1Thb10 1wb2! 1Twe0 1wa0 0u22! 1wb0 1Two0 0u20! 1wb1 0n1o1! 1a1s0 1Twa0 1Sa0c0 0u24! 1Twb0 0u17! 0u11! 1a1c0 0Tu4 0n2o1! 1a2s0 0u21! 1Ta1c0 1r0 1wt1! 1a3w1 1r2 1r1 0u9! 1a2c0 1Tra0 1Tr0 1wt0! 1Thb20 1Ta0c1 1Ts0 1a3z0 0u23! 1r3 1Ta2c0 0n0o1! 1r4 1a3c0 1Sa1c0 1p0! 1Gc0 1a3s0 1Ta3c1 1Ta1c1 1Th0 0d1 1a1c1 1Ta3c0 0z2 1s0 1a0c1 1sp0 1Sa2c0 1h0 1Gg0 1p1 1Tn00 0e2 1s00! 1Ta2c1 1Tu0 1Sa3c0 1n00 1s10! 1a2c1 1a3c1 1n01 1Tn10 1s01 1Tn20 1p2 1n02! 1Tu2 1n10 1s11 1n20 1u0! 1n11 0u25 1u2! 1n21 1Tu1 1n12! 1n0e0 1n22! 1n0e1 1Tn11 1n1e1 1Tn01 1Tn0e0 1n1e0 1u1! 1Tn0e1 1n2e0 1p3! 1n2e1 1Tn1e0 1v0 1Tn1e1 1q0! 1Tn21 1Tn2e0 1Tn2e1 1n0o0! 1Tsw0 1s02 1n1o0 1Gq0 1Svs0 1n2o0 1s12 1sw0 1l00 1Svs1 2Gr1 1l10
2x00! 2x10 2x30! 2x20 2Ta00 2x70! 2x60 1Xq0 2Ta10 1Xc0 2x40! 2a0w1 2x50 1Ti1 1Tj0 1Ti0 1Tk0 1i0! 1f0! 2a0z0 1vs0 1Ti2 2Ta20 1in0 2a1w1 2a0c0 1g0! 1in1 2a0s0 1Gg1 1in2! 2x80! 2a0w0 2a1z0 2Ta0c0 2a1w0 1k0 1ine1 1ine0 2x90! 2a1s0 2Gr0 1Tin0 1Tine0 1Tine1 1Tg0 2a2w1 2a1c0 1ino0 2a2w0 2Ta1c0 2a2z0 2x100! 2x110 2Ta30 2Sa0c0 1f2! 2a2s0 2Sa1c0 1j0! 1f1! 2a2c0 2Ta1c1 1Tk1 1l01 2Ta0c1 1l11 1g2! 2Ta2c0 1ino1! 2b0 1k1! 2a3w0 1g1! 2b2 2a0c1 2a3w1 2b1 2a3z0 2a1c1 2wo2! 2Thb11 2Ta3c1 2we2! 2Thb01 2we0 2we1 2wa2! 2Tn00 2wo1 2Thb10 2wb2! 2wo0 2Twe0 2Sa2c0 2wa1 2wa0 2b3! 2Two0 2wb1 2wb0 2Twa0 2wt1! 2a3s0 2a3c0 2Twb0 2Ta2c1 2Tu0 2r0 2u0! 1k2 2Ta3c0 2a2c1 2wt0! 2Tra0 2r2 2r1 2n00 2Tn10 2Tr0 2n01 1k3 2Sa3c0 2n10 2Ts0 2n02! 2Tu1 2r3 2Thb00 2a3c1 2n11 2p0! 2r4 2Tn20 2u1 2n12 2Th0 2n0e0 2Tu2 2n0e2 2Tn11 2Tn01 2n20 2Tn0e0 2n1e2 2Thb20 2Thb21 2n1e0 2sp0! 2h0 2n21 2Gg0 2u2 2n0e1 2n22! 2n1e1 2p1 2s10! 2Tn0e1 2s00 2Tn0e2 2Tn1e0 2Tn1e1 2p2 2Tn1e2 2n2e0 2n2e1 2q0! 2n2e2 2Tn21 2p3! 2Tn2e0 2s0 2Tn2e1 2n1o0! 2s01 2n0o0! 2Tn2e2 2v0 2Gq0 2s02 2s11 2Svs1 2n2o0 2Gc0 2s12 2l00 2Svs0 2l10
3x10! 3x00 3x30! 2vs0 3x20 3Ta00 2Xq0 2Tsw0 3x50! 2Ti0 2g0 2Ti1 3x40 2Tj0 2Gg1 3Ta10 3x70! 2in0 3a0w1 3Gr1 2i0! 2sw0 3x60! 2in1 3a0z0 2Ti2 3Gr0 2l01 2Tg0 2in2 3a0s0 2f0! 2Xc0 2ine1 2ine0 2Tin0 2ine2 3x80! 3a1w1 2Tine0 3a0c0 2Tine1 2Tine2 3Ta20 3a1z0 3x90! 3a1w0 2ino0 3a1s0 3x100! 3x110 3Ta0c0 3a2w1 3a1c0 2Tk0 3Sa0c0 3a2z0 2j0! 3Ta30 3a2w0 3a0w0 2g2! 3a2c0 2f2! 2f1! 3Ta1c0 3a2s0 2ino1! 3b0 3Ta0c1 3a3w0 3Ta2c0 2k0 3b2 3a3w1 2k1! 3b1 2g1! 3Sa1c0 2l11 3a0c1 3we2! 3a3z0 3wo2! 3we1 3wa2! 2Tk1 3we0 3wb2! 3Thb10 3Ta1c1 3wo0 3wo1 3Sa2c0 3Twe0 3wa1 3b3! 3wa0 3Two0 3wb1 3wb0 3wt0! 3Twa0 3a3c0 3Twb0 3Ta2c1 3a1c1 3Ta3c1 3a3s0 3Tn00 3Tu0 3r0 2k2 3Ta3c0 3a2c1 3u0! 3r1 3r2 3wt1! 3n00 2k3 3Tn10 3Tra0 3n01 3Tr0 3Sa3c0 3n10 3Thb21 3n02! 3Thb01 3Ts0 3r3 3Thb00 3n11 3Thb02 3a3c1 3Th0 3p0! 3sp0 3n12 3Tn20 3n0e0 3Tu2 3n0e3 3Tu1 3h0 3n1e3 3n20 3n0e2 3Thb12 3Thb11 3u1! 3Thb22 3Tn01 3u2 3Tn0e0 3n21 3Thb20 3n0e1 3n22! 3n1e0 3n1e1 3Tn11 3p1 3Tn0e1 3s10! 3Tn0e2 3s00 3Tn0e3 4Gr1 3Tn1e0 3n1e2 3Tn1e1 3p2 3n2e0 3Tn1e2 3Tn1e3 3n2e1 3q0! 3n2e2 3Tn21 3p3! 3Tn2e0 3n2e3 3Tn2e1 3n0o0! 3s01 3Tn2e2 3Gq0 3n1o0! 3v0 3Tn2e3 3s11 3s02 3Svs1 3r4 3n2o0 3s12 3Gc0 3s0 3Svs0 3l00 3Tsw0 3l10
4x00! 3vs0 3Gg0 4x10 4x60! 3l11 4x20 4Ta00 4x30! 3Xq0 3Ti0 3Ti1 3g0 4x50! 4a0w1 4Ta10 3l01 3Gg1 3in0 4a0z0 3i0 3sw0 3in1 4x40 3Tj0 3in2! 3Ti2 4x70! 4Gr0 3Tg0 4x90! 3ine0 3Xc0 3ine1 3ine2 3ine3 3Tin0 3Tine0 3Tine1 4a1w1 3Tine2 4x80! 4a0s0 3Tine3 4Ta20 4a1z0 4a0c0 3f0! 3ino0 4a1s0 4x100! 4Ta0c0 4x110 3f2! 4a2w1 3Tk0 3j0! 4a1c0 4Sa0c0 3Tk1 4Ta30 4a2z0 3g1! 4a0w0 3ino1! 4a2w0 3g2! 4a1w0 4a2s0 4Ta1c0 4a2c0 4Ta0c1 4a3w0 4b0 4Ta2c0 3k0 4a3w1 4b2 3k1! 4b1 4Sa1c0 4a3z0 4a0c1 4we2! 4we1 4wb2! 4we0 4wo2! 4wo0 4Ta3c1 4wa2! 4Ta1c1 4wo1 4b3! 4Twe0 4wb0 3f1! 4wa0 4Two0 4wa1 4wb1 4a3s0 4Twa0 4Sa2c0 4Twb0 4wt1! 4a1c1 4a3c0 4Tn00 4Tu0 4wt0! 4r0 4Ta2c1 3k2 4Ta3c0 4n00 4u0! 4r1 4r2 4n01 4a2c1 4Tra0 3k3 4Tr0 4n02 4Sa3c0 4Thb01 4Tn10 4Thb00 4Thb02 4r3 4Thb22 4a3c1 4Ts0 4n0e0 4p0! 4Thb20 4Thb10 4Thb12 4n10 4Tn20 4n0e2 4Tu1 4n0e4 4Thb11 4Th0 4n11 4n0e3 4Tu2 4n20 4Thb13 4Thb23 4n12 4Thb03 4Tn01 4u2! 4sp0 4Thb21 4Gg0 4n21 4u1 4Tn11 4Tn0e0 4h0 4n22! 4n1e2 4n0e1 4s00! 4p1 4n1e0 4s10! 4Tn0e1 4n1e4 4Tn0e2 4n1e1 4Tn0e3 4p2 4Tn0e4 4n1e3 4Tn1e0 4Tn1e1 4n2e0 4Tn1e2 4p3! 4n2e1 4Tn1e3 4Tn1e4 4q0! 4n2e2 4Tn21 4Tn2e0 4n0o0! 4n2e3 4Tn2e1 4Gq0 4n1o0! 4n2e4 4Tn2e2 4s01 4Tn2e3 4v0 4Tn2e4 4s11 4s02 4Svs1 4s0 4n2o0 4r4 4Tsw0 4s12 4Svs0 4l00 4Gc0 4l10
5x00! 5x10 5x70! 4vs0 5x30 5Ta00 5x20! 4Xq0 4Ti0 4Ti1 4g0 4Tj0 5a0w1 5x60! 4in0 4Gg1 5Ta10 4i0 5a0z0 4in1 5x40 4in2! 5x50! 4Ti2 5Gr0 4Tg0 4ine0 4ine1 5a1w1 4ine3 5x80! 4ine2 4ine4 4Tin0 4Tine0 5Gr1 4Tine1 4sw0 4Xc0 4Tine2 5a1z0 4Tine3 4Tine4 5a0c0 5Ta20 5x90! 5a0s0 4f0! 4ino0 5a1c0 4Tk1 4Tk0 5x100 5x110! 5Ta0c0 5a2w1 4f2! 5a1s0 4j0! 5Ta30 4k0 5a2z0 5a0w0 4g1! 5a1w0 4f1! 5a2w0 5a2s0 5Ta1c0 4g2! 4k1! 5Sa0c0 5a2c0 4ino1! 5Ta0c1 5Sa1c0 4l01 5b0 5Ta2c0 5a3w0 5b2 5a3w1 5b1 4l11 5a3z0 5wa2! 5we1 5wb2! 5wb0 5we0 5we2! 5Ta1c1 5wo2! 5Thb24 5wo1 5Thb12 5b3! 5Thb11 5Twe0 5wo0 5wb1 5wt0! 5wa0 5Two0 5wa1 5a0c1 5a1c1 5Twa0 5Sa2c0 5a3c0 5Twb0 5Tn00 5a3s0 5Tu0 5Ta2c1 5Thb04 5r0 5Ta3c1 5u0! 5n00 5Ta3c0 4k2 5r2 5r1 5n01 5a2c1 5Tra0 4k3 5Tr0 5n02 5Sa3c0 5r3 5Tn10 5Thb01 5wt1! 5Thb02 5Tu1 5n10 5Tn01 5a3c1 5Thb14 5p0! 5Th0 5n0e4 5Tn20 5n11 5n0e3 5Thb00 5Thb03 5n0e0 5Ts0 5n12 5Tu2 5h0 5Tn0e0 5n20 5Thb22 5n0e1 5u2! 5u1! 5n1e4 5n21 5n1e0 5Thb10 5n0e2 5Thb13 5Thb20 5Thb21 5n22! 5Tn11 5n0e5 5Tn0e1 5Thb23 5p1 5Tn0e2 5s10! 5Tn0e3 5sp0 5Tn0e4 5n1e1 6Gr1 5Tn0e5 5n1e2 5Tn1e0 5p2 5n2e0 5s00! 5n2e1 5q0! 5n2e3 5Tn21 5Tn2e0 5p3! 5n2e2 5Tn1e1 5Tn2e1 5n0o0! 5n2e4 5Gq0 5n2e5 5Tn2e2 5Tn2e3 5n1e3 5Tn1e2 5Tn2e4 5n1e5 5Tn2e5 5s01 5Tn1e3 5v0 5Tn1e4 5Tn1e5 6Gr0 5n2o0! 5s11 5s02 5Svs1 5n1o0 5r4 5s12 5l00 5Svs0 5s0 5Gc0 5l10 5Tsw0
6x10! 6x00 5Gg0 6x20! 5vs0 6x30 6Ta00 5Xq0 6x40! 5Ti0 5Ti1 5g0 6Ta10 6a0w1 5sw0 5Gg1 5in0 6a0z0 5i0 5in1 6x60! 6x50 5Tj0 5Ti2 5in2! 6x70! 5Tg0 5ine1 5ine0 5f0! 5ine3 5ine2 5ine4 5Tin0 5Tine0 5Tine1 5ine5 5Tine2 5Xc0 6a0c0 5Tine3 5Tine4 5Tine5 6x90! 6Ta20 6a1w1 6a0s0 5ino0 6a1z0 6x80 6x110! 5Tk0 6a1c0 6Ta0c0 6x100! 6a2w1 6a1w0 6a0w0 5j0! 6a2w0 5g2! 6Ta30 5f2! 6a2z0 6a1s0 5f1! 6a2c0 6Ta1c0 6Sa0c0 5k0 6a2s0 5g1! 5k1! 6b0 6a3w0 6Ta2c0 6b2 6a3w1 6b1 6a3z0 6we0 6we2! 6we1 6wb2! 6wo0 6wo2! 6wo1 6wa2! 6Twe0 6wa0 6Sa1c0 6wa1 6b3! 6Two0 6wb0 6Sa2c0 6wb1 5ino1! 6Twa0 6a3c0 6wt1! 6Twb0 6Ta0c1 6a3s0 6Ta2c1 6Ta1c1 6wt0! 5l01 6r0 6Ta3c0 6r2 6r1 5l11 6Tra0 6Tr0 6Sa3c0 6Tz3 6r3 6a0c1 6s0 6p0! 6a2c1 6a1c1 6Ta3c1 6Tz1 6Ts0 6a3c1 6Th0 6z3 6Tz2 6Tz0 6h0 6sp0! 6p1 6s10! 6z0 6Tp0 6z1 6Tu2 6s00! 6z2 6Tu1 6p2 6s11 6Tu0 6p3! 6q0 6s01 6u2! 6v0 6u1! 6Gq0 6Tsw0 6s12 6s02 6Svs0 6sw0 6u0! 6Svs1 6y0 6y1! 6vs0 6j0 6Xq0 6j1 6Yj0 6Sj0
"""


def ordered():
    ops = plan()
    depend(ops)
    at = {o["id"]: i for i, o in enumerate(ops)}
    order = [at[w.strip("!")] for w in ORDER.split()]
    assert sorted(order) == list(range(len(ops)))
    last, other, done, opened = {}, {}, set(), set()
    for n, (i, w) in enumerate(zip(order, ORDER.split())):
        o = ops[i]
        assert o["dep"] <= done
        done.add(i)
        o["pos"] = n
        if o["kind"] == "mm":
            assert not (o["args"][1] and o["banks"][0] in opened)
            (opened.discard if o["args"][2] else opened.add)(o["banks"][0])
        if w[-1] == "!":
            o["eng"], o["kind"], o["args"] = "s", "act", o["alt"]
        for b in o["banks"]:
            if b in last and ops[last[b]]["eng"] != o["eng"]:
                other[b] = last[b]
            if b in other:
                o["dep"].add(other[b])
            last[b] = i
    return ops, order


_CACHE = {}


def rank_program(g, core, T, topo):
    rank = T.rank_of(core)
    if rank is None:
        return
    if not _CACHE:
        _CACHE["ops"], _CACHE["order"] = ordered()
    ops, order = _CACHE["ops"], _CACHE["order"]
    cores = list(T.cores)
    n = len(cores)
    Q = {"v": g.vector, "s": g.scalar, "t": g.tensor, "g": g, "y": g.sync}

    def ap(a):
        if not is_ap(a):
            return a
        if a[0] == "@":
            return ap(a[1]).indirect(ap(a[2]))
        if a[0] in ("in", "out"):
            return T[a[1]][:]
        return T[a[0]][slice(a[1], a[2]), slice(a[3], a[4]) if a[5] == 1 else slice(a[3], a[4], a[5])]

    def maskof(es):
        return sum(1 << e for e in es)

    def peers(kind):
        return list(range(1, n)) if kind == "c" else [1]

    def share(src, dst, kind, d):
        es = topo.engines(src, dst)
        if kind == "c":
            k = len(es) // 4
            return es[:2 * k] if d == 1 else es[k * d:k * (d + 1)]
        return es

    needed = set()
    for o in ops:
        needed |= o["dep"] - o["soft"]
    count = {e: 0 for e in "vstg"}
    mark, known, totals, clock = {}, {e: {} for e in Q}, {}, {}
    nd = [0]
    for i in order:
        o = ops[i]
        e, k, a = o["eng"], o["kind"], o["args"]
        if k == "recv":
            tot = sum(len(share(cores[(rank - d) % n], core, a[0], d)) for d in peers(a[0]))
            mark[i] = ("r%s%d" % a, tot)
            totals[mark[i][0]] = tot
            clock[i] = {}
            continue
        q, kn = Q[e], known[e]
        want = {}
        for j in o["dep"] - o["soft"]:
            s, v = mark[j]
            if v > want.get(s, (0, 0))[0]:
                want[s] = (v, j)
        for s, (v, j) in sorted(want.items(), key=lambda x: -ops[x[1][1]]["pos"]):
            if kn.get(s, 0) < v:
                q.wait_ge(T.sem[s], v)
                kn[s] = v
                for s2, v2 in clock[j].items():
                    if kn.get(s2, 0) < v2:
                        kn[s2] = v2
        clock[i] = dict(kn)
        if k == "send":
            kind, t, src = a
            tr = []
            for d in peers(kind):
                dst = cores[(rank + d) % n]
                rid, pid, _ = topo.addr(dst)
                es = share(core, dst, kind, d)
                tr.append((rid, pid, es, landing(kind, t, src, d)))
                totals["sent"] = totals.get("sent", 0) + len(es)
            sem = T.sem["r%s%d" % (kind, t)]
            if len(tr) == 1:
                rid, pid, es, land = tr[0]
                g.remote_dma(ap(land), ap(src), sem, T.sem.sent, pid, rid, maskof(es))
            else:
                g.remote_dma_fused([RemoteDMATransfer(dst_ids=[DstId(rid=rid, pnc=pid)], dma_engine_mask=maskof(es), remote_sem=sem,
                                                      src=ap(src), dst=ap(land)) for rid, pid, es, land in tr], local_sem=T.sem.sent)
            continue
        if k == "dma":
            s = "d%d" % nd[0]
            nd[0] += 1
            q.dma_start(ap(a[0]), ap(a[1])).then_inc(T.sem[s], 16)
            mark[i] = (s, 16)
            totals[s] = 16
            continue
        if k == "cp":
            r = q.tensor_copy(ap(a[0]), ap(a[1]))
        elif k == "tt":
            r = q.tensor_tensor(ap(a[0]), ap(a[1]), ap(a[2]), a[3])
        elif k == "ts":
            if a[5] is None:
                r = q.tensor_scalar(ap(a[0]), ap(a[1]), ap(a[2]), None, a[4])
            else:
                r = q.tensor_scalar(ap(a[0]), ap(a[1]), ap(a[2]), ap(a[3]), a[4], a[5])
        elif k == "scan":
            r = q.tensor_tensor_scan(ap(a[0]), ap(a[1]), ap(a[2]), a[5], a[3], a[4])
        elif k == "mset":
            r = q.memset(ap(a[0]), a[1])
        elif k == "red":
            r = q.tensor_reduce(ap(a[0]), ap(a[1]), AxisListType.X, ALU.add, negate=True)
        elif k == "act":
            if a[0][0] == "@":
                r = q.activation(ap(a[0]), ap(a[1]), a[2])
            elif len(a) > 5:
                r = q.activation(ap(a[0]), ap(a[1]), a[2], bias=ap(a[3]), scale=ap(a[4]), accum_out=ap(a[5]))
            else:
                r = q.activation(ap(a[0]), ap(a[1]), a[2], bias=ap(a[3]), scale=ap(a[4]))
        elif k == "side":
            if a[2] is None:
                r = q.affine_select(ap(a[0]), ap(a[1]), [[0, width(a[0])]], ALU.is_ge, 0.0, 0, 0)
            else:
                r = q.affine_select(ap(a[0]), ap(a[1]), [[-1, width(a[0])]], ALU.not_equal, a[2], -a[3], 1)
        elif k == "iota":
            if SCRATCH[a[0][0]][2] == I32:
                r = q.iota(ap(a[0]), a[1], a[2], a[3])
            else:
                r = q.iota(ap(a[0]), a[1], a[2], a[3], allow_small_or_imprecise_dtypes=True)
        else:
            its = a[0]
            for m, (x, l, y) in enumerate(its):
                r = q.matmul(ap(x), ap(l), ap(y), a[1] == "each" or (a[1] and m == 0), a[1] == "each" or (a[2] and m == len(its) - 1))
        if i in needed:
            count[e] += 1
            r.then_inc(T.sem["e" + e], 1)
            mark[i] = ("e" + e, count[e])
            totals["e" + e] = count[e]
    for s, v in totals.items():
        if known["g"].get(s, 0) < v:
            g.wait_ge(T.sem[s], v)
